import numpy as np
import ml_dtypes


def mxq(x, axis, fmt="e4m3"):
    dtype, down = {"e4m3": (ml_dtypes.float8_e4m3fn, 7), "e5m2": (ml_dtypes.float8_e5m2, 14)}[fmt]
    v = np.moveaxis(np.asarray(x, np.float32).astype(ml_dtypes.bfloat16).astype(np.float64), axis, -1)
    blocks = v.reshape(v.shape[:-1] + (-1, 32))
    amax = np.abs(blocks).max(-1, keepdims=True)
    byte = np.maximum(np.where(amax > 0, np.frexp(amax)[1] - 1 + 127, 0) - down, 1)
    scale = np.exp2(byte - 127.0)
    codes = (blocks / scale).astype(np.float32).astype(dtype).astype(np.float64)
    return np.moveaxis((codes * scale).reshape(v.shape), -1, axis)


WIDE = False


def mx_kscale(k):
    if not WIDE:
        return np.ones(k)
    levels = np.array([10, -10, 5, -5, 0])
    if k % 512:
        return np.exp2(np.random.permutation(np.resize(levels, k // 32))).repeat(32)
    a = np.empty((k // 512, 16))
    for p in range(k // 512):
        a[p, :8] = np.random.permutation(np.resize(levels, 8))
        for g in range(8):
            far = levels[np.abs(levels - a[p, g]) >= 10]
            a[p, g + 8] = far[np.random.randint(len(far))]
    return np.exp2(a.ravel()).repeat(32)


def f64(x):
    return np.asarray(x).astype(np.float64)


def striped(idx):
    return np.tile(idx.reshape(-1, 16).T, (8, 1)).astype(np.uint16)


def unstriped(offs):
    return offs[:16].T.reshape(-1).astype(np.int64)


E2M1 = np.array([0.0, 0.5, 1.0, 1.5, 2.0, 3.0, 4.0, 6.0, -0.0, -0.5, -1.0, -1.5, -2.0, -3.0, -4.0, -6.0])


def pack_weight(w, fmt):
    k, n = w.shape
    w = f64(np.asarray(w, np.float32).astype(ml_dtypes.bfloat16)).reshape(k // 32, 32, n)
    amax = np.abs(w).max(1)
    if fmt == "e4m3":
        byte = np.frexp(amax)[1] - 1 + 127 - 7
    else:
        mant, ex = np.frexp(amax / 6.0)
        byte = np.where(mant > 0.5, ex, ex - 1) + 127
    byte = np.clip(np.where(amax > 0, byte, 1), 1, 254)
    scaled = (w * np.exp2(127.0 - byte)[:, None, :]).reshape(k, n).astype(np.float32)
    by_word = np.ascontiguousarray(scaled.reshape(k // 512, 128, 4, n).transpose(0, 1, 3, 2))
    if fmt == "e4m3":
        words = by_word.astype(ml_dtypes.float8_e4m3fn).view(np.uint8)
    else:
        c = by_word.astype(ml_dtypes.float4_e2m1fn).view(np.uint8) & 0xF
        words = (c[..., 0::2] | (c[..., 1::2] << 4)).reshape(k // 512, 128, 2 * n)
    return np.ascontiguousarray(words), np.ascontiguousarray(byte.astype(np.uint8).reshape(k // 512, 16, n))


def unpack_weight(words, scales, fmt):
    g, _, n = scales.shape
    words = np.ascontiguousarray(words).reshape(g, 128, n, -1)
    if fmt == "e4m3":
        vals = words.view(ml_dtypes.float8_e4m3fn).astype(np.float64)
    else:
        nib = np.empty((g, 128, n, 4), np.uint8)
        nib[..., 0::2] = words & 0xF
        nib[..., 1::2] = words >> 4
        vals = E2M1[nib]
    vals = vals * np.repeat(np.exp2(scales.astype(np.float64) - 127.0), 8, axis=1)[..., None]
    return vals.transpose(0, 1, 3, 2).reshape(g * 512, n)


def gelu(v):
    return 0.5 * v * (1.0 + np.tanh(np.sqrt(2.0 / np.pi) * (v + 0.044715 * v**3)))


K, T, S, H, N = 512, 4096, 1024, 1024, 384

def setup_inputs():
    n = np.random.standard_normal
    s = mx_kscale(K)[:, None]
    u = mx_kscale(H)[:, None]
    tab_words, tab_scales = pack_weight(n((K, T)) * s, "e4m3")
    w2_words, w2_scales = pack_weight(0.7 * n((K, H)) / np.sqrt(K) / s, "e2m1")
    w3_words, w3_scales = pack_weight(0.7 * n((K, H)) / np.sqrt(K) / s, "e4m3")
    return {
        "tab_words": tab_words, "tab_scales": tab_scales,
        "offs": striped(np.random.permutation(T)[:S]),
        "offs2": striped(np.random.permutation(T)[:S]),
        "offs3": striped(np.random.permutation(T)[:S]),
        "w1": (0.7 * n((K, H)) / np.sqrt(K) / s).astype(np.float32),
        "w2_words": w2_words, "w2_scales": w2_scales,
        "w3_words": w3_words, "w3_scales": w3_scales,
        "g": (np.exp(0.3 * n(H)) * u[:, 0]).astype(np.float32),
        "w4": (0.8 * n((H, N)) / np.sqrt(H) / u).astype(np.float32),
    }

def reference(tab_words, tab_scales, offs, offs2, offs3, w1, w2_words, w2_scales, w3_words, w3_scales, g, w4):
    v = unpack_weight(tab_words, tab_scales, "e4m3")[:, unstriped(offs)]
    va = unpack_weight(tab_words, tab_scales, "e4m3")[:, unstriped(offs2)]
    vb = unpack_weight(tab_words, tab_scales, "e4m3")[:, unstriped(offs3)]
    w2 = unpack_weight(w2_words, w2_scales, "e2m1")
    w3 = unpack_weight(w3_words, w3_scales, "e4m3")
    c = mxq(f64(w1), 0, "e4m3").T @ v
    a = w2.T @ va
    b = w3.T @ vb
    h = (a - c) * (b - c) * f64(g)[:, None]
    y = mxq(f64(w4), 0, "e4m3").T @ mxq(h, 0, "e4m3")
    return np.tanh(y)

@@ -1,0 +1,294 @@
+from contextlib import ExitStack
+
+import concourse.mybir as mybir
+from concourse.masks import make_identity
+
+K, T, S, H, N = 512, 4096, 1024, 1024, 384
+FLOPS = 3 * 2 * K * H * S + 2 * H * N * S
+
+F32 = mybir.dt.float32
+BF16 = mybir.dt.bfloat16
+I32 = mybir.dt.int32
+U32 = mybir.dt.uint32
+U16 = mybir.dt.uint16
+U8 = mybir.dt.uint8
+FP8X4 = mybir.dt.float8_e4m3fn_x4
+FP4X4 = mybir.dt.float4_e2m1fn_x4
+COPY = mybir.ActivationFunctionType.Copy
+TANH = mybir.ActivationFunctionType.Tanh
+MULT = mybir.AluOpType.mult
+ADD = mybir.AluOpType.add
+
+P = 128
+SEG = 256
+CHUNK = 128
+HALF = 512
+
+
+def tile_list_bond_angle_features_kernel(
+    tc, tab_words, tab_scales, offs, offs2, offs3, w1, w2_words, w2_scales, w3_words, w3_scales, g, w4, out
+):
+    nc = tc.nc
+    with ExitStack() as ctx:
+        keep = ctx.enter_context(tc.tile_pool(name="keep", bufs=1))
+        ring = ctx.enter_context(tc.tile_pool(name="ring", bufs=3))
+        acc_pool = ctx.enter_context(tc.psum_pool(name="acc", bufs=6))
+        y_pool = ctx.enter_context(tc.psum_pool(name="ybank", bufs=2))
+
+        lists = [keep.tile([P, S // 16], U16, name=f"list{l}") for l in range(3)]
+        tab_s = keep.tile([P, T // 4], I32, align_bytes=64)
+        tab_w = keep.tile([P, T], I32, align_bytes=64)
+        ws_raw = keep.tile([P, 2, H // 4], I32, align_bytes=64)
+        w1_raw = keep.tile([P, 4, H], F32, align_bytes=64)
+        w2_raw = keep.tile([P, H // 2], I32, align_bytes=64)
+        w3_raw = keep.tile([P, H], I32, align_bytes=64)
+        w4_raw = keep.tile([P, 8, N], F32, align_bytes=64)
+        g_rows = keep.tile([P, P], F32, align_bytes=64)
+        ident = keep.tile([P, P], F32, align_bytes=64)
+        g_col = keep.tile([P, 8], F32, align_bytes=64)
+        warm = keep.tile([P, 8], F32, align_bytes=64)
+        warm2 = keep.tile([P, 8], F32, align_bytes=64)
+
+        nc.vector.memset(tab_s[:], 0)
+        nc.vector.memset(ws_raw[:], 0)
+        nc.gpsimd.memset(warm[:], 0.0)
+        nc.scalar.activation(warm2[:], warm[:], TANH)
+        nc.gpsimd.memset(g_rows[:], 0.0)
+        make_identity(nc, ident[:])
+
+        for tile, src in zip(lists, (offs, offs2, offs3)):
+            nc.sync.dma_start(tile[:], src)
+        for q in range(4):
+            nc.sync.dma_start(tab_s[32 * q : 32 * q + 4, :], tab_scales[0, 4 * q : 4 * q + 4, :].bitcast(I32))
+        nc.sync.dma_start(w1_raw[:], w1.rearrange("(p j) c -> p j c", j=4))
+        for q in range(4):
+            nc.sync.dma_start(ws_raw[32 * q : 32 * q + 4, 0, :], w2_scales[0, 4 * q : 4 * q + 4, :].bitcast(I32))
+        for q in range(4):
+            nc.sync.dma_start(ws_raw[32 * q : 32 * q + 4, 1, :], w3_scales[0, 4 * q : 4 * q + 4, :].bitcast(I32))
+        nc.sync.dma_start(w2_raw[:], w2_words[0].bitcast(I32))
+        nc.sync.dma_start(w3_raw[:], w3_words[0].rearrange("p e i -> p (e i)").bitcast(I32))
+        nc.sync.dma_start(
+            g_rows[0:8, :].rearrange("u (q i) -> u q i", i=8), g.rearrange("(q u i) -> u q i", u=8, i=8)
+        )
+        nc.sync.dma_start(tab_w[:], tab_words[0].rearrange("p t i -> p (t i)").bitcast(I32))
+        w4_view = w4.rearrange("(q u i) n -> u q i n", u=8, i=8)
+        for u in range(8):
+            nc.sync.dma_start(w4_raw[:, u, :], w4_view[u])
+
+        v_words = [keep.tile([P, S], U32, align_bytes=64, name=f"v_words{l}") for l in range(3)]
+        v_scales = [keep.tile([P, S], U8, align_bytes=64, name=f"v_scales{l}") for l in range(3)]
+
+        def gather(dst, window, half):
+            for l in range(3):
+                cols = slice(half * HALF, (half + 1) * HALF)
+                offsets = lists[l][:, half * HALF // 16 : (half + 1) * HALF // 16]
+                nc.vector.tensor_copy(dst[l][:, cols], window.indirect(offsets))
+
+        gather(v_scales, tab_s[:].bitcast(U8), 0)
+        gather(v_scales, tab_s[:].bitcast(U8), 1)
+
+        w1_bf = keep.tile([P, 8, 16, 8, 4], BF16, align_bytes=64)
+        w1_q = keep.tile([P, H], U32, align_bytes=64)
+        w1_s = keep.tile([P, H], U8, align_bytes=64)
+        w1_view = w1_raw[:].rearrange("p j (q u i) -> p u q i j", u=8, i=8)
+        w1_flat = w1_bf[:].rearrange("p u q i j -> p (u q i j)")
+        for u in range(8):
+            nc.scalar.activation(w1_bf[:, u], w1_view[:, u], COPY, scale=-1.0)
+            if u % 2 == 1:
+                cols = slice((u - 1) * P, (u + 1) * P)
+                nc.vector.quantize_mx(
+                    w1_q[:, cols].bitcast(FP8X4), w1_s[:, cols], w1_flat[:, 4 * cols.start : 4 * cols.stop]
+                )
+
+        g_bank = y_pool.tile([P, 3 * CHUNK], F32, tag="y")
+        nc.tensor.transpose(g_bank[:, 0:P], g_rows[:], ident[:])
+        nc.scalar.copy(g_col[:], g_bank[:, 0:8])
+
+        ws_p = keep.tile([P, 2, H // 4], I32, align_bytes=64)
+        w2_p = keep.tile([P, H // 2], I32, align_bytes=64)
+        w3_p = keep.tile([P, H], I32, align_bytes=64)
+        nc.vector.tensor_copy(
+            ws_p[:].rearrange("p w (u q e) -> p w u q e", u=8, e=2),
+            ws_raw[:].rearrange("p w (q u e) -> p w u q e", u=8, e=2),
+        )
+        nc.vector.tensor_copy(
+            w2_p[:].rearrange("p (u q e) -> p u q e", u=8, e=4),
+            w2_raw[:].rearrange("p (q u e) -> p u q e", u=8, e=4),
+        )
+        nc.vector.tensor_copy(
+            w3_p[:].rearrange("p (u q e) -> p u q e", u=8, e=8),
+            w3_raw[:].rearrange("p (q u e) -> p u q e", u=8, e=8),
+        )
+
+        gather(v_words, tab_w[:].bitcast(U32), 0)
+
+        def weight(l, u):
+            cols = slice(u * P, (u + 1) * P)
+            if l == 0:
+                return w1_q[:, cols].bitcast(FP8X4), w1_s[:, cols]
+            scale = ws_p[:, l - 1, u * 32 : (u + 1) * 32].bitcast(U8)
+            if l == 1:
+                return w2_p[:, u * 64 : (u + 1) * 64].bitcast(U8).bitcast(FP4X4), scale
+            return w3_p[:, cols].bitcast(FP8X4), scale
+
+        def project(dst, ls, u, tok):
+            for n, l in enumerate(ls):
+                codes, scale = weight(l, u)
+                nc.tensor.matmul_mx(
+                    dst,
+                    lhsT=codes,
+                    lhsT_scale=scale,
+                    rhs=v_words[l][:, tok].bitcast(FP8X4),
+                    rhs_scale=v_scales[l][:, tok],
+                    start=(n == 0),
+                    stop=(n == len(ls) - 1),
+                )
+
+        w4_bf = keep.tile([P, 2, N, 4], BF16, align_bytes=64)
+        w4_q = keep.tile([P, 2 * N], U32, align_bytes=64)
+        w4_s = keep.tile([P, 2 * N], U8, align_bytes=64)
+
+        def cast_w4(b):
+            nc.scalar.activation(
+                w4_bf[:, b].rearrange("p (c i) t -> p c t i", i=4),
+                w4_raw[:, 4 * b : 4 * b + 4, :].rearrange("p t (c i) -> p c t i", i=4),
+                COPY,
+            )
+
+        def quant_w4():
+            flat = w4_bf[:].rearrange("p b n t -> p (b n t)")
+            for lo, hi in ((0, 512), (512, 768)):
+                nc.vector.quantize_mx(w4_q[:, lo:hi].bitcast(FP8X4), w4_s[:, lo:hi], flat[:, 4 * lo : 4 * hi])
+
+        h_q = keep.tile([P, 2, S], U32, align_bytes=64)
+        h_s = keep.tile([P, 2, S], U8, align_bytes=64)
+        state = {}
+
+        def seg_tok(seg):
+            return slice(seg * SEG, (seg + 1) * SEG)
+
+        def once_pair(seg, b, tp):
+            if tp == 0:
+                state["d1", seg, b] = ring.tile([P, 4, SEG], F32, name="d1", align_bytes=64)
+                state["d2", seg, b] = ring.tile([P, 4, SEG], F32, name="d2", align_bytes=64)
+            d1, d2 = state["d1", seg, b], state["d2", seg, b]
+            banks = [acc_pool.tile([P, 2, SEG], F32, name="acc") for l in range(3)]
+            for l in range(3):
+                for e in range(2):
+                    project(banks[l][:, e, :], [l], 4 * b + 2 * tp + e, seg_tok(seg))
+            x = ring.tile([P, 2, SEG], F32, name="x", align_bytes=64)
+            xg = ring.tile([P, 2, SEG], F32, name="xg", align_bytes=64)
+            nc.scalar.copy(x[:], banks[0][:])
+            for e in range(2):
+                u = 4 * b + 2 * tp + e
+                nc.scalar.activation(xg[:, e, :], banks[0][:, e, :], COPY, scale=g_col[:, u : u + 1])
+            nc.vector.tensor_tensor(d1[:, 2 * tp : 2 * tp + 2, :], banks[1][:], x[:], ADD)
+            for e in range(2):
+                u = 4 * b + 2 * tp + e
+                nc.vector.scalar_tensor_tensor(
+                    d2[:, 2 * tp + e, :], banks[2][:, e, :], g_col[:, u : u + 1], xg[:, e, :], MULT, ADD
+                )
+
+        def interleaved(ap):
+            return ap.rearrange("p t (c i) -> p c t i", i=4)
+
+        def h_view(h, lo, hi):
+            return h[:, lo:hi, :].rearrange("p (c i) t -> p c t i", i=4)
+
+        def once_final(seg, b):
+            h = ring.tile([P, SEG, 4], BF16, name="h", align_bytes=64)
+            state["h", seg, b] = h
+            nc.vector.tensor_tensor(
+                h_view(h, 0, SEG), interleaved(state["d1", seg, b][:]), interleaved(state["d2", seg, b][:]), MULT
+            )
+
+        def twice_side(seg, b, tp):
+            if tp == 0:
+                state["d2", seg, b] = ring.tile([P, 4, SEG], F32, name="d2", align_bytes=64)
+                state["h", seg, b] = ring.tile([P, SEG, 4], BF16, name="h", align_bytes=64)
+            d2 = state["d2", seg, b]
+            bank = acc_pool.tile([P, 2, SEG], F32, name="acc")
+            for e in range(2):
+                project(bank[:, e, :], [0, 2], 4 * b + 2 * tp + e, seg_tok(seg))
+            for e in range(2):
+                u = 4 * b + 2 * tp + e
+                nc.scalar.activation(d2[:, 2 * tp + e, :], bank[:, e, :], COPY, scale=g_col[:, u : u + 1])
+
+        def twice_final(seg, b, c):
+            bank = acc_pool.tile([P, 4, CHUNK], F32, name="acc")
+            tok = slice(seg * SEG + c * CHUNK, seg * SEG + (c + 1) * CHUNK)
+            for t in range(4):
+                project(bank[:, t, :], [0, 1], 4 * b + t, tok)
+            nc.vector.tensor_tensor(
+                h_view(state["h", seg, b], c * CHUNK, (c + 1) * CHUNK),
+                interleaved(bank[:]),
+                interleaved(state["d2", seg, b][:, :, c * CHUNK : (c + 1) * CHUNK]),
+                MULT,
+            )
+
+        def quant_h(seg, b, lo, hi):
+            tok = slice(seg * SEG + lo, seg * SEG + hi)
+            nc.vector.quantize_mx(
+                h_q[:, b, tok].bitcast(FP8X4),
+                h_s[:, b, tok],
+                state["h", seg, b][:, lo:hi, :].rearrange("p n t -> p (n t)"),
+            )
+
+        out_view = out.rearrange("(m p) s -> p m s", p=P)
+
+        def mix(seg, c, store):
+            tok = slice(seg * SEG + c * CHUNK, seg * SEG + (c + 1) * CHUNK)
+            bank = y_pool.tile([P, 3 * CHUNK], F32, tag="y")
+            for m in range(3):
+                for b in range(2):
+                    cols = slice(b * N + m * P, b * N + (m + 1) * P)
+                    nc.tensor.matmul_mx(
+                        bank[:, m * CHUNK : (m + 1) * CHUNK],
+                        lhsT=w4_q[:, cols].bitcast(FP8X4),
+                        lhsT_scale=w4_s[:, cols],
+                        rhs=h_q[:, b, tok].bitcast(FP8X4),
+                        rhs_scale=h_s[:, b, tok],
+                        start=(b == 0),
+                        stop=(b == 1),
+                    )
+            if c == 0:
+                state["res", seg] = ring.tile([P, 3, SEG], F32, name="res", align_bytes=64)
+            res = state["res", seg]
+            nc.scalar.activation(
+                res[:, :, c * CHUNK : (c + 1) * CHUNK], bank[:].rearrange("p (m s) -> p m s", m=3), TANH
+            )
+            if store is not None:
+                lo, hi = store
+                nc.sync.dma_start(out_view[:, :, seg * SEG + lo : seg * SEG + hi], res[:, :, lo:hi])
+
+        once_pair(0, 0, 0)
+        once_pair(0, 0, 1)
+        once_pair(0, 1, 0)
+        once_final(0, 0)
+        cast_w4(0)
+        once_pair(0, 1, 1)
+        quant_h(0, 0, 0, SEG)
+        cast_w4(1)
+        for seg in range(1, 4):
+            once_pair(seg, 0, 0)
+            if seg == 1:
+                once_final(0, 1)
+                gather(v_words, tab_w[:].bitcast(U32), 1)
+                quant_w4()
+                quant_h(0, 1, 0, SEG)
+            else:
+                quant_h(seg - 1, 1, 0, SEG)
+            twice_side(seg, 1, 0)
+            once_pair(seg, 0, 1)
+            mix(seg - 1, 0, None)
+            mix(seg - 1, 1, (0, SEG))
+            twice_side(seg, 1, 1)
+            once_final(seg, 0)
+            twice_final(seg, 1, 0)
+            quant_h(seg, 0, 0, SEG)
+            if seg == 3:
+                quant_h(3, 1, 0, CHUNK)
+            twice_final(seg, 1, 1)
+        mix(3, 0, (0, CHUNK))
+        quant_h(3, 1, CHUNK, SEG)
+        mix(3, 1, (CHUNK, SEG))

@@ -18,11 +18,13 @@ COPY = mybir.ActivationFunctionType.Copy
 TANH = mybir.ActivationFunctionType.Tanh
 MULT = mybir.AluOpType.mult
 ADD = mybir.AluOpType.add
+IS_EQUAL = mybir.AluOpType.is_equal
 
 P = 128
 SEG = 256
 CHUNK = 128
 HALF = 512
+X_SLOTS = 6
 
 
 def tile_list_bond_angle_features_kernel(
@@ -31,21 +33,27 @@ def tile_list_bond_angle_features_kernel(
     nc = tc.nc
     with ExitStack() as ctx:
         keep = ctx.enter_context(tc.tile_pool(name="keep", bufs=1))
-        ring = ctx.enter_context(tc.tile_pool(name="ring", bufs=3))
-        acc_pool = ctx.enter_context(tc.psum_pool(name="acc", bufs=6))
-        y_pool = ctx.enter_context(tc.psum_pool(name="ybank", bufs=2))
+        psum = ctx.enter_context(tc.psum_pool(name="psum", bufs=1))
+        banks = [psum.tile([P, 512], F32, name=f"bank{k}") for k in range(8)]
+        uses = []
+
+        def take_bank():
+            uses.append(len(uses))
+            return banks[uses[-1] % 8]
 
         lists = [keep.tile([P, S // 16], U16, name=f"list{l}") for l in range(3)]
         tab_s = keep.tile([P, T // 4], I32, align_bytes=64)
         tab_w = keep.tile([P, T], I32, align_bytes=64)
-        ws_raw = keep.tile([P, 2, H // 4], I32, align_bytes=64)
-        w1_raw = keep.tile([P, 4, H], F32, align_bytes=64)
-        w2_raw = keep.tile([P, H // 2], I32, align_bytes=64)
-        w3_raw = keep.tile([P, H], I32, align_bytes=64)
+        ws_raw = keep.tile([P, 2, H // 4], I32, align_bytes=64, tag="reuse0")
+        w1_raw = keep.tile([P, 2, 4, H // 2], F32, align_bytes=64)
+        w2_raw = keep.tile([P, H // 2], I32, align_bytes=64, tag="reuse1")
+        w3_raw = keep.tile([P, H], I32, align_bytes=64, tag="reuse2")
         w4_raw = keep.tile([P, 8, N], F32, align_bytes=64)
         g_rows = keep.tile([P, P], F32, align_bytes=64)
         ident = keep.tile([P, P], F32, align_bytes=64)
         g_col = keep.tile([P, 8], F32, align_bytes=64)
+        g_safe = keep.tile([P, 8], F32, align_bytes=64)
+        g_inv = keep.tile([P, 8], F32, align_bytes=64)
         warm = keep.tile([P, 8], F32, align_bytes=64)
         warm2 = keep.tile([P, 8], F32, align_bytes=64)
 
@@ -60,67 +68,104 @@ def tile_list_bond_angle_features_kernel(
             nc.sync.dma_start(tile[:], src)
         for q in range(4):
             nc.sync.dma_start(tab_s[32 * q : 32 * q + 4, :], tab_scales[0, 4 * q : 4 * q + 4, :].bitcast(I32))
-        nc.sync.dma_start(w1_raw[:], w1.rearrange("(p j) c -> p j c", j=4))
-        for q in range(4):
-            nc.sync.dma_start(ws_raw[32 * q : 32 * q + 4, 0, :], w2_scales[0, 4 * q : 4 * q + 4, :].bitcast(I32))
-        for q in range(4):
-            nc.sync.dma_start(ws_raw[32 * q : 32 * q + 4, 1, :], w3_scales[0, 4 * q : 4 * q + 4, :].bitcast(I32))
+        w1_rows = w1.rearrange("(p j) (b c) -> b p j c", j=4, b=2)
+        g_view = g.rearrange("(b q t i) -> b t q i", b=2, t=4, i=8)
+        w4_view = w4.rearrange("(b q t i) n -> b t q i n", b=2, t=4, i=8)
+
+        def load_scale_rows(w, src):
+            for q in range(4):
+                nc.sync.dma_start(ws_raw[32 * q : 32 * q + 4, w, :], src[0, 4 * q : 4 * q + 4, :].bitcast(I32))
+
+        nc.sync.dma_start(w1_raw[:, 0], w1_rows[0])
+        for b in range(2):
+            nc.sync.dma_start(g_rows[4 * b : 4 * b + 4, :].rearrange("t (q i) -> t q i", i=8), g_view[b])
+        load_scale_rows(0, w2_scales)
+        nc.sync.dma_start(tab_w[:], tab_words[0].rearrange("p t i -> p (t i)").bitcast(I32))
         nc.sync.dma_start(w2_raw[:], w2_words[0].bitcast(I32))
         nc.sync.dma_start(w3_raw[:], w3_words[0].rearrange("p e i -> p (e i)").bitcast(I32))
-        nc.sync.dma_start(
-            g_rows[0:8, :].rearrange("u (q i) -> u q i", i=8), g.rearrange("(q u i) -> u q i", u=8, i=8)
-        )
-        nc.sync.dma_start(tab_w[:], tab_words[0].rearrange("p t i -> p (t i)").bitcast(I32))
-        w4_view = w4.rearrange("(q u i) n -> u q i n", u=8, i=8)
+        load_scale_rows(1, w3_scales)
+        nc.sync.dma_start(w1_raw[:, 1], w1_rows[1])
         for u in range(8):
-            nc.sync.dma_start(w4_raw[:, u, :], w4_view[u])
+            nc.sync.dma_start(w4_raw[:, u, :], w4_view[u // 4, u % 4])
 
-        v_words = [keep.tile([P, S], U32, align_bytes=64, name=f"v_words{l}") for l in range(3)]
+        v_words = {}
         v_scales = [keep.tile([P, S], U8, align_bytes=64, name=f"v_scales{l}") for l in range(3)]
-
-        def gather(dst, window, half):
-            for l in range(3):
-                cols = slice(half * HALF, (half + 1) * HALF)
-                offsets = lists[l][:, half * HALF // 16 : (half + 1) * HALF // 16]
-                nc.vector.tensor_copy(dst[l][:, cols], window.indirect(offsets))
-
-        gather(v_scales, tab_s[:].bitcast(U8), 0)
-        gather(v_scales, tab_s[:].bitcast(U8), 1)
-
-        w1_bf = keep.tile([P, 8, 16, 8, 4], BF16, align_bytes=64)
-        w1_q = keep.tile([P, H], U32, align_bytes=64)
-        w1_s = keep.tile([P, H], U8, align_bytes=64)
-        w1_view = w1_raw[:].rearrange("p j (q u i) -> p u q i j", u=8, i=8)
-        w1_flat = w1_bf[:].rearrange("p u q i j -> p (u q i j)")
-        for u in range(8):
-            nc.scalar.activation(w1_bf[:, u], w1_view[:, u], COPY, scale=-1.0)
-            if u % 2 == 1:
-                cols = slice((u - 1) * P, (u + 1) * P)
-                nc.vector.quantize_mx(
-                    w1_q[:, cols].bitcast(FP8X4), w1_s[:, cols], w1_flat[:, 4 * cols.start : 4 * cols.stop]
-                )
-
-        g_bank = y_pool.tile([P, 3 * CHUNK], F32, tag="y")
+        g_bank = take_bank()
         nc.tensor.transpose(g_bank[:, 0:P], g_rows[:], ident[:])
         nc.scalar.copy(g_col[:], g_bank[:, 0:8])
+        for l in range(3):
+            if l == 2:
+                nc.vector.scalar_tensor_tensor(g_safe[:], g_col[:], 0.0, g_col[:], IS_EQUAL, ADD)
+            nc.vector.tensor_copy(v_scales[l][:], tab_s[:].bitcast(U8).indirect(lists[l][:]))
+
+        def gather_words(half, l):
+            tag = f"reuse{l}" if half else f"first{l}"
+            v_words[l, half] = keep.tile([P, HALF], U32, align_bytes=64, name=f"v_words{l}_{half}", tag=tag)
+            offsets = lists[l][:, half * HALF // 16 : (half + 1) * HALF // 16]
+            nc.vector.tensor_copy(v_words[l, half][:], tab_w[:].bitcast(U32).indirect(offsets))
+
+        w1_bf = [keep.tile([P, 4, 16, 8, 4], BF16, align_bytes=64, name=f"w1_bf{b}", tag=f"cast{b}") for b in range(2)]
+        w1_q = keep.tile([P, H], U32, align_bytes=64)
+        w1_s = keep.tile([P, H], U8, align_bytes=64)
+        w1_view = w1_raw[:].rearrange("p b j (q t i) -> p b t q i j", t=4, i=8)
+
+        def cast_w1(b):
+            for t in range(4):
+                nc.scalar.activation(w1_bf[b][:, t], w1_view[:, b, t], COPY, scale=-1.0)
+
+        def quant_w1(b):
+            cols = slice(b * 4 * P, (b + 1) * 4 * P)
+            nc.vector.quantize_mx(
+                w1_q[:, cols].bitcast(FP8X4), w1_s[:, cols], w1_bf[b][:].rearrange("p t q i j -> p (t q i j)")
+            )
+
+        stage = keep.tile([P, 4, SEG, 4], BF16, align_bytes=64)
+        stage_cols = stage[:].rearrange("p s n t -> p (s n) t")
+        h_bf = stage[:, 1:4]
+        late = {}
+        w4_s = keep.tile([P, 2 * N], U8, align_bytes=64)
+
+        def cast_w4(b, lo, hi):
+            col = b * N + lo
+            at = col if col < 2 * SEG else col + SEG
+            nc.scalar.activation(
+                stage_cols[:, at : at + hi - lo, :].rearrange("p (c i) t -> p c t i", i=4),
+                w4_raw[:, 4 * b : 4 * b + 4, lo:hi].rearrange("p t (c i) -> p c t i", i=4),
+                COPY,
+            )
+
+        def quant_w4():
+            w4_q = keep.tile([P, 2 * N], U32, align_bytes=64, tag="cast1")
+            late["w4_q"] = w4_q
+            for lo, hi, at in ((2 * SEG, 3 * SEG, 3 * SEG), (0, 2 * SEG, 0)):
+                nc.vector.quantize_mx(
+                    w4_q[:, lo:hi].bitcast(FP8X4),
+                    w4_s[:, lo:hi],
+                    stage_cols[:, at : at + hi - lo, :].rearrange("p n t -> p (n t)"),
+                )
+
+        cast_w1(0)
+        quant_w1(0)
+        gather_words(0, 0)
+        nc.vector.reciprocal(g_inv[:], g_safe[:])
+        gather_words(0, 1)
+        gather_words(0, 2)
 
         ws_p = keep.tile([P, 2, H // 4], I32, align_bytes=64)
         w2_p = keep.tile([P, H // 2], I32, align_bytes=64)
         w3_p = keep.tile([P, H], I32, align_bytes=64)
         nc.vector.tensor_copy(
-            ws_p[:].rearrange("p w (u q e) -> p w u q e", u=8, e=2),
-            ws_raw[:].rearrange("p w (q u e) -> p w u q e", u=8, e=2),
+            ws_p[:].rearrange("p w (b t q e) -> p (w b) t q e", b=2, t=4, e=2),
+            ws_raw[:].rearrange("p w (b q t e) -> p (w b) t q e", b=2, t=4, e=2),
         )
         nc.vector.tensor_copy(
-            w2_p[:].rearrange("p (u q e) -> p u q e", u=8, e=4),
-            w2_raw[:].rearrange("p (q u e) -> p u q e", u=8, e=4),
+            w2_p[:].rearrange("p (b t q e) -> p b t q e", b=2, t=4, e=4),
+            w2_raw[:].rearrange("p (b q t e) -> p b t q e", b=2, t=4, e=4),
         )
         nc.vector.tensor_copy(
-            w3_p[:].rearrange("p (u q e) -> p u q e", u=8, e=8),
-            w3_raw[:].rearrange("p (q u e) -> p u q e", u=8, e=8),
+            w3_p[:].rearrange("p (b t q e) -> p b t q e", b=2, t=4, e=8),
+            w3_raw[:].rearrange("p (b q t e) -> p b t q e", b=2, t=4, e=8),
         )
-
-        gather(v_words, tab_w[:].bitcast(U32), 0)
 
         def weight(l, u):
             cols = slice(u * P, (u + 1) * P)
@@ -138,76 +183,86 @@ def tile_list_bond_angle_features_kernel(
                     dst,
                     lhsT=codes,
                     lhsT_scale=scale,
-                    rhs=v_words[l][:, tok].bitcast(FP8X4),
+                    rhs=v_words[l, tok.start // HALF][:, tok.start % HALF : (tok.stop - 1) % HALF + 1].bitcast(FP8X4),
                     rhs_scale=v_scales[l][:, tok],
                     start=(n == 0),
                     stop=(n == len(ls) - 1),
                 )
 
-        w4_bf = keep.tile([P, 2, N, 4], BF16, align_bytes=64)
-        w4_q = keep.tile([P, 2 * N], U32, align_bytes=64)
-        w4_s = keep.tile([P, 2 * N], U8, align_bytes=64)
-
-        def cast_w4(b):
-            nc.scalar.activation(
-                w4_bf[:, b].rearrange("p (c i) t -> p c t i", i=4),
-                w4_raw[:, 4 * b : 4 * b + 4, :].rearrange("p t (c i) -> p c t i", i=4),
-                COPY,
-            )
-
-        def quant_w4():
-            flat = w4_bf[:].rearrange("p b n t -> p (b n t)")
-            for lo, hi in ((0, 512), (512, 768)):
-                nc.vector.quantize_mx(w4_q[:, lo:hi].bitcast(FP8X4), w4_s[:, lo:hi], flat[:, 4 * lo : 4 * hi])
-
-        h_q = keep.tile([P, 2, S], U32, align_bytes=64)
-        h_s = keep.tile([P, 2, S], U8, align_bytes=64)
+        h_q = keep.tile([P, 4, 2, SEG], U32, align_bytes=64)
+        h_s = {}
+        x_all = keep.tile([P, X_SLOTS, 2, SEG], F32, align_bytes=64)
+        side_all = keep.tile([P, 2, 4, SEG], F32, align_bytes=64)
+        res_all = keep.tile([P, 4, 3, SEG], F32, align_bytes=64)
+        both_all = [
+            keep.tile([P, 2, 4, SEG], F32, align_bytes=64, name=f"arms{k}", tag=("cast1", "cast0", "arms")[k]) for k in range(3)
+        ]
         state = {}
+
+        def part(seg, b):
+            return 1 if b == 0 else 2 * (seg % 2)
+
+        def slot(seg, b):
+            return part(seg, b) - seg % 2
 
         def seg_tok(seg):
             return slice(seg * SEG, (seg + 1) * SEG)
 
-        def once_pair(seg, b, tp):
-            if tp == 0:
-                state["d1", seg, b] = ring.tile([P, 4, SEG], F32, name="d1", align_bytes=64)
-                state["d2", seg, b] = ring.tile([P, 4, SEG], F32, name="d2", align_bytes=64)
-            d1, d2 = state["d1", seg, b], state["d2", seg, b]
-            banks = [acc_pool.tile([P, 2, SEG], F32, name="acc") for l in range(3)]
-            for l in range(3):
-                for e in range(2):
-                    project(banks[l][:, e, :], [l], 4 * b + 2 * tp + e, seg_tok(seg))
-            x = ring.tile([P, 2, SEG], F32, name="x", align_bytes=64)
-            xg = ring.tile([P, 2, SEG], F32, name="xg", align_bytes=64)
-            nc.scalar.copy(x[:], banks[0][:])
+        def centre(seg, b, tp):
+            bank = take_bank()[:].rearrange("p (e n) -> p e n", e=2)
+            for e in range(2):
+                project(bank[:, e, :], [0], 4 * b + 2 * tp + e, seg_tok(seg))
+            k = 2 * (seg + b + (seg > 0)) + tp
+            xg = [x_all[:, k % X_SLOTS, e] for e in range(2)]
+            if seg > 0 and tp == (seg < 3):
+                xg[0] = keep.tile([P, SEG], F32, align_bytes=64, name=f"xg_tie{seg}", tag=f"tie{seg - 1}")[:]
+                if seg == 3:
+                    xg[1] = keep.tile([P, SEG], F32, align_bytes=64, name="xg_tie_last", tag="tie3")[:]
             for e in range(2):
                 u = 4 * b + 2 * tp + e
-                nc.scalar.activation(xg[:, e, :], banks[0][:, e, :], COPY, scale=g_col[:, u : u + 1])
-            nc.vector.tensor_tensor(d1[:, 2 * tp : 2 * tp + 2, :], banks[1][:], x[:], ADD)
+                nc.scalar.activation(xg[e], bank[:, e, :], COPY, scale=g_col[:, u : u + 1])
+            state["x", seg, b, tp] = xg
+
+        def once_pair(seg, b, tp):
+            if tp == 0:
+                both = both_all[0 if seg + b == 0 else 1 + (seg + 1) % 2]
+                state["d1", seg, b], state["d2", seg, b] = both[:, 0], both[:, 1]
+            d1, d2 = state["d1", seg, b], state["d2", seg, b]
+            xg = state["x", seg, b, tp]
+            arms = [take_bank()[:].rearrange("p (e n) -> p e n", e=2) for l in range(2)]
+            for l in range(2):
+                for e in range(2):
+                    project(arms[l][:, e, :], [l + 1], 4 * b + 2 * tp + e, seg_tok(seg))
             for e in range(2):
                 u = 4 * b + 2 * tp + e
                 nc.vector.scalar_tensor_tensor(
-                    d2[:, 2 * tp + e, :], banks[2][:, e, :], g_col[:, u : u + 1], xg[:, e, :], MULT, ADD
+                    d1[:, 2 * tp + e, :], arms[0][:, e, :], g_col[:, u : u + 1], xg[e], MULT, ADD
+                )
+            for e in range(2):
+                u = 4 * b + 2 * tp + e
+                nc.vector.scalar_tensor_tensor(
+                    d2[:, 2 * tp + e, :], xg[e], g_inv[:, u : u + 1], arms[1][:, e, :], MULT, ADD
                 )
 
         def interleaved(ap):
             return ap.rearrange("p t (c i) -> p c t i", i=4)
 
-        def h_view(h, lo, hi):
-            return h[:, lo:hi, :].rearrange("p (c i) t -> p c t i", i=4)
+        def h_view(seg, b, lo, hi):
+            return h_bf[:, part(seg, b), lo:hi, :].rearrange("p (c i) t -> p c t i", i=4)
 
-        def once_final(seg, b):
-            h = ring.tile([P, SEG, 4], BF16, name="h", align_bytes=64)
-            state["h", seg, b] = h
-            nc.vector.tensor_tensor(
-                h_view(h, 0, SEG), interleaved(state["d1", seg, b][:]), interleaved(state["d2", seg, b][:]), MULT
+        def once_final(engine, seg, b, lo, hi):
+            engine.tensor_tensor(
+                h_view(seg, b, lo, hi),
+                interleaved(state["d1", seg, b][:, :, lo:hi]),
+                interleaved(state["d2", seg, b][:, :, lo:hi]),
+                MULT,
             )
 
         def twice_side(seg, b, tp):
             if tp == 0:
-                state["d2", seg, b] = ring.tile([P, 4, SEG], F32, name="d2", align_bytes=64)
-                state["h", seg, b] = ring.tile([P, SEG, 4], BF16, name="h", align_bytes=64)
+                state["d2", seg, b] = side_all[:, seg % 2]
             d2 = state["d2", seg, b]
-            bank = acc_pool.tile([P, 2, SEG], F32, name="acc")
+            bank = take_bank()[:].rearrange("p (e n) -> p e n", e=2)
             for e in range(2):
                 project(bank[:, e, :], [0, 2], 4 * b + 2 * tp + e, seg_tok(seg))
             for e in range(2):
@@ -215,80 +270,108 @@ def tile_list_bond_angle_features_kernel(
                 nc.scalar.activation(d2[:, 2 * tp + e, :], bank[:, e, :], COPY, scale=g_col[:, u : u + 1])
 
         def twice_final(seg, b, c):
-            bank = acc_pool.tile([P, 4, CHUNK], F32, name="acc")
+            bank = take_bank()[:].rearrange("p (t n) -> p t n", t=4)
             tok = slice(seg * SEG + c * CHUNK, seg * SEG + (c + 1) * CHUNK)
             for t in range(4):
                 project(bank[:, t, :], [0, 1], 4 * b + t, tok)
             nc.vector.tensor_tensor(
-                h_view(state["h", seg, b], c * CHUNK, (c + 1) * CHUNK),
-                interleaved(bank[:]),
+                h_view(seg, b, c * CHUNK, (c + 1) * CHUNK),
+                interleaved(bank),
                 interleaved(state["d2", seg, b][:, :, c * CHUNK : (c + 1) * CHUNK]),
                 MULT,
             )
 
-        def quant_h(seg, b, lo, hi):
-            tok = slice(seg * SEG + lo, seg * SEG + hi)
+        def quant_seg(seg):
+            first = seg % 2
+            h_s[seg] = keep.tile([P, 2, SEG], U8, align_bytes=64, name=f"h_s{seg}", tag=f"tie{seg}")
             nc.vector.quantize_mx(
-                h_q[:, b, tok].bitcast(FP8X4),
-                h_s[:, b, tok],
-                state["h", seg, b][:, lo:hi, :].rearrange("p n t -> p (n t)"),
+                h_q[:, seg].rearrange("p b n -> p (b n)").bitcast(FP8X4),
+                h_s[seg][:].rearrange("p b n -> p (b n)"),
+                h_bf[:, first : first + 2].rearrange("p b n t -> p (b n t)"),
+            )
+
+        def quant_part(seg, b, lo, hi):
+            if seg not in h_s:
+                h_s[seg] = keep.tile([P, 2, SEG], U8, align_bytes=64, name=f"h_s{seg}", tag="tie3")
+            nc.vector.quantize_mx(
+                h_q[:, seg, slot(seg, b), lo:hi].bitcast(FP8X4),
+                h_s[seg][:, slot(seg, b), lo:hi],
+                h_bf[:, part(seg, b), lo:hi, :].rearrange("p n t -> p (n t)"),
             )
 
         out_view = out.rearrange("(m p) s -> p m s", p=P)
 
         def mix(seg, c, store):
-            tok = slice(seg * SEG + c * CHUNK, seg * SEG + (c + 1) * CHUNK)
-            bank = y_pool.tile([P, 3 * CHUNK], F32, tag="y")
+            tok = slice(c * CHUNK, (c + 1) * CHUNK)
+            bank = take_bank()
             for m in range(3):
                 for b in range(2):
                     cols = slice(b * N + m * P, b * N + (m + 1) * P)
                     nc.tensor.matmul_mx(
                         bank[:, m * CHUNK : (m + 1) * CHUNK],
-                        lhsT=w4_q[:, cols].bitcast(FP8X4),
+                        lhsT=late["w4_q"][:, cols].bitcast(FP8X4),
                         lhsT_scale=w4_s[:, cols],
-                        rhs=h_q[:, b, tok].bitcast(FP8X4),
-                        rhs_scale=h_s[:, b, tok],
+                        rhs=h_q[:, seg, slot(seg, b), tok].bitcast(FP8X4),
+                        rhs_scale=h_s[seg][:, slot(seg, b), tok],
                         start=(b == 0),
                         stop=(b == 1),
                     )
-            if c == 0:
-                state["res", seg] = ring.tile([P, 3, SEG], F32, name="res", align_bytes=64)
-            res = state["res", seg]
+            res = res_all[:, seg]
             nc.scalar.activation(
-                res[:, :, c * CHUNK : (c + 1) * CHUNK], bank[:].rearrange("p (m s) -> p m s", m=3), TANH
+                res[:, :, c * CHUNK : (c + 1) * CHUNK], bank[:, 0 : 3 * CHUNK].rearrange("p (m s) -> p m s", m=3), TANH
             )
             if store is not None:
                 lo, hi = store
                 nc.sync.dma_start(out_view[:, :, seg * SEG + lo : seg * SEG + hi], res[:, :, lo:hi])
 
+        centre(0, 0, 0)
+        centre(0, 0, 1)
+        centre(1, 0, 0)
+        cast_w1(1)
+        for l in range(3):
+            gather_words(1, l)
+        quant_w1(1)
         once_pair(0, 0, 0)
+        cast_w4(0, 0, N)
+        centre(0, 1, 0)
+        centre(0, 1, 1)
         once_pair(0, 0, 1)
+        once_final(nc.gpsimd, 0, 0, 0, SEG)
+        cast_w4(1, 0, P)
+        cast_w4(1, P, N)
+        twice_side(1, 1, 0)
         once_pair(0, 1, 0)
-        once_final(0, 0)
-        cast_w4(0)
+        twice_side(1, 1, 1)
         once_pair(0, 1, 1)
-        quant_h(0, 0, 0, SEG)
-        cast_w4(1)
+        quant_w4()
+        once_final(nc.gpsimd, 0, 1, 0, SEG)
+        centre(1, 0, 1)
         for seg in range(1, 4):
-            once_pair(seg, 0, 0)
-            if seg == 1:
-                once_final(0, 1)
-                gather(v_words, tab_w[:].bitcast(U32), 1)
-                quant_w4()
-                quant_h(0, 1, 0, SEG)
-            else:
-                quant_h(seg - 1, 1, 0, SEG)
-            twice_side(seg, 1, 0)
-            once_pair(seg, 0, 1)
-            mix(seg - 1, 0, None)
-            mix(seg - 1, 1, (0, SEG))
-            twice_side(seg, 1, 1)
-            once_final(seg, 0)
             twice_final(seg, 1, 0)
-            quant_h(seg, 0, 0, SEG)
-            if seg == 3:
-                quant_h(3, 1, 0, CHUNK)
+            if seg < 3:
+                centre(seg + 1, 0, 0)
             twice_final(seg, 1, 1)
+            if seg > 1:
+                mix(seg - 2, 0, None)
+            once_pair(seg, 0, 0)
+            if seg < 3:
+                twice_side(seg + 1, 1, 0)
+            if seg > 1:
+                mix(seg - 2, 1, (0, SEG))
+            if seg < 3:
+                once_pair(seg, 0, 1)
+                quant_seg(seg - 1)
+                once_final(nc.gpsimd, seg, 0, 0, SEG)
+                twice_side(seg + 1, 1, 1)
+                centre(seg + 1, 0, 1)
+        quant_seg(2)
+        quant_part(3, 1, 0, SEG)
+        once_pair(3, 0, 1)
+        mix(2, 0, None)
+        mix(2, 1, (0, SEG))
+        once_final(nc.vector, 3, 0, 0, CHUNK)
+        once_final(nc.vector, 3, 0, CHUNK, SEG)
+        quant_part(3, 0, 0, CHUNK)
         mix(3, 0, (0, CHUNK))
-        quant_h(3, 1, CHUNK, SEG)
+        quant_part(3, 0, CHUNK, SEG)
         mix(3, 1, (CHUNK, SEG))

@@ -58,27 +58,27 @@ def tile_list_bond_angle_features_kernel(
         warm2 = keep.tile([P, 8], F32, align_bytes=64)
 
         nc.vector.memset(tab_s[:], 0)
+        nc.vector.memset(g_rows[:], 0.0)
+        nc.vector.memset(warm[:], 0.0)
         nc.vector.memset(ws_raw[:], 0)
-        nc.gpsimd.memset(warm[:], 0.0)
         nc.scalar.activation(warm2[:], warm[:], TANH)
-        nc.gpsimd.memset(g_rows[:], 0.0)
         make_identity(nc, ident[:])
 
         for tile, src in zip(lists, (offs, offs2, offs3)):
             nc.sync.dma_start(tile[:], src)
-        for q in range(4):
-            nc.sync.dma_start(tab_s[32 * q : 32 * q + 4, :], tab_scales[0, 4 * q : 4 * q + 4, :].bitcast(I32))
+        for r in range(4):
+            nc.sync.dma_start(tab_s[r:P:32, :], tab_scales[0, r:16:4, :].bitcast(I32))
         w1_rows = w1.rearrange("(p j) (b c) -> b p j c", j=4, b=2)
         g_view = g.rearrange("(b q t i) -> b t q i", b=2, t=4, i=8)
         w4_view = w4.rearrange("(b q t i) n -> b t q i n", b=2, t=4, i=8)
 
         def load_scale_rows(w, src):
-            for q in range(4):
-                nc.sync.dma_start(ws_raw[32 * q : 32 * q + 4, w, :], src[0, 4 * q : 4 * q + 4, :].bitcast(I32))
+            for r in range(4):
+                nc.sync.dma_start(ws_raw[r:P:32, w, :], src[0, r:16:4, :].bitcast(I32))
 
-        nc.sync.dma_start(w1_raw[:, 0], w1_rows[0])
         for b in range(2):
             nc.sync.dma_start(g_rows[4 * b : 4 * b + 4, :].rearrange("t (q i) -> t q i", i=8), g_view[b])
+        nc.sync.dma_start(w1_raw[:, 0], w1_rows[0])
         load_scale_rows(0, w2_scales)
         nc.sync.dma_start(tab_w[:], tab_words[0].rearrange("p t i -> p (t i)").bitcast(I32))
         nc.sync.dma_start(w2_raw[:], w2_words[0].bitcast(I32))
@@ -107,11 +107,11 @@ def tile_list_bond_angle_features_kernel(
         w1_bf = [keep.tile([P, 4, 16, 8, 4], BF16, align_bytes=64, name=f"w1_bf{b}", tag=f"cast{b}") for b in range(2)]
         w1_q = keep.tile([P, H], U32, align_bytes=64)
         w1_s = keep.tile([P, H], U8, align_bytes=64)
-        w1_view = w1_raw[:].rearrange("p b j (q t i) -> p b t q i j", t=4, i=8)
+        w1_view = w1_raw[:].rearrange("p b j (q t i) -> p b t q j i", t=4, i=8)
 
         def cast_w1(b):
             for t in range(4):
-                nc.scalar.activation(w1_bf[b][:, t], w1_view[:, b, t], COPY, scale=-1.0)
+                nc.scalar.activation(w1_bf[b][:, t].rearrange("p q i j -> p q j i"), w1_view[:, b, t], COPY, scale=-1.0)
 
         def quant_w1(b):
             cols = slice(b * 4 * P, (b + 1) * 4 * P)
@@ -129,8 +129,8 @@ def tile_list_bond_angle_features_kernel(
             col = b * N + lo
             at = col if col < 2 * SEG else col + SEG
             nc.scalar.activation(
-                stage_cols[:, at : at + hi - lo, :].rearrange("p (c i) t -> p c t i", i=4),
-                w4_raw[:, 4 * b : 4 * b + 4, lo:hi].rearrange("p t (c i) -> p c t i", i=4),
+                stage_cols[:, at : at + hi - lo, :].rearrange("p (c i) t -> p c t i", i=2),
+                w4_raw[:, 4 * b : 4 * b + 4, lo:hi].rearrange("p t (c i) -> p c t i", i=2),
                 COPY,
             )
 
@@ -245,10 +245,10 @@ def tile_list_bond_angle_features_kernel(
                 )
 
         def interleaved(ap):
-            return ap.rearrange("p t (c i) -> p c t i", i=4)
+            return ap.rearrange("p t (c i) -> p c t i", i=2)
 
         def h_view(seg, b, lo, hi):
-            return h_bf[:, part(seg, b), lo:hi, :].rearrange("p (c i) t -> p c t i", i=4)
+            return h_bf[:, part(seg, b), lo:hi, :].rearrange("p (c i) t -> p c t i", i=2)
 
         def once_final(engine, seg, b, lo, hi):
             engine.tensor_tensor(
@@ -300,6 +300,31 @@ def tile_list_bond_angle_features_kernel(
             )
 
         out_view = out.rearrange("(m p) s -> p m s", p=P)
+
+        def mix_pass(dst, seg, c, m, b, start, stop):
+            tok = slice(c * CHUNK, (c + 1) * CHUNK)
+            cols = slice(b * N + m * P, b * N + (m + 1) * P)
+            nc.tensor.matmul_mx(
+                dst,
+                lhsT=late["w4_q"][:, cols].bitcast(FP8X4),
+                lhsT_scale=w4_s[:, cols],
+                rhs=h_q[:, seg, slot(seg, b), tok].bitcast(FP8X4),
+                rhs_scale=h_s[seg][:, slot(seg, b), tok],
+                start=start,
+                stop=stop,
+            )
+
+        def last_open(c):
+            for m in range(3):
+                state["y", c, m] = take_bank()
+                mix_pass(state["y", c, m][:, 0:CHUNK], 3, c, m, 1, True, False)
+
+        def last_close(c):
+            cols = slice(c * CHUNK, (c + 1) * CHUNK)
+            for m in range(3):
+                mix_pass(state["y", c, m][:, 0:CHUNK], 3, c, m, 0, False, True)
+                nc.scalar.activation(res_all[:, 3, m, cols], state["y", c, m][:, 0:CHUNK], TANH)
+            nc.sync.dma_start(out_view[:, :, 3 * SEG + cols.start : 3 * SEG + cols.stop], res_all[:, 3, :, cols])
 
         def mix(seg, c, store):
             tok = slice(c * CHUNK, (c + 1) * CHUNK)
@@ -369,9 +394,11 @@ def tile_list_bond_angle_features_kernel(
         once_pair(3, 0, 1)
         mix(2, 0, None)
         mix(2, 1, (0, SEG))
+        last_open(0)
+        last_open(1)
         once_final(nc.vector, 3, 0, 0, CHUNK)
         once_final(nc.vector, 3, 0, CHUNK, SEG)
         quant_part(3, 0, 0, CHUNK)
-        mix(3, 0, (0, CHUNK))
+        last_close(0)
         quant_part(3, 0, CHUNK, SEG)
-        mix(3, 1, (CHUNK, SEG))
+        last_close(1)

@@ -21,10 +21,8 @@ ADD = mybir.AluOpType.add
 IS_EQUAL = mybir.AluOpType.is_equal
 
 P = 128
-SEG = 256
 CHUNK = 128
 HALF = 512
-X_SLOTS = 6
 
 
 def tile_list_bond_angle_features_kernel(
@@ -35,370 +33,311 @@ def tile_list_bond_angle_features_kernel(
         keep = ctx.enter_context(tc.tile_pool(name="keep", bufs=1))
         psum = ctx.enter_context(tc.psum_pool(name="psum", bufs=1))
         banks = [psum.tile([P, 512], F32, name=f"bank{k}") for k in range(8)]
-        uses = []
+        turns = {"scalar": [], "shared": []}
 
-        def take_bank():
-            uses.append(len(uses))
-            return banks[uses[-1] % 8]
+        def scalar_bank():
+            turns["scalar"].append(0)
+            return banks[len(turns["scalar"]) % 2]
+
+        def shared_bank():
+            turns["shared"].append(0)
+            return banks[2 + len(turns["shared"]) % 6]
+
+        def sb(shape, dtype, name, tag=None):
+            return keep.tile(shape, dtype, align_bytes=64, name=name, tag=tag or name)
 
         lists = [keep.tile([P, S // 16], U16, name=f"list{l}") for l in range(3)]
-        tab_s = keep.tile([P, T // 4], I32, align_bytes=64)
-        tab_w = keep.tile([P, T], I32, align_bytes=64)
-        ws_raw = keep.tile([P, 2, H // 4], I32, align_bytes=64, tag="reuse0")
-        w1_raw = keep.tile([P, 2, 4, H // 2], F32, align_bytes=64)
-        w2_raw = keep.tile([P, H // 2], I32, align_bytes=64, tag="reuse1")
-        w3_raw = keep.tile([P, H], I32, align_bytes=64, tag="reuse2")
-        w4_raw = keep.tile([P, 8, N], F32, align_bytes=64)
-        g_rows = keep.tile([P, P], F32, align_bytes=64)
-        ident = keep.tile([P, P], F32, align_bytes=64)
-        g_col = keep.tile([P, 8], F32, align_bytes=64)
-        g_safe = keep.tile([P, 8], F32, align_bytes=64)
-        g_inv = keep.tile([P, 8], F32, align_bytes=64)
-        warm = keep.tile([P, 8], F32, align_bytes=64)
-        warm2 = keep.tile([P, 8], F32, align_bytes=64)
+        tab_s = sb([P, T // 4], I32, "tab_s")
+        tab_w = sb([P, T], I32, "tab_w")
+        ws_raw = sb([P, 2, H // 4], I32, "ws_raw")
+        w1_raw = [sb([P, 4, H // 2], F32, f"w1_raw{b}") for b in range(2)]
+        w2_raw = sb([P, H // 2], I32, "w2_raw")
+        w3_raw = sb([P, H], I32, "w3_raw")
+        w4_raw = [sb([P, 4, N], F32, f"w4_raw{b}") for b in range(2)]
+        g_rows = sb([P, P], F32, "g_rows")
+        ident = sb([P, P], F32, "ident")
+        g_col = sb([P, 8], F32, "g_col")
+        g_safe = sb([P, 8], F32, "g_safe")
+        g_inv = sb([P, 8], F32, "g_inv")
+        warm = sb([P, 8], F32, "warm")
+        warm2 = sb([P, 8], F32, "warm2")
 
         nc.vector.memset(tab_s[:], 0)
-        nc.vector.memset(g_rows[:], 0.0)
         nc.vector.memset(warm[:], 0.0)
         nc.vector.memset(ws_raw[:], 0)
         nc.scalar.activation(warm2[:], warm[:], TANH)
-        make_identity(nc, ident[:])
 
-        for tile, src in zip(lists, (offs, offs2, offs3)):
-            nc.sync.dma_start(tile[:], src)
-        for r in range(4):
-            nc.sync.dma_start(tab_s[r:P:32, :], tab_scales[0, r:16:4, :].bitcast(I32))
         w1_rows = w1.rearrange("(p j) (b c) -> b p j c", j=4, b=2)
         g_view = g.rearrange("(b q t i) -> b t q i", b=2, t=4, i=8)
         w4_view = w4.rearrange("(b q t i) n -> b t q i n", b=2, t=4, i=8)
 
-        def load_scale_rows(w, src):
-            for r in range(4):
+        nc.gpsimd.memset(g_rows[:], 0.0)
+        make_identity(nc, ident[:])
+
+        def load_scale_rows(w, src, rows):
+            for r in rows:
                 nc.sync.dma_start(ws_raw[r:P:32, w, :], src[0, r:16:4, :].bitcast(I32))
 
+        nc.sync.dma_start(lists[0][:], offs)
+        for r in range(4):
+            nc.sync.dma_start(tab_s[r:P:32, :], tab_scales[0, r:16:4, :].bitcast(I32))
+        nc.sync.dma_start(lists[1][:], offs2)
         for b in range(2):
             nc.sync.dma_start(g_rows[4 * b : 4 * b + 4, :].rearrange("t (q i) -> t q i", i=8), g_view[b])
-        nc.sync.dma_start(w1_raw[:, 0], w1_rows[0])
-        load_scale_rows(0, w2_scales)
+        nc.sync.dma_start(lists[2][:], offs3)
         nc.sync.dma_start(tab_w[:], tab_words[0].rearrange("p t i -> p (t i)").bitcast(I32))
+        nc.sync.dma_start(w1_raw[0][:], w1_rows[0])
         nc.sync.dma_start(w2_raw[:], w2_words[0].bitcast(I32))
         nc.sync.dma_start(w3_raw[:], w3_words[0].rearrange("p e i -> p (e i)").bitcast(I32))
-        load_scale_rows(1, w3_scales)
-        nc.sync.dma_start(w1_raw[:, 1], w1_rows[1])
+        load_scale_rows(0, w2_scales, range(4))
+        nc.sync.dma_start(w1_raw[1][:], w1_rows[1])
+        load_scale_rows(1, w3_scales, range(4))
         for u in range(8):
-            nc.sync.dma_start(w4_raw[:, u, :], w4_view[u // 4, u % 4])
+            nc.sync.dma_start(w4_raw[u // 4][:, u % 4, :], w4_view[u // 4, u % 4])
 
         v_words = {}
-        v_scales = [keep.tile([P, S], U8, align_bytes=64, name=f"v_scales{l}") for l in range(3)]
-        g_bank = take_bank()
+        state = {}
+        v_scales = [sb([P, S], U8, f"v_scales{l}") for l in range(3)]
+        g_bank = scalar_bank()
         nc.tensor.transpose(g_bank[:, 0:P], g_rows[:], ident[:])
         nc.scalar.copy(g_col[:], g_bank[:, 0:8])
         for l in range(3):
-            if l == 2:
-                nc.vector.scalar_tensor_tensor(g_safe[:], g_col[:], 0.0, g_col[:], IS_EQUAL, ADD)
             nc.vector.tensor_copy(v_scales[l][:], tab_s[:].bitcast(U8).indirect(lists[l][:]))
+            if l == 0:
+                nc.vector.scalar_tensor_tensor(g_safe[:], g_col[:], 0.0, g_col[:], IS_EQUAL, ADD)
+            if l == 1:
+                nc.vector.reciprocal(g_inv[:], g_safe[:])
 
-        def gather_words(half, l):
-            tag = f"reuse{l}" if half else f"first{l}"
-            v_words[l, half] = keep.tile([P, HALF], U32, align_bytes=64, name=f"v_words{l}_{half}", tag=tag)
+        def gather_words(half, l, tag=None):
+            v_words[l, half] = sb([P, HALF], U32, f"v_words{l}_{half}", tag)
             offsets = lists[l][:, half * HALF // 16 : (half + 1) * HALF // 16]
             nc.vector.tensor_copy(v_words[l, half][:], tab_w[:].bitcast(U32).indirect(offsets))
 
-        w1_bf = [keep.tile([P, 4, 16, 8, 4], BF16, align_bytes=64, name=f"w1_bf{b}", tag=f"cast{b}") for b in range(2)]
-        w1_q = keep.tile([P, H], U32, align_bytes=64)
-        w1_s = keep.tile([P, H], U8, align_bytes=64)
-        w1_view = w1_raw[:].rearrange("p b j (q t i) -> p b t q j i", t=4, i=8)
+        w1_bf = [sb([P, 4, 16, 8, 4], BF16, f"w1_bf{b}") for b in range(2)]
+        w1_q = [sb([P, H // 2], U32, f"w1_q{b}") for b in range(2)]
+        w1_s = [sb([P, H // 2], U8, f"w1_s{b}") for b in range(2)]
 
         def cast_w1(b):
+            src = w1_raw[b][:].rearrange("p j (q t i) -> p t q j i", t=4, i=8)
             for t in range(4):
-                nc.scalar.activation(w1_bf[b][:, t].rearrange("p q i j -> p q j i"), w1_view[:, b, t], COPY, scale=-1.0)
+                nc.scalar.activation(w1_bf[b][:, t].rearrange("p q i j -> p q j i"), src[:, t], COPY, scale=-1.0)
 
         def quant_w1(b):
-            cols = slice(b * 4 * P, (b + 1) * 4 * P)
             nc.vector.quantize_mx(
-                w1_q[:, cols].bitcast(FP8X4), w1_s[:, cols], w1_bf[b][:].rearrange("p t q i j -> p (t q i j)")
+                w1_q[b][:].bitcast(FP8X4), w1_s[b][:], w1_bf[b][:].rearrange("p t q i j -> p (t q i j)")
             )
 
-        stage = keep.tile([P, 4, SEG, 4], BF16, align_bytes=64)
-        stage_cols = stage[:].rearrange("p s n t -> p (s n) t")
-        h_bf = stage[:, 1:4]
-        late = {}
-        w4_s = keep.tile([P, 2 * N], U8, align_bytes=64)
+        w4_bf = sb([P, 2 * N, 4], BF16, "w4_bf")
+        w4_q = sb([P, 2 * N], U32, "w4_q")
+        w4_s = sb([P, 2 * N], U8, "w4_s")
 
-        def cast_w4(b, lo, hi):
-            col = b * N + lo
-            at = col if col < 2 * SEG else col + SEG
-            nc.scalar.activation(
-                stage_cols[:, at : at + hi - lo, :].rearrange("p (c i) t -> p c t i", i=2),
-                w4_raw[:, 4 * b : 4 * b + 4, lo:hi].rearrange("p t (c i) -> p c t i", i=2),
-                COPY,
+        def cast_w4(b):
+            nc.gpsimd.tensor_scalar(
+                w4_bf[:, b * N : (b + 1) * N, :].rearrange("p (c i) t -> p c t i", i=2),
+                w4_raw[b][:].rearrange("p t (c i) -> p c t i", i=2),
+                1.0,
+                0.0,
+                MULT,
+                ADD,
             )
 
         def quant_w4():
-            w4_q = keep.tile([P, 2 * N], U32, align_bytes=64, tag="cast1")
-            late["w4_q"] = w4_q
-            for lo, hi, at in ((2 * SEG, 3 * SEG, 3 * SEG), (0, 2 * SEG, 0)):
+            for lo, hi in ((0, 512), (512, 768)):
                 nc.vector.quantize_mx(
-                    w4_q[:, lo:hi].bitcast(FP8X4),
-                    w4_s[:, lo:hi],
-                    stage_cols[:, at : at + hi - lo, :].rearrange("p n t -> p (n t)"),
+                    w4_q[:, lo:hi].bitcast(FP8X4), w4_s[:, lo:hi], w4_bf[:, lo:hi, :].rearrange("p n t -> p (n t)")
                 )
 
-        cast_w1(0)
-        quant_w1(0)
-        gather_words(0, 0)
-        nc.vector.reciprocal(g_inv[:], g_safe[:])
-        gather_words(0, 1)
-        gather_words(0, 2)
+        ws_p = sb([P, 2, H // 4], I32, "ws_p")
+        w2_p = sb([P, H // 2], I32, "w2_p")
+        w3_p = sb([P, H], I32, "w3_p")
 
-        ws_p = keep.tile([P, 2, H // 4], I32, align_bytes=64)
-        w2_p = keep.tile([P, H // 2], I32, align_bytes=64)
-        w3_p = keep.tile([P, H], I32, align_bytes=64)
-        nc.vector.tensor_copy(
-            ws_p[:].rearrange("p w (b t q e) -> p (w b) t q e", b=2, t=4, e=2),
-            ws_raw[:].rearrange("p w (b q t e) -> p (w b) t q e", b=2, t=4, e=2),
-        )
-        nc.vector.tensor_copy(
-            w2_p[:].rearrange("p (b t q e) -> p b t q e", b=2, t=4, e=4),
-            w2_raw[:].rearrange("p (b q t e) -> p b t q e", b=2, t=4, e=4),
-        )
-        nc.vector.tensor_copy(
-            w3_p[:].rearrange("p (b t q e) -> p b t q e", b=2, t=4, e=8),
-            w3_raw[:].rearrange("p (b q t e) -> p b t q e", b=2, t=4, e=8),
-        )
+        def deal_packed():
+            nc.vector.tensor_copy(
+                w2_p[:].rearrange("p (b t q e) -> p b t q e", b=2, t=4, e=4),
+                w2_raw[:].rearrange("p (b q t e) -> p b t q e", b=2, t=4, e=4),
+            )
+            nc.vector.tensor_copy(
+                w3_p[:].rearrange("p (b t q e) -> p b t q e", b=2, t=4, e=8),
+                w3_raw[:].rearrange("p (b q t e) -> p b t q e", b=2, t=4, e=8),
+            )
+            nc.vector.tensor_copy(
+                ws_p[:].rearrange("p w (b t q e) -> p (w b) t q e", b=2, t=4, e=2),
+                ws_raw[:].rearrange("p w (b q t e) -> p (w b) t q e", b=2, t=4, e=2),
+            )
 
-        def weight(l, u):
-            cols = slice(u * P, (u + 1) * P)
+        def weight(l, b, t):
+            u = 4 * b + t
             if l == 0:
-                return w1_q[:, cols].bitcast(FP8X4), w1_s[:, cols]
+                return w1_q[b][:, t * P : (t + 1) * P].bitcast(FP8X4), w1_s[b][:, t * P : (t + 1) * P]
             scale = ws_p[:, l - 1, u * 32 : (u + 1) * 32].bitcast(U8)
             if l == 1:
                 return w2_p[:, u * 64 : (u + 1) * 64].bitcast(U8).bitcast(FP4X4), scale
-            return w3_p[:, cols].bitcast(FP8X4), scale
+            return w3_p[:, u * P : (u + 1) * P].bitcast(FP8X4), scale
 
-        def project(dst, ls, u, tok):
+        def project(dst, ls, b, t, lo, hi):
             for n, l in enumerate(ls):
-                codes, scale = weight(l, u)
+                codes, scale = weight(l, b, t)
                 nc.tensor.matmul_mx(
                     dst,
                     lhsT=codes,
                     lhsT_scale=scale,
-                    rhs=v_words[l, tok.start // HALF][:, tok.start % HALF : (tok.stop - 1) % HALF + 1].bitcast(FP8X4),
-                    rhs_scale=v_scales[l][:, tok],
+                    rhs=v_words[l, lo // HALF][:, lo % HALF : lo % HALF + hi - lo].bitcast(FP8X4),
+                    rhs_scale=v_scales[l][:, lo:hi],
                     start=(n == 0),
                     stop=(n == len(ls) - 1),
                 )
 
-        h_q = keep.tile([P, 4, 2, SEG], U32, align_bytes=64)
-        h_s = {}
-        x_all = keep.tile([P, X_SLOTS, 2, SEG], F32, align_bytes=64)
-        side_all = keep.tile([P, 2, 4, SEG], F32, align_bytes=64)
-        res_all = keep.tile([P, 4, 3, SEG], F32, align_bytes=64)
-        both_all = [
-            keep.tile([P, 2, 4, SEG], F32, align_bytes=64, name=f"arms{k}", tag=("cast1", "cast0", "arms")[k]) for k in range(3)
-        ]
-        state = {}
-
-        def part(seg, b):
-            return 1 if b == 0 else 2 * (seg % 2)
-
-        def slot(seg, b):
-            return part(seg, b) - seg % 2
-
-        def seg_tok(seg):
-            return slice(seg * SEG, (seg + 1) * SEG)
-
-        def centre(seg, b, tp):
-            bank = take_bank()[:].rearrange("p (e n) -> p e n", e=2)
-            for e in range(2):
-                project(bank[:, e, :], [0], 4 * b + 2 * tp + e, seg_tok(seg))
-            k = 2 * (seg + b + (seg > 0)) + tp
-            xg = [x_all[:, k % X_SLOTS, e] for e in range(2)]
-            if seg > 0 and tp == (seg < 3):
-                xg[0] = keep.tile([P, SEG], F32, align_bytes=64, name=f"xg_tie{seg}", tag=f"tie{seg - 1}")[:]
-                if seg == 3:
-                    xg[1] = keep.tile([P, SEG], F32, align_bytes=64, name="xg_tie_last", tag="tie3")[:]
-            for e in range(2):
-                u = 4 * b + 2 * tp + e
-                nc.scalar.activation(xg[e], bank[:, e, :], COPY, scale=g_col[:, u : u + 1])
-            state["x", seg, b, tp] = xg
-
-        def once_pair(seg, b, tp):
-            if tp == 0:
-                both = both_all[0 if seg + b == 0 else 1 + (seg + 1) % 2]
-                state["d1", seg, b], state["d2", seg, b] = both[:, 0], both[:, 1]
-            d1, d2 = state["d1", seg, b], state["d2", seg, b]
-            xg = state["x", seg, b, tp]
-            arms = [take_bank()[:].rearrange("p (e n) -> p e n", e=2) for l in range(2)]
-            for l in range(2):
-                for e in range(2):
-                    project(arms[l][:, e, :], [l + 1], 4 * b + 2 * tp + e, seg_tok(seg))
-            for e in range(2):
-                u = 4 * b + 2 * tp + e
-                nc.vector.scalar_tensor_tensor(
-                    d1[:, 2 * tp + e, :], arms[0][:, e, :], g_col[:, u : u + 1], xg[e], MULT, ADD
-                )
-            for e in range(2):
-                u = 4 * b + 2 * tp + e
-                nc.vector.scalar_tensor_tensor(
-                    d2[:, 2 * tp + e, :], xg[e], g_inv[:, u : u + 1], arms[1][:, e, :], MULT, ADD
-                )
-
-        def interleaved(ap):
-            return ap.rearrange("p t (c i) -> p c t i", i=2)
-
-        def h_view(seg, b, lo, hi):
-            return h_bf[:, part(seg, b), lo:hi, :].rearrange("p (c i) t -> p c t i", i=2)
-
-        def once_final(engine, seg, b, lo, hi):
-            engine.tensor_tensor(
-                h_view(seg, b, lo, hi),
-                interleaved(state["d1", seg, b][:, :, lo:hi]),
-                interleaved(state["d2", seg, b][:, :, lo:hi]),
-                MULT,
-            )
-
-        def twice_side(seg, b, tp):
-            if tp == 0:
-                state["d2", seg, b] = side_all[:, seg % 2]
-            d2 = state["d2", seg, b]
-            bank = take_bank()[:].rearrange("p (e n) -> p e n", e=2)
-            for e in range(2):
-                project(bank[:, e, :], [0, 2], 4 * b + 2 * tp + e, seg_tok(seg))
-            for e in range(2):
-                u = 4 * b + 2 * tp + e
-                nc.scalar.activation(d2[:, 2 * tp + e, :], bank[:, e, :], COPY, scale=g_col[:, u : u + 1])
-
-        def twice_final(seg, b, c):
-            bank = take_bank()[:].rearrange("p (t n) -> p t n", t=4)
-            tok = slice(seg * SEG + c * CHUNK, seg * SEG + (c + 1) * CHUNK)
-            for t in range(4):
-                project(bank[:, t, :], [0, 1], 4 * b + t, tok)
-            nc.vector.tensor_tensor(
-                h_view(seg, b, c * CHUNK, (c + 1) * CHUNK),
-                interleaved(bank),
-                interleaved(state["d2", seg, b][:, :, c * CHUNK : (c + 1) * CHUNK]),
-                MULT,
-            )
-
-        def quant_seg(seg):
-            first = seg % 2
-            h_s[seg] = keep.tile([P, 2, SEG], U8, align_bytes=64, name=f"h_s{seg}", tag=f"tie{seg}")
-            nc.vector.quantize_mx(
-                h_q[:, seg].rearrange("p b n -> p (b n)").bitcast(FP8X4),
-                h_s[seg][:].rearrange("p b n -> p (b n)"),
-                h_bf[:, first : first + 2].rearrange("p b n t -> p (b n t)"),
-            )
-
-        def quant_part(seg, b, lo, hi):
-            if seg not in h_s:
-                h_s[seg] = keep.tile([P, 2, SEG], U8, align_bytes=64, name=f"h_s{seg}", tag="tie3")
-            nc.vector.quantize_mx(
-                h_q[:, seg, slot(seg, b), lo:hi].bitcast(FP8X4),
-                h_s[seg][:, slot(seg, b), lo:hi],
-                h_bf[:, part(seg, b), lo:hi, :].rearrange("p n t -> p (n t)"),
-            )
-
         out_view = out.rearrange("(m p) s -> p m s", p=P)
 
-        def mix_pass(dst, seg, c, m, b, start, stop):
-            tok = slice(c * CHUNK, (c + 1) * CHUNK)
-            cols = slice(b * N + m * P, b * N + (m + 1) * P)
-            nc.tensor.matmul_mx(
-                dst,
-                lhsT=late["w4_q"][:, cols].bitcast(FP8X4),
-                lhsT_scale=w4_s[:, cols],
-                rhs=h_q[:, seg, slot(seg, b), tok].bitcast(FP8X4),
-                rhs_scale=h_s[seg][:, slot(seg, b), tok],
-                start=start,
-                stop=stop,
+        def gain(col, b, t):
+            return col[:, 4 * b + t : 4 * b + t + 1]
+
+        def scaled_read(ls, b, ts, lo, hi, dst):
+            bank = scalar_bank()[:].rearrange("p (e n) -> p e n", e=len(ts))
+            for e, t in enumerate(ts):
+                project(bank[:, e, :], ls, b, t, lo, hi)
+            for e, t in enumerate(ts):
+                nc.scalar.activation(dst[:, e, :], bank[:, e, :], COPY, scale=gain(g_col, b, t))
+
+        def centre(b, ts, lo, hi, tag=None):
+            if ts[0] % 2 == 0:
+                state["xx"] = sb([P, 2, hi - lo], F32, f"x{b}_{ts[0]}_{lo}", tag)
+            x = state["xx"][:, ts[0] % 2 : ts[-1] % 2 + 1, :]
+            state["x", b, ts[0], lo] = x
+            scaled_read([0], b, ts, lo, hi, x)
+
+        def arms(b, ts, lo, hi, tag=None):
+            if ts[0] == 0:
+                state["d", b, lo] = sb([P, 2, 4, hi - lo], F32, f"d{b}_{lo}", tag)
+            d, x = state["d", b, lo], state["x", b, ts[0], lo]
+            pair = [shared_bank()[:].rearrange("p (e n) -> p e n", e=len(ts)) for l in range(2)]
+            for l in range(2):
+                for e, t in enumerate(ts):
+                    project(pair[l][:, e, :], [l + 1], b, t, lo, hi)
+            for e, t in enumerate(ts):
+                nc.vector.scalar_tensor_tensor(d[:, 0, t, :], pair[0][:, e, :], gain(g_col, b, t), x[:, e, :], MULT, ADD)
+            for e, t in enumerate(ts):
+                nc.vector.scalar_tensor_tensor(d[:, 1, t, :], x[:, e, :], gain(g_inv, b, t), pair[1][:, e, :], MULT, ADD)
+
+        def woven(ap):
+            return ap.rearrange("p t (c i) -> p c t i", i=2)
+
+        def h_view(ap):
+            return ap.rearrange("p (c i) t -> p c t i", i=2)
+
+        ha_bf = [sb([P, HALF, 4], BF16, f"ha_bf{b}") for b in range(2)]
+        ha_q = sb([P, 2, HALF], U32, "ha_q")
+        hc_bf = {c: sb([P, 2, CHUNK, 4], BF16, f"hc_bf{c}") for c in range(4, 8)}
+        hc_q = {c: sb([P, 2, CHUNK], U32, f"hc_q{c}") for c in range(4, 8)}
+        side = {1: sb([P, 4, HALF], F32, "side1"), 0: sb([P, 4, HALF // 2], F32, "side0")}
+        side_lo = {1: HALF, 0: HALF + HALF // 2}
+        res = sb([P, 3, S], F32, "res")
+
+        def h_dst(b, c):
+            return ha_bf[b][:, c * CHUNK : (c + 1) * CHUNK, :] if c < 4 else hc_bf[c][:, b]
+
+        def product(engine, b, lo, c):
+            d = state["d", b, lo]
+            cols = slice(c * CHUNK - lo, (c + 1) * CHUNK - lo)
+            engine.tensor_tensor(h_view(h_dst(b, c)), woven(d[:, 0, :, cols]), woven(d[:, 1, :, cols]), MULT)
+
+        def second_arm(b, ts):
+            scaled_read([0, 2], b, ts, side_lo[b], S, side[b][:, ts[0] : ts[-1] + 1, :])
+
+        def first_arm(b, c):
+            bank = shared_bank()[:].rearrange("p (t n) -> p t n", t=4)
+            for t in range(4):
+                project(bank[:, t, :], [0, 1], b, t, c * CHUNK, (c + 1) * CHUNK)
+            cols = slice(c * CHUNK - side_lo[b], (c + 1) * CHUNK - side_lo[b])
+            nc.vector.tensor_tensor(h_view(h_dst(b, c)), woven(bank), woven(side[b][:, :, cols]), MULT)
+
+        def quant_a(b, lo, hi, tag):
+            plane = sb([P, hi - lo], U8, f"ha_s{b}_{lo}", tag)
+            for at in range(lo, hi, 256):
+                state["s", b, at] = plane[:, at - lo : at - lo + 256]
+            nc.vector.quantize_mx(
+                ha_q[:, b, lo:hi].bitcast(FP8X4), plane[:], ha_bf[b][:, lo:hi, :].rearrange("p n t -> p (n t)")
             )
 
-        def last_open(c):
-            for m in range(3):
-                state["y", c, m] = take_bank()
-                mix_pass(state["y", c, m][:, 0:CHUNK], 3, c, m, 1, True, False)
-
-        def last_close(c):
-            cols = slice(c * CHUNK, (c + 1) * CHUNK)
-            for m in range(3):
-                mix_pass(state["y", c, m][:, 0:CHUNK], 3, c, m, 0, False, True)
-                nc.scalar.activation(res_all[:, 3, m, cols], state["y", c, m][:, 0:CHUNK], TANH)
-            nc.sync.dma_start(out_view[:, :, 3 * SEG + cols.start : 3 * SEG + cols.stop], res_all[:, 3, :, cols])
-
-        def mix(seg, c, store):
-            tok = slice(c * CHUNK, (c + 1) * CHUNK)
-            bank = take_bank()
-            for m in range(3):
-                for b in range(2):
-                    cols = slice(b * N + m * P, b * N + (m + 1) * P)
-                    nc.tensor.matmul_mx(
-                        bank[:, m * CHUNK : (m + 1) * CHUNK],
-                        lhsT=late["w4_q"][:, cols].bitcast(FP8X4),
-                        lhsT_scale=w4_s[:, cols],
-                        rhs=h_q[:, seg, slot(seg, b), tok].bitcast(FP8X4),
-                        rhs_scale=h_s[seg][:, slot(seg, b), tok],
-                        start=(b == 0),
-                        stop=(b == 1),
-                    )
-            res = res_all[:, seg]
-            nc.scalar.activation(
-                res[:, :, c * CHUNK : (c + 1) * CHUNK], bank[:, 0 : 3 * CHUNK].rearrange("p (m s) -> p m s", m=3), TANH
+        def quant_c(c, tag=None):
+            plane = sb([P, 2, CHUNK], U8, f"hc_s{c}", tag)
+            for b in range(2):
+                state["s", b, c * CHUNK] = plane[:, b]
+            nc.vector.quantize_mx(
+                hc_q[c][:].rearrange("p b n -> p (b n)").bitcast(FP8X4),
+                plane[:].rearrange("p b n -> p (b n)"),
+                hc_bf[c][:].rearrange("p b n t -> p (b n t)"),
             )
-            if store is not None:
-                lo, hi = store
-                nc.sync.dma_start(out_view[:, :, seg * SEG + lo : seg * SEG + hi], res[:, :, lo:hi])
 
-        centre(0, 0, 0)
-        centre(0, 0, 1)
-        centre(1, 0, 0)
-        cast_w1(1)
+        def mix(lo, hi):
+            width = hi - lo
+            for ms in ([0, 1, 2],) if width == CHUNK else ([0, 1], [2]):
+                bank = shared_bank()[:, 0 : len(ms) * width].rearrange("p (m s) -> p m s", m=len(ms))
+                for e, m in enumerate(ms):
+                    for b in range(2):
+                        cols = slice(b * N + m * P, b * N + (m + 1) * P)
+                        codes = ha_q[:, b, lo:hi] if lo < HALF else hc_q[lo // CHUNK][:, b]
+                        nc.tensor.matmul_mx(
+                            bank[:, e, :],
+                            lhsT=w4_q[:, cols].bitcast(FP8X4),
+                            lhsT_scale=w4_s[:, cols],
+                            rhs=codes.bitcast(FP8X4),
+                            rhs_scale=state["s", b, lo],
+                            start=(b == 0),
+                            stop=(b == 1),
+                        )
+                nc.scalar.activation(res[:, ms[0] : ms[-1] + 1, lo:hi], bank, TANH)
+            nc.sync.dma_start(out_view[:, :, lo:hi], res[:, :, lo:hi])
+
+        cast_w1(0)
         for l in range(3):
-            gather_words(1, l)
+            gather_words(0, l)
+        gather_words(1, 0)
+        quant_w1(0)
+        deal_packed()
+        cast_w1(1)
+        for t in range(4):
+            centre(0, [t], 0, HALF, "w1_raw1" if t == 0 else None)
+        gather_words(1, 1, "w1_bf0")
+        gather_words(1, 2, "w3_raw")
         quant_w1(1)
-        once_pair(0, 0, 0)
-        cast_w4(0, 0, N)
-        centre(0, 1, 0)
-        centre(0, 1, 1)
-        once_pair(0, 0, 1)
-        once_final(nc.gpsimd, 0, 0, 0, SEG)
-        cast_w4(1, 0, P)
-        cast_w4(1, P, N)
-        twice_side(1, 1, 0)
-        once_pair(0, 1, 0)
-        twice_side(1, 1, 1)
-        once_pair(0, 1, 1)
+        cast_w4(0)
+        cast_w4(1)
+        for t in range(4):
+            arms(0, [t], 0, HALF, "w1_bf1")
+            centre(1, [t], 0, HALF)
+        for c in range(4):
+            product(nc.gpsimd, 0, 0, c)
+        for t in range(4):
+            arms(1, [t], 0, HALF)
+            second_arm(1, [t])
+        second_arm(0, [0, 1])
+        second_arm(0, [2, 3])
+        for c in range(4):
+            product(nc.gpsimd, 1, 0, c)
         quant_w4()
-        once_final(nc.gpsimd, 0, 1, 0, SEG)
-        centre(1, 0, 1)
-        for seg in range(1, 4):
-            twice_final(seg, 1, 0)
-            if seg < 3:
-                centre(seg + 1, 0, 0)
-            twice_final(seg, 1, 1)
-            if seg > 1:
-                mix(seg - 2, 0, None)
-            once_pair(seg, 0, 0)
-            if seg < 3:
-                twice_side(seg + 1, 1, 0)
-            if seg > 1:
-                mix(seg - 2, 1, (0, SEG))
-            if seg < 3:
-                once_pair(seg, 0, 1)
-                quant_seg(seg - 1)
-                once_final(nc.gpsimd, seg, 0, 0, SEG)
-                twice_side(seg + 1, 1, 1)
-                centre(seg + 1, 0, 1)
-        quant_seg(2)
-        quant_part(3, 1, 0, SEG)
-        once_pair(3, 0, 1)
-        mix(2, 0, None)
-        mix(2, 1, (0, SEG))
-        last_open(0)
-        last_open(1)
-        once_final(nc.vector, 3, 0, 0, CHUNK)
-        once_final(nc.vector, 3, 0, CHUNK, SEG)
-        quant_part(3, 0, 0, CHUNK)
-        last_close(0)
-        quant_part(3, 0, CHUNK, SEG)
-        last_close(1)
+        centre(0, [0, 1], HALF, HALF + 256)
+        centre(0, [2, 3], HALF, HALF + 256)
+        first_arm(1, 6)
+        first_arm(0, 6)
+        first_arm(1, 7)
+        quant_c(6)
+        first_arm(0, 7)
+        mix(6 * CHUNK, 7 * CHUNK)
+        quant_a(0, 0, HALF, "hc_bf6")
+        first_arm(1, 4)
+        quant_c(7)
+        first_arm(1, 5)
+        mix(7 * CHUNK, 8 * CHUNK)
+        arms(0, [0, 1], HALF, HALF + 256)
+        arms(0, [2, 3], HALF, HALF + 256)
+        quant_a(1, 0, 256, "x0_0_512")
+        mix(0, 256)
+        product(nc.gpsimd, 0, HALF, 4)
+        quant_a(1, 256, HALF, "x0_2_512")
+        product(nc.vector, 0, HALF, 5)
+        mix(256, HALF)
+        quant_c(5)
+        mix(5 * CHUNK, 6 * CHUNK)
+        quant_c(4, "hc_bf5")
+        mix(4 * CHUNK, 5 * CHUNK)

@@ -37,11 +37,11 @@ def tile_list_bond_angle_features_kernel(
 
         def scalar_bank():
             turns["scalar"].append(0)
-            return banks[len(turns["scalar"]) % 2]
+            return banks[len(turns["scalar"]) % 3]
 
         def shared_bank():
             turns["shared"].append(0)
-            return banks[2 + len(turns["shared"]) % 6]
+            return banks[3 + len(turns["shared"]) % 5]
 
         def sb(shape, dtype, name, tag=None):
             return keep.tile(shape, dtype, align_bytes=64, name=name, tag=tag or name)
@@ -108,10 +108,9 @@ def tile_list_bond_angle_features_kernel(
             if l == 1:
                 nc.vector.reciprocal(g_inv[:], g_safe[:])
 
-        def gather_words(half, l, tag=None):
-            v_words[l, half] = sb([P, HALF], U32, f"v_words{l}_{half}", tag)
-            offsets = lists[l][:, half * HALF // 16 : (half + 1) * HALF // 16]
-            nc.vector.tensor_copy(v_words[l, half][:], tab_w[:].bitcast(U32).indirect(offsets))
+        def gather_words(l, tag=None):
+            v_words[l] = sb([P, S], U32, f"v_words{l}", tag)
+            nc.vector.tensor_copy(v_words[l][:], tab_w[:].bitcast(U32).indirect(lists[l][:]))
 
         w1_bf = [sb([P, 4, 16, 8, 4], BF16, f"w1_bf{b}") for b in range(2)]
         w1_q = [sb([P, H // 2], U32, f"w1_q{b}") for b in range(2)]
@@ -129,19 +128,18 @@ def tile_list_bond_angle_features_kernel(
 
         w4_bf = sb([P, 2 * N, 4], BF16, "w4_bf")
         w4_q = sb([P, 2 * N], U32, "w4_q")
-        w4_s = sb([P, 2 * N], U8, "w4_s")
+        late = {}
 
         def cast_w4(b):
-            nc.gpsimd.tensor_scalar(
+            nc.scalar.activation(
                 w4_bf[:, b * N : (b + 1) * N, :].rearrange("p (c i) t -> p c t i", i=2),
                 w4_raw[b][:].rearrange("p t (c i) -> p c t i", i=2),
-                1.0,
-                0.0,
-                MULT,
-                ADD,
+                COPY,
             )
 
-        def quant_w4():
+        def quant_w4(tag):
+            w4_s = sb([P, 2 * N], U8, "w4_s", tag)
+            late["w4_s"] = w4_s
             for lo, hi in ((0, 512), (512, 768)):
                 nc.vector.quantize_mx(
                     w4_q[:, lo:hi].bitcast(FP8X4), w4_s[:, lo:hi], w4_bf[:, lo:hi, :].rearrange("p n t -> p (n t)")
@@ -181,7 +179,7 @@ def tile_list_bond_angle_features_kernel(
                     dst,
                     lhsT=codes,
                     lhsT_scale=scale,
-                    rhs=v_words[l, lo // HALF][:, lo % HALF : lo % HALF + hi - lo].bitcast(FP8X4),
+                    rhs=v_words[l][:, lo:hi].bitcast(FP8X4),
                     rhs_scale=v_scales[l][:, lo:hi],
                     start=(n == 0),
                     stop=(n == len(ls) - 1),
@@ -200,9 +198,9 @@ def tile_list_bond_angle_features_kernel(
                 nc.scalar.activation(dst[:, e, :], bank[:, e, :], COPY, scale=gain(g_col, b, t))
 
         def centre(b, ts, lo, hi, tag=None):
-            if ts[0] % 2 == 0:
-                state["xx"] = sb([P, 2, hi - lo], F32, f"x{b}_{ts[0]}_{lo}", tag)
-            x = state["xx"][:, ts[0] % 2 : ts[-1] % 2 + 1, :]
+            if ts[0] == 0:
+                state["xx", b, lo] = sb([P, 4, hi - lo], F32, f"x{b}_{lo}", tag)
+            x = state["xx", b, lo][:, ts[0] : ts[-1] + 1, :]
             state["x", b, ts[0], lo] = x
             scaled_read([0], b, ts, lo, hi, x)
 
@@ -225,16 +223,20 @@ def tile_list_bond_angle_features_kernel(
         def h_view(ap):
             return ap.rearrange("p (c i) t -> p c t i", i=2)
 
-        ha_bf = [sb([P, HALF, 4], BF16, f"ha_bf{b}") for b in range(2)]
-        ha_q = sb([P, 2, HALF], U32, "ha_q")
-        hc_bf = {c: sb([P, 2, CHUNK, 4], BF16, f"hc_bf{c}") for c in range(4, 8)}
-        hc_q = {c: sb([P, 2, CHUNK], U32, f"hc_q{c}") for c in range(4, 8)}
+        h_bf = {}
+        h_q = sb([P, 2, S], U32, "h_q")
         side = {1: sb([P, 4, HALF], F32, "side1"), 0: sb([P, 4, HALF // 2], F32, "side0")}
         side_lo = {1: HALF, 0: HALF + HALF // 2}
         res = sb([P, 3, S], F32, "res")
 
+        def stage(b, lo, hi, tag=None):
+            tile = sb([P, hi - lo, 4], BF16, f"h_bf{b}_{lo}", tag)
+            for c in range(lo // CHUNK, hi // CHUNK):
+                h_bf[b, c] = (tile, lo)
+
         def h_dst(b, c):
-            return ha_bf[b][:, c * CHUNK : (c + 1) * CHUNK, :] if c < 4 else hc_bf[c][:, b]
+            tile, lo = h_bf[b, c]
+            return tile[:, c * CHUNK - lo : (c + 1) * CHUNK - lo, :]
 
         def product(engine, b, lo, c):
             d = state["d", b, lo]
@@ -251,22 +253,12 @@ def tile_list_bond_angle_features_kernel(
             cols = slice(c * CHUNK - side_lo[b], (c + 1) * CHUNK - side_lo[b])
             nc.vector.tensor_tensor(h_view(h_dst(b, c)), woven(bank), woven(side[b][:, :, cols]), MULT)
 
-        def quant_a(b, lo, hi, tag):
-            plane = sb([P, hi - lo], U8, f"ha_s{b}_{lo}", tag)
-            for at in range(lo, hi, 256):
-                state["s", b, at] = plane[:, at - lo : at - lo + 256]
+        def quant(b, lo, hi, tag=None):
+            plane = sb([P, hi - lo], U8, f"h_s{b}_{lo}", tag)
+            for at in range(lo, hi, CHUNK):
+                state["s", b, at] = (plane, lo)
             nc.vector.quantize_mx(
-                ha_q[:, b, lo:hi].bitcast(FP8X4), plane[:], ha_bf[b][:, lo:hi, :].rearrange("p n t -> p (n t)")
-            )
-
-        def quant_c(c, tag=None):
-            plane = sb([P, 2, CHUNK], U8, f"hc_s{c}", tag)
-            for b in range(2):
-                state["s", b, c * CHUNK] = plane[:, b]
-            nc.vector.quantize_mx(
-                hc_q[c][:].rearrange("p b n -> p (b n)").bitcast(FP8X4),
-                plane[:].rearrange("p b n -> p (b n)"),
-                hc_bf[c][:].rearrange("p b n t -> p (b n t)"),
+                h_q[:, b, lo:hi].bitcast(FP8X4), plane[:], h_bf[b, lo // CHUNK][0][:].rearrange("p n t -> p (n t)")
             )
 
         def mix(lo, hi):
@@ -276,13 +268,13 @@ def tile_list_bond_angle_features_kernel(
                 for e, m in enumerate(ms):
                     for b in range(2):
                         cols = slice(b * N + m * P, b * N + (m + 1) * P)
-                        codes = ha_q[:, b, lo:hi] if lo < HALF else hc_q[lo // CHUNK][:, b]
+                        plane, at = state["s", b, lo]
                         nc.tensor.matmul_mx(
                             bank[:, e, :],
                             lhsT=w4_q[:, cols].bitcast(FP8X4),
-                            lhsT_scale=w4_s[:, cols],
-                            rhs=codes.bitcast(FP8X4),
-                            rhs_scale=state["s", b, lo],
+                            lhsT_scale=late["w4_s"][:, cols],
+                            rhs=h_q[:, b, lo:hi].bitcast(FP8X4),
+                            rhs_scale=plane[:, lo - at : hi - at],
                             start=(b == 0),
                             stop=(b == 1),
                         )
@@ -290,54 +282,71 @@ def tile_list_bond_angle_features_kernel(
             nc.sync.dma_start(out_view[:, :, lo:hi], res[:, :, lo:hi])
 
         cast_w1(0)
-        for l in range(3):
-            gather_words(0, l)
-        gather_words(1, 0)
+        gather_words(0)
+        gather_words(1)
         quant_w1(0)
         deal_packed()
         cast_w1(1)
-        for t in range(4):
-            centre(0, [t], 0, HALF, "w1_raw1" if t == 0 else None)
-        gather_words(1, 1, "w1_bf0")
-        gather_words(1, 2, "w3_raw")
+        centre(0, [0, 1], 0, 256, "w1_raw1")
+        centre(0, [2, 3], 0, 256)
+        gather_words(2, "w1_bf0")
         quant_w1(1)
-        cast_w4(0)
-        cast_w4(1)
-        for t in range(4):
-            arms(0, [t], 0, HALF, "w1_bf1")
-            centre(1, [t], 0, HALF)
-        for c in range(4):
+        arms(0, [0, 1], 0, 256, "w1_bf1")
+        centre(1, [0], 0, HALF)
+        arms(0, [2, 3], 0, 256)
+        centre(1, [1], 0, HALF)
+        stage(0, 0, 256)
+        for c in range(2):
             product(nc.gpsimd, 0, 0, c)
         for t in range(4):
             arms(1, [t], 0, HALF)
-            second_arm(1, [t])
-        second_arm(0, [0, 1])
-        second_arm(0, [2, 3])
+            if t < 2:
+                centre(1, [t + 2], 0, HALF)
+            else:
+                centre(0, [t - 2], 256, 768)
+        stage(1, 0, HALF)
         for c in range(4):
             product(nc.gpsimd, 1, 0, c)
-        quant_w4()
-        centre(0, [0, 1], HALF, HALF + 256)
-        centre(0, [2, 3], HALF, HALF + 256)
-        first_arm(1, 6)
+        cast_w4(0)
+        arms(0, [0], 256, 768)
+        centre(0, [2], 256, 768)
+        centre(0, [3], 256, 768)
+        arms(0, [1], 256, 768)
+        second_arm(0, [0, 1])
+        second_arm(0, [2, 3])
+        arms(0, [2], 256, 768)
+        second_arm(1, [0])
+        second_arm(1, [1])
+        arms(0, [3], 256, 768)
+        second_arm(1, [2])
+        second_arm(1, [3])
+        cast_w4(1)
+        stage(0, 256, 384)
+        product(nc.gpsimd, 0, 256, 2)
+        stage(0, 768, S)
+        stage(1, HALF, S)
         first_arm(0, 6)
-        first_arm(1, 7)
-        quant_c(6)
         first_arm(0, 7)
-        mix(6 * CHUNK, 7 * CHUNK)
-        quant_a(0, 0, HALF, "hc_bf6")
-        first_arm(1, 4)
-        quant_c(7)
-        first_arm(1, 5)
-        mix(7 * CHUNK, 8 * CHUNK)
-        arms(0, [0, 1], HALF, HALF + 256)
-        arms(0, [2, 3], HALF, HALF + 256)
-        quant_a(1, 0, 256, "x0_0_512")
+        for c in (6, 7, 4, 5):
+            first_arm(1, c)
+        quant_w4("side0")
+        quant(0, 0, 256, "side1")
+        quant(1, 0, HALF, "w4_bf")
         mix(0, 256)
-        product(nc.gpsimd, 0, HALF, 4)
-        quant_a(1, 256, HALF, "x0_2_512")
-        product(nc.vector, 0, HALF, 5)
-        mix(256, HALF)
-        quant_c(5)
-        mix(5 * CHUNK, 6 * CHUNK)
-        quant_c(4, "hc_bf5")
-        mix(4 * CHUNK, 5 * CHUNK)
+        quant(0, 768, S, "h_bf0_0")
+        quant(1, HALF, S, "h_bf1_0")
+        mix(768, S)
+        stage(0, 384, HALF, "h_bf0_768")
+        product(nc.vector, 0, 256, 3)
+        quant(0, 256, 384, "h_bf1_512")
+        mix(256, 384)
+        stage(0, HALF, 640, "h_bf0_256")
+        product(nc.vector, 0, 256, 4)
+        quant(0, 384, HALF)
+        mix(384, HALF)
+        stage(0, 640, 768, "h_bf0_768")
+        product(nc.vector, 0, 256, 5)
+        quant(0, HALF, 640)
+        mix(HALF, 640)
+        quant(0, 640, 768)
+        mix(640, 768)

@@ -57,7 +57,6 @@ def tile_list_bond_angle_features_kernel(
         g_rows = sb([P, P], F32, "g_rows")
         ident = sb([P, P], F32, "ident")
         g_col = sb([P, 8], F32, "g_col")
-        g_safe = sb([P, 8], F32, "g_safe")
         g_inv = sb([P, 8], F32, "g_inv")
         warm = sb([P, 8], F32, "warm")
         warm2 = sb([P, 8], F32, "warm2")
@@ -82,16 +81,16 @@ def tile_list_bond_angle_features_kernel(
         for r in range(4):
             nc.sync.dma_start(tab_s[r:P:32, :], tab_scales[0, r:16:4, :].bitcast(I32))
         nc.sync.dma_start(lists[1][:], offs2)
-        for b in range(2):
-            nc.sync.dma_start(g_rows[4 * b : 4 * b + 4, :].rearrange("t (q i) -> t q i", i=8), g_view[b])
         nc.sync.dma_start(lists[2][:], offs3)
         nc.sync.dma_start(tab_w[:], tab_words[0].rearrange("p t i -> p (t i)").bitcast(I32))
+        for b in range(2):
+            nc.sync.dma_start(g_rows[4 * b : 4 * b + 4, :].rearrange("t (q i) -> t q i", i=8), g_view[b])
+        load_scale_rows(0, w2_scales, range(4))
         nc.sync.dma_start(w1_raw[0][:], w1_rows[0])
         nc.sync.dma_start(w2_raw[:], w2_words[0].bitcast(I32))
-        nc.sync.dma_start(w3_raw[:], w3_words[0].rearrange("p e i -> p (e i)").bitcast(I32))
-        load_scale_rows(0, w2_scales, range(4))
-        nc.sync.dma_start(w1_raw[1][:], w1_rows[1])
         load_scale_rows(1, w3_scales, range(4))
+        nc.sync.dma_start(w3_raw[:], w3_words[0].rearrange("p e i -> p (e i)").bitcast(I32))
+        nc.sync.dma_start(w1_raw[1][:], w1_rows[1])
         for u in range(8):
             nc.sync.dma_start(w4_raw[u // 4][:, u % 4, :], w4_view[u // 4, u % 4])
 
@@ -103,25 +102,25 @@ def tile_list_bond_angle_features_kernel(
         nc.scalar.copy(g_col[:], g_bank[:, 0:8])
         for l in range(3):
             nc.vector.tensor_copy(v_scales[l][:], tab_s[:].bitcast(U8).indirect(lists[l][:]))
-            if l == 0:
-                nc.vector.scalar_tensor_tensor(g_safe[:], g_col[:], 0.0, g_col[:], IS_EQUAL, ADD)
-            if l == 1:
-                nc.vector.reciprocal(g_inv[:], g_safe[:])
 
-        def gather_words(l, tag=None):
+        def gather_words(l, pieces, tag=None):
             v_words[l] = sb([P, S], U32, f"v_words{l}", tag)
-            nc.vector.tensor_copy(v_words[l][:], tab_w[:].bitcast(U32).indirect(lists[l][:]))
+            width = S // pieces
+            for lo in range(0, S, width):
+                offsets = lists[l][:, lo // 16 : (lo + width) // 16]
+                nc.vector.tensor_copy(v_words[l][:, lo : lo + width], tab_w[:].bitcast(U32).indirect(offsets))
 
         w1_bf = [sb([P, 4, 16, 8, 4], BF16, f"w1_bf{b}") for b in range(2)]
         w1_q = [sb([P, H // 2], U32, f"w1_q{b}") for b in range(2)]
-        w1_s = [sb([P, H // 2], U8, f"w1_s{b}") for b in range(2)]
+        w1_s = {}
 
         def cast_w1(b):
             src = w1_raw[b][:].rearrange("p j (q t i) -> p t q j i", t=4, i=8)
             for t in range(4):
                 nc.scalar.activation(w1_bf[b][:, t].rearrange("p q i j -> p q j i"), src[:, t], COPY, scale=-1.0)
 
-        def quant_w1(b):
+        def quant_w1(b, tag=None):
+            w1_s[b] = sb([P, H // 2], U8, f"w1_s{b}", tag)
             nc.vector.quantize_mx(
                 w1_q[b][:].bitcast(FP8X4), w1_s[b][:], w1_bf[b][:].rearrange("p t q i j -> p (t q i j)")
             )
@@ -198,9 +197,9 @@ def tile_list_bond_angle_features_kernel(
                 nc.scalar.activation(dst[:, e, :], bank[:, e, :], COPY, scale=gain(g_col, b, t))
 
         def centre(b, ts, lo, hi, tag=None):
-            if ts[0] == 0:
-                state["xx", b, lo] = sb([P, 4, hi - lo], F32, f"x{b}_{lo}", tag)
-            x = state["xx", b, lo][:, ts[0] : ts[-1] + 1, :]
+            if ts[0] == 0 and lo == 0:
+                state["xx", b] = sb([P, 4, side_lo[b]], F32, f"x{b}", tag)
+            x = state["xx", b][:, ts[0] : ts[-1] + 1, lo:hi]
             state["x", b, ts[0], lo] = x
             scaled_read([0], b, ts, lo, hi, x)
 
@@ -282,32 +281,25 @@ def tile_list_bond_angle_features_kernel(
             nc.sync.dma_start(out_view[:, :, lo:hi], res[:, :, lo:hi])
 
         cast_w1(0)
-        gather_words(0)
-        gather_words(1)
+        gather_words(0, 1)
+        g_safe = sb([P, 8], F32, "g_safe", "tab_s")
+        nc.vector.scalar_tensor_tensor(g_safe[:], g_col[:], 0.0, g_col[:], IS_EQUAL, ADD)
+        gather_words(1, 1)
+        nc.vector.reciprocal(g_inv[:], g_safe[:])
         quant_w1(0)
         deal_packed()
         cast_w1(1)
         centre(0, [0, 1], 0, 256, "w1_raw1")
         centre(0, [2, 3], 0, 256)
-        gather_words(2, "w1_bf0")
+        gather_words(2, 1, "w1_bf0")
         quant_w1(1)
+        centre(0, [0], 256, 768)
         arms(0, [0, 1], 0, 256, "w1_bf1")
-        centre(1, [0], 0, HALF)
+        centre(0, [1], 256, 768)
         arms(0, [2, 3], 0, 256)
-        centre(1, [1], 0, HALF)
         stage(0, 0, 256)
         for c in range(2):
             product(nc.gpsimd, 0, 0, c)
-        for t in range(4):
-            arms(1, [t], 0, HALF)
-            if t < 2:
-                centre(1, [t + 2], 0, HALF)
-            else:
-                centre(0, [t - 2], 256, 768)
-        stage(1, 0, HALF)
-        for c in range(4):
-            product(nc.gpsimd, 1, 0, c)
-        cast_w4(0)
         arms(0, [0], 256, 768)
         centre(0, [2], 256, 768)
         centre(0, [3], 256, 768)
@@ -315,38 +307,54 @@ def tile_list_bond_angle_features_kernel(
         second_arm(0, [0, 1])
         second_arm(0, [2, 3])
         arms(0, [2], 256, 768)
-        second_arm(1, [0])
-        second_arm(1, [1])
         arms(0, [3], 256, 768)
-        second_arm(1, [2])
-        second_arm(1, [3])
-        cast_w4(1)
-        stage(0, 256, 384)
-        product(nc.gpsimd, 0, 256, 2)
+        stage(0, 256, 768)
+        for c in range(2, 6):
+            product(nc.gpsimd, 0, 256, c)
+        centre(1, [0], 0, HALF)
+        centre(1, [1], 0, HALF)
         stage(0, 768, S)
-        stage(1, HALF, S)
         first_arm(0, 6)
         first_arm(0, 7)
-        for c in (6, 7, 4, 5):
-            first_arm(1, c)
-        quant_w4("side0")
-        quant(0, 0, 256, "side1")
-        quant(1, 0, HALF, "w4_bf")
-        mix(0, 256)
-        quant(0, 768, S, "h_bf0_0")
-        quant(1, HALF, S, "h_bf1_0")
+        cast_w4(0)
+        arms(1, [0], 0, HALF)
+        centre(1, [2], 0, HALF)
+        centre(1, [3], 0, HALF)
+        arms(1, [1], 0, HALF)
+        second_arm(1, [0])
+        second_arm(1, [1])
+        arms(1, [2], 0, HALF)
+        second_arm(1, [2])
+        second_arm(1, [3])
+        arms(1, [3], 0, HALF)
+        cast_w4(1)
+        stage(1, 768, S)
+        first_arm(1, 6)
+        first_arm(1, 7)
+        quant_w4("d0_256")
+        stage(1, HALF, 768)
+        quant(0, 768, S, "w4_bf")
+        first_arm(1, 4)
+        quant(1, 768, S)
         mix(768, S)
-        stage(0, 384, HALF, "h_bf0_768")
-        product(nc.vector, 0, 256, 3)
-        quant(0, 256, 384, "h_bf1_512")
+        first_arm(1, 5)
+        quant(0, 256, 768, "h_bf0_768")
+        stage(1, 0, CHUNK, "h_bf1_768")
+        product(nc.vector, 1, 0, 0)
+        quant(1, HALF, 768)
+        mix(HALF, 768)
+        quant(0, 0, 256, "h_bf0_256")
+        stage(1, CHUNK, 256, "h_bf1_512")
+        product(nc.vector, 1, 0, 1)
+        quant(1, 0, CHUNK)
+        mix(0, CHUNK)
+        stage(1, 256, 384, "h_bf0_0")
+        product(nc.vector, 1, 0, 2)
+        quant(1, CHUNK, 256)
+        mix(CHUNK, 256)
+        stage(1, 384, HALF, "h_bf1_768")
+        product(nc.vector, 1, 0, 3)
+        quant(1, 256, 384)
         mix(256, 384)
-        stage(0, HALF, 640, "h_bf0_256")
-        product(nc.vector, 0, 256, 4)
-        quant(0, 384, HALF)
+        quant(1, 384, HALF)
         mix(384, HALF)
-        stage(0, 640, 768, "h_bf0_768")
-        product(nc.vector, 0, 256, 5)
-        quant(0, HALF, 640)
-        mix(HALF, 640)
-        quant(0, 640, 768)
-        mix(640, 768)

@@ -23,6 +23,7 @@ IS_EQUAL = mybir.AluOpType.is_equal
 P = 128
 CHUNK = 128
 HALF = 512
+ZERO_SPLIT = 640
 
 
 def tile_list_bond_angle_features_kernel(
@@ -58,19 +59,18 @@ def tile_list_bond_angle_features_kernel(
         ident = sb([P, P], F32, "ident")
         g_col = sb([P, 8], F32, "g_col")
         g_inv = sb([P, 8], F32, "g_inv")
-        warm = sb([P, 8], F32, "warm")
-        warm2 = sb([P, 8], F32, "warm2")
+        zeros = sb([P, P], F32, "zeros")
 
-        nc.vector.memset(tab_s[:], 0)
-        nc.vector.memset(warm[:], 0.0)
+        nc.gpsimd.memset(tab_s[:, 0:ZERO_SPLIT], 0)
+        nc.vector.memset(tab_s[:, ZERO_SPLIT:], 0)
+        nc.vector.memset(zeros[:], 0.0)
         nc.vector.memset(ws_raw[:], 0)
-        nc.scalar.activation(warm2[:], warm[:], TANH)
+        nc.scalar.activation(g_rows[:], zeros[:], TANH)
 
         w1_rows = w1.rearrange("(p j) (b c) -> b p j c", j=4, b=2)
         g_view = g.rearrange("(b q t i) -> b t q i", b=2, t=4, i=8)
         w4_view = w4.rearrange("(b q t i) n -> b t q i n", b=2, t=4, i=8)
 
-        nc.gpsimd.memset(g_rows[:], 0.0)
         make_identity(nc, ident[:])
 
         def load_scale_rows(w, src, rows):
@@ -100,6 +100,9 @@ def tile_list_bond_angle_features_kernel(
         g_bank = scalar_bank()
         nc.tensor.transpose(g_bank[:, 0:P], g_rows[:], ident[:])
         nc.scalar.copy(g_col[:], g_bank[:, 0:8])
+        g_centre = [sb([P, 8], F32, f"g_centre{b}") for b in range(2)]
+        for b in range(2):
+            nc.scalar.copy(g_centre[b][:], g_bank[:, 0:8])
         for l in range(3):
             nc.vector.tensor_copy(v_scales[l][:], tab_s[:].bitcast(U8).indirect(lists[l][:]))
 
@@ -110,11 +113,12 @@ def tile_list_bond_angle_features_kernel(
                 offsets = lists[l][:, lo // 16 : (lo + width) // 16]
                 nc.vector.tensor_copy(v_words[l][:, lo : lo + width], tab_w[:].bitcast(U32).indirect(offsets))
 
-        w1_bf = [sb([P, 4, 16, 8, 4], BF16, f"w1_bf{b}") for b in range(2)]
+        w1_bf = {}
         w1_q = [sb([P, H // 2], U32, f"w1_q{b}") for b in range(2)]
         w1_s = {}
 
-        def cast_w1(b):
+        def cast_w1(b, tag=None):
+            w1_bf[b] = sb([P, 4, 16, 8, 4], BF16, f"w1_bf{b}", tag)
             src = w1_raw[b][:].rearrange("p j (q t i) -> p t q j i", t=4, i=8)
             for t in range(4):
                 nc.scalar.activation(w1_bf[b][:, t].rearrange("p q i j -> p q j i"), src[:, t], COPY, scale=-1.0)
@@ -125,23 +129,31 @@ def tile_list_bond_angle_features_kernel(
                 w1_q[b][:].bitcast(FP8X4), w1_s[b][:], w1_bf[b][:].rearrange("p t q i j -> p (t q i j)")
             )
 
-        w4_bf = sb([P, 2 * N, 4], BF16, "w4_bf")
+        w4_bf = {}
         w4_q = sb([P, 2 * N], U32, "w4_q")
         late = {}
 
-        def cast_w4(b):
-            nc.scalar.activation(
-                w4_bf[:, b * N : (b + 1) * N, :].rearrange("p (c i) t -> p c t i", i=2),
-                w4_raw[b][:].rearrange("p t (c i) -> p c t i", i=2),
-                COPY,
-            )
+        def pairs_of(k, lo, hi):
+            return w4_bf[k][:, lo:hi, :].rearrange("p (c i) t -> p c t i", i=2)
+
+        def rows_of(b, lo, hi):
+            return w4_raw[b][:, :, lo:hi].rearrange("p t (c i) -> p c t i", i=2)
+
+        def cast_w4_scalar(tag):
+            w4_bf[0] = sb([P, 512, 4], BF16, "w4_bf0", tag)
+            nc.scalar.activation(pairs_of(0, 0, N), rows_of(0, 0, N), COPY)
+            nc.scalar.activation(pairs_of(0, N, 512), rows_of(1, 0, P), COPY)
+
+        def cast_w4_gpsimd(tag):
+            w4_bf[1] = sb([P, 256, 4], BF16, "w4_bf1", tag)
+            nc.gpsimd.tensor_scalar(pairs_of(1, 0, 256), rows_of(1, P, N), 1.0, 0.0, MULT, ADD)
 
         def quant_w4(tag):
             w4_s = sb([P, 2 * N], U8, "w4_s", tag)
             late["w4_s"] = w4_s
-            for lo, hi in ((0, 512), (512, 768)):
+            for k, (lo, hi) in enumerate(((0, 512), (512, 768))):
                 nc.vector.quantize_mx(
-                    w4_q[:, lo:hi].bitcast(FP8X4), w4_s[:, lo:hi], w4_bf[:, lo:hi, :].rearrange("p n t -> p (n t)")
+                    w4_q[:, lo:hi].bitcast(FP8X4), w4_s[:, lo:hi], w4_bf[k][:].rearrange("p n t -> p (n t)")
                 )
 
         ws_p = sb([P, 2, H // 4], I32, "ws_p")
@@ -189,19 +201,19 @@ def tile_list_bond_angle_features_kernel(
         def gain(col, b, t):
             return col[:, 4 * b + t : 4 * b + t + 1]
 
-        def scaled_read(ls, b, ts, lo, hi, dst):
+        def scaled_read(col, ls, b, ts, lo, hi, dst):
             bank = scalar_bank()[:].rearrange("p (e n) -> p e n", e=len(ts))
             for e, t in enumerate(ts):
                 project(bank[:, e, :], ls, b, t, lo, hi)
             for e, t in enumerate(ts):
-                nc.scalar.activation(dst[:, e, :], bank[:, e, :], COPY, scale=gain(g_col, b, t))
+                nc.scalar.activation(dst[:, e, :], bank[:, e, :], COPY, scale=gain(col, b, t))
 
-        def centre(b, ts, lo, hi, tag=None):
+        def centre(b, ts, lo, hi, col):
             if ts[0] == 0 and lo == 0:
-                state["xx", b] = sb([P, 4, side_lo[b]], F32, f"x{b}", tag)
+                state["xx", b] = sb([P, 4, side_lo[b]], F32, f"x{b}")
             x = state["xx", b][:, ts[0] : ts[-1] + 1, lo:hi]
             state["x", b, ts[0], lo] = x
-            scaled_read([0], b, ts, lo, hi, x)
+            scaled_read(col, [0], b, ts, lo, hi, x)
 
         def arms(b, ts, lo, hi, tag=None):
             if ts[0] == 0:
@@ -242,8 +254,8 @@ def tile_list_bond_angle_features_kernel(
             cols = slice(c * CHUNK - lo, (c + 1) * CHUNK - lo)
             engine.tensor_tensor(h_view(h_dst(b, c)), woven(d[:, 0, :, cols]), woven(d[:, 1, :, cols]), MULT)
 
-        def second_arm(b, ts):
-            scaled_read([0, 2], b, ts, side_lo[b], S, side[b][:, ts[0] : ts[-1] + 1, :])
+        def second_arm(b, ts, col):
+            scaled_read(col, [0, 2], b, ts, side_lo[b], S, side[b][:, ts[0] : ts[-1] + 1, :])
 
         def first_arm(b, c):
             bank = shared_bank()[:].rearrange("p (t n) -> p t n", t=4)
@@ -280,6 +292,30 @@ def tile_list_bond_angle_features_kernel(
                 nc.scalar.activation(res[:, ms[0] : ms[-1] + 1, lo:hi], bank, TANH)
             nc.sync.dma_start(out_view[:, :, lo:hi], res[:, :, lo:hi])
 
+        def mix_pass(dst, m, b, lo, hi):
+            cols = slice(b * N + m * P, b * N + (m + 1) * P)
+            plane, at = state["s", b, lo]
+            nc.tensor.matmul_mx(
+                dst,
+                lhsT=w4_q[:, cols].bitcast(FP8X4),
+                lhsT_scale=late["w4_s"][:, cols],
+                rhs=h_q[:, b, lo:hi].bitcast(FP8X4),
+                rhs_scale=plane[:, lo - at : hi - at],
+                start=(b == 0),
+                stop=(b == 1),
+            )
+
+        def last_open(lo, hi):
+            for m in range(3):
+                state["y", m] = scalar_bank()[:, 0 : hi - lo]
+                mix_pass(state["y", m], m, 0, lo, hi)
+
+        def last_close(lo, hi):
+            for m in range(3):
+                mix_pass(state["y", m], m, 1, lo, hi)
+                nc.scalar.activation(res[:, m, lo:hi], state["y", m], TANH)
+            nc.scalar.dma_start(out_view[:, :, lo:hi], res[:, :, lo:hi])
+
         cast_w1(0)
         gather_words(0, 1)
         g_safe = sb([P, 8], F32, "g_safe", "tab_s")
@@ -288,73 +324,70 @@ def tile_list_bond_angle_features_kernel(
         nc.vector.reciprocal(g_inv[:], g_safe[:])
         quant_w1(0)
         deal_packed()
-        cast_w1(1)
-        centre(0, [0, 1], 0, 256, "w1_raw1")
-        centre(0, [2, 3], 0, 256)
-        gather_words(2, 1, "w1_bf0")
-        quant_w1(1)
-        centre(0, [0], 256, 768)
-        arms(0, [0, 1], 0, 256, "w1_bf1")
-        centre(0, [1], 256, 768)
+        centre(0, [0, 1], 0, 256, g_centre[0])
+        centre(0, [2, 3], 0, 256, g_centre[0])
+        gather_words(2, 2, "w1_bf0")
+        centre(0, [0], 256, 768, g_centre[0])
+        arms(0, [0, 1], 0, 256)
+        centre(0, [1], 256, 768, g_centre[0])
         arms(0, [2, 3], 0, 256)
         stage(0, 0, 256)
         for c in range(2):
             product(nc.gpsimd, 0, 0, c)
+        centre(0, [2], 256, 768, g_col)
         arms(0, [0], 256, 768)
-        centre(0, [2], 256, 768)
-        centre(0, [3], 256, 768)
+        centre(0, [3], 256, 768, g_col)
+        cast_w1(1, "g_centre0")
         arms(0, [1], 256, 768)
-        second_arm(0, [0, 1])
-        second_arm(0, [2, 3])
+        second_arm(0, [0, 1], g_col)
+        second_arm(0, [2, 3], g_col)
         arms(0, [2], 256, 768)
+        quant_w1(1, "d0_0")
+        cast_w4_gpsimd("g_centre0")
         arms(0, [3], 256, 768)
         stage(0, 256, 768)
         for c in range(2, 6):
             product(nc.gpsimd, 0, 256, c)
-        centre(1, [0], 0, HALF)
-        centre(1, [1], 0, HALF)
+        centre(1, [0], 0, HALF, g_centre[1])
+        centre(1, [1], 0, HALF, g_centre[1])
         stage(0, 768, S)
         first_arm(0, 6)
         first_arm(0, 7)
-        cast_w4(0)
         arms(1, [0], 0, HALF)
-        centre(1, [2], 0, HALF)
-        centre(1, [3], 0, HALF)
+        centre(1, [2], 0, HALF, g_centre[1])
+        centre(1, [3], 0, HALF, g_centre[1])
         arms(1, [1], 0, HALF)
-        second_arm(1, [0])
-        second_arm(1, [1])
+        second_arm(1, [0], g_col)
+        second_arm(1, [1], g_col)
         arms(1, [2], 0, HALF)
-        second_arm(1, [2])
-        second_arm(1, [3])
+        second_arm(1, [2], g_col)
+        second_arm(1, [3], g_col)
         arms(1, [3], 0, HALF)
-        cast_w4(1)
-        stage(1, 768, S)
-        first_arm(1, 6)
-        first_arm(1, 7)
-        quant_w4("d0_256")
-        stage(1, HALF, 768)
-        quant(0, 768, S, "w4_bf")
-        first_arm(1, 4)
-        quant(1, 768, S)
+        cast_w4_scalar("g_centre1")
+        stage(1, 0, CHUNK)
+        product(nc.gpsimd, 1, 0, 0)
+        stage(1, HALF, S)
+        for c in range(4, 8):
+            first_arm(1, c)
+        quant(0, 768, S, "side1")
+        quant(0, 0, 256, "h_bf0_768")
+        quant(1, HALF, S)
+        quant_w4("h_bf0_0")
         mix(768, S)
-        first_arm(1, 5)
-        quant(0, 256, 768, "h_bf0_768")
-        stage(1, 0, CHUNK, "h_bf1_768")
-        product(nc.vector, 1, 0, 0)
-        quant(1, HALF, 768)
+        quant(0, 256, 768, "h_bf1_512")
         mix(HALF, 768)
-        quant(0, 0, 256, "h_bf0_256")
-        stage(1, CHUNK, 256, "h_bf1_512")
+        stage(1, CHUNK, 256, "g_centre0")
         product(nc.vector, 1, 0, 1)
-        quant(1, 0, CHUNK)
+        quant(1, 0, CHUNK, "g_centre1")
         mix(0, CHUNK)
-        stage(1, 256, 384, "h_bf0_0")
+        stage(1, 256, 384, "h_bf0_256")
         product(nc.vector, 1, 0, 2)
         quant(1, CHUNK, 256)
         mix(CHUNK, 256)
-        stage(1, 384, HALF, "h_bf1_768")
+        stage(1, 384, HALF, "g_centre0")
         product(nc.vector, 1, 0, 3)
         quant(1, 256, 384)
         mix(256, 384)
+        last_open(384, HALF)
         quant(1, 384, HALF)
-        mix(384, HALF)
+        last_close(384, HALF)

@@ -1,7 +1,6 @@
 from contextlib import ExitStack
 
 import concourse.mybir as mybir
-from concourse.masks import make_identity
 
 K, T, S, H, N = 512, 4096, 1024, 1024, 384
 FLOPS = 3 * 2 * K * H * S + 2 * H * N * S
@@ -19,11 +18,11 @@ TANH = mybir.ActivationFunctionType.Tanh
 MULT = mybir.AluOpType.mult
 ADD = mybir.AluOpType.add
 IS_EQUAL = mybir.AluOpType.is_equal
+NOT_EQUAL = mybir.AluOpType.not_equal
 
 P = 128
 CHUNK = 128
 HALF = 512
-ZERO_SPLIT = 640
 
 
 def tile_list_bond_angle_features_kernel(
@@ -50,7 +49,7 @@ def tile_list_bond_angle_features_kernel(
         lists = [keep.tile([P, S // 16], U16, name=f"list{l}") for l in range(3)]
         tab_s = sb([P, T // 4], I32, "tab_s")
         tab_w = sb([P, T], I32, "tab_w")
-        ws_raw = sb([P, 2, H // 4], I32, "ws_raw")
+        ws_raw = sb([P, H // 4], I32, "ws_raw")
         w1_raw = [sb([P, 4, H // 2], F32, f"w1_raw{b}") for b in range(2)]
         w2_raw = sb([P, H // 2], I32, "w2_raw")
         w3_raw = sb([P, H], I32, "w3_raw")
@@ -58,24 +57,25 @@ def tile_list_bond_angle_features_kernel(
         g_rows = sb([P, P], F32, "g_rows")
         ident = sb([P, P], F32, "ident")
         g_col = sb([P, 8], F32, "g_col")
+        g_safe = sb([P, 8], F32, "g_safe")
         g_inv = sb([P, 8], F32, "g_inv")
         zeros = sb([P, P], F32, "zeros")
 
-        nc.gpsimd.memset(tab_s[:, 0:ZERO_SPLIT], 0)
-        nc.vector.memset(tab_s[:, ZERO_SPLIT:], 0)
+        nc.vector.memset(tab_s[:], 0)
         nc.vector.memset(zeros[:], 0.0)
         nc.vector.memset(ws_raw[:], 0)
         nc.scalar.activation(g_rows[:], zeros[:], TANH)
+        nc.gpsimd.affine_select(
+            out=ident[:], in_=zeros[:], compare_op=NOT_EQUAL, fill=1.0, base=0, pattern=[[-1, P]], channel_multiplier=1
+        )
 
         w1_rows = w1.rearrange("(p j) (b c) -> b p j c", j=4, b=2)
         g_view = g.rearrange("(b q t i) -> b t q i", b=2, t=4, i=8)
         w4_view = w4.rearrange("(b q t i) n -> b t q i n", b=2, t=4, i=8)
 
-        make_identity(nc, ident[:])
-
-        def load_scale_rows(w, src, rows):
-            for r in rows:
-                nc.sync.dma_start(ws_raw[r:P:32, w, :], src[0, r:16:4, :].bitcast(I32))
+        def load_scale_rows(k, src):
+            for r in range(4):
+                nc.sync.dma_start(ws_raw[k + r : P : 32, :], src[0, r:16:4, :].bitcast(I32))
 
         nc.sync.dma_start(lists[0][:], offs)
         for r in range(4):
@@ -85,103 +85,75 @@ def tile_list_bond_angle_features_kernel(
         nc.sync.dma_start(tab_w[:], tab_words[0].rearrange("p t i -> p (t i)").bitcast(I32))
         for b in range(2):
             nc.sync.dma_start(g_rows[4 * b : 4 * b + 4, :].rearrange("t (q i) -> t q i", i=8), g_view[b])
-        load_scale_rows(0, w2_scales, range(4))
         nc.sync.dma_start(w1_raw[0][:], w1_rows[0])
-        nc.sync.dma_start(w2_raw[:], w2_words[0].bitcast(I32))
-        load_scale_rows(1, w3_scales, range(4))
-        nc.sync.dma_start(w3_raw[:], w3_words[0].rearrange("p e i -> p (e i)").bitcast(I32))
+        load_scale_rows(0, w2_scales)
         nc.sync.dma_start(w1_raw[1][:], w1_rows[1])
+        load_scale_rows(4, w3_scales)
+        nc.sync.dma_start(w2_raw[:], w2_words[0].bitcast(I32))
+        nc.sync.dma_start(w3_raw[:], w3_words[0].rearrange("p e i -> p (e i)").bitcast(I32))
         for u in range(8):
             nc.sync.dma_start(w4_raw[u // 4][:, u % 4, :], w4_view[u // 4, u % 4])
 
-        v_words = {}
-        state = {}
+        v_words = [sb([P, S], U32, f"v_words{l}") for l in range(3)]
         v_scales = [sb([P, S], U8, f"v_scales{l}") for l in range(3)]
         g_bank = scalar_bank()
         nc.tensor.transpose(g_bank[:, 0:P], g_rows[:], ident[:])
         nc.scalar.copy(g_col[:], g_bank[:, 0:8])
-        g_centre = [sb([P, 8], F32, f"g_centre{b}") for b in range(2)]
-        for b in range(2):
-            nc.scalar.copy(g_centre[b][:], g_bank[:, 0:8])
         for l in range(3):
             nc.vector.tensor_copy(v_scales[l][:], tab_s[:].bitcast(U8).indirect(lists[l][:]))
 
-        def gather_words(l, pieces, tag=None):
-            v_words[l] = sb([P, S], U32, f"v_words{l}", tag)
-            width = S // pieces
-            for lo in range(0, S, width):
-                offsets = lists[l][:, lo // 16 : (lo + width) // 16]
-                nc.vector.tensor_copy(v_words[l][:, lo : lo + width], tab_w[:].bitcast(U32).indirect(offsets))
+        def gather_words(l):
+            nc.vector.tensor_copy(v_words[l][:], tab_w[:].bitcast(U32).indirect(lists[l][:]))
 
-        w1_bf = {}
+        w1_bf = [sb([P, 4, 16, 8, 4], BF16, f"w1_bf{b}") for b in range(2)]
         w1_q = [sb([P, H // 2], U32, f"w1_q{b}") for b in range(2)]
-        w1_s = {}
+        w1_s = [sb([P, H // 2], U8, f"w1_s{b}") for b in range(2)]
 
-        def cast_w1(b, tag=None):
-            w1_bf[b] = sb([P, 4, 16, 8, 4], BF16, f"w1_bf{b}", tag)
+        def cast_w1(b):
             src = w1_raw[b][:].rearrange("p j (q t i) -> p t q j i", t=4, i=8)
             for t in range(4):
                 nc.scalar.activation(w1_bf[b][:, t].rearrange("p q i j -> p q j i"), src[:, t], COPY, scale=-1.0)
 
-        def quant_w1(b, tag=None):
-            w1_s[b] = sb([P, H // 2], U8, f"w1_s{b}", tag)
+        def quant_w1(b):
             nc.vector.quantize_mx(
                 w1_q[b][:].bitcast(FP8X4), w1_s[b][:], w1_bf[b][:].rearrange("p t q i j -> p (t q i j)")
             )
 
-        w4_bf = {}
+        w4_bf = sb([P, 2 * N, 4], BF16, "w4_bf")
         w4_q = sb([P, 2 * N], U32, "w4_q")
-        late = {}
+        w4_s = sb([P, 2 * N], U8, "w4_s")
 
-        def pairs_of(k, lo, hi):
-            return w4_bf[k][:, lo:hi, :].rearrange("p (c i) t -> p c t i", i=2)
+        def cast_w4(b):
+            nc.scalar.activation(
+                w4_bf[:, b * N : (b + 1) * N, :].rearrange("p (c i) t -> p c t i", i=4),
+                w4_raw[b][:].rearrange("p t (c i) -> p c t i", i=4),
+                COPY,
+            )
 
-        def rows_of(b, lo, hi):
-            return w4_raw[b][:, :, lo:hi].rearrange("p t (c i) -> p c t i", i=2)
-
-        def cast_w4_scalar(tag):
-            w4_bf[0] = sb([P, 512, 4], BF16, "w4_bf0", tag)
-            nc.scalar.activation(pairs_of(0, 0, N), rows_of(0, 0, N), COPY)
-            nc.scalar.activation(pairs_of(0, N, 512), rows_of(1, 0, P), COPY)
-
-        def cast_w4_gpsimd(tag):
-            w4_bf[1] = sb([P, 256, 4], BF16, "w4_bf1", tag)
-            nc.gpsimd.tensor_scalar(pairs_of(1, 0, 256), rows_of(1, P, N), 1.0, 0.0, MULT, ADD)
-
-        def quant_w4(tag):
-            w4_s = sb([P, 2 * N], U8, "w4_s", tag)
-            late["w4_s"] = w4_s
-            for k, (lo, hi) in enumerate(((0, 512), (512, 768))):
+        def quant_w4():
+            for lo, hi in ((0, 512), (512, 768)):
                 nc.vector.quantize_mx(
-                    w4_q[:, lo:hi].bitcast(FP8X4), w4_s[:, lo:hi], w4_bf[k][:].rearrange("p n t -> p (n t)")
+                    w4_q[:, lo:hi].bitcast(FP8X4), w4_s[:, lo:hi], w4_bf[:, lo:hi, :].rearrange("p n t -> p (n t)")
                 )
 
-        ws_p = sb([P, 2, H // 4], I32, "ws_p")
+        ws_p = sb([P, H // 4], I32, "ws_p")
         w2_p = sb([P, H // 2], I32, "w2_p")
         w3_p = sb([P, H], I32, "w3_p")
 
         def deal_packed():
-            nc.vector.tensor_copy(
-                w2_p[:].rearrange("p (b t q e) -> p b t q e", b=2, t=4, e=4),
-                w2_raw[:].rearrange("p (b q t e) -> p b t q e", b=2, t=4, e=4),
-            )
-            nc.vector.tensor_copy(
-                w3_p[:].rearrange("p (b t q e) -> p b t q e", b=2, t=4, e=8),
-                w3_raw[:].rearrange("p (b q t e) -> p b t q e", b=2, t=4, e=8),
-            )
-            nc.vector.tensor_copy(
-                ws_p[:].rearrange("p w (b t q e) -> p (w b) t q e", b=2, t=4, e=2),
-                ws_raw[:].rearrange("p w (b q t e) -> p (w b) t q e", b=2, t=4, e=2),
-            )
+            for dst, src, e in ((ws_p, ws_raw, 2), (w2_p, w2_raw, 4), (w3_p, w3_raw, 8)):
+                nc.vector.tensor_copy(
+                    dst[:].rearrange("p (b t q e) -> p b t q e", b=2, t=4, e=e),
+                    src[:].rearrange("p (b q t e) -> p b t q e", b=2, t=4, e=e),
+                )
 
         def weight(l, b, t):
             u = 4 * b + t
             if l == 0:
                 return w1_q[b][:, t * P : (t + 1) * P].bitcast(FP8X4), w1_s[b][:, t * P : (t + 1) * P]
-            scale = ws_p[:, l - 1, u * 32 : (u + 1) * 32].bitcast(U8)
             if l == 1:
-                return w2_p[:, u * 64 : (u + 1) * 64].bitcast(U8).bitcast(FP4X4), scale
-            return w3_p[:, u * P : (u + 1) * P].bitcast(FP8X4), scale
+                return w2_p[:, u * 64 : (u + 1) * 64].bitcast(U8).bitcast(FP4X4), ws_p[:, u * 32 : (u + 1) * 32].bitcast(U8)
+            return w3_p[:, u * P : (u + 1) * P].bitcast(FP8X4), ws_p[4:P, u * 32 : (u + 1) * 32].bitcast(U8)
 
         def project(dst, ls, b, t, lo, hi):
             for n, l in enumerate(ls):
@@ -201,32 +173,22 @@ def tile_list_bond_angle_features_kernel(
         def gain(col, b, t):
             return col[:, 4 * b + t : 4 * b + t + 1]
 
-        def scaled_read(col, ls, b, ts, lo, hi, dst):
+        def scaled_read(dst, ls, b, ts, lo, hi):
             bank = scalar_bank()[:].rearrange("p (e n) -> p e n", e=len(ts))
             for e, t in enumerate(ts):
                 project(bank[:, e, :], ls, b, t, lo, hi)
             for e, t in enumerate(ts):
-                nc.scalar.activation(dst[:, e, :], bank[:, e, :], COPY, scale=gain(col, b, t))
+                nc.scalar.activation(dst[:, t, :], bank[:, e, :], COPY, scale=gain(g_col, b, t))
 
-        def centre(b, ts, lo, hi, col):
-            if ts[0] == 0 and lo == 0:
-                state["xx", b] = sb([P, 4, side_lo[b]], F32, f"x{b}")
-            x = state["xx", b][:, ts[0] : ts[-1] + 1, lo:hi]
-            state["x", b, ts[0], lo] = x
-            scaled_read(col, [0], b, ts, lo, hi, x)
-
-        def arms(b, ts, lo, hi, tag=None):
-            if ts[0] == 0:
-                state["d", b, lo] = sb([P, 2, 4, hi - lo], F32, f"d{b}_{lo}", tag)
-            d, x = state["d", b, lo], state["x", b, ts[0], lo]
+        def arms(d, x, b, ts, lo, hi):
             pair = [shared_bank()[:].rearrange("p (e n) -> p e n", e=len(ts)) for l in range(2)]
             for l in range(2):
                 for e, t in enumerate(ts):
                     project(pair[l][:, e, :], [l + 1], b, t, lo, hi)
             for e, t in enumerate(ts):
-                nc.vector.scalar_tensor_tensor(d[:, 0, t, :], pair[0][:, e, :], gain(g_col, b, t), x[:, e, :], MULT, ADD)
+                nc.vector.scalar_tensor_tensor(d[:, 0, t, :], pair[0][:, e, :], gain(g_col, b, t), x[:, t, :], MULT, ADD)
             for e, t in enumerate(ts):
-                nc.vector.scalar_tensor_tensor(d[:, 1, t, :], x[:, e, :], gain(g_inv, b, t), pair[1][:, e, :], MULT, ADD)
+                nc.vector.scalar_tensor_tensor(d[:, 1, t, :], x[:, t, :], gain(g_inv, b, t), pair[1][:, e, :], MULT, ADD)
 
         def woven(ap):
             return ap.rearrange("p t (c i) -> p c t i", i=2)
@@ -234,160 +196,117 @@ def tile_list_bond_angle_features_kernel(
         def h_view(ap):
             return ap.rearrange("p (c i) t -> p c t i", i=2)
 
-        h_bf = {}
-        h_q = sb([P, 2, S], U32, "h_q")
-        side = {1: sb([P, 4, HALF], F32, "side1"), 0: sb([P, 4, HALF // 2], F32, "side0")}
-        side_lo = {1: HALF, 0: HALF + HALF // 2}
-        res = sb([P, 3, S], F32, "res")
+        def product(engine, dst, d, lo, hi):
+            engine.tensor_tensor(h_view(dst), woven(d[:, 0, :, lo:hi]), woven(d[:, 1, :, lo:hi]), MULT)
 
-        def stage(b, lo, hi, tag=None):
-            tile = sb([P, hi - lo, 4], BF16, f"h_bf{b}_{lo}", tag)
-            for c in range(lo // CHUNK, hi // CHUNK):
-                h_bf[b, c] = (tile, lo)
-
-        def h_dst(b, c):
-            tile, lo = h_bf[b, c]
-            return tile[:, c * CHUNK - lo : (c + 1) * CHUNK - lo, :]
-
-        def product(engine, b, lo, c):
-            d = state["d", b, lo]
-            cols = slice(c * CHUNK - lo, (c + 1) * CHUNK - lo)
-            engine.tensor_tensor(h_view(h_dst(b, c)), woven(d[:, 0, :, cols]), woven(d[:, 1, :, cols]), MULT)
-
-        def second_arm(b, ts, col):
-            scaled_read(col, [0, 2], b, ts, side_lo[b], S, side[b][:, ts[0] : ts[-1] + 1, :])
-
-        def first_arm(b, c):
+        def first_arm(dst, l, b, c, side, at):
             bank = shared_bank()[:].rearrange("p (t n) -> p t n", t=4)
             for t in range(4):
-                project(bank[:, t, :], [0, 1], b, t, c * CHUNK, (c + 1) * CHUNK)
-            cols = slice(c * CHUNK - side_lo[b], (c + 1) * CHUNK - side_lo[b])
-            nc.vector.tensor_tensor(h_view(h_dst(b, c)), woven(bank), woven(side[b][:, :, cols]), MULT)
+                project(bank[:, t, :], [0, l], b, t, c * CHUNK, (c + 1) * CHUNK)
+            nc.vector.tensor_tensor(h_view(dst), woven(bank), woven(side[:, :, c * CHUNK - at : (c + 1) * CHUNK - at]), MULT)
 
-        def quant(b, lo, hi, tag=None):
-            plane = sb([P, hi - lo], U8, f"h_s{b}_{lo}", tag)
-            for at in range(lo, hi, CHUNK):
-                state["s", b, at] = (plane, lo)
-            nc.vector.quantize_mx(
-                h_q[:, b, lo:hi].bitcast(FP8X4), plane[:], h_bf[b, lo // CHUNK][0][:].rearrange("p n t -> p (n t)")
-            )
+        spans = ((0, 512), (512, 768), (768, 896), (896, 1024))
+        h_bf = [sb([P, 2, hi - lo, 4], BF16, f"h_bf{lo}") for lo, hi in spans]
+        h_q = [sb([P, 2, hi - lo], U32, f"h_q{lo}") for lo, hi in spans]
+        h_s = [sb([P, 2, hi - lo], U8, f"h_s{lo}") for lo, hi in spans]
+        res = sb([P, 3, S], F32, "res")
 
-        def mix(lo, hi):
-            width = hi - lo
-            for ms in ([0, 1, 2],) if width == CHUNK else ([0, 1], [2]):
-                bank = shared_bank()[:, 0 : len(ms) * width].rearrange("p (m s) -> p m s", m=len(ms))
-                for e, m in enumerate(ms):
-                    for b in range(2):
-                        cols = slice(b * N + m * P, b * N + (m + 1) * P)
-                        plane, at = state["s", b, lo]
-                        nc.tensor.matmul_mx(
-                            bank[:, e, :],
-                            lhsT=w4_q[:, cols].bitcast(FP8X4),
-                            lhsT_scale=late["w4_s"][:, cols],
-                            rhs=h_q[:, b, lo:hi].bitcast(FP8X4),
-                            rhs_scale=plane[:, lo - at : hi - at],
-                            start=(b == 0),
-                            stop=(b == 1),
-                        )
-                nc.scalar.activation(res[:, ms[0] : ms[-1] + 1, lo:hi], bank, TANH)
-            nc.sync.dma_start(out_view[:, :, lo:hi], res[:, :, lo:hi])
+        def quant(k, b=None):
+            if b is None:
+                nc.vector.quantize_mx(
+                    h_q[k][:].rearrange("p b n -> p (b n)").bitcast(FP8X4),
+                    h_s[k][:].rearrange("p b n -> p (b n)"),
+                    h_bf[k][:].rearrange("p b n t -> p (b n t)"),
+                )
+            else:
+                nc.vector.quantize_mx(
+                    h_q[k][:, b, :].bitcast(FP8X4), h_s[k][:, b, :], h_bf[k][:, b].rearrange("p n t -> p (n t)")
+                )
 
-        def mix_pass(dst, m, b, lo, hi):
+        def mix_pass(dst, k, m, b):
             cols = slice(b * N + m * P, b * N + (m + 1) * P)
-            plane, at = state["s", b, lo]
             nc.tensor.matmul_mx(
                 dst,
                 lhsT=w4_q[:, cols].bitcast(FP8X4),
-                lhsT_scale=late["w4_s"][:, cols],
-                rhs=h_q[:, b, lo:hi].bitcast(FP8X4),
-                rhs_scale=plane[:, lo - at : hi - at],
+                lhsT_scale=w4_s[:, cols],
+                rhs=h_q[k][:, b, :].bitcast(FP8X4),
+                rhs_scale=h_s[k][:, b, :],
                 start=(b == 0),
                 stop=(b == 1),
             )
 
-        def last_open(lo, hi):
-            for m in range(3):
-                state["y", m] = scalar_bank()[:, 0 : hi - lo]
-                mix_pass(state["y", m], m, 0, lo, hi)
-
-        def last_close(lo, hi):
-            for m in range(3):
-                mix_pass(state["y", m], m, 1, lo, hi)
-                nc.scalar.activation(res[:, m, lo:hi], state["y", m], TANH)
-            nc.scalar.dma_start(out_view[:, :, lo:hi], res[:, :, lo:hi])
+        def mix(k, groups):
+            lo, hi = spans[k]
+            for ms in groups:
+                bank = scalar_bank()[:, 0 : len(ms) * (hi - lo)].rearrange("p (m s) -> p m s", m=len(ms))
+                for e, m in enumerate(ms):
+                    for b in range(2):
+                        mix_pass(bank[:, e, :], k, m, b)
+                nc.scalar.activation(res[:, ms[0] : ms[-1] + 1, lo:hi], bank, TANH)
+                nc.sync.dma_start(out_view[:, ms[0] : ms[-1] + 1, lo:hi], res[:, ms[0] : ms[-1] + 1, lo:hi])
 
         cast_w1(0)
-        gather_words(0, 1)
-        g_safe = sb([P, 8], F32, "g_safe", "tab_s")
+        gather_words(0)
         nc.vector.scalar_tensor_tensor(g_safe[:], g_col[:], 0.0, g_col[:], IS_EQUAL, ADD)
-        gather_words(1, 1)
+        gather_words(1)
         nc.vector.reciprocal(g_inv[:], g_safe[:])
+        cast_w1(1)
+        gather_words(2)
         quant_w1(0)
         deal_packed()
-        centre(0, [0, 1], 0, 256, g_centre[0])
-        centre(0, [2, 3], 0, 256, g_centre[0])
-        gather_words(2, 2, "w1_bf0")
-        centre(0, [0], 256, 768, g_centre[0])
-        arms(0, [0, 1], 0, 256)
-        centre(0, [1], 256, 768, g_centre[0])
-        arms(0, [2, 3], 0, 256)
-        stage(0, 0, 256)
-        for c in range(2):
-            product(nc.gpsimd, 0, 0, c)
-        centre(0, [2], 256, 768, g_col)
-        arms(0, [0], 256, 768)
-        centre(0, [3], 256, 768, g_col)
-        cast_w1(1, "g_centre0")
-        arms(0, [1], 256, 768)
-        second_arm(0, [0, 1], g_col)
-        second_arm(0, [2, 3], g_col)
-        arms(0, [2], 256, 768)
-        quant_w1(1, "d0_0")
-        cast_w4_gpsimd("g_centre0")
-        arms(0, [3], 256, 768)
-        stage(0, 256, 768)
-        for c in range(2, 6):
-            product(nc.gpsimd, 0, 256, c)
-        centre(1, [0], 0, HALF, g_centre[1])
-        centre(1, [1], 0, HALF, g_centre[1])
-        stage(0, 768, S)
-        first_arm(0, 6)
-        first_arm(0, 7)
-        arms(1, [0], 0, HALF)
-        centre(1, [2], 0, HALF, g_centre[1])
-        centre(1, [3], 0, HALF, g_centre[1])
-        arms(1, [1], 0, HALF)
-        second_arm(1, [0], g_col)
-        second_arm(1, [1], g_col)
-        arms(1, [2], 0, HALF)
-        second_arm(1, [2], g_col)
-        second_arm(1, [3], g_col)
-        arms(1, [3], 0, HALF)
-        cast_w4_scalar("g_centre1")
-        stage(1, 0, CHUNK)
-        product(nc.gpsimd, 1, 0, 0)
-        stage(1, HALF, S)
-        for c in range(4, 8):
-            first_arm(1, c)
-        quant(0, 768, S, "side1")
-        quant(0, 0, 256, "h_bf0_768")
-        quant(1, HALF, S)
-        quant_w4("h_bf0_0")
-        mix(768, S)
-        quant(0, 256, 768, "h_bf1_512")
-        mix(HALF, 768)
-        stage(1, CHUNK, 256, "g_centre0")
-        product(nc.vector, 1, 0, 1)
-        quant(1, 0, CHUNK, "g_centre1")
-        mix(0, CHUNK)
-        stage(1, 256, 384, "h_bf0_256")
-        product(nc.vector, 1, 0, 2)
-        quant(1, CHUNK, 256)
-        mix(CHUNK, 256)
-        stage(1, 384, HALF, "g_centre0")
-        product(nc.vector, 1, 0, 3)
-        quant(1, 256, 384)
-        mix(256, 384)
-        last_open(384, HALF)
-        quant(1, 384, HALF)
-        last_close(384, HALF)
+        quant_w1(1)
+
+        x_a = [sb([P, 4, HALF], F32, "x_a0", "w1_raw1"), sb([P, 4, HALF], F32, "x_a1")]
+        x_b = sb([P, 4, 256], F32, "x_b")
+        d_a = [sb([P, 2, 4, HALF], F32, f"d_a{b}") for b in range(2)]
+        d_b = sb([P, 2, 4, 256], F32, "d_b")
+        side1 = sb([P, 4, HALF], F32, "side1")
+        side0 = sb([P, 4, 256], F32, "side0")
+
+        scaled_read(x_a[0], [0], 0, [0], 0, HALF)
+        scaled_read(x_a[0], [0], 0, [1], 0, HALF)
+        for t in range(4):
+            arms(d_a[0], x_a[0], 0, [t], 0, HALF)
+            if t < 2:
+                scaled_read(x_a[0], [0], 0, [t + 2], 0, HALF)
+            scaled_read(x_a[1], [0], 1, [t], 0, HALF)
+        scaled_read(x_b, [0], 0, [0, 1], HALF, 768)
+        scaled_read(x_b, [0], 0, [2, 3], HALF, 768)
+        cast_w4(0)
+        cast_w4(1)
+        for t in range(4):
+            arms(d_a[1], x_a[1], 1, [t], 0, HALF)
+            if t < 2:
+                product(nc.vector, h_bf[0][:, 0, t * 256 : (t + 1) * 256], d_a[0], t * 256, (t + 1) * 256)
+            if t == 2:
+                quant(0, 0)
+            scaled_read(side1, [0, 1], 1, [t], HALF, S)
+        arms(d_b, x_b, 0, [0, 1], HALF, 768)
+        scaled_read(side0, [0, 2], 0, [0, 1], 768, S)
+        scaled_read(side0, [0, 2], 0, [2, 3], 768, S)
+        for t in range(2):
+            product(nc.vector, h_bf[0][:, 1, t * 256 : (t + 1) * 256], d_a[1], t * 256, (t + 1) * 256)
+        quant_w4()
+        quant(0, 1)
+        arms(d_b, x_b, 0, [2, 3], HALF, 768)
+        mix(0, ([0], [1], [2]))
+        first_arm(h_bf[1][:, 1, 0:CHUNK], 2, 1, 4, side1, HALF)
+        product(nc.vector, h_bf[1][:, 0], d_b, 0, 256)
+        first_arm(h_bf[1][:, 1, CHUNK:256], 2, 1, 5, side1, HALF)
+        first_arm(h_bf[2][:, 0], 1, 0, 6, side0, 768)
+        quant(1)
+        first_arm(h_bf[2][:, 1], 2, 1, 6, side1, HALF)
+        mix(1, ([0, 1], [2]))
+        first_arm(h_bf[3][:, 0], 1, 0, 7, side0, 768)
+        quant(2)
+        first_arm(h_bf[3][:, 1], 2, 1, 7, side1, HALF)
+        mix(2, ([0, 1, 2],))
+        quant(3, 0)
+        last = [shared_bank()[:, 0:CHUNK] for m in range(3)]
+        for m in range(3):
+            mix_pass(last[m], 3, m, 0)
+        quant(3, 1)
+        for m in range(3):
+            mix_pass(last[m], 3, m, 1)
+            nc.scalar.activation(res[:, m, 896:S], last[m], TANH)
+        nc.scalar.dma_start(out_view[:, :, 896:S], res[:, :, 896:S])

@@ -41,7 +41,7 @@ def tile_list_bond_angle_features_kernel(
 
         def shared_bank():
             turns["shared"].append(0)
-            return banks[3 + len(turns["shared"]) % 5]
+            return banks[3 + (len(turns["shared"]) + 2) % 5]
 
         def sb(shape, dtype, name, tag=None):
             return keep.tile(shape, dtype, align_bytes=64, name=name, tag=tag or name)
@@ -63,6 +63,8 @@ def tile_list_bond_angle_features_kernel(
 
         nc.vector.memset(tab_s[:], 0)
         nc.vector.memset(zeros[:], 0.0)
+        planes = sb([P, 3, S // 4], I32, "planes")
+        nc.vector.memset(planes[:], 0)
         nc.vector.memset(ws_raw[:], 0)
         nc.scalar.activation(g_rows[:], zeros[:], TANH)
         nc.gpsimd.affine_select(
@@ -75,34 +77,43 @@ def tile_list_bond_angle_features_kernel(
 
         def load_scale_rows(k, src):
             for r in range(4):
-                nc.sync.dma_start(ws_raw[k + r : P : 32, :], src[0, r:16:4, :].bitcast(I32))
+                nc.scalar.dma_start(ws_raw[k + r : P : 32, :], src[0, r:16:4, :].bitcast(I32))
 
         nc.sync.dma_start(lists[0][:], offs)
-        for r in range(4):
-            nc.sync.dma_start(tab_s[r:P:32, :], tab_scales[0, r:16:4, :].bitcast(I32))
+        nc.sync.dma_start(tab_s[0:P:8, :], tab_scales[0].bitcast(I32))
         nc.sync.dma_start(lists[1][:], offs2)
         nc.sync.dma_start(lists[2][:], offs3)
         nc.sync.dma_start(tab_w[:], tab_words[0].rearrange("p t i -> p (t i)").bitcast(I32))
         for b in range(2):
-            nc.sync.dma_start(g_rows[4 * b : 4 * b + 4, :].rearrange("t (q i) -> t q i", i=8), g_view[b])
-        nc.sync.dma_start(w1_raw[0][:], w1_rows[0])
+            nc.scalar.dma_start(g_rows[4 * b : 4 * b + 4, :].rearrange("t (q i) -> t q i", i=8), g_view[b])
         load_scale_rows(0, w2_scales)
-        nc.sync.dma_start(w1_raw[1][:], w1_rows[1])
         load_scale_rows(4, w3_scales)
+        nc.sync.dma_start(w1_raw[0][:], w1_rows[0])
+        nc.sync.dma_start(w1_raw[1][:], w1_rows[1])
         nc.sync.dma_start(w2_raw[:], w2_words[0].bitcast(I32))
         nc.sync.dma_start(w3_raw[:], w3_words[0].rearrange("p e i -> p (e i)").bitcast(I32))
-        for u in range(8):
-            nc.sync.dma_start(w4_raw[u // 4][:, u % 4, :], w4_view[u // 4, u % 4])
 
-        v_words = [sb([P, S], U32, f"v_words{l}") for l in range(3)]
-        v_scales = [sb([P, S], U8, f"v_scales{l}") for l in range(3)]
+        v_words = {}
+        picked = sb([P, 3, S], U8, "picked")
+        v_scales = [planes[:, l, :].bitcast(U8) for l in range(3)]
         g_bank = scalar_bank()
         nc.tensor.transpose(g_bank[:, 0:P], g_rows[:], ident[:])
         nc.scalar.copy(g_col[:], g_bank[:, 0:8])
+        g_hold = [sb([P, 8], F32, f"g_hold{k}") for k in range(3)]
+        for k in range(3):
+            nc.scalar.copy(g_hold[k][:], g_bank[:, 0:8])
         for l in range(3):
-            nc.vector.tensor_copy(v_scales[l][:], tab_s[:].bitcast(U8).indirect(lists[l][:]))
+            nc.vector.tensor_copy(picked[:, l, :], tab_s[:].bitcast(U8).indirect(lists[l][:]))
+        for r in range(4):
+            nc.sync.dma_start(
+                planes[r:P:32].rearrange("p l s -> p (l s)"),
+                picked[8 * r : P : 32].rearrange("p l s -> p (l s)").bitcast(I32),
+            )
+        for u in range(8):
+            nc.sync.dma_start(w4_raw[u // 4][:, u % 4, :], w4_view[u // 4, u % 4])
 
-        def gather_words(l):
+        def gather_words(l, tag=None):
+            v_words[l] = sb([P, S], U32, f"v_words{l}", tag)
             nc.vector.tensor_copy(v_words[l][:], tab_w[:].bitcast(U32).indirect(lists[l][:]))
 
         w1_bf = [sb([P, 4, 16, 8, 4], BF16, f"w1_bf{b}") for b in range(2)]
@@ -112,25 +123,36 @@ def tile_list_bond_angle_features_kernel(
         def cast_w1(b):
             src = w1_raw[b][:].rearrange("p j (q t i) -> p t q j i", t=4, i=8)
             for t in range(4):
-                nc.scalar.activation(w1_bf[b][:, t].rearrange("p q i j -> p q j i"), src[:, t], COPY, scale=-1.0)
+                for i in (0, 4):
+                    nc.scalar.activation(
+                        w1_bf[b][:, t, :, i : i + 4].rearrange("p q i j -> p q j i"),
+                        src[:, t, :, :, i : i + 4],
+                        COPY,
+                        scale=-1.0,
+                    )
 
         def quant_w1(b):
             nc.vector.quantize_mx(
                 w1_q[b][:].bitcast(FP8X4), w1_s[b][:], w1_bf[b][:].rearrange("p t q i j -> p (t q i j)")
             )
 
-        w4_bf = sb([P, 2 * N, 4], BF16, "w4_bf")
         w4_q = sb([P, 2 * N], U32, "w4_q")
-        w4_s = sb([P, 2 * N], U8, "w4_s")
+        late = {}
 
-        def cast_w4(b):
+        def cast_w4(b, tag=None):
+            if b == 0:
+                late["w4_bf"] = sb([P, 2 * N, 4], BF16, "w4_bf", tag)
+            w4_bf = late["w4_bf"]
             nc.scalar.activation(
                 w4_bf[:, b * N : (b + 1) * N, :].rearrange("p (c i) t -> p c t i", i=4),
                 w4_raw[b][:].rearrange("p t (c i) -> p c t i", i=4),
                 COPY,
             )
 
-        def quant_w4():
+        def quant_w4(tag=None):
+            w4_s = sb([P, 2 * N], U8, "w4_s", tag)
+            late["w4_s"] = w4_s
+            w4_bf = late["w4_bf"]
             for lo, hi in ((0, 512), (512, 768)):
                 nc.vector.quantize_mx(
                     w4_q[:, lo:hi].bitcast(FP8X4), w4_s[:, lo:hi], w4_bf[:, lo:hi, :].rearrange("p n t -> p (n t)")
@@ -173,22 +195,28 @@ def tile_list_bond_angle_features_kernel(
         def gain(col, b, t):
             return col[:, 4 * b + t : 4 * b + t + 1]
 
-        def scaled_read(dst, ls, b, ts, lo, hi):
-            bank = scalar_bank()[:].rearrange("p (e n) -> p e n", e=len(ts))
+        def scaled_read(dst, ls, b, ts, lo, hi, col=g_col, bank=None):
+            bank = (scalar_bank() if bank is None else banks[bank])[:].rearrange("p (e n) -> p e n", e=len(ts))
             for e, t in enumerate(ts):
                 project(bank[:, e, :], ls, b, t, lo, hi)
             for e, t in enumerate(ts):
-                nc.scalar.activation(dst[:, t, :], bank[:, e, :], COPY, scale=gain(g_col, b, t))
+                if isinstance(dst, tuple):
+                    for half in range(2):
+                        nc.scalar.activation(
+                            dst[half][t], bank[:, e, half * 256 : (half + 1) * 256], COPY, scale=gain(col, b, t)
+                        )
+                else:
+                    nc.scalar.activation(dst[t], bank[:, e, :], COPY, scale=gain(col, b, t))
 
-        def arms(d, x, b, ts, lo, hi):
+        def arms(d, x, b, ts, lo, hi, col=g_col):
             pair = [shared_bank()[:].rearrange("p (e n) -> p e n", e=len(ts)) for l in range(2)]
             for l in range(2):
                 for e, t in enumerate(ts):
                     project(pair[l][:, e, :], [l + 1], b, t, lo, hi)
             for e, t in enumerate(ts):
-                nc.vector.scalar_tensor_tensor(d[:, 0, t, :], pair[0][:, e, :], gain(g_col, b, t), x[:, t, :], MULT, ADD)
+                nc.vector.scalar_tensor_tensor(d[0][:, t, :], pair[0][:, e, :], gain(col, b, t), x[t], MULT, ADD)
             for e, t in enumerate(ts):
-                nc.vector.scalar_tensor_tensor(d[:, 1, t, :], x[:, t, :], gain(g_inv, b, t), pair[1][:, e, :], MULT, ADD)
+                nc.vector.scalar_tensor_tensor(d[1][:, t, :], x[t], gain(g_inv, b, t), pair[1][:, e, :], MULT, ADD)
 
         def woven(ap):
             return ap.rearrange("p t (c i) -> p c t i", i=2)
@@ -197,7 +225,7 @@ def tile_list_bond_angle_features_kernel(
             return ap.rearrange("p (c i) t -> p c t i", i=2)
 
         def product(engine, dst, d, lo, hi):
-            engine.tensor_tensor(h_view(dst), woven(d[:, 0, :, lo:hi]), woven(d[:, 1, :, lo:hi]), MULT)
+            engine.tensor_tensor(h_view(dst), woven(d[0][:, :, lo:hi]), woven(d[1][:, :, lo:hi]), MULT)
 
         def first_arm(dst, l, b, c, side, at):
             bank = shared_bank()[:].rearrange("p (t n) -> p t n", t=4)
@@ -206,12 +234,22 @@ def tile_list_bond_angle_features_kernel(
             nc.vector.tensor_tensor(h_view(dst), woven(bank), woven(side[:, :, c * CHUNK - at : (c + 1) * CHUNK - at]), MULT)
 
         spans = ((0, 512), (512, 768), (768, 896), (896, 1024))
-        h_bf = [sb([P, 2, hi - lo, 4], BF16, f"h_bf{lo}") for lo, hi in spans]
+        h_bf = [None] + [sb([P, 2, hi - lo, 4], BF16, f"h_bf{lo}") for lo, hi in spans[1:]]
         h_q = [sb([P, 2, hi - lo], U32, f"h_q{lo}") for lo, hi in spans]
-        h_s = [sb([P, 2, hi - lo], U8, f"h_s{lo}") for lo, hi in spans]
+        h_s = {}
+        h_a = {}
+        s_a = {}
+
+        def quant_a(b, lo, hi):
+            nc.vector.quantize_mx(
+                h_q[0][:, b, lo:hi].bitcast(FP8X4), s_a[b][:, lo:hi], h_a[b][:, lo:hi].rearrange("p n t -> p (n t)")
+            )
+
         res = sb([P, 3, S], F32, "res")
 
-        def quant(k, b=None):
+        def quant(k, b=None, tag=None):
+            if not b:
+                h_s[k] = sb([P, 2, spans[k][1] - spans[k][0]], U8, f"h_s{k}", tag)
             if b is None:
                 nc.vector.quantize_mx(
                     h_q[k][:].rearrange("p b n -> p (b n)").bitcast(FP8X4),
@@ -223,25 +261,27 @@ def tile_list_bond_angle_features_kernel(
                     h_q[k][:, b, :].bitcast(FP8X4), h_s[k][:, b, :], h_bf[k][:, b].rearrange("p n t -> p (n t)")
                 )
 
-        def mix_pass(dst, k, m, b):
+        def mix_pass(dst, k, m, b, part=slice(None)):
             cols = slice(b * N + m * P, b * N + (m + 1) * P)
             nc.tensor.matmul_mx(
                 dst,
                 lhsT=w4_q[:, cols].bitcast(FP8X4),
-                lhsT_scale=w4_s[:, cols],
-                rhs=h_q[k][:, b, :].bitcast(FP8X4),
-                rhs_scale=h_s[k][:, b, :],
+                lhsT_scale=late["w4_s"][:, cols],
+                rhs=h_q[k][:, b, part].bitcast(FP8X4),
+                rhs_scale=h_s[k][:, b, part] if k else s_a[b][:, part],
                 start=(b == 0),
                 stop=(b == 1),
             )
 
-        def mix(k, groups):
-            lo, hi = spans[k]
+        def mix(k, groups, lo=None, hi=None):
+            part = slice(lo, hi)
+            if k:
+                lo, hi = spans[k]
             for ms in groups:
                 bank = scalar_bank()[:, 0 : len(ms) * (hi - lo)].rearrange("p (m s) -> p m s", m=len(ms))
                 for e, m in enumerate(ms):
                     for b in range(2):
-                        mix_pass(bank[:, e, :], k, m, b)
+                        mix_pass(bank[:, e, :], k, m, b, part)
                 nc.scalar.activation(res[:, ms[0] : ms[-1] + 1, lo:hi], bank, TANH)
                 nc.sync.dma_start(out_view[:, ms[0] : ms[-1] + 1, lo:hi], res[:, ms[0] : ms[-1] + 1, lo:hi])
 
@@ -251,62 +291,88 @@ def tile_list_bond_angle_features_kernel(
         gather_words(1)
         nc.vector.reciprocal(g_inv[:], g_safe[:])
         cast_w1(1)
-        gather_words(2)
         quant_w1(0)
         deal_packed()
         quant_w1(1)
+        gather_words(2, "w1_bf1")
 
-        x_a = [sb([P, 4, HALF], F32, "x_a0", "w1_raw1"), sb([P, 4, HALF], F32, "x_a1")]
-        x_b = sb([P, 4, 256], F32, "x_b")
-        d_a = [sb([P, 2, 4, HALF], F32, f"d_a{b}") for b in range(2)]
-        d_b = sb([P, 2, 4, 256], F32, "d_b")
-        side1 = sb([P, 4, HALF], F32, "side1")
+        def by_tile(tile):
+            return [tile[:, t, :] for t in range(4)]
+
+        x_0 = sb([P, 4, 768], F32, "x_0", "w1_raw1")
+        x_a0 = by_tile(x_0[:, :, 0:HALF])
+        x_b = by_tile(x_0[:, :, HALF:768])
+        d_a = [[sb([P, 4, HALF], F32, f"d_a{b}_{k}") for k in range(2)] for b in range(2)]
+        d_b = [sb([P, 4, 256], F32, f"d_b{k}") for k in range(2)]
+        side1 = [sb([P, 4, 256], F32, f"side1_{k}") for k in range(2)]
         side0 = sb([P, 4, 256], F32, "side0")
 
-        scaled_read(x_a[0], [0], 0, [0], 0, HALF)
-        scaled_read(x_a[0], [0], 0, [1], 0, HALF)
-        for t in range(4):
-            arms(d_a[0], x_a[0], 0, [t], 0, HALF)
-            if t < 2:
-                scaled_read(x_a[0], [0], 0, [t + 2], 0, HALF)
-            scaled_read(x_a[1], [0], 1, [t], 0, HALF)
-        scaled_read(x_b, [0], 0, [0, 1], HALF, 768)
-        scaled_read(x_b, [0], 0, [2, 3], HALF, 768)
-        cast_w4(0)
-        cast_w4(1)
-        for t in range(4):
-            arms(d_a[1], x_a[1], 1, [t], 0, HALF)
-            if t < 2:
-                product(nc.vector, h_bf[0][:, 0, t * 256 : (t + 1) * 256], d_a[0], t * 256, (t + 1) * 256)
-            if t == 2:
-                quant(0, 0)
-            scaled_read(side1, [0, 1], 1, [t], HALF, S)
+        def chunk(c):
+            return slice(c * CHUNK, (c + 1) * CHUNK)
+
+        scaled_read(x_b, [0], 0, [0, 1], HALF, 768, g_col, 3)
+        scaled_read(x_b, [0], 0, [2, 3], HALF, 768, g_col, 4)
+        scaled_read(x_a0, [0], 0, [0], 0, HALF, g_col, 5)
+        scaled_read(x_a0, [0], 0, [1], 0, HALF)
+        scaled_read(x_a0, [0], 0, [2], 0, HALF)
+        scaled_read(x_a0, [0], 0, [3], 0, HALF, g_hold[2])
         arms(d_b, x_b, 0, [0, 1], HALF, 768)
-        scaled_read(side0, [0, 2], 0, [0, 1], 768, S)
-        scaled_read(side0, [0, 2], 0, [2, 3], 768, S)
-        for t in range(2):
-            product(nc.vector, h_bf[0][:, 1, t * 256 : (t + 1) * 256], d_a[1], t * 256, (t + 1) * 256)
-        quant_w4()
-        quant(0, 1)
         arms(d_b, x_b, 0, [2, 3], HALF, 768)
-        mix(0, ([0], [1], [2]))
-        first_arm(h_bf[1][:, 1, 0:CHUNK], 2, 1, 4, side1, HALF)
-        product(nc.vector, h_bf[1][:, 0], d_b, 0, 256)
-        first_arm(h_bf[1][:, 1, CHUNK:256], 2, 1, 5, side1, HALF)
+        for c in range(2):
+            product(nc.gpsimd, h_bf[1][:, 0, chunk(c)], d_b, c * CHUNK, (c + 1) * CHUNK)
+        cast_w4(0, "g_hold2")
+        cast_w4(1)
+        x_a1 = by_tile(sb([P, 4, HALF], F32, "x_a1", "w4_raw1"))
+        for t in range(4):
+            arms(d_a[0], x_a0, 0, [t], 0, HALF, g_hold[0] if t == 2 else g_col)
+            scaled_read(x_a1, [0], 1, [t], 0, HALF)
+        quant_w4("g_hold0")
+        h_a[0] = sb([P, HALF, 4], BF16, "h_a0", "g_hold2")
+        for c in range(4):
+            product(nc.gpsimd, h_a[0][:, chunk(c)], d_a[0], c * CHUNK, (c + 1) * CHUNK)
+        for t in range(4):
+            arms(d_a[1], x_a1, 1, [t], 0, HALF, g_hold[1])
+            if t < 2:
+                for e in range(2):
+                    scaled_read((by_tile(side1[0]), by_tile(side1[1])), [0, 1], 1, [2 * t + e], HALF, S)
+            if t == 2:
+                scaled_read(by_tile(side0), [0, 2], 0, [0, 1], 768, S)
+                scaled_read(by_tile(side0), [0, 2], 0, [2, 3], 768, S)
+        first_arm(h_bf[2][:, 1], 2, 1, 6, side1[1], 768)
         first_arm(h_bf[2][:, 0], 1, 0, 6, side0, 768)
-        quant(1)
-        first_arm(h_bf[2][:, 1], 2, 1, 6, side1, HALF)
-        mix(1, ([0, 1], [2]))
-        first_arm(h_bf[3][:, 0], 1, 0, 7, side0, 768)
-        quant(2)
-        first_arm(h_bf[3][:, 1], 2, 1, 7, side1, HALF)
+        first_arm(h_bf[1][:, 1, 0:CHUNK], 2, 1, 4, side1[0], HALF)
+        first_arm(h_bf[1][:, 1, CHUNK:256], 2, 1, 5, side1[0], HALF)
+        s_a[0] = sb([P, HALF], U8, "s_a0", "side1_0")
+        s_a[1] = sb([P, HALF], U8, "s_a1")
+        h_a[1] = sb([P, HALF, 4], BF16, "h_a1", "d_a0_1")
+        quant(2, None, "d_a0_0")
         mix(2, ([0, 1, 2],))
-        quant(3, 0)
+        quant_a(0, 0, HALF)
+        quant(1)
+        mix(1, ([0, 1], [2]))
+
+        def product_a1(c):
+            product(nc.vector, h_a[1][:, chunk(c)], d_a[1], c * CHUNK, (c + 1) * CHUNK)
+
+        first_arm(h_bf[3][:, 1], 2, 1, 7, side1[1], 768)
+        product_a1(0)
+        first_arm(h_bf[3][:, 0], 1, 0, 7, side0, 768)
+        quant_a(1, 0, CHUNK)
+        mix(0, ([0, 1, 2],), 0, CHUNK)
+        product_a1(1)
+        quant(3)
+        mix(3, ([0, 1, 2],))
+        product_a1(2)
+        quant_a(1, CHUNK, 256)
+        mix(0, ([0, 1, 2],), CHUNK, 256)
+        product_a1(3)
+        quant_a(1, 256, 384)
+        mix(0, ([0, 1, 2],), 256, 384)
         last = [shared_bank()[:, 0:CHUNK] for m in range(3)]
         for m in range(3):
-            mix_pass(last[m], 3, m, 0)
-        quant(3, 1)
+            mix_pass(last[m], 0, m, 0, chunk(3))
+        quant_a(1, 384, HALF)
         for m in range(3):
-            mix_pass(last[m], 3, m, 1)
-            nc.scalar.activation(res[:, m, 896:S], last[m], TANH)
-        nc.scalar.dma_start(out_view[:, :, 896:S], res[:, :, 896:S])
+            mix_pass(last[m], 0, m, 1, chunk(3))
+            nc.scalar.activation(res[:, m, chunk(3)], last[m], TANH)
+        nc.scalar.dma_start(out_view[:, :, chunk(3)], res[:, :, chunk(3)])

@@ -79,6 +79,7 @@ def tile_list_bond_angle_features_kernel(
             for r in range(4):
                 nc.scalar.dma_start(ws_raw[k + r : P : 32, :], src[0, r:16:4, :].bitcast(I32))
 
+        nc.sync.dma_start(w2_raw[:], w2_words[0].bitcast(I32))
         nc.sync.dma_start(lists[0][:], offs)
         nc.sync.dma_start(tab_s[0:P:8, :], tab_scales[0].bitcast(I32))
         nc.sync.dma_start(lists[1][:], offs2)
@@ -90,12 +91,22 @@ def tile_list_bond_angle_features_kernel(
         load_scale_rows(4, w3_scales)
         nc.sync.dma_start(w1_raw[0][:], w1_rows[0])
         nc.sync.dma_start(w1_raw[1][:], w1_rows[1])
-        nc.sync.dma_start(w2_raw[:], w2_words[0].bitcast(I32))
         nc.sync.dma_start(w3_raw[:], w3_words[0].rearrange("p e i -> p (e i)").bitcast(I32))
 
         v_words = {}
         picked = sb([P, 3, S], U8, "picked")
         v_scales = [planes[:, l, :].bitcast(U8) for l in range(3)]
+        ws_p = sb([P, H // 4], I32, "ws_p")
+        w2_p = sb([P, H // 2], I32, "w2_p")
+        w3_p = sb([P, H], I32, "w3_p")
+
+        def deal(dst, src, e):
+            nc.vector.tensor_copy(
+                dst[:].rearrange("p (b t q e) -> p b t q e", b=2, t=4, e=e),
+                src[:].rearrange("p (b q t e) -> p b t q e", b=2, t=4, e=e),
+            )
+
+        deal(w2_p, w2_raw, 4)
         g_bank = scalar_bank()
         nc.tensor.transpose(g_bank[:, 0:P], g_rows[:], ident[:])
         nc.scalar.copy(g_col[:], g_bank[:, 0:8])
@@ -112,9 +123,11 @@ def tile_list_bond_angle_features_kernel(
         for u in range(8):
             nc.sync.dma_start(w4_raw[u // 4][:, u % 4, :], w4_view[u // 4, u % 4])
 
-        def gather_words(l, tag=None):
+        def gather_words(l, tag=None, parts=((0, S),)):
             v_words[l] = sb([P, S], U32, f"v_words{l}", tag)
-            nc.vector.tensor_copy(v_words[l][:], tab_w[:].bitcast(U32).indirect(lists[l][:]))
+            for lo, hi in parts:
+                offsets = lists[l][:, lo // 16 : hi // 16]
+                nc.vector.tensor_copy(v_words[l][:, lo:hi], tab_w[:].bitcast(U32).indirect(offsets))
 
         w1_bf = [sb([P, 4, 16, 8, 4], BF16, f"w1_bf{b}") for b in range(2)]
         w1_q = [sb([P, H // 2], U32, f"w1_q{b}") for b in range(2)]
@@ -158,17 +171,6 @@ def tile_list_bond_angle_features_kernel(
                     w4_q[:, lo:hi].bitcast(FP8X4), w4_s[:, lo:hi], w4_bf[:, lo:hi, :].rearrange("p n t -> p (n t)")
                 )
 
-        ws_p = sb([P, H // 4], I32, "ws_p")
-        w2_p = sb([P, H // 2], I32, "w2_p")
-        w3_p = sb([P, H], I32, "w3_p")
-
-        def deal_packed():
-            for dst, src, e in ((ws_p, ws_raw, 2), (w2_p, w2_raw, 4), (w3_p, w3_raw, 8)):
-                nc.vector.tensor_copy(
-                    dst[:].rearrange("p (b t q e) -> p b t q e", b=2, t=4, e=e),
-                    src[:].rearrange("p (b q t e) -> p b t q e", b=2, t=4, e=e),
-                )
-
         def weight(l, b, t):
             u = 4 * b + t
             if l == 0:
@@ -208,8 +210,8 @@ def tile_list_bond_angle_features_kernel(
                 else:
                     nc.scalar.activation(dst[t], bank[:, e, :], COPY, scale=gain(col, b, t))
 
-        def arms(d, x, b, ts, lo, hi, col=g_col):
-            pair = [shared_bank()[:].rearrange("p (e n) -> p e n", e=len(ts)) for l in range(2)]
+        def arms(d, x, b, ts, lo, hi, col=g_col, own=None):
+            pair = [(shared_bank() if own is None else banks[own + l])[:].rearrange("p (e n) -> p e n", e=len(ts)) for l in range(2)]
             for l in range(2):
                 for e, t in enumerate(ts):
                     project(pair[l][:, e, :], [l + 1], b, t, lo, hi)
@@ -227,13 +229,18 @@ def tile_list_bond_angle_features_kernel(
         def product(engine, dst, d, lo, hi):
             engine.tensor_tensor(h_view(dst), woven(d[0][:, :, lo:hi]), woven(d[1][:, :, lo:hi]), MULT)
 
-        def first_arm(dst, l, b, c, side, at):
+        def open_arm(l, b, c):
             bank = shared_bank()[:].rearrange("p (t n) -> p t n", t=4)
             for t in range(4):
                 project(bank[:, t, :], [0, l], b, t, c * CHUNK, (c + 1) * CHUNK)
+            return bank
+
+        def first_arm(dst, l, b, c, side, at, bank=None):
+            if bank is None:
+                bank = open_arm(l, b, c)
             nc.vector.tensor_tensor(h_view(dst), woven(bank), woven(side[:, :, c * CHUNK - at : (c + 1) * CHUNK - at]), MULT)
 
-        spans = ((0, 512), (512, 768), (768, 896), (896, 1024))
+        spans = ((0, 512), (512, 768), (768, 1024))
         h_bf = [None] + [sb([P, 2, hi - lo, 4], BF16, f"h_bf{lo}") for lo, hi in spans[1:]]
         h_q = [sb([P, 2, hi - lo], U32, f"h_q{lo}") for lo, hi in spans]
         h_s = {}
@@ -292,9 +299,10 @@ def tile_list_bond_angle_features_kernel(
         nc.vector.reciprocal(g_inv[:], g_safe[:])
         cast_w1(1)
         quant_w1(0)
-        deal_packed()
+        deal(ws_p, ws_raw, 2)
+        deal(w3_p, w3_raw, 8)
+        gather_words(2, "w3_raw", ((HALF, S), (0, HALF)))
         quant_w1(1)
-        gather_words(2, "w1_bf1")
 
         def by_tile(tile):
             return [tile[:, t, :] for t in range(4)]
@@ -313,11 +321,11 @@ def tile_list_bond_angle_features_kernel(
         scaled_read(x_b, [0], 0, [0, 1], HALF, 768, g_col, 3)
         scaled_read(x_b, [0], 0, [2, 3], HALF, 768, g_col, 4)
         scaled_read(x_a0, [0], 0, [0], 0, HALF, g_col, 5)
-        scaled_read(x_a0, [0], 0, [1], 0, HALF)
-        scaled_read(x_a0, [0], 0, [2], 0, HALF)
-        scaled_read(x_a0, [0], 0, [3], 0, HALF, g_hold[2])
-        arms(d_b, x_b, 0, [0, 1], HALF, 768)
-        arms(d_b, x_b, 0, [2, 3], HALF, 768)
+        arms(d_b, x_b, 0, [0, 1], HALF, 768, g_col, 6)
+        arms(d_b, x_b, 0, [2, 3], HALF, 768, g_col, 0)
+        scaled_read(x_a0, [0], 0, [1], 0, HALF, g_col, 3)
+        scaled_read(x_a0, [0], 0, [2], 0, HALF, g_col, 4)
+        scaled_read(x_a0, [0], 0, [3], 0, HALF, g_hold[2], 5)
         for c in range(2):
             product(nc.gpsimd, h_bf[1][:, 0, chunk(c)], d_b, c * CHUNK, (c + 1) * CHUNK)
         cast_w4(0, "g_hold2")
@@ -338,41 +346,40 @@ def tile_list_bond_angle_features_kernel(
             if t == 2:
                 scaled_read(by_tile(side0), [0, 2], 0, [0, 1], 768, S)
                 scaled_read(by_tile(side0), [0, 2], 0, [2, 3], 768, S)
-        first_arm(h_bf[2][:, 1], 2, 1, 6, side1[1], 768)
-        first_arm(h_bf[2][:, 0], 1, 0, 6, side0, 768)
-        first_arm(h_bf[1][:, 1, 0:CHUNK], 2, 1, 4, side1[0], HALF)
-        first_arm(h_bf[1][:, 1, CHUNK:256], 2, 1, 5, side1[0], HALF)
+        for c in (6, 7):
+            first_arm(h_bf[2][:, 1, chunk(c - 6)], 2, 1, c, side1[1], 768)
+            first_arm(h_bf[2][:, 0, chunk(c - 6)], 1, 0, c, side0, 768)
+        quant(2, None, "d_a0_0")
+        mix(2, ([0, 1], [2]))
+        for c in (4, 5):
+            first_arm(h_bf[1][:, 1, chunk(c - 4)], 2, 1, c, side1[0], HALF)
         s_a[0] = sb([P, HALF], U8, "s_a0", "side1_0")
         s_a[1] = sb([P, HALF], U8, "s_a1")
-        h_a[1] = sb([P, HALF, 4], BF16, "h_a1", "d_a0_1")
-        quant(2, None, "d_a0_0")
-        mix(2, ([0, 1, 2],))
-        quant_a(0, 0, HALF)
-        quant(1)
-        mix(1, ([0, 1], [2]))
+        h_c = {}
 
-        def product_a1(c):
-            product(nc.vector, h_a[1][:, chunk(c)], d_a[1], c * CHUNK, (c + 1) * CHUNK)
+        def product_a1(c, tag):
+            h_c[c] = sb([P, CHUNK, 4], BF16, f"h_c{c}", tag)
+            product(nc.vector, h_c[c][:], d_a[1], c * CHUNK, (c + 1) * CHUNK)
 
-        first_arm(h_bf[3][:, 1], 2, 1, 7, side1[1], 768)
-        product_a1(0)
-        first_arm(h_bf[3][:, 0], 1, 0, 7, side0, 768)
-        quant_a(1, 0, CHUNK)
-        mix(0, ([0, 1, 2],), 0, CHUNK)
-        product_a1(1)
-        quant(3)
-        mix(3, ([0, 1, 2],))
-        product_a1(2)
-        quant_a(1, CHUNK, 256)
-        mix(0, ([0, 1, 2],), CHUNK, 256)
-        product_a1(3)
-        quant_a(1, 256, 384)
-        mix(0, ([0, 1, 2],), 256, 384)
+        def quant_a1(c):
+            nc.vector.quantize_mx(
+                h_q[0][:, 1, chunk(c)].bitcast(FP8X4), s_a[1][:, chunk(c)], h_c[c][:].rearrange("p n t -> p (n t)")
+            )
+
+        for c in range(4):
+            product_a1(c, ("d_a0_1", "h_bf512")[c % 2])
+            if c == 0:
+                quant(1)
+                mix(1, ([0, 1], [2]))
+            quant_a(0, c * CHUNK, (c + 1) * CHUNK)
+            if c < 3:
+                quant_a1(c)
+                mix(0, ([0, 1, 2],), c * CHUNK, (c + 1) * CHUNK)
         last = [shared_bank()[:, 0:CHUNK] for m in range(3)]
         for m in range(3):
             mix_pass(last[m], 0, m, 0, chunk(3))
-        quant_a(1, 384, HALF)
+        quant_a1(3)
         for m in range(3):
             mix_pass(last[m], 0, m, 1, chunk(3))
             nc.scalar.activation(res[:, m, chunk(3)], last[m], TANH)
-        nc.scalar.dma_start(out_view[:, :, chunk(3)], res[:, :, chunk(3)])
+            (nc.scalar if m == 2 else nc.sync).dma_start(out_view[:, m, chunk(3)], res[:, m, chunk(3)])

@@ -41,7 +41,7 @@ def tile_list_bond_angle_features_kernel(
 
         def shared_bank():
             turns["shared"].append(0)
-            return banks[3 + (len(turns["shared"]) + 2) % 5]
+            return banks[3 + (len(turns["shared"]) + 1) % 5]
 
         def sb(shape, dtype, name, tag=None):
             return keep.tile(shape, dtype, align_bytes=64, name=name, tag=tag or name)
@@ -61,7 +61,7 @@ def tile_list_bond_angle_features_kernel(
         g_inv = sb([P, 8], F32, "g_inv")
         zeros = sb([P, P], F32, "zeros")
 
-        nc.vector.memset(tab_s[:], 0)
+        nc.vector.memset(tab_s[0:112, :], 0)
         nc.vector.memset(zeros[:], 0.0)
         planes = sb([P, 3, S // 4], I32, "planes")
         nc.vector.memset(planes[:], 0)
@@ -79,9 +79,8 @@ def tile_list_bond_angle_features_kernel(
             for r in range(4):
                 nc.scalar.dma_start(ws_raw[k + r : P : 32, :], src[0, r:16:4, :].bitcast(I32))
 
-        nc.sync.dma_start(w2_raw[:], w2_words[0].bitcast(I32))
+        nc.sync.dma_start(tab_s[112:P, :], tab_scales[0].bitcast(I32))
         nc.sync.dma_start(lists[0][:], offs)
-        nc.sync.dma_start(tab_s[0:P:8, :], tab_scales[0].bitcast(I32))
         nc.sync.dma_start(lists[1][:], offs2)
         nc.sync.dma_start(lists[2][:], offs3)
         nc.sync.dma_start(tab_w[:], tab_words[0].rearrange("p t i -> p (t i)").bitcast(I32))
@@ -91,6 +90,7 @@ def tile_list_bond_angle_features_kernel(
         load_scale_rows(4, w3_scales)
         nc.sync.dma_start(w1_raw[0][:], w1_rows[0])
         nc.sync.dma_start(w1_raw[1][:], w1_rows[1])
+        nc.sync.dma_start(w2_raw[:], w2_words[0].bitcast(I32))
         nc.sync.dma_start(w3_raw[:], w3_words[0].rearrange("p e i -> p (e i)").bitcast(I32))
 
         v_words = {}
@@ -106,7 +106,6 @@ def tile_list_bond_angle_features_kernel(
                 src[:].rearrange("p (b q t e) -> p b t q e", b=2, t=4, e=e),
             )
 
-        deal(w2_p, w2_raw, 4)
         g_bank = scalar_bank()
         nc.tensor.transpose(g_bank[:, 0:P], g_rows[:], ident[:])
         nc.scalar.copy(g_col[:], g_bank[:, 0:8])
@@ -118,7 +117,7 @@ def tile_list_bond_angle_features_kernel(
         for r in range(4):
             nc.sync.dma_start(
                 planes[r:P:32].rearrange("p l s -> p (l s)"),
-                picked[8 * r : P : 32].rearrange("p l s -> p (l s)").bitcast(I32),
+                picked[112 + r : P : 4].rearrange("p l s -> p (l s)").bitcast(I32),
             )
         for u in range(8):
             nc.sync.dma_start(w4_raw[u // 4][:, u % 4, :], w4_view[u // 4, u % 4])
@@ -149,7 +148,6 @@ def tile_list_bond_angle_features_kernel(
                 w1_q[b][:].bitcast(FP8X4), w1_s[b][:], w1_bf[b][:].rearrange("p t q i j -> p (t q i j)")
             )
 
-        w4_q = sb([P, 2 * N], U32, "w4_q")
         late = {}
 
         def cast_w4(b, tag=None):
@@ -162,8 +160,10 @@ def tile_list_bond_angle_features_kernel(
                 COPY,
             )
 
-        def quant_w4(tag=None):
-            w4_s = sb([P, 2 * N], U8, "w4_s", tag)
+        def quant_w4(tag_q, tag_s):
+            w4_q = sb([P, 2 * N], U32, "w4_q", tag_q)
+            late["w4_q"] = w4_q
+            w4_s = sb([P, 2 * N], U8, "w4_s", tag_s)
             late["w4_s"] = w4_s
             w4_bf = late["w4_bf"]
             for lo, hi in ((0, 512), (512, 768)):
@@ -220,6 +220,13 @@ def tile_list_bond_angle_features_kernel(
             for e, t in enumerate(ts):
                 nc.vector.scalar_tensor_tensor(d[1][:, t, :], x[t], gain(g_inv, b, t), pair[1][:, e, :], MULT, ADD)
 
+        def lone_arm(d, x, b, ts, lo, hi, own):
+            bank = banks[own][:].rearrange("p (e n) -> p e n", e=len(ts))
+            for e, t in enumerate(ts):
+                project(bank[:, e, :], [2], b, t, lo, hi)
+            for e, t in enumerate(ts):
+                nc.vector.scalar_tensor_tensor(d[:, t, :], x[t], gain(g_inv, b, t), bank[:, e, :], MULT, ADD)
+
         def woven(ap):
             return ap.rearrange("p t (c i) -> p c t i", i=2)
 
@@ -229,8 +236,8 @@ def tile_list_bond_angle_features_kernel(
         def product(engine, dst, d, lo, hi):
             engine.tensor_tensor(h_view(dst), woven(d[0][:, :, lo:hi]), woven(d[1][:, :, lo:hi]), MULT)
 
-        def open_arm(l, b, c):
-            bank = shared_bank()[:].rearrange("p (t n) -> p t n", t=4)
+        def open_arm(l, b, c, own=None):
+            bank = (shared_bank() if own is None else own)[:].rearrange("p (t n) -> p t n", t=4)
             for t in range(4):
                 project(bank[:, t, :], [0, l], b, t, c * CHUNK, (c + 1) * CHUNK)
             return bank
@@ -272,7 +279,7 @@ def tile_list_bond_angle_features_kernel(
             cols = slice(b * N + m * P, b * N + (m + 1) * P)
             nc.tensor.matmul_mx(
                 dst,
-                lhsT=w4_q[:, cols].bitcast(FP8X4),
+                lhsT=late["w4_q"][:, cols].bitcast(FP8X4),
                 lhsT_scale=late["w4_s"][:, cols],
                 rhs=h_q[k][:, b, part].bitcast(FP8X4),
                 rhs_scale=h_s[k][:, b, part] if k else s_a[b][:, part],
@@ -300,6 +307,7 @@ def tile_list_bond_angle_features_kernel(
         cast_w1(1)
         quant_w1(0)
         deal(ws_p, ws_raw, 2)
+        deal(w2_p, w2_raw, 4)
         deal(w3_p, w3_raw, 8)
         gather_words(2, "w3_raw", ((HALF, S), (0, HALF)))
         quant_w1(1)
@@ -307,52 +315,55 @@ def tile_list_bond_angle_features_kernel(
         def by_tile(tile):
             return [tile[:, t, :] for t in range(4)]
 
-        x_0 = sb([P, 4, 768], F32, "x_0", "w1_raw1")
+        x_0 = sb([P, 4, 1024], F32, "x_0", "w1_raw1")
         x_a0 = by_tile(x_0[:, :, 0:HALF])
         x_b = by_tile(x_0[:, :, HALF:768])
+        y_b = by_tile(x_0[:, :, 768:1024])
+        x_a1 = by_tile(sb([P, 4, HALF], F32, "x_a1"))
         d_a = [[sb([P, 4, HALF], F32, f"d_a{b}_{k}") for k in range(2)] for b in range(2)]
-        d_b = [sb([P, 4, 256], F32, f"d_b{k}") for k in range(2)]
+        d_b = [sb([P, 4, 256], F32, "d_b0", "w1_bf1"), sb([P, 4, 256], F32, "d_b1")]
         side1 = [sb([P, 4, 256], F32, f"side1_{k}") for k in range(2)]
         side0 = sb([P, 4, 256], F32, "side0")
 
         def chunk(c):
             return slice(c * CHUNK, (c + 1) * CHUNK)
 
-        scaled_read(x_b, [0], 0, [0, 1], HALF, 768, g_col, 3)
-        scaled_read(x_b, [0], 0, [2, 3], HALF, 768, g_col, 4)
-        scaled_read(x_a0, [0], 0, [0], 0, HALF, g_col, 5)
-        arms(d_b, x_b, 0, [0, 1], HALF, 768, g_col, 6)
-        arms(d_b, x_b, 0, [2, 3], HALF, 768, g_col, 0)
-        scaled_read(x_a0, [0], 0, [1], 0, HALF, g_col, 3)
-        scaled_read(x_a0, [0], 0, [2], 0, HALF, g_col, 4)
-        scaled_read(x_a0, [0], 0, [3], 0, HALF, g_hold[2], 5)
+        for k, ts in enumerate(([0, 1], [2, 3])):
+            scaled_read(x_b, [0], 0, ts, HALF, 768, g_col, 3 + k)
+            scaled_read(y_b, [1], 0, ts, HALF, 768, g_col, (5, 0)[k])
+            pair = slice(ts[0], ts[1] + 1)
+            nc.gpsimd.tensor_tensor(d_b[0][:, pair, :], x_0[:, pair, HALF:768], x_0[:, pair, 768:1024], ADD)
+        for k, ts in enumerate(([0, 1], [2, 3])):
+            lone_arm(d_b[1], x_b, 0, ts, HALF, 768, 6 + k)
+        for t in range(4):
+            scaled_read(x_a0, [0], 0, [t], 0, HALF, g_col, 1 + t)
         for c in range(2):
             product(nc.gpsimd, h_bf[1][:, 0, chunk(c)], d_b, c * CHUNK, (c + 1) * CHUNK)
-        cast_w4(0, "g_hold2")
-        cast_w4(1)
-        x_a1 = by_tile(sb([P, 4, HALF], F32, "x_a1", "w4_raw1"))
         for t in range(4):
-            arms(d_a[0], x_a0, 0, [t], 0, HALF, g_hold[0] if t == 2 else g_col)
+            arms(d_a[0], x_a0, 0, [t], 0, HALF, g_hold[0])
             scaled_read(x_a1, [0], 1, [t], 0, HALF)
-        quant_w4("g_hold0")
-        h_a[0] = sb([P, HALF, 4], BF16, "h_a0", "g_hold2")
+        h_a[0] = sb([P, HALF, 4], BF16, "h_a0")
         for c in range(4):
             product(nc.gpsimd, h_a[0][:, chunk(c)], d_a[0], c * CHUNK, (c + 1) * CHUNK)
         for t in range(4):
-            arms(d_a[1], x_a1, 1, [t], 0, HALF, g_hold[1])
             if t < 2:
                 for e in range(2):
                     scaled_read((by_tile(side1[0]), by_tile(side1[1])), [0, 1], 1, [2 * t + e], HALF, S)
             if t == 2:
                 scaled_read(by_tile(side0), [0, 2], 0, [0, 1], 768, S)
-                scaled_read(by_tile(side0), [0, 2], 0, [2, 3], 768, S)
+                scaled_read(by_tile(side0), [0, 2], 0, [2, 3], 768, S, g_hold[2])
+            arms(d_a[1], x_a1, 1, [t], 0, HALF, g_hold[1])
+        cast_w4(0, "g_hold2")
+        cast_w4(1)
         for c in (6, 7):
             first_arm(h_bf[2][:, 1, chunk(c - 6)], 2, 1, c, side1[1], 768)
             first_arm(h_bf[2][:, 0, chunk(c - 6)], 1, 0, c, side0, 768)
-        quant(2, None, "d_a0_0")
+        spent = [banks[3 + (len(turns["shared"]) + k) % 5] for k in range(2)]
+        quant_w4("d_a0_0", "side0")
+        quant(2, None, "d_a0_1")
         mix(2, ([0, 1], [2]))
         for c in (4, 5):
-            first_arm(h_bf[1][:, 1, chunk(c - 4)], 2, 1, c, side1[0], HALF)
+            first_arm(h_bf[1][:, 1, chunk(c - 4)], 2, 1, c, side1[0], HALF, open_arm(2, 1, c, spent[c - 4]))
         s_a[0] = sb([P, HALF], U8, "s_a0", "side1_0")
         s_a[1] = sb([P, HALF], U8, "s_a1")
         h_c = {}
@@ -367,7 +378,7 @@ def tile_list_bond_angle_features_kernel(
             )
 
         for c in range(4):
-            product_a1(c, ("d_a0_1", "h_bf512")[c % 2])
+            product_a1(c, ("g_hold2", "h_bf512")[c % 2])
             if c == 0:
                 quant(1)
                 mix(1, ([0, 1], [2]))

@@ -342,13 +342,14 @@ def tile_list_bond_angle_features_kernel(
         for t in range(4):
             arms(d_a[0], x_a0, 0, [t], 0, HALF, g_hold[0])
             scaled_read(x_a1, [0], 1, [t], 0, HALF)
+            if t >= 2:
+                scaled_read((by_tile(side1[0]), by_tile(side1[1])), [0, 1], 1, [t - 2], HALF, S)
         h_a[0] = sb([P, HALF, 4], BF16, "h_a0")
         for c in range(4):
             product(nc.gpsimd, h_a[0][:, chunk(c)], d_a[0], c * CHUNK, (c + 1) * CHUNK)
         for t in range(4):
             if t < 2:
-                for e in range(2):
-                    scaled_read((by_tile(side1[0]), by_tile(side1[1])), [0, 1], 1, [2 * t + e], HALF, S)
+                scaled_read((by_tile(side1[0]), by_tile(side1[1])), [0, 1], 1, [t + 2], HALF, S)
             if t == 2:
                 scaled_read(by_tile(side0), [0, 2], 0, [0, 1], 768, S)
                 scaled_read(by_tile(side0), [0, 2], 0, [2, 3], 768, S, g_hold[2])

@@ -49,69 +49,73 @@ def tile_list_bond_angle_features_kernel(
         lists = [keep.tile([P, S // 16], U16, name=f"list{l}") for l in range(3)]
         tab_s = sb([P, T // 4], I32, "tab_s")
         tab_w = sb([P, T], I32, "tab_w")
-        ws_raw = sb([P, H // 4], I32, "ws_raw")
+        ws_raw = [sb([P, H // 4], I32, f"ws_raw{k}") for k in range(2)]
         w1_raw = [sb([P, 4, H // 2], F32, f"w1_raw{b}") for b in range(2)]
         w2_raw = sb([P, H // 2], I32, "w2_raw")
         w3_raw = sb([P, H], I32, "w3_raw")
         w4_raw = [sb([P, 4, N], F32, f"w4_raw{b}") for b in range(2)]
-        g_rows = sb([P, P], F32, "g_rows")
+        g_rows = sb([P, 2 * P], F32, "g_rows")
         ident = sb([P, P], F32, "ident")
         g_col = sb([P, 8], F32, "g_col")
         g_safe = sb([P, 8], F32, "g_safe")
         g_inv = sb([P, 8], F32, "g_inv")
-        zeros = sb([P, P], F32, "zeros")
+        zeros = sb([P, 2 * P], F32, "zeros")
 
-        nc.vector.memset(tab_s[0:112, :], 0)
+        for k in range(2):
+            nc.gpsimd.memset(ws_raw[k][:], 0)
         nc.vector.memset(zeros[:], 0.0)
+        nc.vector.memset(tab_s[0:112, :], 0)
         planes = sb([P, 3, S // 4], I32, "planes")
         nc.vector.memset(planes[:], 0)
-        nc.vector.memset(ws_raw[:], 0)
-        nc.scalar.activation(g_rows[:], zeros[:], TANH)
+        nc.scalar.activation(g_rows[0 : P - 4, :], zeros[0 : P - 4, :], TANH)
         nc.gpsimd.affine_select(
-            out=ident[:], in_=zeros[:], compare_op=NOT_EQUAL, fill=1.0, base=0, pattern=[[-1, P]], channel_multiplier=1
+            out=ident[:], in_=zeros[:, 0:P], compare_op=NOT_EQUAL, fill=1.0, base=0, pattern=[[-1, P]], channel_multiplier=1
         )
 
         w1_rows = w1.rearrange("(p j) (b c) -> b p j c", j=4, b=2)
-        g_view = g.rearrange("(b q t i) -> b t q i", b=2, t=4, i=8)
+        g_view = g.rearrange("(q t i) -> t q i", t=4, i=8)
         w4_view = w4.rearrange("(b q t i) n -> b t q i n", b=2, t=4, i=8)
 
-        def load_scale_rows(k, src):
-            for r in range(4):
-                nc.scalar.dma_start(ws_raw[k + r : P : 32, :], src[0, r:16:4, :].bitcast(I32))
+        def load_scale_rows(k, src, rows):
+            for r in rows:
+                nc.sync.dma_start(ws_raw[k][r:P:32, :], src[0, r:16:4, :].bitcast(I32))
 
         nc.sync.dma_start(tab_s[112:P, :], tab_scales[0].bitcast(I32))
         nc.sync.dma_start(lists[0][:], offs)
         nc.sync.dma_start(lists[1][:], offs2)
         nc.sync.dma_start(lists[2][:], offs3)
-        nc.sync.dma_start(tab_w[:], tab_words[0].rearrange("p t i -> p (t i)").bitcast(I32))
-        for b in range(2):
-            nc.scalar.dma_start(g_rows[4 * b : 4 * b + 4, :].rearrange("t (q i) -> t q i", i=8), g_view[b])
-        load_scale_rows(0, w2_scales)
-        load_scale_rows(4, w3_scales)
         nc.sync.dma_start(w1_raw[0][:], w1_rows[0])
-        nc.sync.dma_start(w1_raw[1][:], w1_rows[1])
+        nc.sync.dma_start(g_rows[P - 4 : P, :].rearrange("t (q i) -> t q i", i=8), g_view)
+        load_scale_rows(0, w2_scales, (0, 1))
+        nc.sync.dma_start(tab_w[:], tab_words[0].rearrange("p t i -> p (t i)").bitcast(I32))
+        load_scale_rows(0, w2_scales, (2, 3))
+        load_scale_rows(1, w3_scales, (0,))
         nc.sync.dma_start(w2_raw[:], w2_words[0].bitcast(I32))
         nc.sync.dma_start(w3_raw[:], w3_words[0].rearrange("p e i -> p (e i)").bitcast(I32))
+        nc.sync.dma_start(w1_raw[1][:], w1_rows[1])
+        load_scale_rows(1, w3_scales, (1,))
 
         v_words = {}
         picked = sb([P, 3, S], U8, "picked")
         v_scales = [planes[:, l, :].bitcast(U8) for l in range(3)]
-        ws_p = sb([P, H // 4], I32, "ws_p")
+        ws_p = [sb([P, H // 4], I32, f"ws_p{k}") for k in range(2)]
         w2_p = sb([P, H // 2], I32, "w2_p")
         w3_p = sb([P, H], I32, "w3_p")
 
         def deal(dst, src, e):
-            nc.vector.tensor_copy(
-                dst[:].rearrange("p (b t q e) -> p b t q e", b=2, t=4, e=e),
-                src[:].rearrange("p (b q t e) -> p b t q e", b=2, t=4, e=e),
+            nc.scalar.copy(
+                dst[:].bitcast(U32).rearrange("p (b t q e) -> p b t q e", b=2, t=4, e=e),
+                src[:].bitcast(U32).rearrange("p (b q t e) -> p b t q e", b=2, t=4, e=e),
             )
 
         g_bank = scalar_bank()
-        nc.tensor.transpose(g_bank[:, 0:P], g_rows[:], ident[:])
-        nc.scalar.copy(g_col[:], g_bank[:, 0:8])
+        for b in range(2):
+            nc.tensor.transpose(g_bank[:, b * P : (b + 1) * P], g_rows[:, b * P : (b + 1) * P], ident[:])
+        g_turned = g_bank[:, 0 : 2 * P].rearrange("p (b c) -> p b c", b=2)[:, :, P - 4 : P]
+        nc.scalar.copy(g_col[:].rearrange("p (b t) -> p b t", b=2), g_turned)
         g_hold = [sb([P, 8], F32, f"g_hold{k}") for k in range(3)]
         for k in range(3):
-            nc.scalar.copy(g_hold[k][:], g_bank[:, 0:8])
+            nc.scalar.copy(g_hold[k][:].rearrange("p (b t) -> p b t", b=2), g_turned)
         for l in range(3):
             nc.vector.tensor_copy(picked[:, l, :], tab_s[:].bitcast(U8).indirect(lists[l][:]))
         for r in range(4):
@@ -119,6 +123,7 @@ def tile_list_bond_angle_features_kernel(
                 planes[r:P:32].rearrange("p l s -> p (l s)"),
                 picked[112 + r : P : 4].rearrange("p l s -> p (l s)").bitcast(I32),
             )
+        load_scale_rows(1, w3_scales, (2, 3))
         for u in range(8):
             nc.sync.dma_start(w4_raw[u // 4][:, u % 4, :], w4_view[u // 4, u % 4])
 
@@ -176,8 +181,8 @@ def tile_list_bond_angle_features_kernel(
             if l == 0:
                 return w1_q[b][:, t * P : (t + 1) * P].bitcast(FP8X4), w1_s[b][:, t * P : (t + 1) * P]
             if l == 1:
-                return w2_p[:, u * 64 : (u + 1) * 64].bitcast(U8).bitcast(FP4X4), ws_p[:, u * 32 : (u + 1) * 32].bitcast(U8)
-            return w3_p[:, u * P : (u + 1) * P].bitcast(FP8X4), ws_p[4:P, u * 32 : (u + 1) * 32].bitcast(U8)
+                return w2_p[:, u * 64 : (u + 1) * 64].bitcast(U8).bitcast(FP4X4), ws_p[0][:, u * 32 : (u + 1) * 32].bitcast(U8)
+            return w3_p[:, u * P : (u + 1) * P].bitcast(FP8X4), ws_p[1][:, u * 32 : (u + 1) * 32].bitcast(U8)
 
         def project(dst, ls, b, t, lo, hi):
             for n, l in enumerate(ls):
@@ -304,21 +309,23 @@ def tile_list_bond_angle_features_kernel(
         nc.vector.scalar_tensor_tensor(g_safe[:], g_col[:], 0.0, g_col[:], IS_EQUAL, ADD)
         gather_words(1)
         nc.vector.reciprocal(g_inv[:], g_safe[:])
-        cast_w1(1)
         quant_w1(0)
-        deal(ws_p, ws_raw, 2)
+        deal(ws_p[0], ws_raw[0], 2)
         deal(w2_p, w2_raw, 4)
         deal(w3_p, w3_raw, 8)
+        cast_w1(1)
+        deal(ws_p[1], ws_raw[1], 2)
         gather_words(2, "w3_raw", ((HALF, S), (0, HALF)))
         quant_w1(1)
 
         def by_tile(tile):
             return [tile[:, t, :] for t in range(4)]
 
-        x_0 = sb([P, 4, 1024], F32, "x_0", "w1_raw1")
+        x_0 = sb([P, 4, 768], F32, "x_0", "w1_raw1")
         x_a0 = by_tile(x_0[:, :, 0:HALF])
-        x_b = by_tile(x_0[:, :, HALF:768])
-        y_b = by_tile(x_0[:, :, 768:1024])
+        x_b0 = sb([P, 4, 256], F32, "x_b0")
+        x_b = by_tile(x_b0)
+        y_b = by_tile(x_0[:, :, HALF:768])
         x_a1 = by_tile(sb([P, 4, HALF], F32, "x_a1"))
         d_a = [[sb([P, 4, HALF], F32, f"d_a{b}_{k}") for k in range(2)] for b in range(2)]
         d_b = [sb([P, 4, 256], F32, "d_b0", "w1_bf1"), sb([P, 4, 256], F32, "d_b1")]
@@ -330,9 +337,10 @@ def tile_list_bond_angle_features_kernel(
 
         for k, ts in enumerate(([0, 1], [2, 3])):
             scaled_read(x_b, [0], 0, ts, HALF, 768, g_col, 3 + k)
+        for k, ts in enumerate(([0, 1], [2, 3])):
             scaled_read(y_b, [1], 0, ts, HALF, 768, g_col, (5, 0)[k])
             pair = slice(ts[0], ts[1] + 1)
-            nc.gpsimd.tensor_tensor(d_b[0][:, pair, :], x_0[:, pair, HALF:768], x_0[:, pair, 768:1024], ADD)
+            nc.gpsimd.tensor_tensor(d_b[0][:, pair, :], x_b0[:, pair, :], x_0[:, pair, HALF:768], ADD)
         for k, ts in enumerate(([0, 1], [2, 3])):
             lone_arm(d_b[1], x_b, 0, ts, HALF, 768, 6 + k)
         for t in range(4):

@@ -254,7 +254,7 @@ def tile_list_bond_angle_features_kernel(
 
         spans = ((0, 512), (512, 768), (768, 1024))
         h_bf = [None] + [sb([P, 2, hi - lo, 4], BF16, f"h_bf{lo}") for lo, hi in spans[1:]]
-        h_q = [sb([P, 2, hi - lo], U32, f"h_q{lo}") for lo, hi in spans]
+        h_q = {k: sb([P, 2, 256], U32, f"h_q{k}") for k in (1, 2)}
         h_s = {}
         h_a = {}
         s_a = {}
@@ -359,21 +359,25 @@ def tile_list_bond_angle_features_kernel(
             if t < 2:
                 scaled_read((by_tile(side1[0]), by_tile(side1[1])), [0, 1], 1, [t + 2], HALF, S)
             if t == 2:
-                scaled_read(by_tile(side0), [0, 2], 0, [0, 1], 768, S)
-                scaled_read(by_tile(side0), [0, 2], 0, [2, 3], 768, S, g_hold[2])
+                scaled_read(by_tile(side0), [0, 1], 0, [0, 1], 768, S)
+                scaled_read(by_tile(side0), [0, 1], 0, [2, 3], 768, S, g_hold[2])
             arms(d_a[1], x_a1, 1, [t], 0, HALF, g_hold[1])
+        h_g = sb([P, 2 * CHUNK, 4], BF16, "h_g")
+        for c in range(2):
+            product(nc.gpsimd, h_g[:, chunk(c)], d_a[1], c * CHUNK, (c + 1) * CHUNK)
         cast_w4(0, "g_hold2")
         cast_w4(1)
         for c in (6, 7):
             first_arm(h_bf[2][:, 1, chunk(c - 6)], 2, 1, c, side1[1], 768)
-            first_arm(h_bf[2][:, 0, chunk(c - 6)], 1, 0, c, side0, 768)
-        spent = [banks[3 + (len(turns["shared"]) + k) % 5] for k in range(2)]
+            first_arm(h_bf[2][:, 0, chunk(c - 6)], 2, 0, c, side0, 768)
+        first_arm(h_bf[1][:, 1, chunk(0)], 2, 1, 4, side1[0], HALF)
+        spent = banks[3 + (len(turns["shared"]) + 1) % 5]
         quant_w4("d_a0_0", "side0")
         quant(2, None, "d_a0_1")
         mix(2, ([0, 1], [2]))
-        for c in (4, 5):
-            first_arm(h_bf[1][:, 1, chunk(c - 4)], 2, 1, c, side1[0], HALF, open_arm(2, 1, c, spent[c - 4]))
-        s_a[0] = sb([P, HALF], U8, "s_a0", "side1_0")
+        first_arm(h_bf[1][:, 1, chunk(1)], 2, 1, 5, side1[0], HALF, open_arm(2, 1, 5, spent))
+        h_q[0] = sb([P, 2, HALF], U32, "h_q0", "side1_0")
+        s_a[0] = sb([P, HALF], U8, "s_a0")
         s_a[1] = sb([P, HALF], U8, "s_a1")
         h_c = {}
 
@@ -381,24 +385,24 @@ def tile_list_bond_angle_features_kernel(
             h_c[c] = sb([P, CHUNK, 4], BF16, f"h_c{c}", tag)
             product(nc.vector, h_c[c][:], d_a[1], c * CHUNK, (c + 1) * CHUNK)
 
-        def quant_a1(c):
-            nc.vector.quantize_mx(
-                h_q[0][:, 1, chunk(c)].bitcast(FP8X4), s_a[1][:, chunk(c)], h_c[c][:].rearrange("p n t -> p (n t)")
-            )
+        def quant_a1(lo, hi, src):
+            nc.vector.quantize_mx(h_q[0][:, 1, lo:hi].bitcast(FP8X4), s_a[1][:, lo:hi], src.rearrange("p n t -> p (n t)"))
 
-        for c in range(4):
-            product_a1(c, ("g_hold2", "h_bf512")[c % 2])
-            if c == 0:
-                quant(1)
-                mix(1, ([0, 1], [2]))
-            quant_a(0, c * CHUNK, (c + 1) * CHUNK)
-            if c < 3:
-                quant_a1(c)
-                mix(0, ([0, 1, 2],), c * CHUNK, (c + 1) * CHUNK)
+        quant_a(0, 0, 256)
+        quant_a1(0, 256, h_g[:])
+        mix(0, ([0, 1], [2]), 0, 256)
+        quant(1)
+        mix(1, ([0, 1], [2]))
+        product_a1(2, "g_hold2")
+        quant_a(0, 256, 384)
+        quant_a1(256, 384, h_c[2][:])
+        mix(0, ([0, 1, 2],), 256, 384)
+        product_a1(3, "h_bf512")
+        quant_a(0, 384, HALF)
         last = [shared_bank()[:, 0:CHUNK] for m in range(3)]
         for m in range(3):
             mix_pass(last[m], 0, m, 0, chunk(3))
-        quant_a1(3)
+        quant_a1(384, HALF, h_c[3][:])
         for m in range(3):
             mix_pass(last[m], 0, m, 1, chunk(3))
             nc.scalar.activation(res[:, m, chunk(3)], last[m], TANH)

@@ -37,11 +37,11 @@ def tile_list_bond_angle_features_kernel(
 
         def scalar_bank():
             turns["scalar"].append(0)
-            return banks[len(turns["scalar"]) % 3]
+            return banks[(len(turns["scalar"]) + 1) % 3]
 
         def shared_bank():
             turns["shared"].append(0)
-            return banks[3 + (len(turns["shared"]) + 1) % 5]
+            return banks[3 + (len(turns["shared"]) + 2) % 5]
 
         def sb(shape, dtype, name, tag=None):
             return keep.tile(shape, dtype, align_bytes=64, name=name, tag=tag or name)
@@ -50,7 +50,7 @@ def tile_list_bond_angle_features_kernel(
         tab_s = sb([P, T // 4], I32, "tab_s")
         tab_w = sb([P, T], I32, "tab_w")
         ws_raw = [sb([P, H // 4], I32, f"ws_raw{k}") for k in range(2)]
-        w1_raw = [sb([P, 4, H // 2], F32, f"w1_raw{b}") for b in range(2)]
+        w1_raw = [sb([P, 4, 512], F32, "w1_raw0"), sb([P, 4, 256], F32, "w1_raw1"), sb([P, 4, 256], F32, "w1_raw2")]
         w2_raw = sb([P, H // 2], I32, "w2_raw")
         w3_raw = sb([P, H], I32, "w3_raw")
         w4_raw = [sb([P, 4, N], F32, f"w4_raw{b}") for b in range(2)]
@@ -72,7 +72,7 @@ def tile_list_bond_angle_features_kernel(
             out=ident[:], in_=zeros[:, 0:P], compare_op=NOT_EQUAL, fill=1.0, base=0, pattern=[[-1, P]], channel_multiplier=1
         )
 
-        w1_rows = w1.rearrange("(p j) (b c) -> b p j c", j=4, b=2)
+        w1_rows = w1.rearrange("(p j) c -> p j c", j=4)
         g_view = g.rearrange("(q t i) -> t q i", t=4, i=8)
         w4_view = w4.rearrange("(b q t i) n -> b t q i n", b=2, t=4, i=8)
 
@@ -84,7 +84,7 @@ def tile_list_bond_angle_features_kernel(
         nc.sync.dma_start(lists[0][:], offs)
         nc.sync.dma_start(lists[1][:], offs2)
         nc.sync.dma_start(lists[2][:], offs3)
-        nc.sync.dma_start(w1_raw[0][:], w1_rows[0])
+        nc.sync.dma_start(w1_raw[0][:], w1_rows[:, :, 0:512])
         nc.sync.dma_start(g_rows[P - 4 : P, :].rearrange("t (q i) -> t q i", i=8), g_view)
         load_scale_rows(0, w2_scales, (0, 1))
         nc.sync.dma_start(tab_w[:], tab_words[0].rearrange("p t i -> p (t i)").bitcast(I32))
@@ -92,8 +92,7 @@ def tile_list_bond_angle_features_kernel(
         load_scale_rows(1, w3_scales, (0,))
         nc.sync.dma_start(w2_raw[:], w2_words[0].bitcast(I32))
         nc.sync.dma_start(w3_raw[:], w3_words[0].rearrange("p e i -> p (e i)").bitcast(I32))
-        nc.sync.dma_start(w1_raw[1][:], w1_rows[1])
-        load_scale_rows(1, w3_scales, (1,))
+        nc.sync.dma_start(w1_raw[1][:], w1_rows[:, :, 512:768])
 
         v_words = {}
         picked = sb([P, 3, S], U8, "picked")
@@ -113,9 +112,9 @@ def tile_list_bond_angle_features_kernel(
             nc.tensor.transpose(g_bank[:, b * P : (b + 1) * P], g_rows[:, b * P : (b + 1) * P], ident[:])
         g_turned = g_bank[:, 0 : 2 * P].rearrange("p (b c) -> p b c", b=2)[:, :, P - 4 : P]
         nc.scalar.copy(g_col[:].rearrange("p (b t) -> p b t", b=2), g_turned)
-        g_hold = [sb([P, 8], F32, f"g_hold{k}") for k in range(3)]
-        for k in range(3):
-            nc.scalar.copy(g_hold[k][:].rearrange("p (b t) -> p b t", b=2), g_turned)
+        g_last = [sb([P, 8], F32, f"g_last{b}") for b in range(2)]
+        for b in range(2):
+            nc.scalar.copy(g_last[b][:].rearrange("p (b t) -> p b t", b=2), g_turned)
         for l in range(3):
             nc.vector.tensor_copy(picked[:, l, :], tab_s[:].bitcast(U8).indirect(lists[l][:]))
         for r in range(4):
@@ -123,7 +122,8 @@ def tile_list_bond_angle_features_kernel(
                 planes[r:P:32].rearrange("p l s -> p (l s)"),
                 picked[112 + r : P : 4].rearrange("p l s -> p (l s)").bitcast(I32),
             )
-        load_scale_rows(1, w3_scales, (2, 3))
+        nc.sync.dma_start(w1_raw[2][:], w1_rows[:, :, 768:1024])
+        load_scale_rows(1, w3_scales, (1, 2, 3))
         for u in range(8):
             nc.sync.dma_start(w4_raw[u // 4][:, u % 4, :], w4_view[u // 4, u % 4])
 
@@ -137,12 +137,12 @@ def tile_list_bond_angle_features_kernel(
         w1_q = [sb([P, H // 2], U32, f"w1_q{b}") for b in range(2)]
         w1_s = [sb([P, H // 2], U8, f"w1_s{b}") for b in range(2)]
 
-        def cast_w1(b):
-            src = w1_raw[b][:].rearrange("p j (q t i) -> p t q j i", t=4, i=8)
+        def cast_w1(k, b, qs):
+            src = w1_raw[k][:].rearrange("p j (q t i) -> p t q j i", t=4, i=8)
             for t in range(4):
                 for i in (0, 4):
                     nc.scalar.activation(
-                        w1_bf[b][:, t, :, i : i + 4].rearrange("p q i j -> p q j i"),
+                        w1_bf[b][:, t, qs, i : i + 4].rearrange("p q i j -> p q j i"),
                         src[:, t, :, :, i : i + 4],
                         COPY,
                         scale=-1.0,
@@ -155,12 +155,10 @@ def tile_list_bond_angle_features_kernel(
 
         late = {}
 
-        def cast_w4(b, tag=None):
-            if b == 0:
-                late["w4_bf"] = sb([P, 2 * N, 4], BF16, "w4_bf", tag)
-            w4_bf = late["w4_bf"]
+        def cast_w4(b):
+            late[b] = sb([P, N, 4], BF16, f"w4_bf{b}", f"g_last{b}")
             nc.scalar.activation(
-                w4_bf[:, b * N : (b + 1) * N, :].rearrange("p (c i) t -> p c t i", i=4),
+                late[b][:].rearrange("p (c i) t -> p c t i", i=4),
                 w4_raw[b][:].rearrange("p t (c i) -> p c t i", i=4),
                 COPY,
             )
@@ -170,11 +168,9 @@ def tile_list_bond_angle_features_kernel(
             late["w4_q"] = w4_q
             w4_s = sb([P, 2 * N], U8, "w4_s", tag_s)
             late["w4_s"] = w4_s
-            w4_bf = late["w4_bf"]
-            for lo, hi in ((0, 512), (512, 768)):
-                nc.vector.quantize_mx(
-                    w4_q[:, lo:hi].bitcast(FP8X4), w4_s[:, lo:hi], w4_bf[:, lo:hi, :].rearrange("p n t -> p (n t)")
-                )
+            for b in range(2):
+                cols = slice(b * N, (b + 1) * N)
+                nc.vector.quantize_mx(w4_q[:, cols].bitcast(FP8X4), w4_s[:, cols], late[b][:].rearrange("p n t -> p (n t)"))
 
         def weight(l, b, t):
             u = 4 * b + t
@@ -206,14 +202,8 @@ def tile_list_bond_angle_features_kernel(
             bank = (scalar_bank() if bank is None else banks[bank])[:].rearrange("p (e n) -> p e n", e=len(ts))
             for e, t in enumerate(ts):
                 project(bank[:, e, :], ls, b, t, lo, hi)
-            for e, t in enumerate(ts):
-                if isinstance(dst, tuple):
-                    for half in range(2):
-                        nc.scalar.activation(
-                            dst[half][t], bank[:, e, half * 256 : (half + 1) * 256], COPY, scale=gain(col, b, t)
-                        )
-                else:
-                    nc.scalar.activation(dst[t], bank[:, e, :], COPY, scale=gain(col, b, t))
+            for e, t in reversed(list(enumerate(ts))):
+                nc.scalar.activation(dst[t], bank[:, e, :], COPY, scale=gain(col, b, t))
 
         def arms(d, x, b, ts, lo, hi, col=g_col, own=None):
             pair = [(shared_bank() if own is None else banks[own + l])[:].rearrange("p (e n) -> p e n", e=len(ts)) for l in range(2)]
@@ -221,15 +211,15 @@ def tile_list_bond_angle_features_kernel(
                 for e, t in enumerate(ts):
                     project(pair[l][:, e, :], [l + 1], b, t, lo, hi)
             for e, t in enumerate(ts):
-                nc.vector.scalar_tensor_tensor(d[0][:, t, :], pair[0][:, e, :], gain(col, b, t), x[t], MULT, ADD)
-            for e, t in enumerate(ts):
                 nc.vector.scalar_tensor_tensor(d[1][:, t, :], x[t], gain(g_inv, b, t), pair[1][:, e, :], MULT, ADD)
+            for e, t in enumerate(ts):
+                nc.vector.scalar_tensor_tensor(d[0][:, t, :], pair[0][:, e, :], gain(col, b, t), x[t], MULT, ADD)
 
-        def lone_arm(d, x, b, ts, lo, hi, own):
-            bank = banks[own][:].rearrange("p (e n) -> p e n", e=len(ts))
+        def lone_arm(d, x, b, ts, lo, hi):
+            bank = shared_bank()[:].rearrange("p (e n) -> p e n", e=len(ts))
             for e, t in enumerate(ts):
                 project(bank[:, e, :], [2], b, t, lo, hi)
-            for e, t in enumerate(ts):
+            for e, t in reversed(list(enumerate(ts))):
                 nc.vector.scalar_tensor_tensor(d[:, t, :], x[t], gain(g_inv, b, t), bank[:, e, :], MULT, ADD)
 
         def woven(ap):
@@ -254,7 +244,7 @@ def tile_list_bond_angle_features_kernel(
 
         spans = ((0, 512), (512, 768), (768, 1024))
         h_bf = [None] + [sb([P, 2, hi - lo, 4], BF16, f"h_bf{lo}") for lo, hi in spans[1:]]
-        h_q = {k: sb([P, 2, 256], U32, f"h_q{k}") for k in (1, 2)}
+        h_q = {1: sb([P, 2, 256], U32, "h_q1")}
         h_s = {}
         h_a = {}
         s_a = {}
@@ -304,7 +294,7 @@ def tile_list_bond_angle_features_kernel(
                 nc.scalar.activation(res[:, ms[0] : ms[-1] + 1, lo:hi], bank, TANH)
                 nc.sync.dma_start(out_view[:, ms[0] : ms[-1] + 1, lo:hi], res[:, ms[0] : ms[-1] + 1, lo:hi])
 
-        cast_w1(0)
+        cast_w1(0, 0, slice(0, 16))
         gather_words(0)
         nc.vector.scalar_tensor_tensor(g_safe[:], g_col[:], 0.0, g_col[:], IS_EQUAL, ADD)
         gather_words(1)
@@ -313,23 +303,24 @@ def tile_list_bond_angle_features_kernel(
         deal(ws_p[0], ws_raw[0], 2)
         deal(w2_p, w2_raw, 4)
         deal(w3_p, w3_raw, 8)
-        cast_w1(1)
+        cast_w1(1, 1, slice(0, 8))
+        cast_w1(2, 1, slice(8, 16))
         deal(ws_p[1], ws_raw[1], 2)
-        gather_words(2, "w3_raw", ((HALF, S), (0, HALF)))
+        gather_words(2, None, ((HALF, S), (0, HALF)))
         quant_w1(1)
 
         def by_tile(tile):
             return [tile[:, t, :] for t in range(4)]
 
-        x_0 = sb([P, 4, 768], F32, "x_0", "w1_raw1")
+        x_0 = sb([P, 4, 768], F32, "x_0", "ws_raw1")
         x_a0 = by_tile(x_0[:, :, 0:HALF])
-        x_b0 = sb([P, 4, 256], F32, "x_b0")
+        x_b0 = sb([P, 4, 256], F32, "x_b0", "w3_raw")
         x_b = by_tile(x_b0)
         y_b = by_tile(x_0[:, :, HALF:768])
         x_a1 = by_tile(sb([P, 4, HALF], F32, "x_a1"))
         d_a = [[sb([P, 4, HALF], F32, f"d_a{b}_{k}") for k in range(2)] for b in range(2)]
         d_b = [sb([P, 4, 256], F32, "d_b0", "w1_bf1"), sb([P, 4, 256], F32, "d_b1")]
-        side1 = [sb([P, 4, 256], F32, f"side1_{k}") for k in range(2)]
+        side1 = sb([P, 4, HALF], F32, "side1")
         side0 = sb([P, 4, 256], F32, "side0")
 
         def chunk(c):
@@ -338,71 +329,60 @@ def tile_list_bond_angle_features_kernel(
         for k, ts in enumerate(([0, 1], [2, 3])):
             scaled_read(x_b, [0], 0, ts, HALF, 768, g_col, 3 + k)
         for k, ts in enumerate(([0, 1], [2, 3])):
-            scaled_read(y_b, [1], 0, ts, HALF, 768, g_col, (5, 0)[k])
+            scaled_read(y_b, [1], 0, ts, HALF, 768, g_col, (5, None)[k])
             pair = slice(ts[0], ts[1] + 1)
             nc.gpsimd.tensor_tensor(d_b[0][:, pair, :], x_b0[:, pair, :], x_0[:, pair, HALF:768], ADD)
         for k, ts in enumerate(([0, 1], [2, 3])):
-            lone_arm(d_b[1], x_b, 0, ts, HALF, 768, 6 + k)
+            lone_arm(d_b[1], x_b, 0, ts, HALF, 768)
         for t in range(4):
-            scaled_read(x_a0, [0], 0, [t], 0, HALF, g_col, 1 + t)
+            scaled_read(x_a0, [0], 0, [t], 0, HALF)
         for c in range(2):
             product(nc.gpsimd, h_bf[1][:, 0, chunk(c)], d_b, c * CHUNK, (c + 1) * CHUNK)
         for t in range(4):
-            arms(d_a[0], x_a0, 0, [t], 0, HALF, g_hold[0])
+            arms(d_a[0], x_a0, 0, [t], 0, HALF)
             scaled_read(x_a1, [0], 1, [t], 0, HALF)
             if t >= 2:
-                scaled_read((by_tile(side1[0]), by_tile(side1[1])), [0, 1], 1, [t - 2], HALF, S)
+                scaled_read(by_tile(side1), [0, 1], 1, [t - 2], HALF, S)
         h_a[0] = sb([P, HALF, 4], BF16, "h_a0")
         for c in range(4):
             product(nc.gpsimd, h_a[0][:, chunk(c)], d_a[0], c * CHUNK, (c + 1) * CHUNK)
         for t in range(4):
+            arms(d_a[1], x_a1, 1, [t], 0, HALF)
             if t < 2:
-                scaled_read((by_tile(side1[0]), by_tile(side1[1])), [0, 1], 1, [t + 2], HALF, S)
-            if t == 2:
-                scaled_read(by_tile(side0), [0, 1], 0, [0, 1], 768, S)
-                scaled_read(by_tile(side0), [0, 1], 0, [2, 3], 768, S, g_hold[2])
-            arms(d_a[1], x_a1, 1, [t], 0, HALF, g_hold[1])
-        h_g = sb([P, 2 * CHUNK, 4], BF16, "h_g")
-        for c in range(2):
-            product(nc.gpsimd, h_g[:, chunk(c)], d_a[1], c * CHUNK, (c + 1) * CHUNK)
-        cast_w4(0, "g_hold2")
-        cast_w4(1)
+                scaled_read(by_tile(side1), [0, 1], 1, [t + 2], HALF, S, (g_col, g_last[0])[t])
+            else:
+                scaled_read(by_tile(side0), [0, 1], 0, [2 * t - 4, 2 * t - 3], 768, S, (g_col, g_last[1])[t - 2])
+            if t % 2:
+                cast_w4(t // 2)
         for c in (6, 7):
-            first_arm(h_bf[2][:, 1, chunk(c - 6)], 2, 1, c, side1[1], 768)
+            first_arm(h_bf[2][:, 1, chunk(c - 6)], 2, 1, c, side1, HALF)
+        first_arm(h_bf[1][:, 1, chunk(0)], 2, 1, 4, side1, HALF)
+        for c in (6, 7):
             first_arm(h_bf[2][:, 0, chunk(c - 6)], 2, 0, c, side0, 768)
-        first_arm(h_bf[1][:, 1, chunk(0)], 2, 1, 4, side1[0], HALF)
-        spent = banks[3 + (len(turns["shared"]) + 1) % 5]
-        quant_w4("d_a0_0", "side0")
-        quant(2, None, "d_a0_1")
+        spent = banks[3 + (len(turns["shared"]) + 2) % 5]
+
+        h_q[2] = sb([P, 2, 256], U32, "h_q2", "d_a0_1")
+        quant(2)
+        quant_w4(None, "side0")
+        h_a[1] = sb([P, HALF, 4], BF16, "h_a1", "g_last0")
         mix(2, ([0, 1], [2]))
-        first_arm(h_bf[1][:, 1, chunk(1)], 2, 1, 5, side1[0], HALF, open_arm(2, 1, 5, spent))
-        h_q[0] = sb([P, 2, HALF], U32, "h_q0", "side1_0")
+        first_arm(h_bf[1][:, 1, chunk(1)], 2, 1, 5, side1, HALF, open_arm(2, 1, 5, spent))
+        h_q[0] = sb([P, 2, HALF], U32, "h_q0", "side1")
         s_a[0] = sb([P, HALF], U8, "s_a0")
         s_a[1] = sb([P, HALF], U8, "s_a1")
-        h_c = {}
-
-        def product_a1(c, tag):
-            h_c[c] = sb([P, CHUNK, 4], BF16, f"h_c{c}", tag)
-            product(nc.vector, h_c[c][:], d_a[1], c * CHUNK, (c + 1) * CHUNK)
-
-        def quant_a1(lo, hi, src):
-            nc.vector.quantize_mx(h_q[0][:, 1, lo:hi].bitcast(FP8X4), s_a[1][:, lo:hi], src.rearrange("p n t -> p (n t)"))
-
-        quant_a(0, 0, 256)
-        quant_a1(0, 256, h_g[:])
-        mix(0, ([0, 1], [2]), 0, 256)
-        quant(1)
-        mix(1, ([0, 1], [2]))
-        product_a1(2, "g_hold2")
-        quant_a(0, 256, 384)
-        quant_a1(256, 384, h_c[2][:])
-        mix(0, ([0, 1, 2],), 256, 384)
-        product_a1(3, "h_bf512")
-        quant_a(0, 384, HALF)
+        for c in range(4):
+            product(nc.vector, h_a[1][:, chunk(c)], d_a[1], c * CHUNK, (c + 1) * CHUNK)
+            if c == 0:
+                quant(1)
+                mix(1, ([0, 1], [2]))
+            quant_a(0, c * CHUNK, (c + 1) * CHUNK)
+            if c < 3:
+                quant_a(1, c * CHUNK, (c + 1) * CHUNK)
+                mix(0, ([0, 1, 2],), c * CHUNK, (c + 1) * CHUNK)
         last = [shared_bank()[:, 0:CHUNK] for m in range(3)]
         for m in range(3):
             mix_pass(last[m], 0, m, 0, chunk(3))
-        quant_a1(384, HALF, h_c[3][:])
+        quant_a(1, 3 * CHUNK, HALF)
         for m in range(3):
             mix_pass(last[m], 0, m, 1, chunk(3))
             nc.scalar.activation(res[:, m, chunk(3)], last[m], TANH)

@@ -37,11 +37,11 @@ def tile_list_bond_angle_features_kernel(
 
         def scalar_bank():
             turns["scalar"].append(0)
-            return banks[(len(turns["scalar"]) + 1) % 3]
+            return banks[(len(turns["scalar"]) + 2) % 4]
 
         def shared_bank():
             turns["shared"].append(0)
-            return banks[3 + (len(turns["shared"]) + 2) % 5]
+            return banks[4 + (len(turns["shared"]) + 3) % 4]
 
         def sb(shape, dtype, name, tag=None):
             return keep.tile(shape, dtype, align_bytes=64, name=name, tag=tag or name)
@@ -223,10 +223,10 @@ def tile_list_bond_angle_features_kernel(
                 nc.vector.scalar_tensor_tensor(d[:, t, :], x[t], gain(g_inv, b, t), bank[:, e, :], MULT, ADD)
 
         def woven(ap):
-            return ap.rearrange("p t (c i) -> p c t i", i=2)
+            return ap.rearrange("p t (c i) -> p c t i", i=4)
 
         def h_view(ap):
-            return ap.rearrange("p (c i) t -> p c t i", i=2)
+            return ap.rearrange("p (c i) t -> p c t i", i=4)
 
         def product(engine, dst, d, lo, hi):
             engine.tensor_tensor(h_view(dst), woven(d[0][:, :, lo:hi]), woven(d[1][:, :, lo:hi]), MULT)
@@ -249,10 +249,9 @@ def tile_list_bond_angle_features_kernel(
         h_a = {}
         s_a = {}
 
-        def quant_a(b, lo, hi):
-            nc.vector.quantize_mx(
-                h_q[0][:, b, lo:hi].bitcast(FP8X4), s_a[b][:, lo:hi], h_a[b][:, lo:hi].rearrange("p n t -> p (n t)")
-            )
+        def quant_a(b, lo, hi, src=None):
+            src = h_a[b][:, lo:hi] if src is None else src
+            nc.vector.quantize_mx(h_q[0][:, b, lo:hi].bitcast(FP8X4), s_a[b][:, lo:hi], src.rearrange("p n t -> p (n t)"))
 
         res = sb([P, 3, S], F32, "res")
 
@@ -327,25 +326,24 @@ def tile_list_bond_angle_features_kernel(
             return slice(c * CHUNK, (c + 1) * CHUNK)
 
         for k, ts in enumerate(([0, 1], [2, 3])):
-            scaled_read(x_b, [0], 0, ts, HALF, 768, g_col, 3 + k)
+            scaled_read(x_b, [0], 0, ts, HALF, 768, g_col, 6 + k)
         for k, ts in enumerate(([0, 1], [2, 3])):
-            scaled_read(y_b, [1], 0, ts, HALF, 768, g_col, (5, None)[k])
+            scaled_read(y_b, [1], 0, ts, HALF, 768, g_col)
             pair = slice(ts[0], ts[1] + 1)
             nc.gpsimd.tensor_tensor(d_b[0][:, pair, :], x_b0[:, pair, :], x_0[:, pair, HALF:768], ADD)
         for k, ts in enumerate(([0, 1], [2, 3])):
             lone_arm(d_b[1], x_b, 0, ts, HALF, 768)
         for t in range(4):
             scaled_read(x_a0, [0], 0, [t], 0, HALF)
-        for c in range(2):
-            product(nc.gpsimd, h_bf[1][:, 0, chunk(c)], d_b, c * CHUNK, (c + 1) * CHUNK)
+        product(nc.gpsimd, h_bf[1][:, 0], d_b, 0, 256)
         for t in range(4):
             arms(d_a[0], x_a0, 0, [t], 0, HALF)
             scaled_read(x_a1, [0], 1, [t], 0, HALF)
             if t >= 2:
                 scaled_read(by_tile(side1), [0, 1], 1, [t - 2], HALF, S)
         h_a[0] = sb([P, HALF, 4], BF16, "h_a0")
-        for c in range(4):
-            product(nc.gpsimd, h_a[0][:, chunk(c)], d_a[0], c * CHUNK, (c + 1) * CHUNK)
+        for lo in (0, 256):
+            product(nc.gpsimd, h_a[0][:, lo : lo + 256], d_a[0], lo, lo + 256)
         for t in range(4):
             arms(d_a[1], x_a1, 1, [t], 0, HALF)
             if t < 2:
@@ -354,35 +352,40 @@ def tile_list_bond_angle_features_kernel(
                 scaled_read(by_tile(side0), [0, 1], 0, [2 * t - 4, 2 * t - 3], 768, S, (g_col, g_last[1])[t - 2])
             if t % 2:
                 cast_w4(t // 2)
+        h_g = sb([P, CHUNK, 4], BF16, "h_g")
+        product(nc.gpsimd, h_g[:], d_a[1], 0, CHUNK)
         for c in (6, 7):
             first_arm(h_bf[2][:, 1, chunk(c - 6)], 2, 1, c, side1, HALF)
-        first_arm(h_bf[1][:, 1, chunk(0)], 2, 1, 4, side1, HALF)
         for c in (6, 7):
             first_arm(h_bf[2][:, 0, chunk(c - 6)], 2, 0, c, side0, 768)
-        spent = banks[3 + (len(turns["shared"]) + 2) % 5]
+        spent = [banks[4 + (len(turns["shared"]) + 2 + k) % 4] for k in range(2)]
 
         h_q[2] = sb([P, 2, 256], U32, "h_q2", "d_a0_1")
         quant(2)
         quant_w4(None, "side0")
-        h_a[1] = sb([P, HALF, 4], BF16, "h_a1", "g_last0")
         mix(2, ([0, 1], [2]))
-        first_arm(h_bf[1][:, 1, chunk(1)], 2, 1, 5, side1, HALF, open_arm(2, 1, 5, spent))
-        h_q[0] = sb([P, 2, HALF], U32, "h_q0", "side1")
+        h_q[0] = sb([P, 2, HALF], U32, "h_q0", "g_last0")
         s_a[0] = sb([P, HALF], U8, "s_a0")
         s_a[1] = sb([P, HALF], U8, "s_a1")
-        for c in range(4):
-            product(nc.vector, h_a[1][:, chunk(c)], d_a[1], c * CHUNK, (c + 1) * CHUNK)
-            if c == 0:
-                quant(1)
-                mix(1, ([0, 1], [2]))
-            quant_a(0, c * CHUNK, (c + 1) * CHUNK)
+        quant_a(0, 0, CHUNK)
+        quant_a(1, 0, CHUNK, h_g[:])
+        mix(0, ([0, 1, 2],), 0, CHUNK)
+        for c in (4, 5):
+            first_arm(h_bf[1][:, 1, chunk(c - 4)], 2, 1, c, side1, HALF, open_arm(2, 1, c, spent[c - 4]))
+        quant_a(0, CHUNK, 256)
+        quant(1)
+        mix(1, ([0, 1], [2]))
+        for c, tag in ((1, "side1"), (2, "h_bf512"), (3, "h_a0")):
+            h_c = sb([P, CHUNK, 4], BF16, f"h_c{c}", tag)
+            product(nc.vector, h_c[:], d_a[1], c * CHUNK, (c + 1) * CHUNK)
             if c < 3:
-                quant_a(1, c * CHUNK, (c + 1) * CHUNK)
+                quant_a(0, (c + 1) * CHUNK, (c + 2) * CHUNK)
+                quant_a(1, c * CHUNK, (c + 1) * CHUNK, h_c[:])
                 mix(0, ([0, 1, 2],), c * CHUNK, (c + 1) * CHUNK)
         last = [shared_bank()[:, 0:CHUNK] for m in range(3)]
         for m in range(3):
             mix_pass(last[m], 0, m, 0, chunk(3))
-        quant_a(1, 3 * CHUNK, HALF)
+        quant_a(1, 384, HALF, h_c[:])
         for m in range(3):
             mix_pass(last[m], 0, m, 1, chunk(3))
             nc.scalar.activation(res[:, m, chunk(3)], last[m], TANH)

@@ -17,12 +17,16 @@ COPY = mybir.ActivationFunctionType.Copy
 TANH = mybir.ActivationFunctionType.Tanh
 MULT = mybir.AluOpType.mult
 ADD = mybir.AluOpType.add
+SUBTRACT = mybir.AluOpType.subtract
 IS_EQUAL = mybir.AluOpType.is_equal
 NOT_EQUAL = mybir.AluOpType.not_equal
 
 P = 128
 CHUNK = 128
+RANGE = 256
 HALF = 512
+SCALE_ROWS = P - 16
+KIB = 1024
 
 
 def tile_list_bond_angle_features_kernel(
@@ -31,146 +35,148 @@ def tile_list_bond_angle_features_kernel(
     nc = tc.nc
     with ExitStack() as ctx:
         keep = ctx.enter_context(tc.tile_pool(name="keep", bufs=1))
+        shared = ctx.enter_context(tc.tile_pool(name="shared", bufs=1))
         psum = ctx.enter_context(tc.psum_pool(name="psum", bufs=1))
         banks = [psum.tile([P, 512], F32, name=f"bank{k}") for k in range(8)]
-        turns = {"scalar": [], "shared": []}
+        turns = {"scalar": [], "vector": []}
 
         def scalar_bank():
             turns["scalar"].append(0)
-            return banks[(len(turns["scalar"]) + 2) % 4]
+            return banks[4 + (len(turns["scalar"]) - 1) % 4]
 
-        def shared_bank():
-            turns["shared"].append(0)
-            return banks[4 + (len(turns["shared"]) + 3) % 4]
+        def vector_bank():
+            turns["vector"].append(0)
+            return banks[(len(turns["vector"]) - 1) % 4]
 
         def sb(shape, dtype, name, tag=None):
             return keep.tile(shape, dtype, align_bytes=64, name=name, tag=tag or name)
+
+        def placed(shape, dtype, name, at):
+            return shared.tile(shape, dtype, align_bytes=64, name=name, offset=at)
 
         lists = [keep.tile([P, S // 16], U16, name=f"list{l}") for l in range(3)]
         tab_s = sb([P, T // 4], I32, "tab_s")
         tab_w = sb([P, T], I32, "tab_w")
         ws_raw = [sb([P, H // 4], I32, f"ws_raw{k}") for k in range(2)]
-        w1_raw = [sb([P, 4, 512], F32, "w1_raw0"), sb([P, 4, 256], F32, "w1_raw1"), sb([P, 4, 256], F32, "w1_raw2")]
+        w1_cuts = (0, 512, 768, 1024)
+        w1_raw = [sb([P, 4, w1_cuts[k + 1] - w1_cuts[k]], F32, f"w1_raw{k}") for k in range(3)]
         w2_raw = sb([P, H // 2], I32, "w2_raw")
-        w3_raw = sb([P, H], I32, "w3_raw")
+        w3_raw = [sb([P, HALF], I32, f"w3_raw{b}") for b in range(2)]
         w4_raw = [sb([P, 4, N], F32, f"w4_raw{b}") for b in range(2)]
-        g_rows = sb([P, 2 * P], F32, "g_rows")
+        g_rows = sb([P, HALF], F32, "g_rows")
+        g_dealt = sb([P, HALF], F32, "g_dealt")
         ident = sb([P, P], F32, "ident")
         g_col = sb([P, 8], F32, "g_col")
+        g_zero = sb([P, 8], F32, "g_zero")
         g_safe = sb([P, 8], F32, "g_safe")
         g_inv = sb([P, 8], F32, "g_inv")
-        zeros = sb([P, 2 * P], F32, "zeros")
+        zeros = sb([P, HALF], F32, "zeros")
+        planes = [sb([P, 3, HALF // 4], I32, f"planes{u}") for u in range(2)]
+        picked = [sb([P, 3, HALF], U8, f"picked{u}") for u in range(2)]
 
         for k in range(2):
             nc.gpsimd.memset(ws_raw[k][:], 0)
         nc.vector.memset(zeros[:], 0.0)
-        nc.vector.memset(tab_s[0:112, :], 0)
-        planes = sb([P, 3, S // 4], I32, "planes")
-        nc.vector.memset(planes[:], 0)
-        nc.scalar.activation(g_rows[0 : P - 4, :], zeros[0 : P - 4, :], TANH)
+        nc.vector.memset(tab_s[0:SCALE_ROWS, :], 0)
+        for u in range(2):
+            nc.vector.memset(planes[u][:], 0)
+        nc.scalar.activation(g_rows[0 : P - 2, :], zeros[0 : P - 2, :], TANH)
         nc.gpsimd.affine_select(
             out=ident[:], in_=zeros[:, 0:P], compare_op=NOT_EQUAL, fill=1.0, base=0, pattern=[[-1, P]], channel_multiplier=1
         )
 
         w1_rows = w1.rearrange("(p j) c -> p j c", j=4)
-        g_view = g.rearrange("(q t i) -> t q i", t=4, i=8)
-        w4_view = w4.rearrange("(b q t i) n -> b t q i n", b=2, t=4, i=8)
+        w3_rows = w3_words[0].rearrange("p e i -> p (e i)").bitcast(I32)
+        w4_view = w4.rearrange("(b q t i) n -> b t q i n", b=2, t=4, i=4)
 
-        def load_scale_rows(k, src, rows):
-            for r in rows:
-                nc.sync.dma_start(ws_raw[k][r:P:32, :], src[0, r:16:4, :].bitcast(I32))
+        def load_w1(k):
+            nc.sync.dma_start(w1_raw[k][:], w1_rows[:, :, w1_cuts[k] : w1_cuts[k + 1]])
 
-        nc.sync.dma_start(tab_s[112:P, :], tab_scales[0].bitcast(I32))
-        nc.sync.dma_start(lists[0][:], offs)
-        nc.sync.dma_start(lists[1][:], offs2)
-        nc.sync.dma_start(lists[2][:], offs3)
-        nc.sync.dma_start(w1_raw[0][:], w1_rows[:, :, 0:512])
-        nc.sync.dma_start(g_rows[P - 4 : P, :].rearrange("t (q i) -> t q i", i=8), g_view)
-        load_scale_rows(0, w2_scales, (0, 1))
+        def load_scale_rows(queue, k, src):
+            for r in range(4):
+                queue.dma_start(ws_raw[k][r:P:32, :], src[0, r:16:4, :].bitcast(I32))
+
+        def pick_scales(l, u):
+            offsets = lists[l][:, u * HALF // 16 : (u + 1) * HALF // 16]
+            nc.vector.tensor_copy(picked[u][:, l, :], tab_s[:].bitcast(U8).indirect(offsets))
+
+        def carry_scales(u):
+            for r in range(4):
+                nc.sync.dma_start(
+                    planes[u][r:P:32].rearrange("p l s -> p (l s)"),
+                    picked[u][SCALE_ROWS + r : P : 4].rearrange("p l s -> p (l s)").bitcast(I32),
+                )
+
+        nc.sync.dma_start(tab_s[SCALE_ROWS:P, :], tab_scales[0].bitcast(I32))
+        for l, src in enumerate((offs, offs2, offs3)):
+            nc.sync.dma_start(lists[l][:], src)
+        load_w1(0)
+        load_w1(1)
+        nc.sync.dma_start(g_rows[P - 2 : P, :], g.rearrange("(b c) -> b c", b=2))
+        load_scale_rows(nc.sync, 0, w2_scales)
+        load_scale_rows(nc.gpsimd, 1, w3_scales)
         nc.sync.dma_start(tab_w[:], tab_words[0].rearrange("p t i -> p (t i)").bitcast(I32))
-        load_scale_rows(0, w2_scales, (2, 3))
-        load_scale_rows(1, w3_scales, (0,))
-        nc.sync.dma_start(w2_raw[:], w2_words[0].bitcast(I32))
-        nc.sync.dma_start(w3_raw[:], w3_words[0].rearrange("p e i -> p (e i)").bitcast(I32))
-        nc.sync.dma_start(w1_raw[1][:], w1_rows[:, :, 512:768])
-
-        v_words = {}
-        picked = sb([P, 3, S], U8, "picked")
-        v_scales = [planes[:, l, :].bitcast(U8) for l in range(3)]
-        ws_p = [sb([P, H // 4], I32, f"ws_p{k}") for k in range(2)]
-        w2_p = sb([P, H // 2], I32, "w2_p")
-        w3_p = sb([P, H], I32, "w3_p")
-
-        def deal(dst, src, e):
-            nc.scalar.copy(
-                dst[:].bitcast(U32).rearrange("p (b t q e) -> p b t q e", b=2, t=4, e=e),
-                src[:].bitcast(U32).rearrange("p (b q t e) -> p b t q e", b=2, t=4, e=e),
-            )
-
-        g_bank = scalar_bank()
-        for b in range(2):
-            nc.tensor.transpose(g_bank[:, b * P : (b + 1) * P], g_rows[:, b * P : (b + 1) * P], ident[:])
-        g_turned = g_bank[:, 0 : 2 * P].rearrange("p (b c) -> p b c", b=2)[:, :, P - 4 : P]
-        nc.scalar.copy(g_col[:].rearrange("p (b t) -> p b t", b=2), g_turned)
-        g_last = [sb([P, 8], F32, f"g_last{b}") for b in range(2)]
-        for b in range(2):
-            nc.scalar.copy(g_last[b][:].rearrange("p (b t) -> p b t", b=2), g_turned)
         for l in range(3):
-            nc.vector.tensor_copy(picked[:, l, :], tab_s[:].bitcast(U8).indirect(lists[l][:]))
-        for r in range(4):
-            nc.sync.dma_start(
-                planes[r:P:32].rearrange("p l s -> p (l s)"),
-                picked[112 + r : P : 4].rearrange("p l s -> p (l s)").bitcast(I32),
-            )
-        nc.sync.dma_start(w1_raw[2][:], w1_rows[:, :, 768:1024])
-        load_scale_rows(1, w3_scales, (1, 2, 3))
+            pick_scales(l, 0)
+        carry_scales(0)
+        nc.sync.dma_start(w2_raw[:], w2_words[0].bitcast(I32))
+        nc.sync.dma_start(w3_raw[0][:], w3_rows[:, 0:HALF])
+        load_w1(2)
+        nc.sync.dma_start(w3_raw[1][:], w3_rows[:, HALF:H])
+        for l in range(3):
+            pick_scales(l, 1)
+        carry_scales(1)
         for u in range(8):
             nc.sync.dma_start(w4_raw[u // 4][:, u % 4, :], w4_view[u // 4, u % 4])
 
-        def gather_words(l, tag=None, parts=((0, S),)):
-            v_words[l] = sb([P, S], U32, f"v_words{l}", tag)
-            for lo, hi in parts:
-                offsets = lists[l][:, lo // 16 : hi // 16]
-                nc.vector.tensor_copy(v_words[l][:, lo:hi], tab_w[:].bitcast(U32).indirect(offsets))
+        ws_p = [sb([P, H // 4], I32, f"ws_p{k}") for k in range(2)]
+        w2_p = sb([P, H // 2], I32, "w2_p")
+        w3_p = [sb([P, HALF], I32, f"w3_p{b}") for b in range(2)]
 
-        w1_bf = [sb([P, 4, 16, 8, 4], BF16, f"w1_bf{b}") for b in range(2)]
-        w1_q = [sb([P, H // 2], U32, f"w1_q{b}") for b in range(2)]
-        w1_s = [sb([P, H // 2], U8, f"w1_s{b}") for b in range(2)]
+        def dealt(dst, src, dtype, b, e):
+            return (
+                dst[:].bitcast(dtype).rearrange("p (b t q e) -> p b t q e", b=b, t=4, e=e),
+                src[:].bitcast(dtype).rearrange("p (b q t e) -> p b t q e", b=b, t=4, e=e),
+            )
 
-        def cast_w1(k, b, qs):
-            src = w1_raw[k][:].rearrange("p j (q t i) -> p t q j i", t=4, i=8)
-            for t in range(4):
-                for i in (0, 4):
-                    nc.scalar.activation(
-                        w1_bf[b][:, t, qs, i : i + 4].rearrange("p q i j -> p q j i"),
-                        src[:, t, :, :, i : i + 4],
-                        COPY,
-                        scale=-1.0,
-                    )
+        nc.scalar.copy(*dealt(g_dealt, g_rows, F32, 1, 4))
+        g_bank = banks[7]
+        for t in range(4):
+            nc.tensor.transpose(g_bank[:, t * P : (t + 1) * P], g_dealt[:, t * P : (t + 1) * P], ident[:])
+        nc.scalar.copy(
+            g_col[:].rearrange("p (b t) -> p t b", b=2), g_bank[:].rearrange("p (t r) -> p t r", t=4)[:, :, P - 2 : P]
+        )
+        nc.gpsimd.tensor_scalar(g_zero[:], g_col[:], 0.0, 0.0, IS_EQUAL, ADD)
+        nc.gpsimd.tensor_tensor(g_safe[:], g_zero[:], g_col[:], ADD)
+
+        w1_bf = [sb([P, 4, 32, 4, 4], BF16, "w1_bf0"), placed([P, 4, 32, 4, 4], BF16, "w1_bf1", 2 * KIB)]
+        w1_q = [sb([P, HALF], U32, f"w1_q{b}") for b in range(2)]
+        w1_s = [sb([P, HALF], U8, f"w1_s{b}") for b in range(2)]
+
+        def cast_w1(k, engine, ts=range(4)):
+            b, lo = divmod(w1_cuts[k], HALF)
+            qs = slice(lo // 16, (lo + w1_cuts[k + 1] - w1_cuts[k]) // 16)
+            src = w1_raw[k][:].rearrange("p j (q t i) -> p t q j i", t=4, i=4)
+            for t in ts:
+                dst = w1_bf[b][:, t, qs].rearrange("p q i j -> p q j i")
+                if engine == "scalar":
+                    nc.scalar.activation(dst, src[:, t], COPY, scale=-1.0)
+                else:
+                    nothing = zeros[:, 0:RANGE].rearrange("p (q j i) -> p q j i", j=4, i=4)
+                    nc.gpsimd.tensor_tensor(dst, nothing, src[:, t], SUBTRACT)
 
         def quant_w1(b):
             nc.vector.quantize_mx(
                 w1_q[b][:].bitcast(FP8X4), w1_s[b][:], w1_bf[b][:].rearrange("p t q i j -> p (t q i j)")
             )
 
-        late = {}
+        v_words = {}
 
-        def cast_w4(b):
-            late[b] = sb([P, N, 4], BF16, f"w4_bf{b}", f"g_last{b}")
-            nc.scalar.activation(
-                late[b][:].rearrange("p (c i) t -> p c t i", i=4),
-                w4_raw[b][:].rearrange("p t (c i) -> p c t i", i=4),
-                COPY,
-            )
-
-        def quant_w4(tag_q, tag_s):
-            w4_q = sb([P, 2 * N], U32, "w4_q", tag_q)
-            late["w4_q"] = w4_q
-            w4_s = sb([P, 2 * N], U8, "w4_s", tag_s)
-            late["w4_s"] = w4_s
-            for b in range(2):
-                cols = slice(b * N, (b + 1) * N)
-                nc.vector.quantize_mx(w4_q[:, cols].bitcast(FP8X4), w4_s[:, cols], late[b][:].rearrange("p n t -> p (n t)"))
+        def pick_words(l, lo, hi, tile=None):
+            tile = sb([P, hi - lo], U32, f"v_words{l}_{lo}")[:] if tile is None else tile
+            for c in range(lo, hi, CHUNK):
+                v_words[l, c] = (tile, lo)
+            nc.vector.tensor_copy(tile, tab_w[:].bitcast(U32).indirect(lists[l][:, lo // 16 : hi // 16]))
 
         def weight(l, b, t):
             u = 4 * b + t
@@ -178,49 +184,35 @@ def tile_list_bond_angle_features_kernel(
                 return w1_q[b][:, t * P : (t + 1) * P].bitcast(FP8X4), w1_s[b][:, t * P : (t + 1) * P]
             if l == 1:
                 return w2_p[:, u * 64 : (u + 1) * 64].bitcast(U8).bitcast(FP4X4), ws_p[0][:, u * 32 : (u + 1) * 32].bitcast(U8)
-            return w3_p[:, u * P : (u + 1) * P].bitcast(FP8X4), ws_p[1][:, u * 32 : (u + 1) * 32].bitcast(U8)
+            return w3_p[b][:, t * P : (t + 1) * P].bitcast(FP8X4), ws_p[1][:, u * 32 : (u + 1) * 32].bitcast(U8)
 
-        def project(dst, ls, b, t, lo, hi):
-            for n, l in enumerate(ls):
-                codes, scale = weight(l, b, t)
-                nc.tensor.matmul_mx(
-                    dst,
-                    lhsT=codes,
-                    lhsT_scale=scale,
-                    rhs=v_words[l][:, lo:hi].bitcast(FP8X4),
-                    rhs_scale=v_scales[l][:, lo:hi],
-                    start=(n == 0),
-                    stop=(n == len(ls) - 1),
-                )
+        def project(dst, l, b, t, lo, hi, start, stop):
+            codes, scale = weight(l, b, t)
+            tile, at = v_words[l, lo]
+            u, col = divmod(lo, HALF)
+            nc.tensor.matmul_mx(
+                dst,
+                lhsT=codes,
+                lhsT_scale=scale,
+                rhs=tile[:, lo - at : hi - at].bitcast(FP8X4),
+                rhs_scale=planes[u][:, l, :].bitcast(U8)[:, col : col + hi - lo],
+                start=start,
+                stop=stop,
+            )
 
-        out_view = out.rearrange("(m p) s -> p m s", p=P)
+        def fill(bank, ls, b, ts, lo, hi):
+            view = bank[:].rearrange("p (e n) -> p e n", e=len(ts))
+            passes = [(e, t, l) for l in ls for e, t in enumerate(ts)]
+            for n, (e, t, l) in enumerate(passes):
+                project(view[:, e, :], l, b, t, lo, hi, n == 0, n == len(passes) - 1)
+            return view
 
         def gain(col, b, t):
             return col[:, 4 * b + t : 4 * b + t + 1]
 
-        def scaled_read(dst, ls, b, ts, lo, hi, col=g_col, bank=None):
-            bank = (scalar_bank() if bank is None else banks[bank])[:].rearrange("p (e n) -> p e n", e=len(ts))
+        def read_scaled(dst, view, b, ts):
             for e, t in enumerate(ts):
-                project(bank[:, e, :], ls, b, t, lo, hi)
-            for e, t in reversed(list(enumerate(ts))):
-                nc.scalar.activation(dst[t], bank[:, e, :], COPY, scale=gain(col, b, t))
-
-        def arms(d, x, b, ts, lo, hi, col=g_col, own=None):
-            pair = [(shared_bank() if own is None else banks[own + l])[:].rearrange("p (e n) -> p e n", e=len(ts)) for l in range(2)]
-            for l in range(2):
-                for e, t in enumerate(ts):
-                    project(pair[l][:, e, :], [l + 1], b, t, lo, hi)
-            for e, t in enumerate(ts):
-                nc.vector.scalar_tensor_tensor(d[1][:, t, :], x[t], gain(g_inv, b, t), pair[1][:, e, :], MULT, ADD)
-            for e, t in enumerate(ts):
-                nc.vector.scalar_tensor_tensor(d[0][:, t, :], pair[0][:, e, :], gain(col, b, t), x[t], MULT, ADD)
-
-        def lone_arm(d, x, b, ts, lo, hi):
-            bank = shared_bank()[:].rearrange("p (e n) -> p e n", e=len(ts))
-            for e, t in enumerate(ts):
-                project(bank[:, e, :], [2], b, t, lo, hi)
-            for e, t in reversed(list(enumerate(ts))):
-                nc.vector.scalar_tensor_tensor(d[:, t, :], x[t], gain(g_inv, b, t), bank[:, e, :], MULT, ADD)
+                nc.scalar.activation(dst[:, t, :], view[:, e, :], COPY, scale=gain(g_col, b, t))
 
         def woven(ap):
             return ap.rearrange("p t (c i) -> p c t i", i=4)
@@ -228,165 +220,163 @@ def tile_list_bond_angle_features_kernel(
         def h_view(ap):
             return ap.rearrange("p (c i) t -> p c t i", i=4)
 
-        def product(engine, dst, d, lo, hi):
-            engine.tensor_tensor(h_view(dst), woven(d[0][:, :, lo:hi]), woven(d[1][:, :, lo:hi]), MULT)
+        h_bf = [placed([P, 2, RANGE, 4], BF16, f"h_bf{r}", at * KIB) for r, at in enumerate((4, 14, 16, 16))]
+        h_q = [sb([P, 2, RANGE], U32, f"h_q{r}") for r in range(4)]
+        h_s = [placed([P, 2, RANGE], U8, f"h_s{r}", at * KIB) for r, at in enumerate((8, 9, 28, 32))]
 
-        def open_arm(l, b, c, own=None):
-            bank = (shared_bank() if own is None else own)[:].rearrange("p (t n) -> p t n", t=4)
-            for t in range(4):
-                project(bank[:, t, :], [0, l], b, t, c * CHUNK, (c + 1) * CHUNK)
-            return bank
+        def h_part(tiles, b, lo, hi):
+            r, col = divmod(lo, RANGE)
+            return tiles[r][:, b, col : col + hi - lo]
 
-        def first_arm(dst, l, b, c, side, at, bank=None):
-            if bank is None:
-                bank = open_arm(l, b, c)
-            nc.vector.tensor_tensor(h_view(dst), woven(bank), woven(side[:, :, c * CHUNK - at : (c + 1) * CHUNK - at]), MULT)
+        def tiles_of(n):
+            return [list(range(t, t + 512 // n)) for t in range(0, 4, 512 // n)]
 
-        spans = ((0, 512), (512, 768), (768, 1024))
-        h_bf = [None] + [sb([P, 2, hi - lo, 4], BF16, f"h_bf{lo}") for lo, hi in spans[1:]]
-        h_q = {1: sb([P, 2, 256], U32, "h_q1")}
-        h_s = {}
-        h_a = {}
-        s_a = {}
+        def doubled(b, lo, hi, bank_of, tag=None, between=None):
+            arm = [sb([P, 4, hi - lo], F32, f"arm0_{b}_{lo}"), sb([P, 4, hi - lo], F32, f"arm1_{b}_{lo}", tag)]
+            for ts in tiles_of(hi - lo):
+                read_scaled(arm[0], fill(bank_of(), [0, 1], b, ts, lo, hi), b, ts)
+            if between:
+                between()
+            for ts in tiles_of(hi - lo):
+                nc.scalar.copy(arm[1][:, ts[0] : ts[-1] + 1, :], fill(bank_of(), [0, 2], b, ts, lo, hi))
+            nc.gpsimd.tensor_tensor(h_view(h_part(h_bf, b, lo, hi)), woven(arm[0][:]), woven(arm[1][:]), MULT)
 
-        def quant_a(b, lo, hi, src=None):
-            src = h_a[b][:, lo:hi] if src is None else src
-            nc.vector.quantize_mx(h_q[0][:, b, lo:hi].bitcast(FP8X4), s_a[b][:, lo:hi], src.rearrange("p n t -> p (n t)"))
+        centre = {}
+        arms = {}
+
+        def read_centre(b, lo, ts):
+            if (b, lo) not in centre:
+                name = f"centre{b}_{lo}"
+                centre[b, lo] = placed([P, 4, RANGE], F32, name, {512: 8, 768: 28}[lo] * KIB) if b == 0 else sb([P, 4, RANGE], F32, name)
+            read_scaled(centre[b, lo], fill(scalar_bank(), [0], b, ts, lo, lo + RANGE), b, ts)
+
+        def make_arms(b, lo, ts):
+            if (b, lo) not in arms:
+                if (b, lo) == (1, 512):
+                    arms[b, lo] = [placed([P, 4, RANGE], F32, f"arm{l}_{b}_{lo}", at * KIB) for l, at in enumerate((20, 12))]
+                else:
+                    arms[b, lo] = [sb([P, 4, RANGE], F32, f"arm{l}_{b}_{lo}") for l in range(2)]
+            x = centre[b, lo]
+            first = fill(vector_bank(), [1], b, ts, lo, lo + RANGE)
+            second = fill(vector_bank(), [2], b, ts, lo, lo + RANGE)
+            for e, t in enumerate(ts):
+                nc.vector.scalar_tensor_tensor(arms[b, lo][1][:, t, :], x[:, t, :], gain(g_inv, b, t), second[:, e, :], MULT, ADD)
+            for e, t in enumerate(ts):
+                nc.vector.scalar_tensor_tensor(arms[b, lo][0][:, t, :], first[:, e, :], gain(g_col, b, t), x[:, t, :], MULT, ADD)
+
+        def product(engine, dst, b, at, lo, hi):
+            a0, a1 = (arm[:, :, lo - at : hi - at] for arm in arms[b, at])
+            engine.tensor_tensor(h_view(dst), woven(a0), woven(a1), MULT)
+
+        w4_bf = [sb([P, N, 4], BF16, "w4_bf0"), placed([P, N, 4], BF16, "w4_bf1", 20 * KIB)]
+        w4_q = sb([P, 2 * N], U32, "w4_q")
+        w4_s = placed([P, 2 * N], U8, "w4_s", 10 * KIB)
+
+        def cast_w4(b, lo, hi):
+            nc.scalar.activation(h_view(w4_bf[b][:, lo:hi]), woven(w4_raw[b][:, :, lo:hi]), COPY)
+
+        def quant_w4(b):
+            cols = slice(b * N, (b + 1) * N)
+            nc.vector.quantize_mx(w4_q[:, cols].bitcast(FP8X4), w4_s[:, cols], w4_bf[b][:].rearrange("p n t -> p (n t)"))
+
+        def quant_range(r):
+            nc.vector.quantize_mx(
+                h_q[r][:].rearrange("p b n -> p (b n)").bitcast(FP8X4),
+                h_s[r][:].rearrange("p b n -> p (b n)"),
+                h_bf[r][:].rearrange("p b n t -> p (b n t)"),
+            )
+
+        def quant_part(src, b, lo, hi):
+            nc.vector.quantize_mx(h_part(h_q, b, lo, hi).bitcast(FP8X4), h_part(h_s, b, lo, hi), src.rearrange("p n t -> p (n t)"))
 
         res = sb([P, 3, S], F32, "res")
+        out_view = out.rearrange("(m p) s -> p m s", p=P)
 
-        def quant(k, b=None, tag=None):
-            if not b:
-                h_s[k] = sb([P, 2, spans[k][1] - spans[k][0]], U8, f"h_s{k}", tag)
-            if b is None:
-                nc.vector.quantize_mx(
-                    h_q[k][:].rearrange("p b n -> p (b n)").bitcast(FP8X4),
-                    h_s[k][:].rearrange("p b n -> p (b n)"),
-                    h_bf[k][:].rearrange("p b n t -> p (b n t)"),
-                )
-            else:
-                nc.vector.quantize_mx(
-                    h_q[k][:, b, :].bitcast(FP8X4), h_s[k][:, b, :], h_bf[k][:, b].rearrange("p n t -> p (n t)")
-                )
-
-        def mix_pass(dst, k, m, b, part=slice(None)):
+        def mix_pass(dst, m, b, lo, hi, start):
             cols = slice(b * N + m * P, b * N + (m + 1) * P)
             nc.tensor.matmul_mx(
                 dst,
-                lhsT=late["w4_q"][:, cols].bitcast(FP8X4),
-                lhsT_scale=late["w4_s"][:, cols],
-                rhs=h_q[k][:, b, part].bitcast(FP8X4),
-                rhs_scale=h_s[k][:, b, part] if k else s_a[b][:, part],
-                start=(b == 0),
-                stop=(b == 1),
+                lhsT=w4_q[:, cols].bitcast(FP8X4),
+                lhsT_scale=w4_s[:, cols],
+                rhs=h_part(h_q, b, lo, hi).bitcast(FP8X4),
+                rhs_scale=h_part(h_s, b, lo, hi),
+                start=start,
+                stop=not start,
             )
 
-        def mix(k, groups, lo=None, hi=None):
-            part = slice(lo, hi)
-            if k:
-                lo, hi = spans[k]
+        def mix(lo, hi, groups):
             for ms in groups:
                 bank = scalar_bank()[:, 0 : len(ms) * (hi - lo)].rearrange("p (m s) -> p m s", m=len(ms))
                 for e, m in enumerate(ms):
                     for b in range(2):
-                        mix_pass(bank[:, e, :], k, m, b, part)
+                        mix_pass(bank[:, e, :], m, b, lo, hi, b == 0)
                 nc.scalar.activation(res[:, ms[0] : ms[-1] + 1, lo:hi], bank, TANH)
                 nc.sync.dma_start(out_view[:, ms[0] : ms[-1] + 1, lo:hi], res[:, ms[0] : ms[-1] + 1, lo:hi])
 
-        cast_w1(0, 0, slice(0, 16))
-        gather_words(0)
-        nc.vector.scalar_tensor_tensor(g_safe[:], g_col[:], 0.0, g_col[:], IS_EQUAL, ADD)
-        gather_words(1)
-        nc.vector.reciprocal(g_inv[:], g_safe[:])
+        cast_w1(0, "scalar")
         quant_w1(0)
-        deal(ws_p[0], ws_raw[0], 2)
-        deal(w2_p, w2_raw, 4)
-        deal(w3_p, w3_raw, 8)
-        cast_w1(1, 1, slice(0, 8))
-        cast_w1(2, 1, slice(8, 16))
-        deal(ws_p[1], ws_raw[1], 2)
-        gather_words(2, None, ((HALF, S), (0, HALF)))
+        nc.vector.reciprocal(g_inv[:], g_safe[:])
+        nc.scalar.copy(*dealt(ws_p[0], ws_raw[0], U32, 2, 1))
+        cast_w1(1, "scalar")
+        nc.scalar.copy(*dealt(w2_p, w2_raw, U32, 2, 2))
+        nc.scalar.copy(*dealt(w3_p[0], w3_raw[0], U32, 1, 4))
+        nc.scalar.copy(*dealt(ws_p[1], ws_raw[1], U32, 2, 1))
+        cast_w1(2, "scalar", (0, 1))
+        cast_w1(2, "gpsimd", (2, 3))
+        nc.gpsimd.tensor_copy(*dealt(w3_p[1], w3_raw[1], U32, 1, 4))
+        for lo in (0, RANGE):
+            for l in range(3):
+                pick_words(l, lo, lo + RANGE)
+        pick_words(0, HALF, S)
         quant_w1(1)
+        v_late = placed([P, 2, HALF], U32, "v_late", 0)
+        pick_words(2, HALF, S, v_late[:, 0, :])
+        pick_words(1, HALF, S, v_late[:, 1, :])
 
-        def by_tile(tile):
-            return [tile[:, t, :] for t in range(4)]
-
-        x_0 = sb([P, 4, 768], F32, "x_0", "ws_raw1")
-        x_a0 = by_tile(x_0[:, :, 0:HALF])
-        x_b0 = sb([P, 4, 256], F32, "x_b0", "w3_raw")
-        x_b = by_tile(x_b0)
-        y_b = by_tile(x_0[:, :, HALF:768])
-        x_a1 = by_tile(sb([P, 4, HALF], F32, "x_a1"))
-        d_a = [[sb([P, 4, HALF], F32, f"d_a{b}_{k}") for k in range(2)] for b in range(2)]
-        d_b = [sb([P, 4, 256], F32, "d_b0", "w1_bf1"), sb([P, 4, 256], F32, "d_b1")]
-        side1 = sb([P, 4, HALF], F32, "side1")
-        side0 = sb([P, 4, 256], F32, "side0")
-
-        def chunk(c):
-            return slice(c * CHUNK, (c + 1) * CHUNK)
-
-        for k, ts in enumerate(([0, 1], [2, 3])):
-            scaled_read(x_b, [0], 0, ts, HALF, 768, g_col, 6 + k)
-        for k, ts in enumerate(([0, 1], [2, 3])):
-            scaled_read(y_b, [1], 0, ts, HALF, 768, g_col)
-            pair = slice(ts[0], ts[1] + 1)
-            nc.gpsimd.tensor_tensor(d_b[0][:, pair, :], x_b0[:, pair, :], x_0[:, pair, HALF:768], ADD)
-        for k, ts in enumerate(([0, 1], [2, 3])):
-            lone_arm(d_b[1], x_b, 0, ts, HALF, 768)
-        for t in range(4):
-            scaled_read(x_a0, [0], 0, [t], 0, HALF)
-        product(nc.gpsimd, h_bf[1][:, 0], d_b, 0, 256)
-        for t in range(4):
-            arms(d_a[0], x_a0, 0, [t], 0, HALF)
-            scaled_read(x_a1, [0], 1, [t], 0, HALF)
-            if t >= 2:
-                scaled_read(by_tile(side1), [0, 1], 1, [t - 2], HALF, S)
-        h_a[0] = sb([P, HALF, 4], BF16, "h_a0")
-        for lo in (0, 256):
-            product(nc.gpsimd, h_a[0][:, lo : lo + 256], d_a[0], lo, lo + 256)
-        for t in range(4):
-            arms(d_a[1], x_a1, 1, [t], 0, HALF)
-            if t < 2:
-                scaled_read(by_tile(side1), [0, 1], 1, [t + 2], HALF, S, (g_col, g_last[0])[t])
-            else:
-                scaled_read(by_tile(side0), [0, 1], 0, [2 * t - 4, 2 * t - 3], 768, S, (g_col, g_last[1])[t - 2])
-            if t % 2:
-                cast_w4(t // 2)
-        h_g = sb([P, CHUNK, 4], BF16, "h_g")
-        product(nc.gpsimd, h_g[:], d_a[1], 0, CHUNK)
-        for c in (6, 7):
-            first_arm(h_bf[2][:, 1, chunk(c - 6)], 2, 1, c, side1, HALF)
-        for c in (6, 7):
-            first_arm(h_bf[2][:, 0, chunk(c - 6)], 2, 0, c, side0, 768)
-        spent = [banks[4 + (len(turns["shared"]) + 2 + k) % 4] for k in range(2)]
-
-        h_q[2] = sb([P, 2, 256], U32, "h_q2", "d_a0_1")
-        quant(2)
-        quant_w4(None, "side0")
-        mix(2, ([0, 1], [2]))
-        h_q[0] = sb([P, 2, HALF], U32, "h_q0", "g_last0")
-        s_a[0] = sb([P, HALF], U8, "s_a0")
-        s_a[1] = sb([P, HALF], U8, "s_a1")
-        quant_a(0, 0, CHUNK)
-        quant_a(1, 0, CHUNK, h_g[:])
-        mix(0, ([0, 1, 2],), 0, CHUNK)
-        for c in (4, 5):
-            first_arm(h_bf[1][:, 1, chunk(c - 4)], 2, 1, c, side1, HALF, open_arm(2, 1, c, spent[c - 4]))
-        quant_a(0, CHUNK, 256)
-        quant(1)
-        mix(1, ([0, 1], [2]))
-        for c, tag in ((1, "side1"), (2, "h_bf512"), (3, "h_a0")):
-            h_c = sb([P, CHUNK, 4], BF16, f"h_c{c}", tag)
-            product(nc.vector, h_c[:], d_a[1], c * CHUNK, (c + 1) * CHUNK)
-            if c < 3:
-                quant_a(0, (c + 1) * CHUNK, (c + 2) * CHUNK)
-                quant_a(1, c * CHUNK, (c + 1) * CHUNK, h_c[:])
-                mix(0, ([0, 1, 2],), c * CHUNK, (c + 1) * CHUNK)
-        last = [shared_bank()[:, 0:CHUNK] for m in range(3)]
+        doubled(0, 0, RANGE, vector_bank, "w1_raw2")
+        pairs = tiles_of(RANGE)
+        plain = [(1, 0), (1, 256), (0, 512), (1, 512), (0, 768)]
+        doubled(0, RANGE, HALF, scalar_bank, None, lambda: read_centre(*plain[0], pairs[0]))
+        read_centre(*plain[0], pairs[1])
+        side = placed([P, 4, RANGE], F32, "side", 24 * KIB)
+        for k, (b, lo) in enumerate(plain):
+            for e, ts in enumerate(pairs):
+                make_arms(b, lo, ts)
+                if k + 1 < len(plain):
+                    read_centre(*plain[k + 1], ts)
+                if k < 2:
+                    cast_w4(k, e * N // 2, (e + 1) * N // 2)
+                if k == 2:
+                    read_scaled(side, fill(scalar_bank(), [0, 1], 1, ts, 768, S), 1, ts)
+                if (k, e) == (4, 0):
+                    mix(256, 512, ([0, 1], [2]))
+            if k == 2:
+                quant_w4(0)
+                quant_w4(1)
+                quant_range(0)
+                mix(0, 256, ([0, 1], [2]))
+                quant_range(1)
+            if k == 4:
+                quant_range(2)
+            hi = lo + (RANGE if k < 4 else CHUNK)
+            product(nc.gpsimd, h_part(h_bf, b, lo, hi), b, lo, lo, hi)
+        for lo in (768, 896):
+            view = fill(vector_bank(), [0, 2], 1, range(4), lo, lo + CHUNK)
+            nc.vector.tensor_tensor(
+                h_view(h_part(h_bf, 1, lo, lo + CHUNK)), woven(view), woven(side[:, :, lo - 768 : lo - 768 + CHUNK]), MULT
+            )
+        mix(512, 768, ([0, 1], [2]))
+        h_last = placed([P, CHUNK, 4], BF16, "h_last", 25 * KIB)
+        product(nc.vector, h_last[:], 0, 768, 896, S)
+        for b in range(2):
+            quant_part(h_part(h_bf, b, 768, 896), b, 768, 896)
+        mix(768, 896, ([0, 1, 2],))
+        quant_part(h_part(h_bf, 1, 896, S), 1, 896, S)
+        last = [vector_bank()[:, 0:CHUNK] for m in range(3)]
         for m in range(3):
-            mix_pass(last[m], 0, m, 0, chunk(3))
-        quant_a(1, 384, HALF, h_c[:])
+            mix_pass(last[m], m, 1, 896, S, True)
+        quant_part(h_last[:], 0, 896, S)
         for m in range(3):
-            mix_pass(last[m], 0, m, 1, chunk(3))
-            nc.scalar.activation(res[:, m, chunk(3)], last[m], TANH)
-            (nc.scalar if m == 2 else nc.sync).dma_start(out_view[:, m, chunk(3)], res[:, m, chunk(3)])
+            mix_pass(last[m], m, 0, 896, S, False)
+            nc.scalar.activation(res[:, m, 896:S], last[m], TANH)
+            (nc.scalar if m == 2 else nc.sync).dma_start(out_view[:, m, 896:S], res[:, m, 896:S])

@@ -59,10 +59,10 @@ def tile_list_bond_angle_features_kernel(
         tab_w = sb([P, T], I32, "tab_w")
         ws_raw = [sb([P, H // 4], I32, f"ws_raw{k}") for k in range(2)]
         w1_cuts = (0, 512, 768, 1024)
-        w1_raw = [sb([P, 4, w1_cuts[k + 1] - w1_cuts[k]], F32, f"w1_raw{k}") for k in range(3)]
+        w1_raw = [sb([P, 4, 512], F32, "w1_raw0"), sb([P, 4, 256], F32, "w1_raw1"), placed([P, 4, 256], F32, "w1_raw2", 2 * KIB)]
         w2_raw = sb([P, H // 2], I32, "w2_raw")
         w3_raw = [sb([P, HALF], I32, f"w3_raw{b}") for b in range(2)]
-        w4_raw = [sb([P, 4, N], F32, f"w4_raw{b}") for b in range(2)]
+        w4_raw = [sb([P, 4, N], F32, "w4_raw0"), placed([P, 4, N], F32, "w4_raw1", 24 * KIB)]
         g_rows = sb([P, HALF], F32, "g_rows")
         g_dealt = sb([P, HALF], F32, "g_dealt")
         ident = sb([P, P], F32, "ident")
@@ -139,17 +139,7 @@ def tile_list_bond_angle_features_kernel(
                 src[:].bitcast(dtype).rearrange("p (b q t e) -> p b t q e", b=b, t=4, e=e),
             )
 
-        nc.scalar.copy(*dealt(g_dealt, g_rows, F32, 1, 4))
-        g_bank = banks[7]
-        for t in range(4):
-            nc.tensor.transpose(g_bank[:, t * P : (t + 1) * P], g_dealt[:, t * P : (t + 1) * P], ident[:])
-        nc.scalar.copy(
-            g_col[:].rearrange("p (b t) -> p t b", b=2), g_bank[:].rearrange("p (t r) -> p t r", t=4)[:, :, P - 2 : P]
-        )
-        nc.gpsimd.tensor_scalar(g_zero[:], g_col[:], 0.0, 0.0, IS_EQUAL, ADD)
-        nc.gpsimd.tensor_tensor(g_safe[:], g_zero[:], g_col[:], ADD)
-
-        w1_bf = [sb([P, 4, 32, 4, 4], BF16, "w1_bf0"), placed([P, 4, 32, 4, 4], BF16, "w1_bf1", 2 * KIB)]
+        w1_bf = [sb([P, 4, 32, 4, 4], BF16, "w1_bf0"), placed([P, 4, 32, 4, 4], BF16, "w1_bf1", 8 * KIB)]
         w1_q = [sb([P, HALF], U32, f"w1_q{b}") for b in range(2)]
         w1_s = [sb([P, HALF], U8, f"w1_s{b}") for b in range(2)]
 
@@ -212,7 +202,7 @@ def tile_list_bond_angle_features_kernel(
 
         def read_scaled(dst, view, b, ts):
             for e, t in enumerate(ts):
-                nc.scalar.activation(dst[:, t, :], view[:, e, :], COPY, scale=gain(g_col, b, t))
+                nc.scalar.activation(dst[t], view[:, e, :], COPY, scale=gain(g_col, b, t))
 
         def woven(ap):
             return ap.rearrange("p t (c i) -> p c t i", i=4)
@@ -220,57 +210,59 @@ def tile_list_bond_angle_features_kernel(
         def h_view(ap):
             return ap.rearrange("p (c i) t -> p c t i", i=4)
 
-        h_bf = [placed([P, 2, RANGE, 4], BF16, f"h_bf{r}", at * KIB) for r, at in enumerate((4, 14, 16, 16))]
+        h_bf = [placed([P, 2, RANGE, 4], BF16, f"h_bf{r}", at * KIB) for r, at in enumerate((8, 16, 16))]
         h_q = [sb([P, 2, RANGE], U32, f"h_q{r}") for r in range(4)]
-        h_s = [placed([P, 2, RANGE], U8, f"h_s{r}", at * KIB) for r, at in enumerate((8, 9, 28, 32))]
+        h_s = [placed([P, 2, RANGE], U8, f"h_s{r}", at) for r, at in enumerate((13 * KIB - 448, 13 * KIB + 128, 20 * KIB, 26 * KIB))]
 
         def h_part(tiles, b, lo, hi):
             r, col = divmod(lo, RANGE)
             return tiles[r][:, b, col : col + hi - lo]
 
-        def tiles_of(n):
-            return [list(range(t, t + 512 // n)) for t in range(0, 4, 512 // n)]
+        pairs = ([0, 1], [2, 3])
 
-        def doubled(b, lo, hi, bank_of, tag=None, between=None):
-            arm = [sb([P, 4, hi - lo], F32, f"arm0_{b}_{lo}"), sb([P, 4, hi - lo], F32, f"arm1_{b}_{lo}", tag)]
-            for ts in tiles_of(hi - lo):
-                read_scaled(arm[0], fill(bank_of(), [0, 1], b, ts, lo, hi), b, ts)
-            if between:
-                between()
-            for ts in tiles_of(hi - lo):
-                nc.scalar.copy(arm[1][:, ts[0] : ts[-1] + 1, :], fill(bank_of(), [0, 2], b, ts, lo, hi))
-            nc.gpsimd.tensor_tensor(h_view(h_part(h_bf, b, lo, hi)), woven(arm[0][:]), woven(arm[1][:]), MULT)
+        def first_arm(dst, bank, b, ts, lo):
+            read_scaled([dst[:, t, :] for t in range(4)], fill(bank, [0, 1], b, ts, lo, lo + RANGE), b, ts)
 
-        centre = {}
-        arms = {}
+        def second_arm(dst, bank, b, ts, lo):
+            nc.scalar.copy(dst[:, ts[0] : ts[1] + 1, :], fill(bank, [0, 2], b, ts, lo, lo + RANGE))
 
-        def read_centre(b, lo, ts):
-            if (b, lo) not in centre:
-                name = f"centre{b}_{lo}"
-                centre[b, lo] = placed([P, 4, RANGE], F32, name, {512: 8, 768: 28}[lo] * KIB) if b == 0 else sb([P, 4, RANGE], F32, name)
-            read_scaled(centre[b, lo], fill(scalar_bank(), [0], b, ts, lo, lo + RANGE), b, ts)
+        plain = [(1, 0), (1, 256), (0, 512), (1, 512), (0, 768)]
+        third = {2: 13 * KIB}
+        centre = []
+        for k in range(5):
+            tiles = [sb([P, RANGE], F32, f"centre{k}_{t}") for t in range(4)]
+            if k in third:
+                tiles[2] = placed([P, RANGE], F32, f"centre{k}_third", third[k])
+            centre.append([tile[:] for tile in tiles])
+        arm_at = {(1, 1): 32 * KIB, (3, 1): 32 * KIB, (3, 0): 24 * KIB}
+        arms = [
+            [placed([P, 4, RANGE], F32, f"arm{k}_{l}", arm_at.get((k, l), (40 + 8 * k + 4 * l) * KIB)) for l in range(2)]
+            for k in range(5)
+        ]
+        filled = {}
 
-        def make_arms(b, lo, ts):
-            if (b, lo) not in arms:
-                if (b, lo) == (1, 512):
-                    arms[b, lo] = [placed([P, 4, RANGE], F32, f"arm{l}_{b}_{lo}", at * KIB) for l, at in enumerate((20, 12))]
-                else:
-                    arms[b, lo] = [sb([P, 4, RANGE], F32, f"arm{l}_{b}_{lo}") for l in range(2)]
-            x = centre[b, lo]
-            first = fill(vector_bank(), [1], b, ts, lo, lo + RANGE)
-            second = fill(vector_bank(), [2], b, ts, lo, lo + RANGE)
-            for e, t in enumerate(ts):
-                nc.vector.scalar_tensor_tensor(arms[b, lo][1][:, t, :], x[:, t, :], gain(g_inv, b, t), second[:, e, :], MULT, ADD)
-            for e, t in enumerate(ts):
-                nc.vector.scalar_tensor_tensor(arms[b, lo][0][:, t, :], first[:, e, :], gain(g_col, b, t), x[:, t, :], MULT, ADD)
+        def read_centre(k, e):
+            b, lo = plain[k]
+            read_scaled(centre[k], fill(scalar_bank(), [0], b, pairs[e], lo, lo + RANGE), b, pairs[e])
 
-        def product(engine, dst, b, at, lo, hi):
-            a0, a1 = (arm[:, :, lo - at : hi - at] for arm in arms[b, at])
-            engine.tensor_tensor(h_view(dst), woven(a0), woven(a1), MULT)
+        def fill_arms(k, e):
+            b, lo = plain[k]
+            filled[k, e] = [fill(vector_bank(), [l], b, pairs[e], lo, lo + RANGE) for l in (2, 1)]
 
-        w4_bf = [sb([P, N, 4], BF16, "w4_bf0"), placed([P, N, 4], BF16, "w4_bf1", 20 * KIB)]
+        def make_arms(k, e):
+            b = plain[k][0]
+            second, first = filled[k, e]
+            for n, t in enumerate(pairs[e]):
+                nc.vector.scalar_tensor_tensor(arms[k][1][:, t, :], centre[k][t], gain(g_inv, b, t), second[:, n, :], MULT, ADD)
+            for n, t in enumerate(pairs[e]):
+                nc.vector.scalar_tensor_tensor(arms[k][0][:, t, :], first[:, n, :], gain(g_col, b, t), centre[k][t], MULT, ADD)
+
+        def product(engine, dst, arm, cols=slice(None)):
+            engine.tensor_tensor(h_view(dst), woven(arm[0][:, :, cols]), woven(arm[1][:, :, cols]), MULT)
+
+        w4_bf = [sb([P, N, 4], BF16, f"w4_bf{b}") for b in range(2)]
         w4_q = sb([P, 2 * N], U32, "w4_q")
-        w4_s = placed([P, 2 * N], U8, "w4_s", 10 * KIB)
+        w4_s = placed([P, 2 * N], U8, "w4_s", 13 * KIB + 704)
 
         def cast_w4(b, lo, hi):
             nc.scalar.activation(h_view(w4_bf[b][:, lo:hi]), woven(w4_raw[b][:, :, lo:hi]), COPY)
@@ -304,9 +296,9 @@ def tile_list_bond_angle_features_kernel(
                 stop=not start,
             )
 
-        def mix(lo, hi, groups):
-            for ms in groups:
-                bank = scalar_bank()[:, 0 : len(ms) * (hi - lo)].rearrange("p (m s) -> p m s", m=len(ms))
+        def mix(lo, hi, groups, at=None):
+            for n, ms in enumerate(groups):
+                bank = (banks[at + n] if at is not None else scalar_bank())[:, 0 : len(ms) * (hi - lo)].rearrange("p (m s) -> p m s", m=len(ms))
                 for e, m in enumerate(ms):
                     for b in range(2):
                         mix_pass(bank[:, e, :], m, b, lo, hi, b == 0)
@@ -315,12 +307,21 @@ def tile_list_bond_angle_features_kernel(
 
         cast_w1(0, "scalar")
         quant_w1(0)
+        nc.scalar.copy(*dealt(g_dealt, g_rows, F32, 1, 4))
+        g_bank = banks[7]
+        for t in range(4):
+            nc.tensor.transpose(g_bank[:, t * P : (t + 1) * P], g_dealt[:, t * P : (t + 1) * P], ident[:])
+        nc.scalar.copy(
+            g_col[:].rearrange("p (b t) -> p t b", b=2), g_bank[:].rearrange("p (t r) -> p t r", t=4)[:, :, P - 2 : P]
+        )
+        nc.gpsimd.tensor_scalar(g_zero[:], g_col[:], 0.0, 0.0, IS_EQUAL, ADD)
+        nc.gpsimd.tensor_tensor(g_safe[:], g_zero[:], g_col[:], ADD)
         nc.vector.reciprocal(g_inv[:], g_safe[:])
-        nc.scalar.copy(*dealt(ws_p[0], ws_raw[0], U32, 2, 1))
         cast_w1(1, "scalar")
+        nc.scalar.copy(*dealt(ws_p[0], ws_raw[0], U32, 2, 1))
+        nc.scalar.copy(*dealt(ws_p[1], ws_raw[1], U32, 2, 1))
         nc.scalar.copy(*dealt(w2_p, w2_raw, U32, 2, 2))
         nc.scalar.copy(*dealt(w3_p[0], w3_raw[0], U32, 1, 4))
-        nc.scalar.copy(*dealt(ws_p[1], ws_raw[1], U32, 2, 1))
         cast_w1(2, "scalar", (0, 1))
         cast_w1(2, "gpsimd", (2, 3))
         nc.gpsimd.tensor_copy(*dealt(w3_p[1], w3_raw[1], U32, 1, 4))
@@ -333,46 +334,67 @@ def tile_list_bond_angle_features_kernel(
         pick_words(2, HALF, S, v_late[:, 0, :])
         pick_words(1, HALF, S, v_late[:, 1, :])
 
-        doubled(0, 0, RANGE, vector_bank, "w1_raw2")
-        pairs = tiles_of(RANGE)
-        plain = [(1, 0), (1, 256), (0, 512), (1, 512), (0, 768)]
-        doubled(0, RANGE, HALF, scalar_bank, None, lambda: read_centre(*plain[0], pairs[0]))
-        read_centre(*plain[0], pairs[1])
-        side = placed([P, 4, RANGE], F32, "side", 24 * KIB)
+        early = [
+            [sb([P, 4, RANGE], F32, "early0_0"), placed([P, 4, RANGE], F32, "early0_1", 4 * KIB)],
+            [sb([P, 4, RANGE], F32, f"early1_{l}") for l in range(2)],
+        ]
+        for ts in pairs:
+            first_arm(early[0][0], vector_bank(), 0, ts, 0)
+        for ts in pairs:
+            second_arm(early[0][1], vector_bank(), 0, ts, 0)
+        product(nc.gpsimd, h_bf[0][:, 0], early[0])
+        for ts in pairs:
+            first_arm(early[1][0], scalar_bank(), 0, ts, RANGE)
+        read_centre(0, 0)
+        for ts in pairs:
+            second_arm(early[1][1], scalar_bank(), 0, ts, RANGE)
+        product(nc.gpsimd, h_bf[1][:, 0], early[1])
+        fill_arms(0, 0)
+        read_centre(0, 1)
+        fill_arms(0, 1)
+
+        side = placed([P, 4, RANGE], F32, "side", 20 * KIB)
+        h_gpsimd = sb([P, CHUNK, 4], BF16, "h_gpsimd")
+        h_last = placed([P, CHUNK, 4], BF16, "h_last", 24 * KIB)
+        h_doubled = sb([P, RANGE, 4], BF16, "h_doubled")
+        late = []
         for k, (b, lo) in enumerate(plain):
-            for e, ts in enumerate(pairs):
-                make_arms(b, lo, ts)
-                if k + 1 < len(plain):
-                    read_centre(*plain[k + 1], ts)
+            for e in range(2):
+                if k < 3:
+                    read_centre(k + 1, e)
+                make_arms(k, e)
+                if k < 4:
+                    fill_arms(k + 1, e)
+                else:
+                    at = 768 + e * CHUNK
+                    late.append(fill(vector_bank(), [0, 2], 1, range(4), at, at + CHUNK))
                 if k < 2:
                     cast_w4(k, e * N // 2, (e + 1) * N // 2)
-                if k == 2:
-                    read_scaled(side, fill(scalar_bank(), [0, 1], 1, ts, 768, S), 1, ts)
-                if (k, e) == (4, 0):
-                    mix(256, 512, ([0, 1], [2]))
             if k == 2:
+                for e in range(2):
+                    read_centre(4, e)
+                for ts in pairs:
+                    first_arm(side, scalar_bank(), 1, ts, 768)
                 quant_w4(0)
                 quant_w4(1)
                 quant_range(0)
-                mix(0, 256, ([0, 1], [2]))
                 quant_range(1)
-            if k == 4:
-                quant_range(2)
-            hi = lo + (RANGE if k < 4 else CHUNK)
-            product(nc.gpsimd, h_part(h_bf, b, lo, hi), b, lo, lo, hi)
-        for lo in (768, 896):
-            view = fill(vector_bank(), [0, 2], 1, range(4), lo, lo + CHUNK)
-            nc.vector.tensor_tensor(
-                h_view(h_part(h_bf, 1, lo, lo + CHUNK)), woven(view), woven(side[:, :, lo - 768 : lo - 768 + CHUNK]), MULT
-            )
+                mix(0, 256, ([0, 1], [2]))
+            if k < 4:
+                product(nc.gpsimd, h_part(h_bf, b, lo, lo + RANGE), arms[k])
+        product(nc.gpsimd, h_gpsimd[:], arms[4], slice(0, CHUNK))
+        for e in range(2):
+            cols = slice(e * CHUNK, (e + 1) * CHUNK)
+            nc.vector.tensor_tensor(h_view(h_doubled[:, cols]), woven(late[e]), woven(side[:, :, cols]), MULT)
+        mix(256, 512, ([0, 1], [2]), 0)
+        quant_range(2)
         mix(512, 768, ([0, 1], [2]))
-        h_last = placed([P, CHUNK, 4], BF16, "h_last", 25 * KIB)
-        product(nc.vector, h_last[:], 0, 768, 896, S)
-        for b in range(2):
-            quant_part(h_part(h_bf, b, 768, 896), b, 768, 896)
+        product(nc.vector, h_last[:], arms[4], slice(CHUNK, RANGE))
+        quant_part(h_gpsimd[:], 0, 768, 896)
+        quant_part(h_doubled[:, 0:CHUNK], 1, 768, 896)
         mix(768, 896, ([0, 1, 2],))
-        quant_part(h_part(h_bf, 1, 896, S), 1, 896, S)
-        last = [vector_bank()[:, 0:CHUNK] for m in range(3)]
+        quant_part(h_doubled[:, CHUNK:RANGE], 1, 896, S)
+        last = [banks[m][:, 0:CHUNK] for m in (2, 3, 5)]
         for m in range(3):
             mix_pass(last[m], m, 1, 896, S, True)
         quant_part(h_last[:], 0, 896, S)

@@ -59,10 +59,10 @@ def tile_list_bond_angle_features_kernel(
         tab_w = sb([P, T], I32, "tab_w")
         ws_raw = [sb([P, H // 4], I32, f"ws_raw{k}") for k in range(2)]
         w1_cuts = (0, 512, 768, 1024)
-        w1_raw = [sb([P, 4, 512], F32, "w1_raw0"), sb([P, 4, 256], F32, "w1_raw1"), placed([P, 4, 256], F32, "w1_raw2", 2 * KIB)]
+        w1_raw = [sb([P, 4, 512], F32, "w1_raw0"), sb([P, 4, 256], F32, "w1_raw1"), sb([P, 4, 256], F32, "w1_raw2")]
         w2_raw = sb([P, H // 2], I32, "w2_raw")
         w3_raw = [sb([P, HALF], I32, f"w3_raw{b}") for b in range(2)]
-        w4_raw = [sb([P, 4, N], F32, "w4_raw0"), placed([P, 4, N], F32, "w4_raw1", 24 * KIB)]
+        w4_raw = [sb([P, 4, N], F32, "w4_raw0"), sb([P, 4, N], F32, "w4_raw1")]
         g_rows = sb([P, HALF], F32, "g_rows")
         g_dealt = sb([P, HALF], F32, "g_dealt")
         ident = sb([P, P], F32, "ident")
@@ -139,7 +139,7 @@ def tile_list_bond_angle_features_kernel(
                 src[:].bitcast(dtype).rearrange("p (b q t e) -> p b t q e", b=b, t=4, e=e),
             )
 
-        w1_bf = [sb([P, 4, 32, 4, 4], BF16, "w1_bf0"), placed([P, 4, 32, 4, 4], BF16, "w1_bf1", 8 * KIB)]
+        w1_bf = [sb([P, 4, 32, 4, 4], BF16, "w1_bf0"), placed([P, 4, 32, 4, 4], BF16, "w1_bf1", 0)]
         w1_q = [sb([P, HALF], U32, f"w1_q{b}") for b in range(2)]
         w1_s = [sb([P, HALF], U8, f"w1_s{b}") for b in range(2)]
 
@@ -210,31 +210,48 @@ def tile_list_bond_angle_features_kernel(
         def h_view(ap):
             return ap.rearrange("p (c i) t -> p c t i", i=4)
 
-        h_bf = [placed([P, 2, RANGE, 4], BF16, f"h_bf{r}", at * KIB) for r, at in enumerate((8, 16, 16))]
-        h_q = [sb([P, 2, RANGE], U32, f"h_q{r}") for r in range(4)]
-        h_s = [placed([P, 2, RANGE], U8, f"h_s{r}", at) for r, at in enumerate((13 * KIB - 448, 13 * KIB + 128, 20 * KIB, 26 * KIB))]
-
-        def h_part(tiles, b, lo, hi):
-            r, col = divmod(lo, RANGE)
-            return tiles[r][:, b, col : col + hi - lo]
+        groups = [
+            ([(0, 0, 256), (1, 0, 256)], 20 * KIB, 12 * KIB + 128),
+            ([(0, 256, 256)], None, 12 * KIB + 704),
+            ([(1, 256, 256)], 20 * KIB, None),
+            ([(0, 768, 128), (0, 896, 128)], None, 32 * KIB),
+            ([(1, 768, 128), (1, 896, 128)], 68 * KIB, 32 * KIB + 512),
+            ([(0, 512, 128)], 20 * KIB, None),
+            ([(1, 512, 128), (1, 640, 128)], None, None),
+            ([(0, 640, 128)], 34 * KIB, None),
+        ]
+        values, quantised, group_of = {}, {}, {}
+        for n, (pieces, values_at, scales_at) in enumerate(groups):
+            width = sum(piece[2] for piece in pieces)
+            h_bf = sb([P, width, 4], BF16, f"h_bf{n}") if values_at is None else placed([P, width, 4], BF16, f"h_bf{n}", values_at)
+            h_s = sb([P, width], U8, f"h_s{n}") if scales_at is None else placed([P, width], U8, f"h_s{n}", scales_at)
+            h_q = sb([P, width], U32, f"h_q{n}")
+            group_of[pieces[0][0], pieces[0][1]] = (h_q, h_s, h_bf)
+            at = 0
+            for b, lo, w in pieces:
+                values[b, lo] = h_bf[:, at : at + w]
+                for c in range(0, w, CHUNK):
+                    quantised[b, lo + c] = (h_q, h_s, at + c)
+                at += w
 
         pairs = ([0, 1], [2, 3])
 
         def first_arm(dst, bank, b, ts, lo):
             read_scaled([dst[:, t, :] for t in range(4)], fill(bank, [0, 1], b, ts, lo, lo + RANGE), b, ts)
 
-        def second_arm(dst, bank, b, ts, lo):
-            nc.scalar.copy(dst[:, ts[0] : ts[1] + 1, :], fill(bank, [0, 2], b, ts, lo, lo + RANGE))
-
-        plain = [(1, 0), (1, 256), (0, 512), (1, 512), (0, 768)]
-        third = {2: 13 * KIB}
+        plain = [(0, 0), (0, 256), (1, 0), (1, 256), (0, 512)]
+        third = {1: 4 * KIB, 2: 7 * KIB, 3: 12 * KIB}
         centre = []
         for k in range(5):
+            if k == 0:
+                centre_first = sb([P, 4, RANGE], F32, "centre_first")
+                centre.append([centre_first[:, t, :] for t in range(4)])
+                continue
             tiles = [sb([P, RANGE], F32, f"centre{k}_{t}") for t in range(4)]
             if k in third:
                 tiles[2] = placed([P, RANGE], F32, f"centre{k}_third", third[k])
             centre.append([tile[:] for tile in tiles])
-        arm_at = {(1, 1): 32 * KIB, (3, 1): 32 * KIB, (3, 0): 24 * KIB}
+        arm_at = {(0, 0): 0, (2, 1): 28 * KIB, (4, 1): 28 * KIB}
         arms = [
             [placed([P, 4, RANGE], F32, f"arm{k}_{l}", arm_at.get((k, l), (40 + 8 * k + 4 * l) * KIB)) for l in range(2)]
             for k in range(5)
@@ -247,22 +264,21 @@ def tile_list_bond_angle_features_kernel(
 
         def fill_arms(k, e):
             b, lo = plain[k]
-            filled[k, e] = [fill(vector_bank(), [l], b, pairs[e], lo, lo + RANGE) for l in (2, 1)]
+            filled[k, e] = [fill(vector_bank(), [l], b, pairs[e], lo, lo + RANGE) for l in ((2, 1) if k else (2,))]
 
         def make_arms(k, e):
             b = plain[k][0]
-            second, first = filled[k, e]
             for n, t in enumerate(pairs[e]):
-                nc.vector.scalar_tensor_tensor(arms[k][1][:, t, :], centre[k][t], gain(g_inv, b, t), second[:, n, :], MULT, ADD)
-            for n, t in enumerate(pairs[e]):
-                nc.vector.scalar_tensor_tensor(arms[k][0][:, t, :], first[:, n, :], gain(g_col, b, t), centre[k][t], MULT, ADD)
+                nc.vector.scalar_tensor_tensor(arms[k][1][:, t, :], centre[k][t], gain(g_inv, b, t), filled[k, e][0][:, n, :], MULT, ADD)
+            for n, t in enumerate(pairs[e] if k else ()):
+                nc.vector.scalar_tensor_tensor(arms[k][0][:, t, :], filled[k, e][1][:, n, :], gain(g_col, b, t), centre[k][t], MULT, ADD)
 
         def product(engine, dst, arm, cols=slice(None)):
             engine.tensor_tensor(h_view(dst), woven(arm[0][:, :, cols]), woven(arm[1][:, :, cols]), MULT)
 
         w4_bf = [sb([P, N, 4], BF16, f"w4_bf{b}") for b in range(2)]
         w4_q = sb([P, 2 * N], U32, "w4_q")
-        w4_s = placed([P, 2 * N], U8, "w4_s", 13 * KIB + 704)
+        w4_s = placed([P, 2 * N], U8, "w4_s", 12 * KIB - 704)
 
         def cast_w4(b, lo, hi):
             nc.scalar.activation(h_view(w4_bf[b][:, lo:hi]), woven(w4_raw[b][:, :, lo:hi]), COPY)
@@ -271,27 +287,22 @@ def tile_list_bond_angle_features_kernel(
             cols = slice(b * N, (b + 1) * N)
             nc.vector.quantize_mx(w4_q[:, cols].bitcast(FP8X4), w4_s[:, cols], w4_bf[b][:].rearrange("p n t -> p (n t)"))
 
-        def quant_range(r):
-            nc.vector.quantize_mx(
-                h_q[r][:].rearrange("p b n -> p (b n)").bitcast(FP8X4),
-                h_s[r][:].rearrange("p b n -> p (b n)"),
-                h_bf[r][:].rearrange("p b n t -> p (b n t)"),
-            )
-
-        def quant_part(src, b, lo, hi):
-            nc.vector.quantize_mx(h_part(h_q, b, lo, hi).bitcast(FP8X4), h_part(h_s, b, lo, hi), src.rearrange("p n t -> p (n t)"))
+        def quant(pieces):
+            h_q, h_s, h_bf = group_of[pieces[0]]
+            nc.vector.quantize_mx(h_q[:].bitcast(FP8X4), h_s[:], h_bf[:].rearrange("p n t -> p (n t)"))
 
         res = sb([P, 3, S], F32, "res")
         out_view = out.rearrange("(m p) s -> p m s", p=P)
 
         def mix_pass(dst, m, b, lo, hi, start):
             cols = slice(b * N + m * P, b * N + (m + 1) * P)
+            h_q, h_s, at = quantised[b, lo]
             nc.tensor.matmul_mx(
                 dst,
                 lhsT=w4_q[:, cols].bitcast(FP8X4),
                 lhsT_scale=w4_s[:, cols],
-                rhs=h_part(h_q, b, lo, hi).bitcast(FP8X4),
-                rhs_scale=h_part(h_s, b, lo, hi),
+                rhs=h_q[:, at : at + hi - lo].bitcast(FP8X4),
+                rhs_scale=h_s[:, at : at + hi - lo],
                 start=start,
                 stop=not start,
             )
@@ -322,83 +333,101 @@ def tile_list_bond_angle_features_kernel(
         nc.scalar.copy(*dealt(ws_p[1], ws_raw[1], U32, 2, 1))
         nc.scalar.copy(*dealt(w2_p, w2_raw, U32, 2, 2))
         nc.scalar.copy(*dealt(w3_p[0], w3_raw[0], U32, 1, 4))
-        cast_w1(2, "scalar", (0, 1))
-        cast_w1(2, "gpsimd", (2, 3))
-        nc.gpsimd.tensor_copy(*dealt(w3_p[1], w3_raw[1], U32, 1, 4))
+        cast_w1(2, "gpsimd", (3,))
         for lo in (0, RANGE):
             for l in range(3):
                 pick_words(l, lo, lo + RANGE)
-        pick_words(0, HALF, S)
-        quant_w1(1)
-        v_late = placed([P, 2, HALF], U32, "v_late", 0)
-        pick_words(2, HALF, S, v_late[:, 0, :])
-        pick_words(1, HALF, S, v_late[:, 1, :])
 
-        early = [
-            [sb([P, 4, RANGE], F32, "early0_0"), placed([P, 4, RANGE], F32, "early0_1", 4 * KIB)],
-            [sb([P, 4, RANGE], F32, f"early1_{l}") for l in range(2)],
-        ]
-        for ts in pairs:
-            first_arm(early[0][0], vector_bank(), 0, ts, 0)
-        for ts in pairs:
-            second_arm(early[0][1], vector_bank(), 0, ts, 0)
-        product(nc.gpsimd, h_bf[0][:, 0], early[0])
-        for ts in pairs:
-            first_arm(early[1][0], scalar_bank(), 0, ts, RANGE)
+        neighbour = sb([P, 4, RANGE], F32, "neighbour")
+
+        def sum_first(e):
+            ts = pairs[e]
+            read_scaled([neighbour[:, t, :] for t in range(4)], fill(scalar_bank(), [1], 0, ts, 0, RANGE), 0, ts)
+            both = slice(ts[0], ts[1] + 1)
+            nc.gpsimd.tensor_tensor(arms[0][0][:, both, :], centre_first[:, both, :], neighbour[:, both, :], ADD)
+
         read_centre(0, 0)
-        for ts in pairs:
-            second_arm(early[1][1], scalar_bank(), 0, ts, RANGE)
-        product(nc.gpsimd, h_bf[1][:, 0], early[1])
-        fill_arms(0, 0)
+        cast_w1(2, "scalar", (0, 1, 2))
+        quant_w1(1)
+        sum_first(0)
         read_centre(0, 1)
-        fill_arms(0, 1)
+        for e in range(2):
+            fill_arms(0, e)
+        sum_first(1)
 
-        side = placed([P, 4, RANGE], F32, "side", 20 * KIB)
-        h_gpsimd = sb([P, CHUNK, 4], BF16, "h_gpsimd")
-        h_last = placed([P, CHUNK, 4], BF16, "h_last", 24 * KIB)
-        h_doubled = sb([P, RANGE, 4], BF16, "h_doubled")
-        late = []
+        doubled = [(0, 768), (0, 896), (1, 768), (1, 896), (1, 512), (1, 640)]
+        side_at = {(0, 768): 16 * KIB, (1, 768): 32 * KIB, (1, 512): 36 * KIB}
+        sides = {key: placed([P, 4, RANGE], F32, f"side{key[0]}_{key[1]}", at) for key, at in side_at.items()}
+        late = {}
+
+        def read_side(b, lo, e):
+            first_arm(sides[b, lo], scalar_bank(), b, pairs[e], lo)
+
+        def fill_doubled(n):
+            b, lo = doubled[n]
+            late[n] = fill(vector_bank(), [0, 2], b, range(4), lo, lo + CHUNK)
+
+        def finish_doubled(n):
+            b, lo = doubled[n]
+            side = sides[b, lo - lo % RANGE][:, :, lo % RANGE : lo % RANGE + CHUNK]
+            nc.vector.tensor_tensor(h_view(values[b, lo]), woven(late[n]), woven(side), MULT)
+
         for k, (b, lo) in enumerate(plain):
+            if k == 3:
+                for e in range(2):
+                    read_centre(4, e)
             for e in range(2):
                 if k < 3:
                     read_centre(k + 1, e)
+                if k == 3:
+                    for pair in range(2):
+                        read_side(e, 768, pair)
                 make_arms(k, e)
                 if k < 4:
                     fill_arms(k + 1, e)
                 else:
-                    at = 768 + e * CHUNK
-                    late.append(fill(vector_bank(), [0, 2], 1, range(4), at, at + CHUNK))
-                if k < 2:
-                    cast_w4(k, e * N // 2, (e + 1) * N // 2)
+                    for n in (2 * e, 2 * e + 1):
+                        fill_doubled(n)
+                if k in (1, 2):
+                    cast_w4(k - 1, e * N // 2, (e + 1) * N // 2)
+            if k == 0:
+                nc.scalar.copy(*dealt(w3_p[1], w3_raw[1], U32, 1, 4))
+            if k == 1:
+                pick_words(0, HALF, S, placed([P, HALF], U32, "v_late0", third[1])[:])
             if k == 2:
-                for e in range(2):
-                    read_centre(4, e)
-                for ts in pairs:
-                    first_arm(side, scalar_bank(), 1, ts, 768)
+                v_late = placed([P, 2, HALF], U32, "v_late", third[2])
+                pick_words(1, HALF, S, v_late[:, 0, :])
+                pick_words(2, HALF, S, v_late[:, 1, :])
+            if k == 3:
+                for pair in range(2):
+                    read_side(1, 512, pair)
                 quant_w4(0)
                 quant_w4(1)
-                quant_range(0)
-                quant_range(1)
+                quant([(0, 256)])
+                quant([(0, 0), (1, 0)])
                 mix(0, 256, ([0, 1], [2]))
             if k < 4:
-                product(nc.gpsimd, h_part(h_bf, b, lo, lo + RANGE), arms[k])
-        product(nc.gpsimd, h_gpsimd[:], arms[4], slice(0, CHUNK))
-        for e in range(2):
-            cols = slice(e * CHUNK, (e + 1) * CHUNK)
-            nc.vector.tensor_tensor(h_view(h_doubled[:, cols]), woven(late[e]), woven(side[:, :, cols]), MULT)
-        mix(256, 512, ([0, 1], [2]), 0)
-        quant_range(2)
-        mix(512, 768, ([0, 1], [2]))
-        product(nc.vector, h_last[:], arms[4], slice(CHUNK, RANGE))
-        quant_part(h_gpsimd[:], 0, 768, 896)
-        quant_part(h_doubled[:, 0:CHUNK], 1, 768, 896)
-        mix(768, 896, ([0, 1, 2],))
-        quant_part(h_doubled[:, CHUNK:RANGE], 1, 896, S)
-        last = [banks[m][:, 0:CHUNK] for m in (2, 3, 5)]
+                product(nc.gpsimd, values[b, lo], arms[k])
+        for n in range(6):
+            finish_doubled(n)
+            if n < 2:
+                fill_doubled(n + 4)
+            if n == 1:
+                quant([(1, 256)])
+                product(nc.gpsimd, values[0, 512], arms[4], slice(0, CHUNK))
+                mix(256, 512, ([0, 1], [2]))
+        quant([(0, 768), (0, 896)])
+        quant([(1, 768), (1, 896)])
+        mix(768, S, ([0, 1], [2]))
+        product(nc.vector, values[0, 640], arms[4], slice(CHUNK, RANGE))
+        quant([(0, 512)])
+        quant([(1, 512), (1, 640)])
+        mix(512, 640, ([0, 1, 2],))
+        last = [vector_bank()[:, 0:CHUNK] for m in range(3)]
         for m in range(3):
-            mix_pass(last[m], m, 1, 896, S, True)
-        quant_part(h_last[:], 0, 896, S)
+            mix_pass(last[m], m, 1, 640, 768, True)
+        quant([(0, 640)])
         for m in range(3):
-            mix_pass(last[m], m, 0, 896, S, False)
-            nc.scalar.activation(res[:, m, 896:S], last[m], TANH)
-            (nc.scalar if m == 2 else nc.sync).dma_start(out_view[:, m, 896:S], res[:, m, 896:S])
+            mix_pass(last[m], m, 0, 640, 768, False)
+            nc.scalar.activation(res[:, m, 640:768], last[m], TANH)
+            (nc.scalar if m == 2 else nc.sync).dma_start(out_view[:, m, 640:768], res[:, m, 640:768])

@@ -51,15 +51,16 @@ def tile_list_bond_angle_features_kernel(
         def sb(shape, dtype, name, tag=None):
             return keep.tile(shape, dtype, align_bytes=64, name=name, tag=tag or name)
 
-        def placed(shape, dtype, name, at):
-            return shared.tile(shape, dtype, align_bytes=64, name=name, offset=at)
+        def placed(shape, dtype, name, at, wider=1):
+            tile = shared.tile([shape[0], wider] + shape[1:], dtype, align_bytes=64, name=name, offset=at)
+            return tile[:, 0]
 
         lists = [keep.tile([P, S // 16], U16, name=f"list{l}") for l in range(3)]
         tab_s = sb([P, T // 4], I32, "tab_s")
         tab_w = sb([P, T], I32, "tab_w")
         ws_raw = [sb([P, H // 4], I32, f"ws_raw{k}") for k in range(2)]
         w1_cuts = (0, 512, 768, 1024)
-        w1_raw = [sb([P, 4, 512], F32, "w1_raw0"), sb([P, 4, 256], F32, "w1_raw1"), sb([P, 4, 256], F32, "w1_raw2")]
+        w1_raw = [sb([P, 4, 512], F32, "w1_raw0"), sb([P, 4, 256], F32, "w1_raw1"), placed([P, 4, 256], F32, "w1_raw2", 4 * KIB, 8)]
         w2_raw = sb([P, H // 2], I32, "w2_raw")
         w3_raw = [sb([P, HALF], I32, f"w3_raw{b}") for b in range(2)]
         w4_raw = [sb([P, 4, N], F32, "w4_raw0"), sb([P, 4, N], F32, "w4_raw1")]
@@ -71,15 +72,14 @@ def tile_list_bond_angle_features_kernel(
         g_safe = sb([P, 8], F32, "g_safe")
         g_inv = sb([P, 8], F32, "g_inv")
         zeros = sb([P, HALF], F32, "zeros")
-        planes = [sb([P, 3, HALF // 4], I32, f"planes{u}") for u in range(2)]
+        planes = sb([P, 3, S // 4], I32, "planes")
         picked = [sb([P, 3, HALF], U8, f"picked{u}") for u in range(2)]
 
         for k in range(2):
             nc.gpsimd.memset(ws_raw[k][:], 0)
         nc.vector.memset(zeros[:], 0.0)
         nc.vector.memset(tab_s[0:SCALE_ROWS, :], 0)
-        for u in range(2):
-            nc.vector.memset(planes[u][:], 0)
+        nc.vector.memset(planes[:], 0)
         nc.scalar.activation(g_rows[0 : P - 2, :], zeros[0 : P - 2, :], TANH)
         nc.gpsimd.affine_select(
             out=ident[:], in_=zeros[:, 0:P], compare_op=NOT_EQUAL, fill=1.0, base=0, pattern=[[-1, P]], channel_multiplier=1
@@ -103,8 +103,7 @@ def tile_list_bond_angle_features_kernel(
         def carry_scales(u):
             for r in range(4):
                 nc.sync.dma_start(
-                    planes[u][r:P:32].rearrange("p l s -> p (l s)"),
-                    picked[u][SCALE_ROWS + r : P : 4].rearrange("p l s -> p (l s)").bitcast(I32),
+                    planes[r:P:32, :, u * HALF // 4 : (u + 1) * HALF // 4], picked[u][SCALE_ROWS + r : P : 4].bitcast(I32)
                 )
 
         nc.sync.dma_start(tab_s[SCALE_ROWS:P, :], tab_scales[0].bitcast(I32))
@@ -120,12 +119,12 @@ def tile_list_bond_angle_features_kernel(
             pick_scales(l, 0)
         carry_scales(0)
         nc.sync.dma_start(w2_raw[:], w2_words[0].bitcast(I32))
-        nc.sync.dma_start(w3_raw[0][:], w3_rows[:, 0:HALF])
         load_w1(2)
-        nc.sync.dma_start(w3_raw[1][:], w3_rows[:, HALF:H])
         for l in range(3):
             pick_scales(l, 1)
         carry_scales(1)
+        for b in range(2):
+            nc.sync.dma_start(w3_raw[b][:], w3_rows[:, b * HALF : (b + 1) * HALF])
         for u in range(8):
             nc.sync.dma_start(w4_raw[u // 4][:, u % 4, :], w4_view[u // 4, u % 4])
 
@@ -179,13 +178,12 @@ def tile_list_bond_angle_features_kernel(
         def project(dst, l, b, t, lo, hi, start, stop):
             codes, scale = weight(l, b, t)
             tile, at = v_words[l, lo]
-            u, col = divmod(lo, HALF)
             nc.tensor.matmul_mx(
                 dst,
                 lhsT=codes,
                 lhsT_scale=scale,
                 rhs=tile[:, lo - at : hi - at].bitcast(FP8X4),
-                rhs_scale=planes[u][:, l, :].bitcast(U8)[:, col : col + hi - lo],
+                rhs_scale=planes[:, l, :].bitcast(U8)[:, lo:hi],
                 start=start,
                 stop=stop,
             )
@@ -210,15 +208,16 @@ def tile_list_bond_angle_features_kernel(
         def h_view(ap):
             return ap.rearrange("p (c i) t -> p c t i", i=4)
 
+        held = 40 * KIB
         groups = [
-            ([(0, 0, 256), (1, 0, 256)], 20 * KIB, 12 * KIB + 128),
-            ([(0, 256, 256)], None, 12 * KIB + 704),
-            ([(1, 256, 256)], 20 * KIB, None),
-            ([(0, 768, 128), (0, 896, 128)], None, 32 * KIB),
-            ([(1, 768, 128), (1, 896, 128)], 68 * KIB, 32 * KIB + 512),
-            ([(0, 512, 128)], 20 * KIB, None),
-            ([(1, 512, 128), (1, 640, 128)], None, None),
-            ([(0, 640, 128)], 34 * KIB, None),
+            ([(0, 256, 256), (1, 256, 256)], None, held + 832),
+            ([(0, 768, 128), (0, 896, 128), (1, 768, 128), (1, 896, 128)], None, held + 1344),
+            ([(0, 512, 128), (0, 640, 128)], None, held + 1856),
+            ([(1, 512, 128)], None, held + 2112),
+            ([(1, 640, 128)], held - 960, None),
+            ([(0, 0, 256)], None, held + 2240),
+            ([(1, 0, 128)], held + 4032, None),
+            ([(1, 128, 128)], held + 2560, None),
         ]
         values, quantised, group_of = {}, {}, {}
         for n, (pieces, values_at, scales_at) in enumerate(groups):
@@ -239,46 +238,23 @@ def tile_list_bond_angle_features_kernel(
         def first_arm(dst, bank, b, ts, lo):
             read_scaled([dst[:, t, :] for t in range(4)], fill(bank, [0, 1], b, ts, lo, lo + RANGE), b, ts)
 
-        plain = [(0, 0), (0, 256), (1, 0), (1, 256), (0, 512)]
-        third = {1: 4 * KIB, 2: 7 * KIB, 3: 12 * KIB}
-        centre = []
-        for k in range(5):
-            if k == 0:
-                centre_first = sb([P, 4, RANGE], F32, "centre_first")
-                centre.append([centre_first[:, t, :] for t in range(4)])
-                continue
-            tiles = [sb([P, RANGE], F32, f"centre{k}_{t}") for t in range(4)]
-            if k in third:
-                tiles[2] = placed([P, RANGE], F32, f"centre{k}_third", third[k])
-            centre.append([tile[:] for tile in tiles])
-        arm_at = {(0, 0): 0, (2, 1): 28 * KIB, (4, 1): 28 * KIB}
-        arms = [
-            [placed([P, 4, RANGE], F32, f"arm{k}_{l}", arm_at.get((k, l), (40 + 8 * k + 4 * l) * KIB)) for l in range(2)]
-            for k in range(5)
-        ]
-        filled = {}
+        def by_tile(tile):
+            return [tile[:, t, :] for t in range(tile.shape[1])]
 
-        def read_centre(k, e):
-            b, lo = plain[k]
-            read_scaled(centre[k], fill(scalar_bank(), [0], b, pairs[e], lo, lo + RANGE), b, pairs[e])
+        def second_arm(dst, x, view, b, ts):
+            for n, t in enumerate(ts):
+                nc.vector.scalar_tensor_tensor(dst[:, t, :], x[t], gain(g_inv, b, t), view[:, n, :], MULT, ADD)
 
-        def fill_arms(k, e):
-            b, lo = plain[k]
-            filled[k, e] = [fill(vector_bank(), [l], b, pairs[e], lo, lo + RANGE) for l in ((2, 1) if k else (2,))]
-
-        def make_arms(k, e):
-            b = plain[k][0]
-            for n, t in enumerate(pairs[e]):
-                nc.vector.scalar_tensor_tensor(arms[k][1][:, t, :], centre[k][t], gain(g_inv, b, t), filled[k, e][0][:, n, :], MULT, ADD)
-            for n, t in enumerate(pairs[e] if k else ()):
-                nc.vector.scalar_tensor_tensor(arms[k][0][:, t, :], filled[k, e][1][:, n, :], gain(g_col, b, t), centre[k][t], MULT, ADD)
+        def first_arm_plain(dst, x, view, b, ts):
+            for n, t in enumerate(ts):
+                nc.vector.scalar_tensor_tensor(dst[:, t, :], view[:, n, :], gain(g_col, b, t), x[t], MULT, ADD)
 
         def product(engine, dst, arm, cols=slice(None)):
             engine.tensor_tensor(h_view(dst), woven(arm[0][:, :, cols]), woven(arm[1][:, :, cols]), MULT)
 
         w4_bf = [sb([P, N, 4], BF16, f"w4_bf{b}") for b in range(2)]
         w4_q = sb([P, 2 * N], U32, "w4_q")
-        w4_s = placed([P, 2 * N], U8, "w4_s", 12 * KIB - 704)
+        w4_s = placed([P, 2 * N], U8, "w4_s", held + 64)
 
         def cast_w4(b, lo, hi):
             nc.scalar.activation(h_view(w4_bf[b][:, lo:hi]), woven(w4_raw[b][:, :, lo:hi]), COPY)
@@ -332,102 +308,135 @@ def tile_list_bond_angle_features_kernel(
         nc.scalar.copy(*dealt(ws_p[0], ws_raw[0], U32, 2, 1))
         nc.scalar.copy(*dealt(ws_p[1], ws_raw[1], U32, 2, 1))
         nc.scalar.copy(*dealt(w2_p, w2_raw, U32, 2, 2))
-        nc.scalar.copy(*dealt(w3_p[0], w3_raw[0], U32, 1, 4))
         cast_w1(2, "gpsimd", (3,))
-        for lo in (0, RANGE):
-            for l in range(3):
-                pick_words(l, lo, lo + RANGE)
+        pick_words(0, 0, RANGE)
+        pick_words(1, 0, RANGE)
+        pick_words(0, RANGE, S)
 
-        neighbour = sb([P, 4, RANGE], F32, "neighbour")
+        spans = {"summed0": (0, 0, 256), "summed1": (0, 256, 512), "long": (1, 256, 768), "short": (1, 0, 256)}
+        centre_pairs = {
+            "summed0": [sb([P, 2, RANGE], F32, "centre_first")[:], placed([P, 2, RANGE], F32, "centre_second", 12 * KIB)],
+            "summed1": [placed([P, 2, RANGE], F32, f"centre_summed1_{e}", (14 + 2 * e) * KIB) for e in range(2)],
+        }
+        neighbour_pairs = {
+            key: [placed([P, 2, RANGE], F32, f"neighbour_{key}_{e}", (at + 2 * e) * KIB) for e in range(2)]
+            for key, at in (("summed0", 26), ("summed1", 30))
+        }
+        centre = {key: by_tile(tiles[0]) + by_tile(tiles[1]) for key, tiles in centre_pairs.items()}
+        centre["long"] = by_tile(placed([P, 4, HALF], F32, "centre_long", 18 * KIB))
+        centre["short"] = by_tile(sb([P, 4, RANGE], F32, "centre_short")[:])
+        neighbour = {key: by_tile(tiles[0]) + by_tile(tiles[1]) for key, tiles in neighbour_pairs.items()}
+        arms = {key: [sb([P, 4, hi - lo], F32, f"arm{l}_{key}") for l in range(2)] for key, (b, lo, hi) in spans.items()}
+        arms["summed0"][0] = placed([P, 4, RANGE], F32, "arm_first", 0)
 
-        def sum_first(e):
-            ts = pairs[e]
-            read_scaled([neighbour[:, t, :] for t in range(4)], fill(scalar_bank(), [1], 0, ts, 0, RANGE), 0, ts)
-            both = slice(ts[0], ts[1] + 1)
-            nc.gpsimd.tensor_tensor(arms[0][0][:, both, :], centre_first[:, both, :], neighbour[:, both, :], ADD)
+        def read(dst, l, key, ts, bank=None):
+            b, lo, hi = spans[key]
+            bank = scalar_bank() if bank is None else bank
+            read_scaled(dst[key], fill(bank, [l], b, ts, lo, hi), b, ts)
+            return bank
 
-        read_centre(0, 0)
+        def cast_quarter(n):
+            cast_w4(n // 2, n % 2 * N // 2, (n % 2 + 1) * N // 2)
+
+        def add_first(key, ts):
+            e = ts[0] // 2
+            nc.gpsimd.tensor_tensor(arms[key][0][:, ts[0] : ts[1] + 1, :], centre_pairs[key][e], neighbour_pairs[key][e], ADD)
+
+        def fill_for_vector(l, key, ts):
+            b, lo, hi = spans[key]
+            return fill(vector_bank(), [l], b, ts, lo, hi)
+
+        read(centre, 0, "summed0", pairs[0])
         cast_w1(2, "scalar", (0, 1, 2))
         quant_w1(1)
-        sum_first(0)
-        read_centre(0, 1)
-        for e in range(2):
-            fill_arms(0, e)
-        sum_first(1)
+        pick_words(1, RANGE, S, placed([P, S - RANGE], U32, "v_late1", 4 * KIB)[:])
+        pick_words(2, 0, S, placed([P, S], U32, "v_late2", 8 * KIB)[:])
+        read(neighbour, 1, "summed0", pairs[0])
+        add_first("summed0", pairs[0])
+        read(centre, 0, "summed0", pairs[1])
+        bank = read(centre, 0, "long", [0])
+        waiting = fill(banks[3], [0], 1, [1], *spans["long"][1:])
+        nc.scalar.copy(*dealt(w3_p[0], w3_raw[0], U32, 1, 4))
+        late_first = fill(banks[2], [0], 0, pairs[0], *spans["summed1"][1:])
+        read(neighbour, 1, "summed0", pairs[1], bank)
+        add_first("summed0", pairs[1])
+        read_scaled(centre["summed1"], late_first, 0, pairs[0])
+        read(neighbour, 1, "summed1", pairs[0])
+        add_first("summed1", pairs[0])
+        first = [fill_for_vector(1, "long", [t]) for t in range(2)]
+        read_scaled(centre["long"], waiting, 1, [1])
+        read(centre, 0, "summed1", pairs[1])
+        read(neighbour, 1, "summed1", pairs[1])
+        add_first("summed1", pairs[1])
+        read(centre, 0, "long", [2])
+        nc.scalar.copy(*dealt(w3_p[1], w3_raw[1], U32, 1, 4))
 
-        doubled = [(0, 768), (0, 896), (1, 768), (1, 896), (1, 512), (1, 640)]
-        side_at = {(0, 768): 16 * KIB, (1, 768): 32 * KIB, (1, 512): 36 * KIB}
-        sides = {key: placed([P, 4, RANGE], F32, f"side{key[0]}_{key[1]}", at) for key, at in side_at.items()}
-        late = {}
+        doubled = [(0, 512), (0, 768), (1, 768), (1, 896), (0, 896), (0, 640)]
+        sides = {key: sb([P, 4, RANGE], F32, f"side{key[0]}_{key[1]}") for key in ((0, 512), (0, 768))}
+        sides[1, 768] = placed([P, 4, RANGE], F32, "side_last", held)
 
-        def read_side(b, lo, e):
-            first_arm(sides[b, lo], scalar_bank(), b, pairs[e], lo)
+        def read_side(key):
+            for ts in pairs:
+                first_arm(sides[key], scalar_bank(), key[0], ts, key[1])
 
-        def fill_doubled(n):
-            b, lo = doubled[n]
-            late[n] = fill(vector_bank(), [0, 2], b, range(4), lo, lo + CHUNK)
-
-        def finish_doubled(n):
-            b, lo = doubled[n]
+        def finish_doubled(b, lo, bank):
+            view = fill(bank, [0, 2], b, range(4), lo, lo + CHUNK)
             side = sides[b, lo - lo % RANGE][:, :, lo % RANGE : lo % RANGE + CHUNK]
-            nc.vector.tensor_tensor(h_view(values[b, lo]), woven(late[n]), woven(side), MULT)
+            return lambda: nc.vector.tensor_tensor(h_view(values[b, lo]), woven(view), woven(side), MULT)
 
-        for k, (b, lo) in enumerate(plain):
-            if k == 3:
-                for e in range(2):
-                    read_centre(4, e)
-            for e in range(2):
-                if k < 3:
-                    read_centre(k + 1, e)
-                if k == 3:
-                    for pair in range(2):
-                        read_side(e, 768, pair)
-                make_arms(k, e)
-                if k < 4:
-                    fill_arms(k + 1, e)
-                else:
-                    for n in (2 * e, 2 * e + 1):
-                        fill_doubled(n)
-                if k in (1, 2):
-                    cast_w4(k - 1, e * N // 2, (e + 1) * N // 2)
-            if k == 0:
-                nc.scalar.copy(*dealt(w3_p[1], w3_raw[1], U32, 1, 4))
-            if k == 1:
-                pick_words(0, HALF, S, placed([P, HALF], U32, "v_late0", third[1])[:])
-            if k == 2:
-                v_late = placed([P, 2, HALF], U32, "v_late", third[2])
-                pick_words(1, HALF, S, v_late[:, 0, :])
-                pick_words(2, HALF, S, v_late[:, 1, :])
-            if k == 3:
-                for pair in range(2):
-                    read_side(1, 512, pair)
-                quant_w4(0)
-                quant_w4(1)
-                quant([(0, 256)])
-                quant([(0, 0), (1, 0)])
-                mix(0, 256, ([0, 1], [2]))
-            if k < 4:
-                product(nc.gpsimd, values[b, lo], arms[k])
-        for n in range(6):
-            finish_doubled(n)
-            if n < 2:
-                fill_doubled(n + 4)
-            if n == 1:
-                quant([(1, 256)])
-                product(nc.gpsimd, values[0, 512], arms[4], slice(0, CHUNK))
-                mix(256, 512, ([0, 1], [2]))
-        quant([(0, 768), (0, 896)])
-        quant([(1, 768), (1, 896)])
+        for t in range(2):
+            first_arm_plain(arms["long"][0], centre["long"], first[t], 1, [t])
+        for n, key in enumerate(("summed0", "summed1")):
+            for ts in pairs:
+                second_arm(arms[key][1], centre[key], fill_for_vector(2, key, ts), 0, ts)
+            product(nc.gpsimd, values[spans[key][:2]], arms[key])
+            if n == 0:
+                read(centre, 0, "long", [3])
+        for ts in pairs:
+            read(centre, 0, "short", ts)
+        cast_quarter(0)
+        for t in range(4):
+            second_arm(arms["long"][1], centre["long"], fill_for_vector(2, "long", [t]), 1, [t])
+            if t >= 2:
+                first_arm_plain(arms["long"][0], centre["long"], fill_for_vector(1, "long", [t]), 1, [t])
+            if t % 2:
+                read_side(doubled[t // 2])
+                cast_quarter(1 + t // 2)
+        product(nc.gpsimd, values[1, 256], arms["long"], slice(0, RANGE))
+        product(nc.gpsimd, values[1, 512], arms["long"], slice(RANGE, RANGE + CHUNK))
+        for n, ts in enumerate(pairs):
+            second_arm(arms["short"][1], centre["short"], fill_for_vector(2, "short", ts), 1, ts)
+            first_arm_plain(arms["short"][0], centre["short"], fill_for_vector(1, "short", ts), 1, ts)
+        read_side((1, 768))
+        cast_quarter(3)
+        for b, lo in doubled[:5]:
+            bank = vector_bank()
+            finish_doubled(b, lo, bank)()
+        last_doubled = finish_doubled(*doubled[5], bank)
+
+        quant_w4(0)
+        quant_w4(1)
+        quant([(0, 256)])
+        mix(256, 512, ([0, 1], [2]))
+        last_doubled()
+        quant([(0, 768)])
         mix(768, S, ([0, 1], [2]))
-        product(nc.vector, values[0, 640], arms[4], slice(CHUNK, RANGE))
+        product(nc.vector, values[1, 640], arms["long"], slice(RANGE + CHUNK, HALF))
         quant([(0, 512)])
-        quant([(1, 512), (1, 640)])
+        quant([(1, 512)])
         mix(512, 640, ([0, 1, 2],))
+        product(nc.vector, values[1, 0], arms["short"], slice(0, CHUNK))
+        quant([(1, 640)])
+        mix(640, 768, ([0, 1, 2],))
+        product(nc.vector, values[1, 128], arms["short"], slice(CHUNK, RANGE))
+        quant([(0, 0)])
+        quant([(1, 0)])
+        mix(0, CHUNK, ([0, 1, 2],))
         last = [vector_bank()[:, 0:CHUNK] for m in range(3)]
         for m in range(3):
-            mix_pass(last[m], m, 1, 640, 768, True)
-        quant([(0, 640)])
+            mix_pass(last[m], m, 0, CHUNK, RANGE, True)
+        quant([(1, 128)])
         for m in range(3):
-            mix_pass(last[m], m, 0, 640, 768, False)
-            nc.scalar.activation(res[:, m, 640:768], last[m], TANH)
-            (nc.scalar if m == 2 else nc.sync).dma_start(out_view[:, m, 640:768], res[:, m, 640:768])
+            mix_pass(last[m], m, 1, CHUNK, RANGE, False)
+            nc.scalar.activation(res[:, m, CHUNK:RANGE], last[m], TANH)
+            (nc.scalar if m == 2 else nc.sync).dma_start(out_view[:, m, CHUNK:RANGE], res[:, m, CHUNK:RANGE])

@@ -62,7 +62,7 @@ def tile_list_bond_angle_features_kernel(
         w1_cuts = (0, 512, 768, 1024)
         w1_raw = [sb([P, 4, 512], F32, "w1_raw0"), sb([P, 4, 256], F32, "w1_raw1"), placed([P, 4, 256], F32, "w1_raw2", 4 * KIB, 8)]
         w2_raw = sb([P, H // 2], I32, "w2_raw")
-        w3_raw = [sb([P, HALF], I32, f"w3_raw{b}") for b in range(2)]
+        w3_raw = sb([P, H], I32, "w3_raw")[:]
         w4_raw = [sb([P, 4, N], F32, "w4_raw0"), sb([P, 4, N], F32, "w4_raw1")]
         g_rows = sb([P, HALF], F32, "g_rows")
         g_dealt = sb([P, HALF], F32, "g_dealt")
@@ -71,16 +71,17 @@ def tile_list_bond_angle_features_kernel(
         g_zero = sb([P, 8], F32, "g_zero")
         g_safe = sb([P, 8], F32, "g_safe")
         g_inv = sb([P, 8], F32, "g_inv")
-        zeros = sb([P, HALF], F32, "zeros")
+        zeros = sb([P, RANGE], F32, "zeros")
         planes = sb([P, 3, S // 4], I32, "planes")
-        picked = [sb([P, 3, HALF], U8, f"picked{u}") for u in range(2)]
+        picked = sb([P, 3, S], U8, "picked")
 
         for k in range(2):
             nc.gpsimd.memset(ws_raw[k][:], 0)
         nc.vector.memset(zeros[:], 0.0)
         nc.vector.memset(tab_s[0:SCALE_ROWS, :], 0)
         nc.vector.memset(planes[:], 0)
-        nc.scalar.activation(g_rows[0 : P - 2, :], zeros[0 : P - 2, :], TANH)
+        for lo in (0, RANGE):
+            nc.scalar.activation(g_rows[0 : P - 2, lo : lo + RANGE], zeros[0 : P - 2, :], TANH)
         nc.gpsimd.affine_select(
             out=ident[:], in_=zeros[:, 0:P], compare_op=NOT_EQUAL, fill=1.0, base=0, pattern=[[-1, P]], channel_multiplier=1
         )
@@ -92,45 +93,37 @@ def tile_list_bond_angle_features_kernel(
         def load_w1(k):
             nc.sync.dma_start(w1_raw[k][:], w1_rows[:, :, w1_cuts[k] : w1_cuts[k + 1]])
 
-        def load_scale_rows(queue, k, src):
-            for r in range(4):
-                queue.dma_start(ws_raw[k][r:P:32, :], src[0, r:16:4, :].bitcast(I32))
-
-        def pick_scales(l, u):
-            offsets = lists[l][:, u * HALF // 16 : (u + 1) * HALF // 16]
-            nc.vector.tensor_copy(picked[u][:, l, :], tab_s[:].bitcast(U8).indirect(offsets))
-
-        def carry_scales(u):
-            for r in range(4):
-                nc.sync.dma_start(
-                    planes[r:P:32, :, u * HALF // 4 : (u + 1) * HALF // 4], picked[u][SCALE_ROWS + r : P : 4].bitcast(I32)
-                )
+        def load_scale_rows(k, src, rows):
+            for r in rows:
+                nc.sync.dma_start(ws_raw[k][r:P:32, :], src[0, r:16:4, :].bitcast(I32))
 
         nc.sync.dma_start(tab_s[SCALE_ROWS:P, :], tab_scales[0].bitcast(I32))
         for l, src in enumerate((offs, offs2, offs3)):
             nc.sync.dma_start(lists[l][:], src)
         load_w1(0)
-        load_w1(1)
         nc.sync.dma_start(g_rows[P - 2 : P, :], g.rearrange("(b c) -> b c", b=2))
-        load_scale_rows(nc.sync, 0, w2_scales)
-        load_scale_rows(nc.gpsimd, 1, w3_scales)
+        load_scale_rows(0, w2_scales, (0, 1))
         nc.sync.dma_start(tab_w[:], tab_words[0].rearrange("p t i -> p (t i)").bitcast(I32))
-        for l in range(3):
-            pick_scales(l, 0)
-        carry_scales(0)
+        load_scale_rows(0, w2_scales, (2, 3))
+        load_scale_rows(1, w3_scales, (0,))
         nc.sync.dma_start(w2_raw[:], w2_words[0].bitcast(I32))
-        load_w1(2)
+        nc.sync.dma_start(w3_raw, w3_rows)
+        load_w1(1)
         for l in range(3):
-            pick_scales(l, 1)
-        carry_scales(1)
-        for b in range(2):
-            nc.sync.dma_start(w3_raw[b][:], w3_rows[:, b * HALF : (b + 1) * HALF])
+            nc.vector.tensor_copy(picked[:, l, :], tab_s[:].bitcast(U8).indirect(lists[l][:]))
+        for r in range(4):
+            nc.sync.dma_start(
+                planes[r:P:32].rearrange("p l s -> p (l s)"),
+                picked[SCALE_ROWS + r : P : 4].rearrange("p l s -> p (l s)").bitcast(I32),
+            )
+        load_w1(2)
+        load_scale_rows(1, w3_scales, (1, 2, 3))
         for u in range(8):
             nc.sync.dma_start(w4_raw[u // 4][:, u % 4, :], w4_view[u // 4, u % 4])
 
         ws_p = [sb([P, H // 4], I32, f"ws_p{k}") for k in range(2)]
         w2_p = sb([P, H // 2], I32, "w2_p")
-        w3_p = [sb([P, HALF], I32, f"w3_p{b}") for b in range(2)]
+        w3_p = sb([P, H], I32, "w3_p")
 
         def dealt(dst, src, dtype, b, e):
             return (
@@ -173,7 +166,7 @@ def tile_list_bond_angle_features_kernel(
                 return w1_q[b][:, t * P : (t + 1) * P].bitcast(FP8X4), w1_s[b][:, t * P : (t + 1) * P]
             if l == 1:
                 return w2_p[:, u * 64 : (u + 1) * 64].bitcast(U8).bitcast(FP4X4), ws_p[0][:, u * 32 : (u + 1) * 32].bitcast(U8)
-            return w3_p[b][:, t * P : (t + 1) * P].bitcast(FP8X4), ws_p[1][:, u * 32 : (u + 1) * 32].bitcast(U8)
+            return w3_p[:, u * P : (u + 1) * P].bitcast(FP8X4), ws_p[1][:, u * 32 : (u + 1) * 32].bitcast(U8)
 
         def project(dst, l, b, t, lo, hi, start, stop):
             codes, scale = weight(l, b, t)
@@ -210,14 +203,14 @@ def tile_list_bond_angle_features_kernel(
 
         held = 40 * KIB
         groups = [
-            ([(0, 256, 256), (1, 256, 256)], None, held + 832),
-            ([(0, 768, 128), (0, 896, 128), (1, 768, 128), (1, 896, 128)], None, held + 1344),
-            ([(0, 512, 128), (0, 640, 128)], None, held + 1856),
-            ([(1, 512, 128)], None, held + 2112),
-            ([(1, 640, 128)], held - 960, None),
-            ([(0, 0, 256)], None, held + 2240),
-            ([(1, 0, 128)], held + 4032, None),
-            ([(1, 128, 128)], held + 2560, None),
+            ([(0, 768, 128), (0, 896, 128), (1, 768, 128), (1, 896, 128)], None, held + 832),
+            ([(0, 0, 256)], None, held + 1344),
+            ([(1, 0, 128)], None, held + 1600),
+            ([(0, 512, 256), (1, 512, 128), (1, 640, 128)], None, None),
+            ([(1, 128, 128)], held - 960, None),
+            ([(0, 256, 256)], None, held + 1856),
+            ([(1, 256, 128)], held + 4032, None),
+            ([(1, 384, 128)], held + 2560, None),
         ]
         values, quantised, group_of = {}, {}, {}
         for n, (pieces, values_at, scales_at) in enumerate(groups):
@@ -263,9 +256,9 @@ def tile_list_bond_angle_features_kernel(
             cols = slice(b * N, (b + 1) * N)
             nc.vector.quantize_mx(w4_q[:, cols].bitcast(FP8X4), w4_s[:, cols], w4_bf[b][:].rearrange("p n t -> p (n t)"))
 
-        def quant(pieces):
+        def quant(pieces, cols=slice(None)):
             h_q, h_s, h_bf = group_of[pieces[0]]
-            nc.vector.quantize_mx(h_q[:].bitcast(FP8X4), h_s[:], h_bf[:].rearrange("p n t -> p (n t)"))
+            nc.vector.quantize_mx(h_q[:, cols].bitcast(FP8X4), h_s[:, cols], h_bf[:, cols].rearrange("p n t -> p (n t)"))
 
         res = sb([P, 3, S], F32, "res")
         out_view = out.rearrange("(m p) s -> p m s", p=P)
@@ -304,139 +297,125 @@ def tile_list_bond_angle_features_kernel(
         nc.gpsimd.tensor_scalar(g_zero[:], g_col[:], 0.0, 0.0, IS_EQUAL, ADD)
         nc.gpsimd.tensor_tensor(g_safe[:], g_zero[:], g_col[:], ADD)
         nc.vector.reciprocal(g_inv[:], g_safe[:])
-        cast_w1(1, "scalar")
         nc.scalar.copy(*dealt(ws_p[0], ws_raw[0], U32, 2, 1))
-        nc.scalar.copy(*dealt(ws_p[1], ws_raw[1], U32, 2, 1))
         nc.scalar.copy(*dealt(w2_p, w2_raw, U32, 2, 2))
+        nc.gpsimd.tensor_copy(*dealt(w3_p, w3_raw, U32, 2, 4))
+        cast_w1(1, "scalar")
         cast_w1(2, "gpsimd", (3,))
-        pick_words(0, 0, RANGE)
-        pick_words(1, 0, RANGE)
-        pick_words(0, RANGE, S)
+        for lo in (HALF, 0):
+            for l in range(2):
+                pick_words(l, lo, lo + HALF)
 
-        spans = {"summed0": (0, 0, 256), "summed1": (0, 256, 512), "long": (1, 256, 768), "short": (1, 0, 256)}
-        centre_pairs = {
-            "summed0": [sb([P, 2, RANGE], F32, "centre_first")[:], placed([P, 2, RANGE], F32, "centre_second", 12 * KIB)],
-            "summed1": [placed([P, 2, RANGE], F32, f"centre_summed1_{e}", (14 + 2 * e) * KIB) for e in range(2)],
+        spans = {"summed": (0, 512, 768), "near": (0, 0, 512), "far": (1, 0, 512)}
+        centre_pairs = [placed([P, 2, RANGE], F32, f"centre_summed{e}", at * KIB) for e, at in enumerate((24, 8))]
+        neighbour_pairs = [placed([P, 2, RANGE], F32, f"neighbour_summed{e}", at * KIB) for e, at in enumerate((26, 10))]
+        centre = {
+            "summed": by_tile(centre_pairs[0]) + by_tile(centre_pairs[1]),
+            "near": by_tile(placed([P, 4, HALF], F32, "centre_near", 12 * KIB)),
+            "far": by_tile(sb([P, 4, HALF], F32, "centre_far")[:]),
         }
-        neighbour_pairs = {
-            key: [placed([P, 2, RANGE], F32, f"neighbour_{key}_{e}", (at + 2 * e) * KIB) for e in range(2)]
-            for key, at in (("summed0", 26), ("summed1", 30))
+        neighbour = {
+            "summed": by_tile(neighbour_pairs[0]) + by_tile(neighbour_pairs[1]),
+            "near": by_tile(placed([P, 1, HALF], F32, "neighbour_near", 20 * KIB)),
         }
-        centre = {key: by_tile(tiles[0]) + by_tile(tiles[1]) for key, tiles in centre_pairs.items()}
-        centre["long"] = by_tile(placed([P, 4, HALF], F32, "centre_long", 18 * KIB))
-        centre["short"] = by_tile(sb([P, 4, RANGE], F32, "centre_short")[:])
-        neighbour = {key: by_tile(tiles[0]) + by_tile(tiles[1]) for key, tiles in neighbour_pairs.items()}
         arms = {key: [sb([P, 4, hi - lo], F32, f"arm{l}_{key}") for l in range(2)] for key, (b, lo, hi) in spans.items()}
-        arms["summed0"][0] = placed([P, 4, RANGE], F32, "arm_first", 0)
 
         def read(dst, l, key, ts, bank=None):
             b, lo, hi = spans[key]
-            bank = scalar_bank() if bank is None else bank
-            read_scaled(dst[key], fill(bank, [l], b, ts, lo, hi), b, ts)
-            return bank
+            read_scaled(dst[key], fill(scalar_bank() if bank is None else bank, [l], b, ts, lo, hi), b, ts)
 
         def cast_quarter(n):
             cast_w4(n // 2, n % 2 * N // 2, (n % 2 + 1) * N // 2)
-
-        def add_first(key, ts):
-            e = ts[0] // 2
-            nc.gpsimd.tensor_tensor(arms[key][0][:, ts[0] : ts[1] + 1, :], centre_pairs[key][e], neighbour_pairs[key][e], ADD)
 
         def fill_for_vector(l, key, ts):
             b, lo, hi = spans[key]
             return fill(vector_bank(), [l], b, ts, lo, hi)
 
-        read(centre, 0, "summed0", pairs[0])
+        arms["summed"][0] = placed([P, 4, RANGE], F32, "arm_first", 0)
+
+        def read_pair(e, at):
+            read(centre, 0, "summed", pairs[e], banks[at])
+            read(neighbour, 1, "summed", pairs[e], banks[at + 1])
+
+        def sum_pair(e):
+            nc.gpsimd.tensor_tensor(arms["summed"][0][:, 2 * e : 2 * e + 2, :], centre_pairs[e], neighbour_pairs[e], ADD)
+
         cast_w1(2, "scalar", (0, 1, 2))
+        nc.gpsimd.tensor_copy(*dealt(ws_p[1], ws_raw[1], U32, 2, 1))
         quant_w1(1)
-        pick_words(1, RANGE, S, placed([P, S - RANGE], U32, "v_late1", 4 * KIB)[:])
-        pick_words(2, 0, S, placed([P, S], U32, "v_late2", 8 * KIB)[:])
-        read(neighbour, 1, "summed0", pairs[0])
-        add_first("summed0", pairs[0])
-        read(centre, 0, "summed0", pairs[1])
-        bank = read(centre, 0, "long", [0])
-        waiting = fill(banks[3], [0], 1, [1], *spans["long"][1:])
-        nc.scalar.copy(*dealt(w3_p[0], w3_raw[0], U32, 1, 4))
-        late_first = fill(banks[2], [0], 0, pairs[0], *spans["summed1"][1:])
-        read(neighbour, 1, "summed0", pairs[1], bank)
-        add_first("summed0", pairs[1])
-        read_scaled(centre["summed1"], late_first, 0, pairs[0])
-        read(neighbour, 1, "summed1", pairs[0])
-        add_first("summed1", pairs[0])
-        first = [fill_for_vector(1, "long", [t]) for t in range(2)]
-        read_scaled(centre["long"], waiting, 1, [1])
-        read(centre, 0, "summed1", pairs[1])
-        read(neighbour, 1, "summed1", pairs[1])
-        add_first("summed1", pairs[1])
-        read(centre, 0, "long", [2])
-        nc.scalar.copy(*dealt(w3_p[1], w3_raw[1], U32, 1, 4))
+        for n, lo in enumerate((HALF, 0)):
+            pick_words(2, lo, lo + HALF, placed([P, HALF], U32, f"v_late{n}", (4 + 2 * n) * KIB))
+        read_pair(0, 0)
+        sum_pair(0)
+        read_pair(1, 2)
+        sum_pair(1)
+        read(centre, 0, "near", [0])
+        read(neighbour, 1, "near", [0])
+        nc.gpsimd.tensor_tensor(arms["near"][0][:, 0, :], centre["near"][0], neighbour["near"][0], ADD)
+        read(centre, 0, "near", [1])
 
-        doubled = [(0, 512), (0, 768), (1, 768), (1, 896), (0, 896), (0, 640)]
-        sides = {key: sb([P, 4, RANGE], F32, f"side{key[0]}_{key[1]}") for key in ((0, 512), (0, 768))}
+        doubled = [(0, 768), (1, 768), (1, 896), (0, 896), (1, 512), (1, 640)]
+        sides = {key: sb([P, 4, RANGE], F32, f"side{key[0]}_{key[1]}") for key in ((1, 512), (0, 768))}
         sides[1, 768] = placed([P, 4, RANGE], F32, "side_last", held)
-
-        def read_side(key):
-            for ts in pairs:
-                first_arm(sides[key], scalar_bank(), key[0], ts, key[1])
 
         def finish_doubled(b, lo, bank):
             view = fill(bank, [0, 2], b, range(4), lo, lo + CHUNK)
             side = sides[b, lo - lo % RANGE][:, :, lo % RANGE : lo % RANGE + CHUNK]
             return lambda: nc.vector.tensor_tensor(h_view(values[b, lo]), woven(view), woven(side), MULT)
 
-        for t in range(2):
-            first_arm_plain(arms["long"][0], centre["long"], first[t], 1, [t])
-        for n, key in enumerate(("summed0", "summed1")):
-            for ts in pairs:
-                second_arm(arms[key][1], centre[key], fill_for_vector(2, key, ts), 0, ts)
-            product(nc.gpsimd, values[spans[key][:2]], arms[key])
-            if n == 0:
-                read(centre, 0, "long", [3])
         for ts in pairs:
-            read(centre, 0, "short", ts)
-        cast_quarter(0)
-        for t in range(4):
-            second_arm(arms["long"][1], centre["long"], fill_for_vector(2, "long", [t]), 1, [t])
-            if t >= 2:
-                first_arm_plain(arms["long"][0], centre["long"], fill_for_vector(1, "long", [t]), 1, [t])
-            if t % 2:
-                read_side(doubled[t // 2])
-                cast_quarter(1 + t // 2)
-        product(nc.gpsimd, values[1, 256], arms["long"], slice(0, RANGE))
-        product(nc.gpsimd, values[1, 512], arms["long"], slice(RANGE, RANGE + CHUNK))
-        for n, ts in enumerate(pairs):
-            second_arm(arms["short"][1], centre["short"], fill_for_vector(2, "short", ts), 1, ts)
-            first_arm_plain(arms["short"][0], centre["short"], fill_for_vector(1, "short", ts), 1, ts)
-        read_side((1, 768))
-        cast_quarter(3)
-        for b, lo in doubled[:5]:
-            bank = vector_bank()
-            finish_doubled(b, lo, bank)()
-        last_doubled = finish_doubled(*doubled[5], bank)
+            second_arm(arms["summed"][1], centre["summed"], fill_for_vector(2, "summed", ts), 0, ts)
+        product(nc.gpsimd, values[0, 512], arms["summed"])
+        order = [("near", t) for t in range(4)] + [("far", t) for t in range(4)]
+        side_steps = [3, 4, 5, 6]
+        for n, (key, t) in enumerate(order):
+            b = spans[key][0]
+            second_arm(arms[key][1], centre[key], fill_for_vector(2, key, [t]), b, [t])
+            if n >= 1:
+                first_arm_plain(arms[key][0], centre[key], fill_for_vector(1, key, [t]), b, [t])
+            if n + 2 < len(order):
+                read(centre, 0, order[n + 2][0], [order[n + 2][1]])
+            if n in side_steps:
+                b, e = divmod(side_steps.index(n), 2)
+                first_arm(sides[b, 768], scalar_bank(), b, pairs[e], 768)
+            if n >= 4:
+                cast_quarter(n - 4)
+            if n == 3:
+                for lo, hi in ((0, 256), (256, 512)):
+                    product(nc.gpsimd, values[0, lo], arms["near"], slice(lo, hi))
+        product(nc.gpsimd, values[1, 0], arms["far"], slice(0, CHUNK))
+        spent = [vector_bank() for n in range(4)]
+        for n in range(4):
+            finish_doubled(*doubled[n], spent[n])()
+        for ts in pairs:
+            first_arm(sides[1, 512], scalar_bank(), 1, ts, 512)
 
         quant_w4(0)
-        quant_w4(1)
-        quant([(0, 256)])
-        mix(256, 512, ([0, 1], [2]))
-        last_doubled()
+        late = [finish_doubled(*doubled[4 + n], spent[2 + n]) for n in range(2)]
         quant([(0, 768)])
+        quant_w4(1)
         mix(768, S, ([0, 1], [2]))
-        product(nc.vector, values[1, 640], arms["long"], slice(RANGE + CHUNK, HALF))
-        quant([(0, 512)])
-        quant([(1, 512)])
-        mix(512, 640, ([0, 1, 2],))
-        product(nc.vector, values[1, 0], arms["short"], slice(0, CHUNK))
-        quant([(1, 640)])
-        mix(640, 768, ([0, 1, 2],))
-        product(nc.vector, values[1, 128], arms["short"], slice(CHUNK, RANGE))
+        late[0]()
         quant([(0, 0)])
+        late[1]()
         quant([(1, 0)])
         mix(0, CHUNK, ([0, 1, 2],))
+        quant([(0, 512)])
+        mix(512, 768, ([0, 1], [2]))
+        product(nc.vector, values[1, 128], arms["far"], slice(128, 256))
+        product(nc.vector, values[1, 256], arms["far"], slice(256, 384))
+        quant([(1, 128)])
+        mix(128, 256, ([0, 1, 2],))
+        quant([(0, 256)], slice(0, CHUNK))
+        quant([(1, 256)])
+        mix(256, 384, ([0, 1, 2],))
+        product(nc.vector, values[1, 384], arms["far"], slice(384, 512))
+        quant([(0, 256)], slice(CHUNK, RANGE))
         last = [vector_bank()[:, 0:CHUNK] for m in range(3)]
         for m in range(3):
-            mix_pass(last[m], m, 0, CHUNK, RANGE, True)
-        quant([(1, 128)])
+            mix_pass(last[m], m, 0, 384, HALF, True)
+        quant([(1, 384)])
         for m in range(3):
-            mix_pass(last[m], m, 1, CHUNK, RANGE, False)
-            nc.scalar.activation(res[:, m, CHUNK:RANGE], last[m], TANH)
-            (nc.scalar if m == 2 else nc.sync).dma_start(out_view[:, m, CHUNK:RANGE], res[:, m, CHUNK:RANGE])
+            mix_pass(last[m], m, 1, 384, HALF, False)
+            nc.scalar.activation(res[:, m, 384:HALF], last[m], TANH)
+            (nc.scalar if m == 2 else nc.sync).dma_start(out_view[:, m, 384:HALF], res[:, m, 384:HALF])

@@ -299,7 +299,7 @@ def tile_list_bond_angle_features_kernel(
         nc.vector.reciprocal(g_inv[:], g_safe[:])
         nc.scalar.copy(*dealt(ws_p[0], ws_raw[0], U32, 2, 1))
         nc.scalar.copy(*dealt(w2_p, w2_raw, U32, 2, 2))
-        nc.gpsimd.tensor_copy(*dealt(w3_p, w3_raw, U32, 2, 4))
+        nc.scalar.copy(*dealt(w3_p, w3_raw, U32, 2, 4))
         cast_w1(1, "scalar")
         cast_w1(2, "gpsimd", (3,))
         for lo in (HALF, 0):
@@ -341,12 +341,12 @@ def tile_list_bond_angle_features_kernel(
             nc.gpsimd.tensor_tensor(arms["summed"][0][:, 2 * e : 2 * e + 2, :], centre_pairs[e], neighbour_pairs[e], ADD)
 
         cast_w1(2, "scalar", (0, 1, 2))
-        nc.gpsimd.tensor_copy(*dealt(ws_p[1], ws_raw[1], U32, 2, 1))
         quant_w1(1)
         for n, lo in enumerate((HALF, 0)):
             pick_words(2, lo, lo + HALF, placed([P, HALF], U32, f"v_late{n}", (4 + 2 * n) * KIB))
         read_pair(0, 0)
         sum_pair(0)
+        nc.scalar.copy(*dealt(ws_p[1], ws_raw[1], U32, 2, 1))
         read_pair(1, 2)
         sum_pair(1)
         read(centre, 0, "near", [0])

@@ -25,8 +25,11 @@ P = 128
 CHUNK = 128
 RANGE = 256
 HALF = 512
+RUN = 4
 SCALE_ROWS = P - 16
 KIB = 1024
+CENTRE, FIRST, SECOND = 0, 1, 2
+PAIRS = ([0, 1], [2, 3])
 
 
 def tile_list_bond_angle_features_kernel(
@@ -37,7 +40,7 @@ def tile_list_bond_angle_features_kernel(
         keep = ctx.enter_context(tc.tile_pool(name="keep", bufs=1))
         shared = ctx.enter_context(tc.tile_pool(name="shared", bufs=1))
         psum = ctx.enter_context(tc.psum_pool(name="psum", bufs=1))
-        banks = [psum.tile([P, 512], F32, name=f"bank{k}") for k in range(8)]
+        banks = [psum.tile([P, HALF], F32, name=f"bank{k}") for k in range(8)]
         turns = {"scalar": [], "vector": []}
 
         def scalar_bank():
@@ -48,22 +51,26 @@ def tile_list_bond_angle_features_kernel(
             turns["vector"].append(0)
             return banks[(len(turns["vector"]) - 1) % 4]
 
-        def sb(shape, dtype, name, tag=None):
-            return keep.tile(shape, dtype, align_bytes=64, name=name, tag=tag or name)
+        def sb(shape, dtype, name):
+            return keep.tile(shape, dtype, align_bytes=64, name=name, tag=name)
 
-        def placed(shape, dtype, name, at, wider=1):
-            tile = shared.tile([shape[0], wider] + shape[1:], dtype, align_bytes=64, name=name, offset=at)
-            return tile[:, 0]
+        def placed(shape, dtype, name, at):
+            return shared.tile(shape, dtype, align_bytes=64, name=name, offset=at)
+
+        at_w1_raw = 0
+        at_w1_second = 22 * KIB
+        at_side = {0: 26 * KIB, 1: 30 * KIB}
 
         lists = [keep.tile([P, S // 16], U16, name=f"list{l}") for l in range(3)]
         tab_s = sb([P, T // 4], I32, "tab_s")
         tab_w = sb([P, T], I32, "tab_w")
         ws_raw = [sb([P, H // 4], I32, f"ws_raw{k}") for k in range(2)]
         w1_cuts = (0, 512, 768, 1024)
-        w1_raw = [sb([P, 4, 512], F32, "w1_raw0"), sb([P, 4, 256], F32, "w1_raw1"), placed([P, 4, 256], F32, "w1_raw2", 4 * KIB, 8)]
+        w1_tile = placed([P, 4 * H], F32, "w1_raw", at_w1_raw)
+        w1_raw = [w1_tile[:, 4 * w1_cuts[k] : 4 * w1_cuts[k + 1]].rearrange("p (j c) -> p j c", j=4) for k in range(3)]
         w2_raw = sb([P, H // 2], I32, "w2_raw")
-        w3_raw = sb([P, H], I32, "w3_raw")[:]
-        w4_raw = [sb([P, 4, N], F32, "w4_raw0"), sb([P, 4, N], F32, "w4_raw1")]
+        w3_raw = sb([P, H], I32, "w3_raw")
+        w4_raw = [sb([P, 4, N], F32, f"w4_raw{b}") for b in range(2)]
         g_rows = sb([P, HALF], F32, "g_rows")
         g_dealt = sb([P, HALF], F32, "g_dealt")
         ident = sb([P, P], F32, "ident")
@@ -87,11 +94,10 @@ def tile_list_bond_angle_features_kernel(
         )
 
         w1_rows = w1.rearrange("(p j) c -> p j c", j=4)
-        w3_rows = w3_words[0].rearrange("p e i -> p (e i)").bitcast(I32)
-        w4_view = w4.rearrange("(b q t i) n -> b t q i n", b=2, t=4, i=4)
+        w4_view = w4.rearrange("(b u t i) n -> b t u i n", b=2, t=4, i=RUN)
 
         def load_w1(k):
-            nc.sync.dma_start(w1_raw[k][:], w1_rows[:, :, w1_cuts[k] : w1_cuts[k + 1]])
+            nc.sync.dma_start(w1_raw[k], w1_rows[:, :, w1_cuts[k] : w1_cuts[k + 1]])
 
         def load_scale_rows(k, src, rows):
             for r in rows:
@@ -107,7 +113,7 @@ def tile_list_bond_angle_features_kernel(
         load_scale_rows(0, w2_scales, (2, 3))
         load_scale_rows(1, w3_scales, (0,))
         nc.sync.dma_start(w2_raw[:], w2_words[0].bitcast(I32))
-        nc.sync.dma_start(w3_raw, w3_rows)
+        nc.sync.dma_start(w3_raw[:], w3_words[0].rearrange("p e i -> p (e i)").bitcast(I32))
         load_w1(1)
         for l in range(3):
             nc.vector.tensor_copy(picked[:, l, :], tab_s[:].bitcast(U8).indirect(lists[l][:]))
@@ -118,99 +124,98 @@ def tile_list_bond_angle_features_kernel(
             )
         load_w1(2)
         load_scale_rows(1, w3_scales, (1, 2, 3))
-        for u in range(8):
-            nc.sync.dma_start(w4_raw[u // 4][:, u % 4, :], w4_view[u // 4, u % 4])
+        for b in range(2):
+            for t in range(4):
+                nc.sync.dma_start(w4_raw[b][:, t, :], w4_view[b, t])
 
         ws_p = [sb([P, H // 4], I32, f"ws_p{k}") for k in range(2)]
         w2_p = sb([P, H // 2], I32, "w2_p")
         w3_p = sb([P, H], I32, "w3_p")
 
-        def dealt(dst, src, dtype, b, e):
-            return (
-                dst[:].bitcast(dtype).rearrange("p (b t q e) -> p b t q e", b=b, t=4, e=e),
-                src[:].bitcast(dtype).rearrange("p (b q t e) -> p b t q e", b=b, t=4, e=e),
+        def deal(dst, src, dtype, b, e):
+            nc.scalar.copy(
+                dst[:].bitcast(dtype).rearrange("p (b t u e) -> p b t u e", b=b, t=4, e=e),
+                src[:].bitcast(dtype).rearrange("p (b u t e) -> p b t u e", b=b, t=4, e=e),
             )
 
-        w1_bf = [sb([P, 4, 32, 4, 4], BF16, "w1_bf0"), placed([P, 4, 32, 4, 4], BF16, "w1_bf1", 0)]
+        w1_bf = [sb([P, 4, 32, RUN, 4], BF16, "w1_bf0"), placed([P, 4, 32, RUN, 4], BF16, "w1_bf1", at_w1_second)]
         w1_q = [sb([P, HALF], U32, f"w1_q{b}") for b in range(2)]
         w1_s = [sb([P, HALF], U8, f"w1_s{b}") for b in range(2)]
 
-        def cast_w1(k, engine, ts=range(4)):
+        def round_w1(k, engine, ts):
             b, lo = divmod(w1_cuts[k], HALF)
-            qs = slice(lo // 16, (lo + w1_cuts[k + 1] - w1_cuts[k]) // 16)
-            src = w1_raw[k][:].rearrange("p j (q t i) -> p t q j i", t=4, i=4)
+            us = slice(lo // 16, (lo + w1_cuts[k + 1] - w1_cuts[k]) // 16)
+            src = w1_raw[k].rearrange("p j (u t i) -> p t u j i", t=4, i=RUN)
             for t in ts:
-                dst = w1_bf[b][:, t, qs].rearrange("p q i j -> p q j i")
+                dst = w1_bf[b][:, t, us].rearrange("p u i j -> p u j i")
                 if engine == "scalar":
                     nc.scalar.activation(dst, src[:, t], COPY, scale=-1.0)
                 else:
-                    nothing = zeros[:, 0:RANGE].rearrange("p (q j i) -> p q j i", j=4, i=4)
-                    nc.gpsimd.tensor_tensor(dst, nothing, src[:, t], SUBTRACT)
+                    nc.gpsimd.tensor_tensor(dst, zeros[:].rearrange("p (u j i) -> p u j i", j=4, i=RUN), src[:, t], SUBTRACT)
 
-        def quant_w1(b):
+        def quantise_w1(b):
             nc.vector.quantize_mx(
-                w1_q[b][:].bitcast(FP8X4), w1_s[b][:], w1_bf[b][:].rearrange("p t q i j -> p (t q i j)")
+                w1_q[b][:].bitcast(FP8X4), w1_s[b][:], w1_bf[b][:].rearrange("p t u i j -> p (t u i j)")
             )
 
         v_words = {}
 
-        def pick_words(l, lo, hi, tile=None):
-            tile = sb([P, hi - lo], U32, f"v_words{l}_{lo}")[:] if tile is None else tile
-            for c in range(lo, hi, CHUNK):
-                v_words[l, c] = (tile, lo)
-            nc.vector.tensor_copy(tile, tab_w[:].bitcast(U32).indirect(lists[l][:, lo // 16 : hi // 16]))
+        def gather_words(l, lo, tile):
+            v_words[l, lo] = tile
+            nc.vector.tensor_copy(tile[:], tab_w[:].bitcast(U32).indirect(lists[l][:, lo // 16 : (lo + HALF) // 16]))
 
         def weight(l, b, t):
-            u = 4 * b + t
-            if l == 0:
+            c = 4 * b + t
+            if l == CENTRE:
                 return w1_q[b][:, t * P : (t + 1) * P].bitcast(FP8X4), w1_s[b][:, t * P : (t + 1) * P]
-            if l == 1:
-                return w2_p[:, u * 64 : (u + 1) * 64].bitcast(U8).bitcast(FP4X4), ws_p[0][:, u * 32 : (u + 1) * 32].bitcast(U8)
-            return w3_p[:, u * P : (u + 1) * P].bitcast(FP8X4), ws_p[1][:, u * 32 : (u + 1) * 32].bitcast(U8)
-
-        def project(dst, l, b, t, lo, hi, start, stop):
-            codes, scale = weight(l, b, t)
-            tile, at = v_words[l, lo]
-            nc.tensor.matmul_mx(
-                dst,
-                lhsT=codes,
-                lhsT_scale=scale,
-                rhs=tile[:, lo - at : hi - at].bitcast(FP8X4),
-                rhs_scale=planes[:, l, :].bitcast(U8)[:, lo:hi],
-                start=start,
-                stop=stop,
-            )
+            scale = ws_p[l - 1][:, c * 32 : (c + 1) * 32].bitcast(U8)
+            if l == FIRST:
+                return w2_p[:, c * 64 : (c + 1) * 64].bitcast(U8).bitcast(FP4X4), scale
+            return w3_p[:, c * P : (c + 1) * P].bitcast(FP8X4), scale
 
         def fill(bank, ls, b, ts, lo, hi):
             view = bank[:].rearrange("p (e n) -> p e n", e=len(ts))
             passes = [(e, t, l) for l in ls for e, t in enumerate(ts)]
+            at = lo - lo % HALF
             for n, (e, t, l) in enumerate(passes):
-                project(view[:, e, :], l, b, t, lo, hi, n == 0, n == len(passes) - 1)
+                codes, scale = weight(l, b, t)
+                nc.tensor.matmul_mx(
+                    view[:, e, :],
+                    lhsT=codes,
+                    lhsT_scale=scale,
+                    rhs=v_words[l, at][:, lo - at : hi - at].bitcast(FP8X4),
+                    rhs_scale=planes[:, l, :].bitcast(U8)[:, lo:hi],
+                    start=n == 0,
+                    stop=n == len(passes) - 1,
+                )
             return view
 
         def gain(col, b, t):
             return col[:, 4 * b + t : 4 * b + t + 1]
 
+        def by_tile(tile):
+            return [tile[:, t, :] for t in range(tile.shape[1])]
+
         def read_scaled(dst, view, b, ts):
             for e, t in enumerate(ts):
                 nc.scalar.activation(dst[t], view[:, e, :], COPY, scale=gain(g_col, b, t))
 
-        def woven(ap):
-            return ap.rearrange("p t (c i) -> p c t i", i=4)
+        def by_runs(ap):
+            return ap.rearrange("p t (c i) -> p c t i", i=RUN)
 
-        def h_view(ap):
-            return ap.rearrange("p (c i) t -> p c t i", i=4)
+        def interleaved(ap):
+            return ap.rearrange("p (c i) t -> p c t i", i=RUN)
 
-        held = 40 * KIB
+        at_scales = at_side[1] + 2 * N
         groups = [
-            ([(0, 768, 128), (0, 896, 128), (1, 768, 128), (1, 896, 128)], None, held + 832),
-            ([(0, 0, 256)], None, held + 1344),
-            ([(1, 0, 128)], None, held + 1600),
+            ([(0, 768, 128), (0, 896, 128), (1, 768, 128), (1, 896, 128)], None, at_scales),
+            ([(0, 0, 256)], None, at_scales + 512),
+            ([(1, 0, 128)], None, at_scales + 768),
             ([(0, 512, 256), (1, 512, 128), (1, 640, 128)], None, None),
-            ([(1, 128, 128)], held - 960, None),
-            ([(0, 256, 256)], None, held + 1856),
-            ([(1, 256, 128)], held + 4032, None),
-            ([(1, 384, 128)], held + 2560, None),
+            ([(1, 128, 128)], at_side[0], None),
+            ([(0, 256, 256)], None, at_scales + 896),
+            ([(1, 256, 128)], at_side[0] + KIB, None),
+            ([(1, 384, 128)], at_side[0] + 2 * KIB, None),
         ]
         values, quantised, group_of = {}, {}, {}
         for n, (pieces, values_at, scales_at) in enumerate(groups):
@@ -226,44 +231,29 @@ def tile_list_bond_angle_features_kernel(
                     quantised[b, lo + c] = (h_q, h_s, at + c)
                 at += w
 
-        pairs = ([0, 1], [2, 3])
-
-        def first_arm(dst, bank, b, ts, lo):
-            read_scaled([dst[:, t, :] for t in range(4)], fill(bank, [0, 1], b, ts, lo, lo + RANGE), b, ts)
-
-        def by_tile(tile):
-            return [tile[:, t, :] for t in range(tile.shape[1])]
-
-        def second_arm(dst, x, view, b, ts):
-            for n, t in enumerate(ts):
-                nc.vector.scalar_tensor_tensor(dst[:, t, :], x[t], gain(g_inv, b, t), view[:, n, :], MULT, ADD)
-
-        def first_arm_plain(dst, x, view, b, ts):
-            for n, t in enumerate(ts):
-                nc.vector.scalar_tensor_tensor(dst[:, t, :], view[:, n, :], gain(g_col, b, t), x[t], MULT, ADD)
-
-        def product(engine, dst, arm, cols=slice(None)):
-            engine.tensor_tensor(h_view(dst), woven(arm[0][:, :, cols]), woven(arm[1][:, :, cols]), MULT)
+        def multiply(engine, dst, arm, cols=slice(None)):
+            engine.tensor_tensor(interleaved(dst), by_runs(arm[0][:, :, cols]), by_runs(arm[1][:, :, cols]), MULT)
 
         w4_bf = [sb([P, N, 4], BF16, f"w4_bf{b}") for b in range(2)]
         w4_q = sb([P, 2 * N], U32, "w4_q")
-        w4_s = placed([P, 2 * N], U8, "w4_s", held + 64)
+        w4_s = placed([P, 2 * N], U8, "w4_s", at_side[1])
 
-        def cast_w4(b, lo, hi):
-            nc.scalar.activation(h_view(w4_bf[b][:, lo:hi]), woven(w4_raw[b][:, :, lo:hi]), COPY)
+        def round_w4(quarter):
+            b, cols = quarter // 2, slice(quarter % 2 * N // 2, (quarter % 2 + 1) * N // 2)
+            nc.scalar.activation(interleaved(w4_bf[b][:, cols]), by_runs(w4_raw[b][:, :, cols]), COPY)
 
-        def quant_w4(b):
+        def quantise_w4(b):
             cols = slice(b * N, (b + 1) * N)
             nc.vector.quantize_mx(w4_q[:, cols].bitcast(FP8X4), w4_s[:, cols], w4_bf[b][:].rearrange("p n t -> p (n t)"))
 
-        def quant(pieces, cols=slice(None)):
-            h_q, h_s, h_bf = group_of[pieces[0]]
+        def quantise_h(b, lo, cols=slice(None)):
+            h_q, h_s, h_bf = group_of[b, lo]
             nc.vector.quantize_mx(h_q[:, cols].bitcast(FP8X4), h_s[:, cols], h_bf[:, cols].rearrange("p n t -> p (n t)"))
 
         res = sb([P, 3, S], F32, "res")
         out_view = out.rearrange("(m p) s -> p m s", p=P)
 
-        def mix_pass(dst, m, b, lo, hi, start):
+        def mix_pass(dst, m, b, lo, hi):
             cols = slice(b * N + m * P, b * N + (m + 1) * P)
             h_q, h_s, at = quantised[b, lo]
             nc.tensor.matmul_mx(
@@ -272,22 +262,22 @@ def tile_list_bond_angle_features_kernel(
                 lhsT_scale=w4_s[:, cols],
                 rhs=h_q[:, at : at + hi - lo].bitcast(FP8X4),
                 rhs_scale=h_s[:, at : at + hi - lo],
-                start=start,
-                stop=not start,
+                start=b == 0,
+                stop=b == 1,
             )
 
-        def mix(lo, hi, groups, at=None):
-            for n, ms in enumerate(groups):
-                bank = (banks[at + n] if at is not None else scalar_bank())[:, 0 : len(ms) * (hi - lo)].rearrange("p (m s) -> p m s", m=len(ms))
+        def mix(lo, hi):
+            for ms in ([0, 1, 2],) if hi - lo == CHUNK else ([0, 1], [2]):
+                bank = scalar_bank()[:, 0 : len(ms) * (hi - lo)].rearrange("p (m s) -> p m s", m=len(ms))
                 for e, m in enumerate(ms):
                     for b in range(2):
-                        mix_pass(bank[:, e, :], m, b, lo, hi, b == 0)
+                        mix_pass(bank[:, e, :], m, b, lo, hi)
                 nc.scalar.activation(res[:, ms[0] : ms[-1] + 1, lo:hi], bank, TANH)
                 nc.sync.dma_start(out_view[:, ms[0] : ms[-1] + 1, lo:hi], res[:, ms[0] : ms[-1] + 1, lo:hi])
 
-        cast_w1(0, "scalar")
-        quant_w1(0)
-        nc.scalar.copy(*dealt(g_dealt, g_rows, F32, 1, 4))
+        round_w1(0, "scalar", range(4))
+        quantise_w1(0)
+        deal(g_dealt, g_rows, F32, 1, RUN)
         g_bank = banks[7]
         for t in range(4):
             nc.tensor.transpose(g_bank[:, t * P : (t + 1) * P], g_dealt[:, t * P : (t + 1) * P], ident[:])
@@ -297,125 +287,130 @@ def tile_list_bond_angle_features_kernel(
         nc.gpsimd.tensor_scalar(g_zero[:], g_col[:], 0.0, 0.0, IS_EQUAL, ADD)
         nc.gpsimd.tensor_tensor(g_safe[:], g_zero[:], g_col[:], ADD)
         nc.vector.reciprocal(g_inv[:], g_safe[:])
-        nc.scalar.copy(*dealt(ws_p[0], ws_raw[0], U32, 2, 1))
-        nc.scalar.copy(*dealt(w2_p, w2_raw, U32, 2, 2))
-        nc.scalar.copy(*dealt(w3_p, w3_raw, U32, 2, 4))
-        cast_w1(1, "scalar")
-        cast_w1(2, "gpsimd", (3,))
+        deal(ws_p[0], ws_raw[0], U32, 2, 1)
+        deal(w2_p, w2_raw, U32, 2, 2)
+        deal(w3_p, w3_raw, U32, 2, 4)
+        round_w1(1, "scalar", range(4))
+        round_w1(2, "gpsimd", (3,))
         for lo in (HALF, 0):
-            for l in range(2):
-                pick_words(l, lo, lo + HALF)
+            for l in (CENTRE, FIRST):
+                gather_words(l, lo, sb([P, HALF], U32, f"v_words{l}_{lo}"))
 
-        spans = {"summed": (0, 512, 768), "near": (0, 0, 512), "far": (1, 0, 512)}
-        centre_pairs = [placed([P, 2, RANGE], F32, f"centre_summed{e}", at * KIB) for e, at in enumerate((24, 8))]
-        neighbour_pairs = [placed([P, 2, RANGE], F32, f"neighbour_summed{e}", at * KIB) for e, at in enumerate((26, 10))]
+        spans = {"short": (0, 512, 768), "near": (0, 0, 512), "far": (1, 0, 512)}
+        v_late = [placed([P, HALF], U32, f"v_late{n}", at_w1_raw + 2 * n * KIB) for n in range(2)]
+        centre_pairs = [placed([P, 2, RANGE], F32, f"centre_short{e}", at_w1_raw + (4 + 2 * e) * KIB) for e in range(2)]
+        neighbour_pairs = [placed([P, 2, RANGE], F32, f"neighbour_short{e}", at_w1_raw + (8 + 2 * e) * KIB) for e in range(2)]
         centre = {
-            "summed": by_tile(centre_pairs[0]) + by_tile(centre_pairs[1]),
-            "near": by_tile(placed([P, 4, HALF], F32, "centre_near", 12 * KIB)),
+            "short": by_tile(centre_pairs[0][:]) + by_tile(centre_pairs[1][:]),
+            "near": by_tile(placed([P, 4, HALF], F32, "centre_near", at_w1_raw + 14 * KIB)[:]),
             "far": by_tile(sb([P, 4, HALF], F32, "centre_far")[:]),
         }
         neighbour = {
-            "summed": by_tile(neighbour_pairs[0]) + by_tile(neighbour_pairs[1]),
-            "near": by_tile(placed([P, 1, HALF], F32, "neighbour_near", 20 * KIB)),
+            "short": by_tile(neighbour_pairs[0][:]) + by_tile(neighbour_pairs[1][:]),
+            "near": [placed([P, HALF], F32, "neighbour_near", at_w1_raw + 12 * KIB)[:]],
         }
-        arms = {key: [sb([P, 4, hi - lo], F32, f"arm{l}_{key}") for l in range(2)] for key, (b, lo, hi) in spans.items()}
+        arms = {key: [sb([P, 4, hi - lo], F32, f"arm{l}_{key}") for l in range(2)] for key, (b, lo, hi) in spans.items() if key != "short"}
+        arms["short"] = [placed([P, 4, RANGE], F32, "arm0_short", at_w1_second), sb([P, 4, RANGE], F32, "arm1_short")]
 
-        def read(dst, l, key, ts, bank=None):
+        def read(dst, l, key, ts, bank):
             b, lo, hi = spans[key]
-            read_scaled(dst[key], fill(scalar_bank() if bank is None else bank, [l], b, ts, lo, hi), b, ts)
+            read_scaled(dst[key], fill(bank, [l], b, ts, lo, hi), b, ts)
 
-        def cast_quarter(n):
-            cast_w4(n // 2, n % 2 * N // 2, (n % 2 + 1) * N // 2)
-
-        def fill_for_vector(l, key, ts):
+        def first_arm(key, ts):
             b, lo, hi = spans[key]
-            return fill(vector_bank(), [l], b, ts, lo, hi)
+            view = fill(vector_bank(), [FIRST], b, ts, lo, hi)
+            for e, t in enumerate(ts):
+                nc.vector.scalar_tensor_tensor(arms[key][0][:, t, :], view[:, e, :], gain(g_col, b, t), centre[key][t], MULT, ADD)
 
-        arms["summed"][0] = placed([P, 4, RANGE], F32, "arm_first", 0)
-
-        def read_pair(e, at):
-            read(centre, 0, "summed", pairs[e], banks[at])
-            read(neighbour, 1, "summed", pairs[e], banks[at + 1])
+        def second_arm(key, ts):
+            b, lo, hi = spans[key]
+            view = fill(vector_bank(), [SECOND], b, ts, lo, hi)
+            for e, t in enumerate(ts):
+                nc.vector.scalar_tensor_tensor(arms[key][1][:, t, :], centre[key][t], gain(g_inv, b, t), view[:, e, :], MULT, ADD)
 
         def sum_pair(e):
-            nc.gpsimd.tensor_tensor(arms["summed"][0][:, 2 * e : 2 * e + 2, :], centre_pairs[e], neighbour_pairs[e], ADD)
+            read(centre, CENTRE, "short", PAIRS[e], banks[2 * e])
+            read(neighbour, FIRST, "short", PAIRS[e], banks[2 * e + 1])
+            nc.gpsimd.tensor_tensor(arms["short"][0][:, 2 * e : 2 * e + 2, :], centre_pairs[e][:], neighbour_pairs[e][:], ADD)
 
-        cast_w1(2, "scalar", (0, 1, 2))
-        quant_w1(1)
+        round_w1(2, "scalar", (0, 1, 2))
+        quantise_w1(1)
         for n, lo in enumerate((HALF, 0)):
-            pick_words(2, lo, lo + HALF, placed([P, HALF], U32, f"v_late{n}", (4 + 2 * n) * KIB))
-        read_pair(0, 0)
+            gather_words(SECOND, lo, v_late[n])
         sum_pair(0)
-        nc.scalar.copy(*dealt(ws_p[1], ws_raw[1], U32, 2, 1))
-        read_pair(1, 2)
+        deal(ws_p[1], ws_raw[1], U32, 2, 1)
         sum_pair(1)
-        read(centre, 0, "near", [0])
-        read(neighbour, 1, "near", [0])
+        read(centre, CENTRE, "near", [0], scalar_bank())
+        read(neighbour, FIRST, "near", [0], scalar_bank())
         nc.gpsimd.tensor_tensor(arms["near"][0][:, 0, :], centre["near"][0], neighbour["near"][0], ADD)
-        read(centre, 0, "near", [1])
+        read(centre, CENTRE, "near", [1], scalar_bank())
 
-        doubled = [(0, 768), (1, 768), (1, 896), (0, 896), (1, 512), (1, 640)]
-        sides = {key: sb([P, 4, RANGE], F32, f"side{key[0]}_{key[1]}") for key in ((1, 512), (0, 768))}
-        sides[1, 768] = placed([P, 4, RANGE], F32, "side_last", held)
+        sides = {(b, 768): placed([P, 4, RANGE], F32, f"side{b}", at_side[b]) for b in range(2)}
+        sides[1, 512] = sb([P, 4, RANGE], F32, "side_late")
 
-        def finish_doubled(b, lo, bank):
-            view = fill(bank, [0, 2], b, range(4), lo, lo + CHUNK)
+        def read_side(b, lo, e):
+            read_scaled(by_tile(sides[b, lo][:]), fill(scalar_bank(), [CENTRE, FIRST], b, PAIRS[e], lo, lo + RANGE), b, PAIRS[e])
+
+        def fill_doubled(b, lo, bank):
+            return b, lo, fill(bank, [CENTRE, SECOND], b, range(4), lo, lo + CHUNK)
+
+        def finish_doubled(b, lo, view):
             side = sides[b, lo - lo % RANGE][:, :, lo % RANGE : lo % RANGE + CHUNK]
-            return lambda: nc.vector.tensor_tensor(h_view(values[b, lo]), woven(view), woven(side), MULT)
+            nc.vector.tensor_tensor(interleaved(values[b, lo]), by_runs(view), by_runs(side), MULT)
 
-        for ts in pairs:
-            second_arm(arms["summed"][1], centre["summed"], fill_for_vector(2, "summed", ts), 0, ts)
-        product(nc.gpsimd, values[0, 512], arms["summed"])
-        order = [("near", t) for t in range(4)] + [("far", t) for t in range(4)]
-        side_steps = [3, 4, 5, 6]
-        for n, (key, t) in enumerate(order):
-            b = spans[key][0]
-            second_arm(arms[key][1], centre[key], fill_for_vector(2, key, [t]), b, [t])
-            if n >= 1:
-                first_arm_plain(arms[key][0], centre[key], fill_for_vector(1, key, [t]), b, [t])
-            if n + 2 < len(order):
-                read(centre, 0, order[n + 2][0], [order[n + 2][1]])
-            if n in side_steps:
-                b, e = divmod(side_steps.index(n), 2)
-                first_arm(sides[b, 768], scalar_bank(), b, pairs[e], 768)
-            if n >= 4:
-                cast_quarter(n - 4)
-            if n == 3:
-                for lo, hi in ((0, 256), (256, 512)):
-                    product(nc.gpsimd, values[0, lo], arms["near"], slice(lo, hi))
-        product(nc.gpsimd, values[1, 0], arms["far"], slice(0, CHUNK))
+        for ts in PAIRS:
+            second_arm("short", ts)
+        multiply(nc.gpsimd, values[0, 512], arms["short"])
+        steps = [("near", t) for t in range(4)] + [("far", t) for t in range(4)]
+        ahead = 2
+        first_side_step = 3
+        for n, (key, t) in enumerate(steps):
+            second_arm(key, [t])
+            if n > 0:
+                first_arm(key, [t])
+            if n + ahead < len(steps):
+                read(centre, CENTRE, steps[n + ahead][0], [steps[n + ahead][1]], scalar_bank())
+            if first_side_step <= n < first_side_step + 4:
+                b, e = divmod(n - first_side_step, 2)
+                read_side(b, 768, e)
+            if key == "far":
+                round_w4(t)
+            if (key, t) == ("near", 3):
+                for lo in (0, RANGE):
+                    multiply(nc.gpsimd, values[0, lo], arms["near"], slice(lo, lo + RANGE))
+        multiply(nc.gpsimd, values[1, 0], arms["far"], slice(0, CHUNK))
         spent = [vector_bank() for n in range(4)]
-        for n in range(4):
-            finish_doubled(*doubled[n], spent[n])()
-        for ts in pairs:
-            first_arm(sides[1, 512], scalar_bank(), 1, ts, 512)
+        for bank, (b, lo) in zip(spent, ((0, 768), (1, 768), (1, 896), (0, 896))):
+            finish_doubled(*fill_doubled(b, lo, bank))
+        for e in range(2):
+            read_side(1, 512, e)
 
-        quant_w4(0)
-        late = [finish_doubled(*doubled[4 + n], spent[2 + n]) for n in range(2)]
-        quant([(0, 768)])
-        quant_w4(1)
-        mix(768, S, ([0, 1], [2]))
-        late[0]()
-        quant([(0, 0)])
-        late[1]()
-        quant([(1, 0)])
-        mix(0, CHUNK, ([0, 1, 2],))
-        quant([(0, 512)])
-        mix(512, 768, ([0, 1], [2]))
-        product(nc.vector, values[1, 128], arms["far"], slice(128, 256))
-        product(nc.vector, values[1, 256], arms["far"], slice(256, 384))
-        quant([(1, 128)])
-        mix(128, 256, ([0, 1, 2],))
-        quant([(0, 256)], slice(0, CHUNK))
-        quant([(1, 256)])
-        mix(256, 384, ([0, 1, 2],))
-        product(nc.vector, values[1, 384], arms["far"], slice(384, 512))
-        quant([(0, 256)], slice(CHUNK, RANGE))
+        quantise_w4(0)
+        late = [fill_doubled(1, lo, bank) for lo, bank in zip((512, 640), spent[2:])]
+        quantise_h(0, 768)
+        quantise_w4(1)
+        mix(768, S)
+        finish_doubled(*late[0])
+        quantise_h(0, 0)
+        finish_doubled(*late[1])
+        quantise_h(1, 0)
+        mix(0, 128)
+        quantise_h(0, 512)
+        mix(512, 768)
+        for lo in (128, 256):
+            multiply(nc.vector, values[1, lo], arms["far"], slice(lo, lo + CHUNK))
+        quantise_h(1, 128)
+        mix(128, 256)
+        quantise_h(0, 256, slice(0, CHUNK))
+        quantise_h(1, 256)
+        mix(256, 384)
+        multiply(nc.vector, values[1, 384], arms["far"], slice(384, HALF))
+        quantise_h(0, 256, slice(CHUNK, RANGE))
         last = [vector_bank()[:, 0:CHUNK] for m in range(3)]
         for m in range(3):
-            mix_pass(last[m], m, 0, 384, HALF, True)
-        quant([(1, 384)])
+            mix_pass(last[m], m, 0, 384, HALF)
+        quantise_h(1, 384)
         for m in range(3):
-            mix_pass(last[m], m, 1, 384, HALF, False)
+            mix_pass(last[m], m, 1, 384, HALF)
             nc.scalar.activation(res[:, m, 384:HALF], last[m], TANH)
             (nc.scalar if m == 2 else nc.sync).dma_start(out_view[:, m, 384:HALF], res[:, m, 384:HALF])

@@ -17,7 +17,6 @@ COPY = mybir.ActivationFunctionType.Copy
 TANH = mybir.ActivationFunctionType.Tanh
 MULT = mybir.AluOpType.mult
 ADD = mybir.AluOpType.add
-SUBTRACT = mybir.AluOpType.subtract
 IS_EQUAL = mybir.AluOpType.is_equal
 NOT_EQUAL = mybir.AluOpType.not_equal
 
@@ -42,14 +41,11 @@ def tile_list_bond_angle_features_kernel(
         psum = ctx.enter_context(tc.psum_pool(name="psum", bufs=1))
         banks = [psum.tile([P, HALF], F32, name=f"bank{k}") for k in range(8)]
         turns = {"scalar": [], "vector": []}
+        rotation = {"scalar": (1, 2, 3, 7), "vector": (4, 5, 6, 0)}
 
-        def scalar_bank():
-            turns["scalar"].append(0)
-            return banks[4 + (len(turns["scalar"]) - 1) % 4]
-
-        def vector_bank():
-            turns["vector"].append(0)
-            return banks[(len(turns["vector"]) - 1) % 4]
+        def bank_for(engine):
+            turns[engine].append(0)
+            return banks[rotation[engine][(len(turns[engine]) - 1) % 4]]
 
         def sb(shape, dtype, name):
             return keep.tile(shape, dtype, align_bytes=64, name=name, tag=name)
@@ -58,8 +54,9 @@ def tile_list_bond_angle_features_kernel(
             return shared.tile(shape, dtype, align_bytes=64, name=name, offset=at)
 
         at_w1_raw = 0
-        at_w1_second = 22 * KIB
-        at_side = {0: 26 * KIB, 1: 30 * KIB}
+        at_w1_second = 19 * KIB
+        at_near_last = 28 * KIB
+        at_side = 30 * KIB
 
         lists = [keep.tile([P, S // 16], U16, name=f"list{l}") for l in range(3)]
         tab_s = sb([P, T // 4], I32, "tab_s")
@@ -111,10 +108,10 @@ def tile_list_bond_angle_features_kernel(
         load_scale_rows(0, w2_scales, (0, 1))
         nc.sync.dma_start(tab_w[:], tab_words[0].rearrange("p t i -> p (t i)").bitcast(I32))
         load_scale_rows(0, w2_scales, (2, 3))
-        load_scale_rows(1, w3_scales, (0,))
+        load_scale_rows(1, w3_scales, (0, 1, 2))
         nc.sync.dma_start(w2_raw[:], w2_words[0].bitcast(I32))
         nc.sync.dma_start(w3_raw[:], w3_words[0].rearrange("p e i -> p (e i)").bitcast(I32))
-        load_w1(1)
+        load_scale_rows(1, w3_scales, (3,))
         for l in range(3):
             nc.vector.tensor_copy(picked[:, l, :], tab_s[:].bitcast(U8).indirect(lists[l][:]))
         for r in range(4):
@@ -122,8 +119,8 @@ def tile_list_bond_angle_features_kernel(
                 planes[r:P:32].rearrange("p l s -> p (l s)"),
                 picked[SCALE_ROWS + r : P : 4].rearrange("p l s -> p (l s)").bitcast(I32),
             )
+        load_w1(1)
         load_w1(2)
-        load_scale_rows(1, w3_scales, (1, 2, 3))
         for b in range(2):
             for t in range(4):
                 nc.sync.dma_start(w4_raw[b][:, t, :], w4_view[b, t])
@@ -140,7 +137,7 @@ def tile_list_bond_angle_features_kernel(
 
         w1_bf = [sb([P, 4, 32, RUN, 4], BF16, "w1_bf0"), placed([P, 4, 32, RUN, 4], BF16, "w1_bf1", at_w1_second)]
         w1_q = [sb([P, HALF], U32, f"w1_q{b}") for b in range(2)]
-        w1_s = [sb([P, HALF], U8, f"w1_s{b}") for b in range(2)]
+        w1_s = [sb([P, HALF], U8, "w1_s0"), placed([P, HALF], U8, "w1_s1", at_near_last)]
 
         def round_w1(k, engine, ts):
             b, lo = divmod(w1_cuts[k], HALF)
@@ -151,7 +148,7 @@ def tile_list_bond_angle_features_kernel(
                 if engine == "scalar":
                     nc.scalar.activation(dst, src[:, t], COPY, scale=-1.0)
                 else:
-                    nc.gpsimd.tensor_tensor(dst, zeros[:].rearrange("p (u j i) -> p u j i", j=4, i=RUN), src[:, t], SUBTRACT)
+                    nc.gpsimd.tensor_scalar(dst, src[:, t], -1.0, 0.0, MULT, ADD)
 
         def quantise_w1(b):
             nc.vector.quantize_mx(
@@ -206,37 +203,38 @@ def tile_list_bond_angle_features_kernel(
         def interleaved(ap):
             return ap.rearrange("p (c i) t -> p c t i", i=RUN)
 
-        at_scales = at_side[1] + 2 * N
+        at_scales = at_side + 2 * N
         groups = [
-            ([(0, 768, 128), (0, 896, 128), (1, 768, 128), (1, 896, 128)], None, at_scales),
-            ([(0, 0, 256)], None, at_scales + 512),
-            ([(1, 0, 128)], None, at_scales + 768),
-            ([(0, 512, 256), (1, 512, 128), (1, 640, 128)], None, None),
-            ([(1, 128, 128)], at_side[0], None),
-            ([(0, 256, 256)], None, at_scales + 896),
-            ([(1, 256, 128)], at_side[0] + KIB, None),
-            ([(1, 384, 128)], at_side[0] + 2 * KIB, None),
+            ([(0, 768, 256), (1, 768, 256)], None, at_scales),
+            ([(1, 0, 128), (0, 0, 256), (1, 128, 128)], at_w1_second + 3 * KIB, at_scales + 512),
+            ([(0, 256, 256)], None, at_scales + 1024),
+            ([(1, 512, 128), (0, 512, 256), (1, 640, 128)], None, at_scales + 1280),
+            ([(1, 256, 256)], at_scales + 1792, None),
         ]
-        values, quantised, group_of = {}, {}, {}
+        h_tiles = {}
         for n, (pieces, values_at, scales_at) in enumerate(groups):
             width = sum(piece[2] for piece in pieces)
             h_bf = sb([P, width, 4], BF16, f"h_bf{n}") if values_at is None else placed([P, width, 4], BF16, f"h_bf{n}", values_at)
             h_s = sb([P, width], U8, f"h_s{n}") if scales_at is None else placed([P, width], U8, f"h_s{n}", scales_at)
             h_q = sb([P, width], U32, f"h_q{n}")
-            group_of[pieces[0][0], pieces[0][1]] = (h_q, h_s, h_bf)
             at = 0
             for b, lo, w in pieces:
-                values[b, lo] = h_bf[:, at : at + w]
                 for c in range(0, w, CHUNK):
-                    quantised[b, lo + c] = (h_q, h_s, at + c)
+                    h_tiles[b, lo + c] = (h_bf, h_q, h_s, at + c)
                 at += w
 
-        def multiply(engine, dst, arm, cols=slice(None)):
-            engine.tensor_tensor(interleaved(dst), by_runs(arm[0][:, :, cols]), by_runs(arm[1][:, :, cols]), MULT)
+        def values(b, lo, hi):
+            h_bf, h_q, h_s, at = h_tiles[b, lo]
+            return h_bf[:, at : at + hi - lo]
 
-        w4_bf = [sb([P, N, 4], BF16, f"w4_bf{b}") for b in range(2)]
+        def multiply(engine, key, lo, hi):
+            b, first, end = spans[key]
+            cols = slice(lo - first, hi - first)
+            engine.tensor_tensor(interleaved(values(b, lo, hi)), by_runs(arms[key][0][:, :, cols]), by_runs(arms[key][1][:, :, cols]), MULT)
+
+        w4_bf = [placed([P, N, 4], BF16, f"w4_bf{b}", at_w1_raw + 12 * b * KIB) for b in range(2)]
         w4_q = sb([P, 2 * N], U32, "w4_q")
-        w4_s = placed([P, 2 * N], U8, "w4_s", at_side[1])
+        w4_s = placed([P, 2 * N], U8, "w4_s", at_side)
 
         def round_w4(quarter):
             b, cols = quarter // 2, slice(quarter % 2 * N // 2, (quarter % 2 + 1) * N // 2)
@@ -246,32 +244,34 @@ def tile_list_bond_angle_features_kernel(
             cols = slice(b * N, (b + 1) * N)
             nc.vector.quantize_mx(w4_q[:, cols].bitcast(FP8X4), w4_s[:, cols], w4_bf[b][:].rearrange("p n t -> p (n t)"))
 
-        def quantise_h(b, lo, cols=slice(None)):
-            h_q, h_s, h_bf = group_of[b, lo]
+        def quantise_h(b, lo, width):
+            h_bf, h_q, h_s, at = h_tiles[b, lo]
+            cols = slice(at, at + width)
             nc.vector.quantize_mx(h_q[:, cols].bitcast(FP8X4), h_s[:, cols], h_bf[:, cols].rearrange("p n t -> p (n t)"))
 
         res = sb([P, 3, S], F32, "res")
         out_view = out.rearrange("(m p) s -> p m s", p=P)
 
-        def mix_pass(dst, m, b, lo, hi):
+        def mix_pass(dst, m, b, lo, hi, first):
             cols = slice(b * N + m * P, b * N + (m + 1) * P)
-            h_q, h_s, at = quantised[b, lo]
+            h_bf, h_q, h_s, at = h_tiles[b, lo]
+            entries = slice(at, at + hi - lo)
             nc.tensor.matmul_mx(
                 dst,
                 lhsT=w4_q[:, cols].bitcast(FP8X4),
                 lhsT_scale=w4_s[:, cols],
-                rhs=h_q[:, at : at + hi - lo].bitcast(FP8X4),
-                rhs_scale=h_s[:, at : at + hi - lo],
-                start=b == 0,
-                stop=b == 1,
+                rhs=h_q[:, entries].bitcast(FP8X4),
+                rhs_scale=h_s[:, entries],
+                start=first,
+                stop=not first,
             )
 
         def mix(lo, hi):
             for ms in ([0, 1, 2],) if hi - lo == CHUNK else ([0, 1], [2]):
-                bank = scalar_bank()[:, 0 : len(ms) * (hi - lo)].rearrange("p (m s) -> p m s", m=len(ms))
+                bank = bank_for("scalar")[:, 0 : len(ms) * (hi - lo)].rearrange("p (m s) -> p m s", m=len(ms))
                 for e, m in enumerate(ms):
                     for b in range(2):
-                        mix_pass(bank[:, e, :], m, b, lo, hi)
+                        mix_pass(bank[:, e, :], m, b, lo, hi, b == 0)
                 nc.scalar.activation(res[:, ms[0] : ms[-1] + 1, lo:hi], bank, TANH)
                 nc.sync.dma_start(out_view[:, ms[0] : ms[-1] + 1, lo:hi], res[:, ms[0] : ms[-1] + 1, lo:hi])
 
@@ -290,127 +290,121 @@ def tile_list_bond_angle_features_kernel(
         deal(ws_p[0], ws_raw[0], U32, 2, 1)
         deal(w2_p, w2_raw, U32, 2, 2)
         deal(w3_p, w3_raw, U32, 2, 4)
-        round_w1(1, "scalar", range(4))
-        round_w1(2, "gpsimd", (3,))
-        for lo in (HALF, 0):
-            for l in (CENTRE, FIRST):
-                gather_words(l, lo, sb([P, HALF], U32, f"v_words{l}_{lo}"))
+        deal(ws_p[1], ws_raw[1], U32, 2, 1)
+        round_w1(1, "gpsimd", range(4))
+        for l, lo in ((CENTRE, 0), (FIRST, 0), (SECOND, 0), (CENTRE, HALF), (FIRST, HALF)):
+            gather_words(l, lo, sb([P, HALF], U32, f"v_words{l}_{lo}"))
 
-        spans = {"short": (0, 512, 768), "near": (0, 0, 512), "far": (1, 0, 512)}
-        v_late = [placed([P, HALF], U32, f"v_late{n}", at_w1_raw + 2 * n * KIB) for n in range(2)]
-        centre_pairs = [placed([P, 2, RANGE], F32, f"centre_short{e}", at_w1_raw + (4 + 2 * e) * KIB) for e in range(2)]
-        neighbour_pairs = [placed([P, 2, RANGE], F32, f"neighbour_short{e}", at_w1_raw + (8 + 2 * e) * KIB) for e in range(2)]
+        spans = {"near": (0, 0, 512), "far": (1, 0, 512), "short": (0, 512, 768)}
         centre = {
-            "short": by_tile(centre_pairs[0][:]) + by_tile(centre_pairs[1][:]),
-            "near": by_tile(placed([P, 4, HALF], F32, "centre_near", at_w1_raw + 14 * KIB)[:]),
-            "far": by_tile(sb([P, 4, HALF], F32, "centre_far")[:]),
+            "near": [sb([P, HALF], F32, f"centre_near{t}")[:] for t in range(3)] + [placed([P, HALF], F32, "centre_near3", at_near_last)[:]],
+            "far": [placed([P, HALF], F32, f"centre_far{t}", at_w1_raw + (12 + 2 * t) * KIB)[:] for t in range(2)]
+            + [sb([P, HALF], F32, f"centre_far{t}")[:] for t in (2, 3)],
+            "short": by_tile(placed([P, 4, RANGE], F32, "centre_short", at_w1_raw)[:]),
         }
         neighbour = {
-            "short": by_tile(neighbour_pairs[0][:]) + by_tile(neighbour_pairs[1][:]),
-            "near": [placed([P, HALF], F32, "neighbour_near", at_w1_raw + 12 * KIB)[:]],
+            "near": [sb([P, HALF], F32, f"neighbour{t}")[:] for t in range(3)]
         }
-        arms = {key: [sb([P, 4, hi - lo], F32, f"arm{l}_{key}") for l in range(2)] for key, (b, lo, hi) in spans.items() if key != "short"}
-        arms["short"] = [placed([P, 4, RANGE], F32, "arm0_short", at_w1_second), sb([P, 4, RANGE], F32, "arm1_short")]
+        arms = {key: [sb([P, 4, HALF], F32, f"arm{l}_{key}") for l in range(2)] for key in ("near", "far")}
+        arms["short"] = [placed([P, 4, RANGE], F32, "arm0_short", at_w1_second - 3 * KIB), sb([P, 4, RANGE], F32, "arm1_short")]
 
         def read(dst, l, key, ts, bank):
             b, lo, hi = spans[key]
             read_scaled(dst[key], fill(bank, [l], b, ts, lo, hi), b, ts)
 
-        def first_arm(key, ts):
+        def first_arm(key, ts, bank):
             b, lo, hi = spans[key]
-            view = fill(vector_bank(), [FIRST], b, ts, lo, hi)
+            view = fill(bank, [FIRST], b, ts, lo, hi)
             for e, t in enumerate(ts):
                 nc.vector.scalar_tensor_tensor(arms[key][0][:, t, :], view[:, e, :], gain(g_col, b, t), centre[key][t], MULT, ADD)
 
-        def second_arm(key, ts):
+        def second_arm(key, ts, bank):
             b, lo, hi = spans[key]
-            view = fill(vector_bank(), [SECOND], b, ts, lo, hi)
+            view = fill(bank, [SECOND], b, ts, lo, hi)
             for e, t in enumerate(ts):
                 nc.vector.scalar_tensor_tensor(arms[key][1][:, t, :], centre[key][t], gain(g_inv, b, t), view[:, e, :], MULT, ADD)
 
-        def sum_pair(e):
-            read(centre, CENTRE, "short", PAIRS[e], banks[2 * e])
-            read(neighbour, FIRST, "short", PAIRS[e], banks[2 * e + 1])
-            nc.gpsimd.tensor_tensor(arms["short"][0][:, 2 * e : 2 * e + 2, :], centre_pairs[e][:], neighbour_pairs[e][:], ADD)
-
-        round_w1(2, "scalar", (0, 1, 2))
-        quantise_w1(1)
-        for n, lo in enumerate((HALF, 0)):
-            gather_words(SECOND, lo, v_late[n])
-        sum_pair(0)
-        deal(ws_p[1], ws_raw[1], U32, 2, 1)
-        sum_pair(1)
-        read(centre, CENTRE, "near", [0], scalar_bank())
-        read(neighbour, FIRST, "near", [0], scalar_bank())
-        nc.gpsimd.tensor_tensor(arms["near"][0][:, 0, :], centre["near"][0], neighbour["near"][0], ADD)
-        read(centre, CENTRE, "near", [1], scalar_bank())
-
-        sides = {(b, 768): placed([P, 4, RANGE], F32, f"side{b}", at_side[b]) for b in range(2)}
-        sides[1, 512] = sb([P, 4, RANGE], F32, "side_late")
+        sides = {
+            (0, 768): placed([P, 4, RANGE], F32, "side_0_768", at_w1_raw + 4 * KIB),
+            (1, 512): placed([P, 4, RANGE], F32, "side_1_512", at_w1_raw + 8 * KIB),
+            (1, 768): placed([P, 4, RANGE], F32, "side_1_768", at_side),
+        }
 
         def read_side(b, lo, e):
-            read_scaled(by_tile(sides[b, lo][:]), fill(scalar_bank(), [CENTRE, FIRST], b, PAIRS[e], lo, lo + RANGE), b, PAIRS[e])
+            read_scaled(by_tile(sides[b, lo][:]), fill(bank_for("scalar"), [CENTRE, FIRST], b, PAIRS[e], lo, lo + RANGE), b, PAIRS[e])
 
-        def fill_doubled(b, lo, bank):
-            return b, lo, fill(bank, [CENTRE, SECOND], b, range(4), lo, lo + CHUNK)
-
-        def finish_doubled(b, lo, view):
+        def doubled(b, lo, bank):
+            view = fill(bank, [CENTRE, SECOND], b, range(4), lo, lo + CHUNK)
             side = sides[b, lo - lo % RANGE][:, :, lo % RANGE : lo % RANGE + CHUNK]
-            nc.vector.tensor_tensor(interleaved(values[b, lo]), by_runs(view), by_runs(side), MULT)
+            nc.vector.tensor_tensor(interleaved(values(b, lo, lo + CHUNK)), by_runs(view), by_runs(side), MULT)
 
+        def near_sum(t, centre_bank, neighbour_bank):
+            read(centre, CENTRE, "near", [t], banks[centre_bank])
+            read(neighbour, FIRST, "near", [t], banks[neighbour_bank])
+            nc.gpsimd.tensor_tensor(arms["near"][0][:, t, :], centre["near"][t], neighbour["near"][t], ADD)
+
+        near_sum(0, 4, 5)
+        near_sum(1, 6, 0)
+        second_arm("near", [0], banks[7])
+        read(centre, CENTRE, "near", [3], banks[3])
+        near_sum(2, 1, 2)
+        for t, k in ((1, 4), (3, 5), (2, 6)):
+            second_arm("near", [t], banks[k])
+        first_arm("near", [3], banks[0])
+        round_w1(2, "scalar", range(4))
         for ts in PAIRS:
-            second_arm("short", ts)
-        multiply(nc.gpsimd, values[0, 512], arms["short"])
-        steps = [("near", t) for t in range(4)] + [("far", t) for t in range(4)]
-        ahead = 2
-        first_side_step = 3
-        for n, (key, t) in enumerate(steps):
-            second_arm(key, [t])
-            if n > 0:
-                first_arm(key, [t])
-            if n + ahead < len(steps):
-                read(centre, CENTRE, steps[n + ahead][0], [steps[n + ahead][1]], scalar_bank())
-            if first_side_step <= n < first_side_step + 4:
-                b, e = divmod(n - first_side_step, 2)
-                read_side(b, 768, e)
-            if key == "far":
-                round_w4(t)
-            if (key, t) == ("near", 3):
-                for lo in (0, RANGE):
-                    multiply(nc.gpsimd, values[0, lo], arms["near"], slice(lo, lo + RANGE))
-        multiply(nc.gpsimd, values[1, 0], arms["far"], slice(0, CHUNK))
-        spent = [vector_bank() for n in range(4)]
-        for bank, (b, lo) in zip(spent, ((0, 768), (1, 768), (1, 896), (0, 896))):
-            finish_doubled(*fill_doubled(b, lo, bank))
-        for e in range(2):
-            read_side(1, 512, e)
+            read(centre, CENTRE, "short", ts, bank_for("scalar"))
+        side_reads = [(b, lo, e) for b, lo in sides for e in range(2)]
+        read_side(*side_reads[0])
+        quantise_w1(1)
+        gather_words(SECOND, HALF, placed([P, HALF], U32, "v_late", at_w1_second + KIB))
+        for lo in (0, RANGE):
+            multiply(nc.gpsimd, "near", lo, lo + RANGE)
 
-        quantise_w4(0)
-        late = [fill_doubled(1, lo, bank) for lo, bank in zip((512, 640), spent[2:])]
-        quantise_h(0, 768)
-        quantise_w4(1)
+        for e, ts in enumerate(PAIRS):
+            first_arm("short", ts, bank_for("vector"))
+            read(centre, CENTRE, "far", [e], bank_for("scalar"))
+        read_side(*side_reads[1])
+        for t in range(4):
+            second_arm("far", [t], bank_for("vector"))
+            first_arm("far", [t], bank_for("vector"))
+            if t == 0:
+                for e, ts in enumerate(PAIRS):
+                    second_arm("short", ts, bank_for("vector"))
+                    read(centre, CENTRE, "far", [2 + e], bank_for("scalar"))
+                multiply(nc.gpsimd, "short", 512, 768)
+            read_side(*side_reads[2 + t])
+            round_w4(t)
+        for lo in (0, CHUNK):
+            multiply(nc.gpsimd, "far", lo, lo + CHUNK)
+        for b, lo in ((0, 768), (1, 512), (0, 896), (1, 768), (1, 896)):
+            spent = bank_for("vector")
+            doubled(b, lo, spent)
+
+        for b in range(2):
+            quantise_w4(b)
+        quantise_h(1, 512, 256)
+        mix(512, 640)
+        quantise_h(0, 768, 512)
         mix(768, S)
-        finish_doubled(*late[0])
-        quantise_h(0, 0)
-        finish_doubled(*late[1])
-        quantise_h(1, 0)
+        quantise_h(1, 0, 256)
         mix(0, 128)
-        quantise_h(0, 512)
-        mix(512, 768)
-        for lo in (128, 256):
-            multiply(nc.vector, values[1, lo], arms["far"], slice(lo, lo + CHUNK))
-        quantise_h(1, 128)
+        doubled(1, 640, spent)
+        quantise_h(0, 128, 256)
         mix(128, 256)
-        quantise_h(0, 256, slice(0, CHUNK))
-        quantise_h(1, 256)
+        quantise_h(0, 640, 256)
+        mix(640, 768)
+        multiply(nc.vector, "far", 256, 384)
+        for b in range(2):
+            quantise_h(b, 256, 128)
         mix(256, 384)
-        multiply(nc.vector, values[1, 384], arms["far"], slice(384, HALF))
-        quantise_h(0, 256, slice(CHUNK, RANGE))
-        last = [vector_bank()[:, 0:CHUNK] for m in range(3)]
+        multiply(nc.vector, "far", 384, HALF)
+        quantise_h(0, 384, 128)
+        last = [bank_for("vector")[:, 0:CHUNK] for m in range(3)]
         for m in range(3):
-            mix_pass(last[m], m, 0, 384, HALF)
-        quantise_h(1, 384)
+            mix_pass(last[m], m, 0, 384, HALF, True)
+        quantise_h(1, 384, 128)
         for m in range(3):
-            mix_pass(last[m], m, 1, 384, HALF)
+            mix_pass(last[m], m, 1, 384, HALF, False)
             nc.scalar.activation(res[:, m, 384:HALF], last[m], TANH)
             (nc.scalar if m == 2 else nc.sync).dma_start(out_view[:, m, 384:HALF], res[:, m, 384:HALF])

@@ -55,8 +55,7 @@ def tile_list_bond_angle_features_kernel(
 
         at_w1_raw = 0
         at_w1_second = 19 * KIB
-        at_near_last = 28 * KIB
-        at_side = 30 * KIB
+        at_side = 24 * KIB
 
         lists = [keep.tile([P, S // 16], U16, name=f"list{l}") for l in range(3)]
         tab_s = sb([P, T // 4], I32, "tab_s")
@@ -110,7 +109,7 @@ def tile_list_bond_angle_features_kernel(
         load_scale_rows(0, w2_scales, (2, 3))
         load_scale_rows(1, w3_scales, (0, 1, 2))
         nc.sync.dma_start(w2_raw[:], w2_words[0].bitcast(I32))
-        nc.sync.dma_start(w3_raw[:], w3_words[0].rearrange("p e i -> p (e i)").bitcast(I32))
+        load_w1(1)
         load_scale_rows(1, w3_scales, (3,))
         for l in range(3):
             nc.vector.tensor_copy(picked[:, l, :], tab_s[:].bitcast(U8).indirect(lists[l][:]))
@@ -119,7 +118,7 @@ def tile_list_bond_angle_features_kernel(
                 planes[r:P:32].rearrange("p l s -> p (l s)"),
                 picked[SCALE_ROWS + r : P : 4].rearrange("p l s -> p (l s)").bitcast(I32),
             )
-        load_w1(1)
+        nc.sync.dma_start(w3_raw[:], w3_words[0].rearrange("p e i -> p (e i)").bitcast(I32))
         load_w1(2)
         for b in range(2):
             for t in range(4):
@@ -137,7 +136,7 @@ def tile_list_bond_angle_features_kernel(
 
         w1_bf = [sb([P, 4, 32, RUN, 4], BF16, "w1_bf0"), placed([P, 4, 32, RUN, 4], BF16, "w1_bf1", at_w1_second)]
         w1_q = [sb([P, HALF], U32, f"w1_q{b}") for b in range(2)]
-        w1_s = [sb([P, HALF], U8, "w1_s0"), placed([P, HALF], U8, "w1_s1", at_near_last)]
+        w1_s = [sb([P, HALF], U8, f"w1_s{b}") for b in range(2)]
 
         def round_w1(k, engine, ts):
             b, lo = divmod(w1_cuts[k], HALF)
@@ -206,7 +205,7 @@ def tile_list_bond_angle_features_kernel(
         at_scales = at_side + 2 * N
         groups = [
             ([(0, 768, 256), (1, 768, 256)], None, at_scales),
-            ([(1, 0, 128), (0, 0, 256), (1, 128, 128)], at_w1_second + 3 * KIB, at_scales + 512),
+            ([(1, 0, 128), (0, 0, 256), (1, 128, 128)], at_w1_second, at_scales + 512),
             ([(0, 256, 256)], None, at_scales + 1024),
             ([(1, 512, 128), (0, 512, 256), (1, 640, 128)], None, at_scales + 1280),
             ([(1, 256, 256)], at_scales + 1792, None),
@@ -232,7 +231,7 @@ def tile_list_bond_angle_features_kernel(
             cols = slice(lo - first, hi - first)
             engine.tensor_tensor(interleaved(values(b, lo, hi)), by_runs(arms[key][0][:, :, cols]), by_runs(arms[key][1][:, :, cols]), MULT)
 
-        w4_bf = [placed([P, N, 4], BF16, f"w4_bf{b}", at_w1_raw + 12 * b * KIB) for b in range(2)]
+        w4_bf = [placed([P, N, 4], BF16, f"w4_bf{b}", at_w1_raw + 14 * b * KIB) for b in range(2)]
         w4_q = sb([P, 2 * N], U32, "w4_q")
         w4_s = placed([P, 2 * N], U8, "w4_s", at_side)
 
@@ -289,16 +288,19 @@ def tile_list_bond_angle_features_kernel(
         nc.vector.reciprocal(g_inv[:], g_safe[:])
         deal(ws_p[0], ws_raw[0], U32, 2, 1)
         deal(w2_p, w2_raw, U32, 2, 2)
-        deal(w3_p, w3_raw, U32, 2, 4)
+        round_w1(1, "scalar", range(4))
         deal(ws_p[1], ws_raw[1], U32, 2, 1)
-        round_w1(1, "gpsimd", range(4))
+        w3_from = w3_raw[:].bitcast(U32).rearrange("p (b u t i) -> p b t u i", b=2, t=4, i=RUN)
+        w3_to = w3_p[:].bitcast(U32).rearrange("p (b t u i) -> p b t u i", b=2, t=4, i=RUN)
+        nc.gpsimd.tensor_copy(w3_to[:, 0], w3_from[:, 0])
+        round_w1(2, "gpsimd", (2, 3))
         for l, lo in ((CENTRE, 0), (FIRST, 0), (SECOND, 0), (CENTRE, HALF), (FIRST, HALF)):
             gather_words(l, lo, sb([P, HALF], U32, f"v_words{l}_{lo}"))
 
         spans = {"near": (0, 0, 512), "far": (1, 0, 512), "short": (0, 512, 768)}
         centre = {
-            "near": [sb([P, HALF], F32, f"centre_near{t}")[:] for t in range(3)] + [placed([P, HALF], F32, "centre_near3", at_near_last)[:]],
-            "far": [placed([P, HALF], F32, f"centre_far{t}", at_w1_raw + (12 + 2 * t) * KIB)[:] for t in range(2)]
+            "near": [sb([P, HALF], F32, f"centre_near{t}")[:] for t in range(4)],
+            "far": [placed([P, HALF], F32, f"centre_far{t}", at_w1_raw + (14 + 2 * t) * KIB)[:] for t in range(2)]
             + [sb([P, HALF], F32, f"centre_far{t}")[:] for t in (2, 3)],
             "short": by_tile(placed([P, 4, RANGE], F32, "centre_short", at_w1_raw)[:]),
         }
@@ -306,7 +308,7 @@ def tile_list_bond_angle_features_kernel(
             "near": [sb([P, HALF], F32, f"neighbour{t}")[:] for t in range(3)]
         }
         arms = {key: [sb([P, 4, HALF], F32, f"arm{l}_{key}") for l in range(2)] for key in ("near", "far")}
-        arms["short"] = [placed([P, 4, RANGE], F32, "arm0_short", at_w1_second - 3 * KIB), sb([P, 4, RANGE], F32, "arm1_short")]
+        arms["short"] = [sb([P, 4, RANGE], F32, f"arm{l}_short") for l in range(2)]
 
         def read(dst, l, key, ts, bank):
             b, lo, hi = spans[key]
@@ -325,9 +327,9 @@ def tile_list_bond_angle_features_kernel(
                 nc.vector.scalar_tensor_tensor(arms[key][1][:, t, :], centre[key][t], gain(g_inv, b, t), view[:, e, :], MULT, ADD)
 
         sides = {
-            (0, 768): placed([P, 4, RANGE], F32, "side_0_768", at_w1_raw + 4 * KIB),
+            (0, 768): placed([P, 4, RANGE], F32, "side_0_768", at_side),
             (1, 512): placed([P, 4, RANGE], F32, "side_1_512", at_w1_raw + 8 * KIB),
-            (1, 768): placed([P, 4, RANGE], F32, "side_1_768", at_side),
+            (1, 768): placed([P, 4, RANGE], F32, "side_1_768", at_w1_raw + 4 * KIB),
         }
 
         def read_side(b, lo, e):
@@ -351,13 +353,14 @@ def tile_list_bond_angle_features_kernel(
         for t, k in ((1, 4), (3, 5), (2, 6)):
             second_arm("near", [t], banks[k])
         first_arm("near", [3], banks[0])
-        round_w1(2, "scalar", range(4))
+        round_w1(2, "scalar", (0, 1))
+        nc.scalar.copy(w3_to[:, 1], w3_from[:, 1])
         for ts in PAIRS:
             read(centre, CENTRE, "short", ts, bank_for("scalar"))
         side_reads = [(b, lo, e) for b, lo in sides for e in range(2)]
         read_side(*side_reads[0])
         quantise_w1(1)
-        gather_words(SECOND, HALF, placed([P, HALF], U32, "v_late", at_w1_second + KIB))
+        gather_words(SECOND, HALF, placed([P, HALF], U32, "v_late", at_w1_raw + 12 * KIB))
         for lo in (0, RANGE):
             multiply(nc.gpsimd, "near", lo, lo + RANGE)
 
@@ -374,12 +377,12 @@ def tile_list_bond_angle_features_kernel(
                     read(centre, CENTRE, "far", [2 + e], bank_for("scalar"))
                 multiply(nc.gpsimd, "short", 512, 768)
             read_side(*side_reads[2 + t])
-            round_w4(t)
+        for quarter in range(4):
+            round_w4(quarter)
         for lo in (0, CHUNK):
             multiply(nc.gpsimd, "far", lo, lo + CHUNK)
-        for b, lo in ((0, 768), (1, 512), (0, 896), (1, 768), (1, 896)):
-            spent = bank_for("vector")
-            doubled(b, lo, spent)
+        for k, (b, lo) in zip((4, 5, 6, 0, 4), ((0, 768), (1, 512), (1, 768), (0, 896), (1, 896))):
+            doubled(b, lo, banks[k])
 
         for b in range(2):
             quantise_w4(b)
@@ -389,18 +392,18 @@ def tile_list_bond_angle_features_kernel(
         mix(768, S)
         quantise_h(1, 0, 256)
         mix(0, 128)
-        doubled(1, 640, spent)
-        quantise_h(0, 128, 256)
-        mix(128, 256)
+        doubled(1, 640, banks[0])
+        multiply(nc.vector, "far", 256, 384)
         quantise_h(0, 640, 256)
         mix(640, 768)
-        multiply(nc.vector, "far", 256, 384)
         for b in range(2):
             quantise_h(b, 256, 128)
         mix(256, 384)
+        quantise_h(0, 128, 256)
+        mix(128, 256)
         multiply(nc.vector, "far", 384, HALF)
         quantise_h(0, 384, 128)
-        last = [bank_for("vector")[:, 0:CHUNK] for m in range(3)]
+        last = [banks[k][:, 0:CHUNK] for k in (5, 6, 4)]
         for m in range(3):
             mix_pass(last[m], m, 0, 384, HALF, True)
         quantise_h(1, 384, 128)

@@ -56,6 +56,7 @@ def tile_list_bond_angle_features_kernel(
         at_w1_raw = 0
         at_w1_second = 19 * KIB
         at_side = 24 * KIB
+        at_far = 30 * KIB
 
         lists = [keep.tile([P, S // 16], U16, name=f"list{l}") for l in range(3)]
         tab_s = sb([P, T // 4], I32, "tab_s")
@@ -108,8 +109,8 @@ def tile_list_bond_angle_features_kernel(
         nc.sync.dma_start(tab_w[:], tab_words[0].rearrange("p t i -> p (t i)").bitcast(I32))
         load_scale_rows(0, w2_scales, (2, 3))
         load_scale_rows(1, w3_scales, (0, 1, 2))
-        nc.sync.dma_start(w2_raw[:], w2_words[0].bitcast(I32))
         load_w1(1)
+        nc.sync.dma_start(w2_raw[:], w2_words[0].bitcast(I32))
         load_scale_rows(1, w3_scales, (3,))
         for l in range(3):
             nc.vector.tensor_copy(picked[:, l, :], tab_s[:].bitcast(U8).indirect(lists[l][:]))
@@ -126,10 +127,10 @@ def tile_list_bond_angle_features_kernel(
 
         ws_p = [sb([P, H // 4], I32, f"ws_p{k}") for k in range(2)]
         w2_p = sb([P, H // 2], I32, "w2_p")
-        w3_p = sb([P, H], I32, "w3_p")
+        w3_p = [sb([P, HALF], I32, "w3_p0"), placed([P, HALF], I32, "w3_p1", at_w1_raw + 14 * KIB)]
 
-        def deal(dst, src, dtype, b, e):
-            nc.scalar.copy(
+        def deal(dst, src, dtype, b, e, copy=nc.scalar.copy):
+            copy(
                 dst[:].bitcast(dtype).rearrange("p (b t u e) -> p b t u e", b=b, t=4, e=e),
                 src[:].bitcast(dtype).rearrange("p (b u t e) -> p b t u e", b=b, t=4, e=e),
             )
@@ -167,7 +168,7 @@ def tile_list_bond_angle_features_kernel(
             scale = ws_p[l - 1][:, c * 32 : (c + 1) * 32].bitcast(U8)
             if l == FIRST:
                 return w2_p[:, c * 64 : (c + 1) * 64].bitcast(U8).bitcast(FP4X4), scale
-            return w3_p[:, c * P : (c + 1) * P].bitcast(FP8X4), scale
+            return w3_p[b][:, t * P : (t + 1) * P].bitcast(FP8X4), scale
 
         def fill(bank, ls, b, ts, lo, hi):
             view = bank[:].rearrange("p (e n) -> p e n", e=len(ts))
@@ -231,7 +232,7 @@ def tile_list_bond_angle_features_kernel(
             cols = slice(lo - first, hi - first)
             engine.tensor_tensor(interleaved(values(b, lo, hi)), by_runs(arms[key][0][:, :, cols]), by_runs(arms[key][1][:, :, cols]), MULT)
 
-        w4_bf = [placed([P, N, 4], BF16, f"w4_bf{b}", at_w1_raw + 14 * b * KIB) for b in range(2)]
+        w4_bf = [placed([P, N, 4], BF16, f"w4_bf{b}", (at_w1_raw, at_far)[b]) for b in range(2)]
         w4_q = sb([P, 2 * N], U32, "w4_q")
         w4_s = placed([P, 2 * N], U8, "w4_s", at_side)
 
@@ -287,20 +288,20 @@ def tile_list_bond_angle_features_kernel(
         nc.gpsimd.tensor_tensor(g_safe[:], g_zero[:], g_col[:], ADD)
         nc.vector.reciprocal(g_inv[:], g_safe[:])
         deal(ws_p[0], ws_raw[0], U32, 2, 1)
-        deal(w2_p, w2_raw, U32, 2, 2)
         round_w1(1, "scalar", range(4))
-        deal(ws_p[1], ws_raw[1], U32, 2, 1)
+        deal(w2_p, w2_raw, U32, 2, 2)
+        deal(ws_p[1], ws_raw[1], U32, 2, 1, nc.gpsimd.tensor_copy)
         w3_from = w3_raw[:].bitcast(U32).rearrange("p (b u t i) -> p b t u i", b=2, t=4, i=RUN)
-        w3_to = w3_p[:].bitcast(U32).rearrange("p (b t u i) -> p b t u i", b=2, t=4, i=RUN)
-        nc.gpsimd.tensor_copy(w3_to[:, 0], w3_from[:, 0])
-        round_w1(2, "gpsimd", (2, 3))
+        w3_to = [tile[:].bitcast(U32).rearrange("p (t u i) -> p t u i", t=4, i=RUN) for tile in w3_p]
+        nc.gpsimd.tensor_copy(w3_to[0], w3_from[:, 0])
+        round_w1(2, "gpsimd", (3,))
         for l, lo in ((CENTRE, 0), (FIRST, 0), (SECOND, 0), (CENTRE, HALF), (FIRST, HALF)):
             gather_words(l, lo, sb([P, HALF], U32, f"v_words{l}_{lo}"))
 
         spans = {"near": (0, 0, 512), "far": (1, 0, 512), "short": (0, 512, 768)}
         centre = {
             "near": [sb([P, HALF], F32, f"centre_near{t}")[:] for t in range(4)],
-            "far": [placed([P, HALF], F32, f"centre_far{t}", at_w1_raw + (14 + 2 * t) * KIB)[:] for t in range(2)]
+            "far": [placed([P, HALF], F32, f"centre_far{t}", at_far + 2 * t * KIB)[:] for t in range(2)]
             + [sb([P, HALF], F32, f"centre_far{t}")[:] for t in (2, 3)],
             "short": by_tile(placed([P, 4, RANGE], F32, "centre_short", at_w1_raw)[:]),
         }
@@ -353,10 +354,10 @@ def tile_list_bond_angle_features_kernel(
         for t, k in ((1, 4), (3, 5), (2, 6)):
             second_arm("near", [t], banks[k])
         first_arm("near", [3], banks[0])
-        round_w1(2, "scalar", (0, 1))
-        nc.scalar.copy(w3_to[:, 1], w3_from[:, 1])
+        round_w1(2, "scalar", (0, 1, 2))
         for ts in PAIRS:
             read(centre, CENTRE, "short", ts, bank_for("scalar"))
+        nc.scalar.copy(w3_to[1], w3_from[:, 1])
         side_reads = [(b, lo, e) for b, lo in sides for e in range(2)]
         read_side(*side_reads[0])
         quantise_w1(1)

@@ -355,11 +355,11 @@ def tile_list_bond_angle_features_kernel(
             second_arm("near", [t], banks[k])
         first_arm("near", [3], banks[0])
         round_w1(2, "scalar", (0, 1, 2))
-        for ts in PAIRS:
-            read(centre, CENTRE, "short", ts, bank_for("scalar"))
         nc.scalar.copy(w3_to[1], w3_from[:, 1])
         side_reads = [(b, lo, e) for b, lo in sides for e in range(2)]
         read_side(*side_reads[0])
+        for ts in PAIRS:
+            read(centre, CENTRE, "short", ts, bank_for("scalar"))
         quantise_w1(1)
         gather_words(SECOND, HALF, placed([P, HALF], U32, "v_late", at_w1_raw + 12 * KIB))
         for lo in (0, RANGE):

from contextlib import ExitStack

import concourse.mybir as mybir

K, T, S, H, N = 512, 4096, 1024, 1024, 384
FLOPS = 3 * 2 * K * H * S + 2 * H * N * S

F32 = mybir.dt.float32
BF16 = mybir.dt.bfloat16
I32 = mybir.dt.int32
U32 = mybir.dt.uint32
U16 = mybir.dt.uint16
U8 = mybir.dt.uint8
FP8X4 = mybir.dt.float8_e4m3fn_x4
FP4X4 = mybir.dt.float4_e2m1fn_x4
COPY = mybir.ActivationFunctionType.Copy
TANH = mybir.ActivationFunctionType.Tanh
MULT = mybir.AluOpType.mult
ADD = mybir.AluOpType.add
IS_EQUAL = mybir.AluOpType.is_equal
NOT_EQUAL = mybir.AluOpType.not_equal

P = 128
CHUNK = 128
RANGE = 256
HALF = 512
RUN = 4
SCALE_ROWS = P - 16
KIB = 1024
CENTRE, FIRST, SECOND = 0, 1, 2
PAIRS = ([0, 1], [2, 3])


def tile_list_bond_angle_features_kernel(
    tc, tab_words, tab_scales, offs, offs2, offs3, w1, w2_words, w2_scales, w3_words, w3_scales, g, w4, out
):
    nc = tc.nc
    with ExitStack() as ctx:
        keep = ctx.enter_context(tc.tile_pool(name="keep", bufs=1))
        shared = ctx.enter_context(tc.tile_pool(name="shared", bufs=1))
        psum = ctx.enter_context(tc.psum_pool(name="psum", bufs=1))
        banks = [psum.tile([P, HALF], F32, name=f"bank{k}") for k in range(8)]
        turns = {"scalar": [], "vector": []}
        rotation = {"scalar": (1, 2, 3, 7), "vector": (4, 5, 6, 0)}

        def bank_for(engine):
            turns[engine].append(0)
            return banks[rotation[engine][(len(turns[engine]) - 1) % 4]]

        def sb(shape, dtype, name):
            return keep.tile(shape, dtype, align_bytes=64, name=name, tag=name)

        def placed(shape, dtype, name, at):
            return shared.tile(shape, dtype, align_bytes=64, name=name, offset=at)

        at_w1_raw = 0
        at_w1_second = 19 * KIB
        at_side = 24 * KIB
        at_far = 30 * KIB

        lists = [keep.tile([P, S // 16], U16, name=f"list{l}") for l in range(3)]
        tab_s = sb([P, T // 4], I32, "tab_s")
        tab_w = sb([P, T], I32, "tab_w")
        ws_raw = [sb([P, H // 4], I32, f"ws_raw{k}") for k in range(2)]
        w1_cuts = (0, 512, 768, 1024)
        w1_tile = placed([P, 4 * H], F32, "w1_raw", at_w1_raw)
        w1_raw = [w1_tile[:, 4 * w1_cuts[k] : 4 * w1_cuts[k + 1]].rearrange("p (j c) -> p j c", j=4) for k in range(3)]
        w2_raw = sb([P, H // 2], I32, "w2_raw")
        w3_raw = sb([P, H], I32, "w3_raw")
        w4_raw = [sb([P, 4, N], F32, f"w4_raw{b}") for b in range(2)]
        g_rows = sb([P, HALF], F32, "g_rows")
        g_dealt = sb([P, HALF], F32, "g_dealt")
        ident = sb([P, P], F32, "ident")
        g_col = sb([P, 8], F32, "g_col")
        g_zero = sb([P, 8], F32, "g_zero")
        g_safe = sb([P, 8], F32, "g_safe")
        g_inv = sb([P, 8], F32, "g_inv")
        zeros = sb([P, RANGE], F32, "zeros")
        planes = sb([P, 3, S // 4], I32, "planes")
        picked = sb([P, 3, S], U8, "picked")

        for k in range(2):
            nc.gpsimd.memset(ws_raw[k][:], 0)
        nc.vector.memset(zeros[:], 0.0)
        nc.vector.memset(tab_s[0:SCALE_ROWS, :], 0)
        nc.vector.memset(planes[:], 0)
        for lo in (0, RANGE):
            nc.scalar.activation(g_rows[0 : P - 2, lo : lo + RANGE], zeros[0 : P - 2, :], TANH)
        nc.gpsimd.affine_select(
            out=ident[:], in_=zeros[:, 0:P], compare_op=NOT_EQUAL, fill=1.0, base=0, pattern=[[-1, P]], channel_multiplier=1
        )

        w1_rows = w1.rearrange("(p j) c -> p j c", j=4)
        w4_view = w4.rearrange("(b u t i) n -> b t u i n", b=2, t=4, i=RUN)

        def load_w1(k):
            nc.sync.dma_start(w1_raw[k], w1_rows[:, :, w1_cuts[k] : w1_cuts[k + 1]])

        def load_scale_rows(k, src, rows):
            for r in rows:
                nc.sync.dma_start(ws_raw[k][r:P:32, :], src[0, r:16:4, :].bitcast(I32))

        nc.sync.dma_start(tab_s[SCALE_ROWS:P, :], tab_scales[0].bitcast(I32))
        for l, src in enumerate((offs, offs2, offs3)):
            nc.sync.dma_start(lists[l][:], src)
        load_w1(0)
        nc.sync.dma_start(g_rows[P - 2 : P, :], g.rearrange("(b c) -> b c", b=2))
        load_scale_rows(0, w2_scales, (0, 1))
        nc.sync.dma_start(tab_w[:], tab_words[0].rearrange("p t i -> p (t i)").bitcast(I32))
        load_scale_rows(0, w2_scales, (2, 3))
        load_scale_rows(1, w3_scales, (0, 1, 2))
        load_w1(1)
        nc.sync.dma_start(w2_raw[:], w2_words[0].bitcast(I32))
        load_scale_rows(1, w3_scales, (3,))
        for l in range(3):
            nc.vector.tensor_copy(picked[:, l, :], tab_s[:].bitcast(U8).indirect(lists[l][:]))
        for r in range(4):
            nc.sync.dma_start(
                planes[r:P:32].rearrange("p l s -> p (l s)"),
                picked[SCALE_ROWS + r : P : 4].rearrange("p l s -> p (l s)").bitcast(I32),
            )
        nc.sync.dma_start(w3_raw[:], w3_words[0].rearrange("p e i -> p (e i)").bitcast(I32))
        load_w1(2)
        for b in range(2):
            for t in range(4):
                nc.sync.dma_start(w4_raw[b][:, t, :], w4_view[b, t])

        ws_p = [sb([P, H // 4], I32, f"ws_p{k}") for k in range(2)]
        w2_p = sb([P, H // 2], I32, "w2_p")
        w3_p = [sb([P, HALF], I32, "w3_p0"), placed([P, HALF], I32, "w3_p1", at_w1_raw + 14 * KIB)]

        def deal(dst, src, dtype, b, e, copy=nc.scalar.copy):
            copy(
                dst[:].bitcast(dtype).rearrange("p (b t u e) -> p b t u e", b=b, t=4, e=e),
                src[:].bitcast(dtype).rearrange("p (b u t e) -> p b t u e", b=b, t=4, e=e),
            )

        w1_bf = [sb([P, 4, 32, RUN, 4], BF16, "w1_bf0"), placed([P, 4, 32, RUN, 4], BF16, "w1_bf1", at_w1_second)]
        w1_q = [sb([P, HALF], U32, f"w1_q{b}") for b in range(2)]
        w1_s = [sb([P, HALF], U8, f"w1_s{b}") for b in range(2)]

        def round_w1(k, engine, ts):
            b, lo = divmod(w1_cuts[k], HALF)
            us = slice(lo // 16, (lo + w1_cuts[k + 1] - w1_cuts[k]) // 16)
            src = w1_raw[k].rearrange("p j (u t i) -> p t u j i", t=4, i=RUN)
            for t in ts:
                dst = w1_bf[b][:, t, us].rearrange("p u i j -> p u j i")
                if engine == "scalar":
                    nc.scalar.activation(dst, src[:, t], COPY, scale=-1.0)
                else:
                    nc.gpsimd.tensor_scalar(dst, src[:, t], -1.0, 0.0, MULT, ADD)

        def quantise_w1(b):
            nc.vector.quantize_mx(
                w1_q[b][:].bitcast(FP8X4), w1_s[b][:], w1_bf[b][:].rearrange("p t u i j -> p (t u i j)")
            )

        v_words = {}

        def gather_words(l, lo, tile):
            v_words[l, lo] = tile
            nc.vector.tensor_copy(tile[:], tab_w[:].bitcast(U32).indirect(lists[l][:, lo // 16 : (lo + HALF) // 16]))

        def weight(l, b, t):
            c = 4 * b + t
            if l == CENTRE:
                return w1_q[b][:, t * P : (t + 1) * P].bitcast(FP8X4), w1_s[b][:, t * P : (t + 1) * P]
            scale = ws_p[l - 1][:, c * 32 : (c + 1) * 32].bitcast(U8)
            if l == FIRST:
                return w2_p[:, c * 64 : (c + 1) * 64].bitcast(U8).bitcast(FP4X4), scale
            return w3_p[b][:, t * P : (t + 1) * P].bitcast(FP8X4), scale

        def fill(bank, ls, b, ts, lo, hi):
            view = bank[:].rearrange("p (e n) -> p e n", e=len(ts))
            passes = [(e, t, l) for l in ls for e, t in enumerate(ts)]
            at = lo - lo % HALF
            for n, (e, t, l) in enumerate(passes):
                codes, scale = weight(l, b, t)
                nc.tensor.matmul_mx(
                    view[:, e, :],
                    lhsT=codes,
                    lhsT_scale=scale,
                    rhs=v_words[l, at][:, lo - at : hi - at].bitcast(FP8X4),
                    rhs_scale=planes[:, l, :].bitcast(U8)[:, lo:hi],
                    start=n == 0,
                    stop=n == len(passes) - 1,
                )
            return view

        def gain(col, b, t):
            return col[:, 4 * b + t : 4 * b + t + 1]

        def by_tile(tile):
            return [tile[:, t, :] for t in range(tile.shape[1])]

        def read_scaled(dst, view, b, ts):
            for e, t in enumerate(ts):
                nc.scalar.activation(dst[t], view[:, e, :], COPY, scale=gain(g_col, b, t))

        def by_runs(ap):
            return ap.rearrange("p t (c i) -> p c t i", i=RUN)

        def interleaved(ap):
            return ap.rearrange("p (c i) t -> p c t i", i=RUN)

        at_scales = at_side + 2 * N
        groups = [
            ([(0, 768, 256), (1, 768, 256)], None, at_scales),
            ([(1, 0, 128), (0, 0, 256), (1, 128, 128)], at_w1_second, at_scales + 512),
            ([(0, 256, 256)], None, at_scales + 1024),
            ([(1, 512, 128), (0, 512, 256), (1, 640, 128)], None, at_scales + 1280),
            ([(1, 256, 256)], at_scales + 1792, None),
        ]
        h_tiles = {}
        for n, (pieces, values_at, scales_at) in enumerate(groups):
            width = sum(piece[2] for piece in pieces)
            h_bf = sb([P, width, 4], BF16, f"h_bf{n}") if values_at is None else placed([P, width, 4], BF16, f"h_bf{n}", values_at)
            h_s = sb([P, width], U8, f"h_s{n}") if scales_at is None else placed([P, width], U8, f"h_s{n}", scales_at)
            h_q = sb([P, width], U32, f"h_q{n}")
            at = 0
            for b, lo, w in pieces:
                for c in range(0, w, CHUNK):
                    h_tiles[b, lo + c] = (h_bf, h_q, h_s, at + c)
                at += w

        def values(b, lo, hi):
            h_bf, h_q, h_s, at = h_tiles[b, lo]
            return h_bf[:, at : at + hi - lo]

        def multiply(engine, key, lo, hi):
            b, first, end = spans[key]
            cols = slice(lo - first, hi - first)
            engine.tensor_tensor(interleaved(values(b, lo, hi)), by_runs(arms[key][0][:, :, cols]), by_runs(arms[key][1][:, :, cols]), MULT)

        w4_bf = [placed([P, N, 4], BF16, f"w4_bf{b}", (at_w1_raw, at_far)[b]) for b in range(2)]
        w4_q = sb([P, 2 * N], U32, "w4_q")
        w4_s = placed([P, 2 * N], U8, "w4_s", at_side)

        def round_w4(quarter):
            b, cols = quarter // 2, slice(quarter % 2 * N // 2, (quarter % 2 + 1) * N // 2)
            nc.scalar.activation(interleaved(w4_bf[b][:, cols]), by_runs(w4_raw[b][:, :, cols]), COPY)

        def quantise_w4(b):
            cols = slice(b * N, (b + 1) * N)
            nc.vector.quantize_mx(w4_q[:, cols].bitcast(FP8X4), w4_s[:, cols], w4_bf[b][:].rearrange("p n t -> p (n t)"))

        def quantise_h(b, lo, width):
            h_bf, h_q, h_s, at = h_tiles[b, lo]
            cols = slice(at, at + width)
            nc.vector.quantize_mx(h_q[:, cols].bitcast(FP8X4), h_s[:, cols], h_bf[:, cols].rearrange("p n t -> p (n t)"))

        res = sb([P, 3, S], F32, "res")
        out_view = out.rearrange("(m p) s -> p m s", p=P)

        def mix_pass(dst, m, b, lo, hi, first):
            cols = slice(b * N + m * P, b * N + (m + 1) * P)
            h_bf, h_q, h_s, at = h_tiles[b, lo]
            entries = slice(at, at + hi - lo)
            nc.tensor.matmul_mx(
                dst,
                lhsT=w4_q[:, cols].bitcast(FP8X4),
                lhsT_scale=w4_s[:, cols],
                rhs=h_q[:, entries].bitcast(FP8X4),
                rhs_scale=h_s[:, entries],
                start=first,
                stop=not first,
            )

        def mix(lo, hi):
            for ms in ([0, 1, 2],) if hi - lo == CHUNK else ([0, 1], [2]):
                bank = bank_for("scalar")[:, 0 : len(ms) * (hi - lo)].rearrange("p (m s) -> p m s", m=len(ms))
                for e, m in enumerate(ms):
                    for b in range(2):
                        mix_pass(bank[:, e, :], m, b, lo, hi, b == 0)
                nc.scalar.activation(res[:, ms[0] : ms[-1] + 1, lo:hi], bank, TANH)
                nc.sync.dma_start(out_view[:, ms[0] : ms[-1] + 1, lo:hi], res[:, ms[0] : ms[-1] + 1, lo:hi])

        round_w1(0, "scalar", range(4))
        quantise_w1(0)
        deal(g_dealt, g_rows, F32, 1, RUN)
        g_bank = banks[7]
        for t in range(4):
            nc.tensor.transpose(g_bank[:, t * P : (t + 1) * P], g_dealt[:, t * P : (t + 1) * P], ident[:])
        nc.scalar.copy(
            g_col[:].rearrange("p (b t) -> p t b", b=2), g_bank[:].rearrange("p (t r) -> p t r", t=4)[:, :, P - 2 : P]
        )
        nc.gpsimd.tensor_scalar(g_zero[:], g_col[:], 0.0, 0.0, IS_EQUAL, ADD)
        nc.gpsimd.tensor_tensor(g_safe[:], g_zero[:], g_col[:], ADD)
        nc.vector.reciprocal(g_inv[:], g_safe[:])
        deal(ws_p[0], ws_raw[0], U32, 2, 1)
        round_w1(1, "scalar", range(4))
        deal(w2_p, w2_raw, U32, 2, 2)
        deal(ws_p[1], ws_raw[1], U32, 2, 1, nc.gpsimd.tensor_copy)
        w3_from = w3_raw[:].bitcast(U32).rearrange("p (b u t i) -> p b t u i", b=2, t=4, i=RUN)
        w3_to = [tile[:].bitcast(U32).rearrange("p (t u i) -> p t u i", t=4, i=RUN) for tile in w3_p]
        nc.gpsimd.tensor_copy(w3_to[0], w3_from[:, 0])
        round_w1(2, "gpsimd", (3,))
        for l, lo in ((CENTRE, 0), (FIRST, 0), (SECOND, 0), (CENTRE, HALF), (FIRST, HALF)):
            gather_words(l, lo, sb([P, HALF], U32, f"v_words{l}_{lo}"))

        spans = {"near": (0, 0, 512), "far": (1, 0, 512), "short": (0, 512, 768)}
        centre = {
            "near": [sb([P, HALF], F32, f"centre_near{t}")[:] for t in range(4)],
            "far": [placed([P, HALF], F32, f"centre_far{t}", at_far + 2 * t * KIB)[:] for t in range(2)]
            + [sb([P, HALF], F32, f"centre_far{t}")[:] for t in (2, 3)],
            "short": by_tile(placed([P, 4, RANGE], F32, "centre_short", at_w1_raw)[:]),
        }
        neighbour = {
            "near": [sb([P, HALF], F32, f"neighbour{t}")[:] for t in range(3)]
        }
        arms = {key: [sb([P, 4, HALF], F32, f"arm{l}_{key}") for l in range(2)] for key in ("near", "far")}
        arms["short"] = [sb([P, 4, RANGE], F32, f"arm{l}_short") for l in range(2)]

        def read(dst, l, key, ts, bank):
            b, lo, hi = spans[key]
            read_scaled(dst[key], fill(bank, [l], b, ts, lo, hi), b, ts)

        def first_arm(key, ts, bank):
            b, lo, hi = spans[key]
            view = fill(bank, [FIRST], b, ts, lo, hi)
            for e, t in enumerate(ts):
                nc.vector.scalar_tensor_tensor(arms[key][0][:, t, :], view[:, e, :], gain(g_col, b, t), centre[key][t], MULT, ADD)

        def second_arm(key, ts, bank):
            b, lo, hi = spans[key]
            view = fill(bank, [SECOND], b, ts, lo, hi)
            for e, t in enumerate(ts):
                nc.vector.scalar_tensor_tensor(arms[key][1][:, t, :], centre[key][t], gain(g_inv, b, t), view[:, e, :], MULT, ADD)

        sides = {
            (0, 768): placed([P, 4, RANGE], F32, "side_0_768", at_side),
            (1, 512): placed([P, 4, RANGE], F32, "side_1_512", at_w1_raw + 8 * KIB),
            (1, 768): placed([P, 4, RANGE], F32, "side_1_768", at_w1_raw + 4 * KIB),
        }

        def read_side(b, lo, e):
            read_scaled(by_tile(sides[b, lo][:]), fill(bank_for("scalar"), [CENTRE, FIRST], b, PAIRS[e], lo, lo + RANGE), b, PAIRS[e])

        def doubled(b, lo, bank):
            view = fill(bank, [CENTRE, SECOND], b, range(4), lo, lo + CHUNK)
            side = sides[b, lo - lo % RANGE][:, :, lo % RANGE : lo % RANGE + CHUNK]
            nc.vector.tensor_tensor(interleaved(values(b, lo, lo + CHUNK)), by_runs(view), by_runs(side), MULT)

        def near_sum(t, centre_bank, neighbour_bank):
            read(centre, CENTRE, "near", [t], banks[centre_bank])
            read(neighbour, FIRST, "near", [t], banks[neighbour_bank])
            nc.gpsimd.tensor_tensor(arms["near"][0][:, t, :], centre["near"][t], neighbour["near"][t], ADD)

        near_sum(0, 4, 5)
        near_sum(1, 6, 0)
        second_arm("near", [0], banks[7])
        read(centre, CENTRE, "near", [3], banks[3])
        near_sum(2, 1, 2)
        for t, k in ((1, 4), (3, 5), (2, 6)):
            second_arm("near", [t], banks[k])
        first_arm("near", [3], banks[0])
        round_w1(2, "scalar", (0, 1, 2))
        nc.scalar.copy(w3_to[1], w3_from[:, 1])
        side_reads = [(b, lo, e) for b, lo in sides for e in range(2)]
        read_side(*side_reads[0])
        for ts in PAIRS:
            read(centre, CENTRE, "short", ts, bank_for("scalar"))
        quantise_w1(1)
        gather_words(SECOND, HALF, placed([P, HALF], U32, "v_late", at_w1_raw + 12 * KIB))
        for lo in (0, RANGE):
            multiply(nc.gpsimd, "near", lo, lo + RANGE)

        for e, ts in enumerate(PAIRS):
            first_arm("short", ts, bank_for("vector"))
            read(centre, CENTRE, "far", [e], bank_for("scalar"))
        read_side(*side_reads[1])
        for t in range(4):
            second_arm("far", [t], bank_for("vector"))
            first_arm("far", [t], bank_for("vector"))
            if t == 0:
                for e, ts in enumerate(PAIRS):
                    second_arm("short", ts, bank_for("vector"))
                    read(centre, CENTRE, "far", [2 + e], bank_for("scalar"))
                multiply(nc.gpsimd, "short", 512, 768)
            read_side(*side_reads[2 + t])
        for quarter in range(4):
            round_w4(quarter)
        for lo in (0, CHUNK):
            multiply(nc.gpsimd, "far", lo, lo + CHUNK)
        for k, (b, lo) in zip((4, 5, 6, 0, 4), ((0, 768), (1, 512), (1, 768), (0, 896), (1, 896))):
            doubled(b, lo, banks[k])

        for b in range(2):
            quantise_w4(b)
        quantise_h(1, 512, 256)
        mix(512, 640)
        quantise_h(0, 768, 512)
        mix(768, S)
        quantise_h(1, 0, 256)
        mix(0, 128)
        doubled(1, 640, banks[0])
        multiply(nc.vector, "far", 256, 384)
        quantise_h(0, 640, 256)
        mix(640, 768)
        for b in range(2):
            quantise_h(b, 256, 128)
        mix(256, 384)
        quantise_h(0, 128, 256)
        mix(128, 256)
        multiply(nc.vector, "far", 384, HALF)
        quantise_h(0, 384, 128)
        last = [banks[k][:, 0:CHUNK] for k in (5, 6, 4)]
        for m in range(3):
            mix_pass(last[m], m, 0, 384, HALF, True)
        quantise_h(1, 384, 128)
        for m in range(3):
            mix_pass(last[m], m, 1, 384, HALF, False)
            nc.scalar.activation(res[:, m, 384:HALF], last[m], TANH)
            (nc.scalar if m == 2 else nc.sync).dma_start(out_view[:, m, 384:HALF], res[:, m, 384:HALF])
